import numpy as np, ml_dtypes
CORES = [48,51,52,55]
N = 4
BF = ml_dtypes.bfloat16
def gentries(a):
    return np.ascontiguousarray(a.reshape(8, 16, -1).transpose(0, 2, 1)).reshape(8, -1)
def gtable(e):
    e = np.asarray(e); return np.ascontiguousarray(e.reshape(8, -1, 16).transpose(0, 2, 1)).reshape(128, -1).astype(np.int32)
V, M, KK, RO, S, TH = 2048, 256, 512, 4, 1, 12
W = V + M * RO
def parts(rng):
    c = rng.integers(-60, 61, (N, 8, 8, V)); s = rng.integers(5, 36, (N, 8, 8, V))
    x = np.stack([c + s, s - c], axis=3).reshape(N, 8, 16, V)
    nb = rng.integers(0, V, (N, 8, 16, V))
    sh = (N, 8, 8, KK // 2); cut = rng.random(sh) < 0.25; h = rng.integers(-60, 61, sh); big = rng.integers(60, 128, (4,) + sh)
    k0 = np.stack([np.where(cut, h, big[0]), big[1]], axis=3).reshape(N, 8, 16, KK // 2)
    k1 = np.stack([big[2], np.where(cut, -h, big[3])], axis=3).reshape(N, 8, 16, KK // 2)
    k = np.stack([k0, k1], axis=-1).reshape(N, 8, 16, KK)
    z = rng.integers(-127, 128, (N, 8, 16, M)); p = rng.integers(0, V, (N, 8, M))
    p = np.where(rng.random(p.shape) < 0.15, p[..., ::-1], p)
    return x, nb, k, z, p, rng.integers(-127, 128, (N, 8, 16))
def distinct(rng):
    return np.argsort(rng.random((8, V)), axis=1)[:, :M]
def pack(x, nb, k, z, p, w):
    b = lambda a: np.ascontiguousarray(a.reshape(N, 128, -1)).astype(np.float32).astype(BF)
    return {"xc": b(x), "nb": np.ascontiguousarray(nb.reshape(N, 128, V)).astype(np.int32), "kc": b(k), "zi": b(z),
            "ps": np.stack([gtable(a) for a in p]), "wt": np.ascontiguousarray(w.reshape(N, 128, 1)).astype(np.int32)}
def setup_inputs(rng):
    return pack(*parts(rng))
def setup_inputs_spread(rng):
    x, nb, k, z, p, w = parts(rng)
    x = 127 - np.floor(255 * rng.random(x.shape) * rng.random((N, 8, 1, V)) ** rng.integers(0, 3, (N, 8, 1, V))).astype(np.int64)
    k = 127 - np.floor(255 * rng.random(k.shape) * rng.random((N, 8, 1, KK)) ** rng.integers(1, 4, (N, 8, 1, KK))).astype(np.int64)
    z = np.rint(z * rng.random((N, 8, 1, M)) ** 2).astype(np.int64); w = np.rint(w * rng.random((N, 8, 16)) ** 2).astype(np.int64)
    p[:, ::2] = np.floor(V * rng.random((N, 4, M)) ** 3).astype(np.int64)
    return pack(x, nb, k, z, np.minimum(p, V - 1), w)
def setup_inputs_ends(rng):
    x, nb, k, z, p, w = parts(rng)
    sg = lambda sh: np.where(rng.random(sh) < 0.5, 127, -127)
    def recs(n, a, b):
        h = rng.random((N, 8, 1, n)); return np.where(h < a, 127, np.where(h < b, -127, sg((N, 8, 16, n))))
    x = recs(V, 0.35, 0.5); k = recs(KK, 0.5, 0.6); w = sg((N, 8, 16)); z = sg((N, 8, 16, M))
    x[..., V - 1] = 127; x[..., V - 2] = 127; x[:, ::2, :, 0] = 127; x[:, 1::2, :, 0] = -127
    for i in (1, M - 1): z[..., i] = w
    for i in (0, M - 2): z[..., i] = -w
    for u in ((16 * 127 * 127) & (KK - 1), (-16 * 127 * 127) & (KK - 1)): k[..., u] = 127; k[..., u ^ 1] = -127
    e = np.where(rng.random(nb.shape) < 0.5, 0, V - 1); nb = np.where(rng.random((N, 8, 1, V)) < 0.72, e, nb)
    nb[..., 0] = np.where(np.arange(16) % 3 == 0, 0, V - 1); nb[..., V - 1] = np.where(np.arange(16) % 4 == 3, V - 1, 0); nb[..., V - 2] = np.where(np.arange(16) % 2 == 0, 0, V - 1)
    p = np.where(rng.random(p.shape) < 0.93, np.where(rng.random(p.shape) < 0.5, 0, V - 1), p); p[..., M - 1] = V - 2
    d = np.argsort(rng.random((8, V - 2)), axis=1)[:, :M] + 1; d[::2, 0] = V - 1; d[::2, M - 1] = 0; d[1::2, 0] = 0; d[1::2, M - 1] = V - 1
    p[N - 1] = d
    return pack(x, nb, k, z, p, w)
def setup_inputs_corners(rng):
    x, nb, k, z, p, w = parts(rng); v = np.arange(V); i = np.arange(M)
    for r in range(N):
        for g in range(8):
            m = (g + r) % 8; o = (3 * g + r) % 8
            if m == 0: nb[r, g] = v
            elif m == 1: nb[r, g] = (v + 1) & (V - 1)
            elif m == 2: nb[r, g] = 0
            elif m == 3: nb[r, g] = V - 1
            elif m == 4: nb[r, g, ::2] = v; nb[r, g, 1::4] = 0; nb[r, g, 3::4] = V - 1
            elif m == 5: nb[r, g] = (v - 1) & (V - 1)
            elif m == 6: nb[r, g] = int(rng.integers(0, V))
            if o < 7: p[r, g] = ((V - 1 + i // 2) & (V - 1), 0 * i + V - 1, 0 * i, i, V - M + i, i // 16, V - 1 - i)[o]
    h = rng.random((N, 8, 1, V)); x = np.where(h < 0.05, -127, np.where(h < 0.1, 127, np.where(h < 0.15, 0, x)))
    h = rng.random((N, 8, 1, KK)); k = np.where(h < 0.1, -127, np.where(h < 0.3, 127, k))
    z[:, 0] = 0; z[:, 3] = 0; z[:, 5] = np.where(rng.random((N, 16, M)) < 0.5, 127, -127); w[:, 2] = 0; w[:, 6] = 127
    return pack(x, nb, k, z, p, w)
def setup_inputs_crowd(rng):
    x, nb, k, z, p, w = parts(rng)
    for r in range(N):
        d = distinct(rng)
        for g in range(8):
            one = (0, V - 1, int(rng.integers(0, V)))[int(rng.integers(0, 3))]
            m = 0 if r == 0 else 3 if r in (1, 3) else (g + r) % 4
            if m == 3: p[r, g] = d[g]
            elif m == 2: p[r, g] = rng.choice(np.array([one, (one + 1) & (V - 1), (one + 7) & (V - 1)]), M)
            else:
                p[r, g] = one
                if m == 1: p[r, g, (0, M - 1)[int(rng.integers(0, 2))]] = (one + 1) & (V - 1)
    p[3, 0, M - 1] = p[3, 0, 0]
    few = rng.integers(0, V, (N, 4)); few[:, 0] = 0; few[:, 1] = V - 1
    for r in range(N):
        for g in (1, 5): nb[r, g] = few[r][rng.integers(0, 4, (16, V))]
    x[:, 6] = np.where(rng.random((N, 16, V)) < 0.02, -127, 127); k[:, 6] = np.where(rng.random((N, 16, KK)) < 0.02, -127, 127)
    return pack(x, nb, k, z, p, w)
def setup_inputs_ties(rng):
    x, nb, k, z, p, w = parts(rng)
    h = rng.random(x.shape); x = np.where(h < 0.2, -1, np.where(h < 0.5, 0, 1))
    h = rng.random(k.shape); k = np.where(h < 0.1, -1, np.where(h < 0.25, 0, np.where(h < 0.4, 1, 127)))
    nb[:, ::2, 8:] = nb[:, ::2, :8]
    return pack(x, nb, k, rng.integers(-3, 4, z.shape), p, rng.integers(-2, 3, w.shape))
def check_inputs(d):
    bad = []
    for key, lo, hi in (("xc", -127, 127), ("nb", 0, V - 1), ("kc", -127, 127), ("zi", -127, 127), ("ps", 0, V - 1), ("wt", -127, 127)):
        a = np.asarray(d[key]).astype(np.float64)
        if not (np.min(a) >= lo and np.max(a) <= hi): bad.append("range of " + key)
        elif np.any(a != np.floor(a)): bad.append("whole numbers in " + key)
    return bad
def relist(child, xa, xb, a, b, other):
    c = child[:, np.arange(16) ^ 1][:, :, None, :]
    oa = np.add.reduce(xa + c >= 0, axis=1, dtype=np.int32); ob = np.add.reduce(xb + c >= 0, axis=1, dtype=np.int32)
    s = np.maximum(oa, ob)
    return np.where(s < TH, other[:, None, :], np.where(ob > oa, b, a)), s
def reference(xc, nb, kc, zi, ps, wt):
    whole = lambda a: a.astype(np.float32).astype(np.int32).reshape(N, 8, 16, -1)
    X = np.zeros((N, 8, 16, W), np.int32); X[..., :V] = whole(xc)
    L = np.zeros((N, 8, 16, W), np.int64); L[..., :V] = nb.reshape(N, 8, 16, V)
    sib = np.tile(np.arange(W), (N, 8, 1)); K = whole(kc); w = wt.astype(np.int64).reshape(N, 8, 16, 1)
    z = whole(zi); p = np.stack([gentries(a) for a in ps]).astype(np.int64); A = np.zeros(N, np.int64)
    before = np.arange(M)[:, None] > np.arange(M)[None, :]
    for t in range(RO):
        n = V + M * t + np.arange(M)
        for r in range(N):
            q = (r + S * t) % N; pp = p[r]; zz = z[r]
            act = ~np.any((pp[:, :, None] == pp[:, None, :]) & before, axis=2)
            u = (np.add.reduce(w[q] * zz, axis=1) + A[q]) & (KK - 1)
            xp = np.take_along_axis(X[q], pp[:, None, :], 2)
            C = np.minimum(xp, np.take_along_axis(K[q], u[:, None, :], 2)); E = np.minimum(xp, np.take_along_axis(K[q], (u ^ 1)[:, None, :], 2))
            a = np.take_along_axis(L[q], pp[:, None, :], 2)
            for g in range(8):
                m = act[g]; X[q, g][:, pp[g, m]] = C[g][:, m]; X[q, g][:, n[m]] = E[g][:, m]; sib[q, g][pp[g, m]] = n[m]
            b = np.take_along_axis(sib[q], a.reshape(8, 16 * M), 1).reshape(8, 16, M)
            xa = np.take_along_axis(X[q], a.reshape(8, 1, 16 * M), 2).reshape(8, 16, 16, M)
            xb = np.take_along_axis(X[q], b.reshape(8, 1, 16 * M), 2).reshape(8, 16, 16, M)
            lc, sc = relist(C, xa, xb, a, b, np.tile(n, (8, 1))); le, se = relist(E, xa, xb, a, b, pp)
            for g in range(8):
                m = act[g]; L[q, g][:, pp[g, m]] = lc[g][:, m]; L[q, g][:, n[m]] = le[g][:, m]
            A[q] = np.sum(act)
            top = np.argmax(sc, axis=1)
            p[r] = np.where(act, np.take_along_axis(lc, top[:, None, :], 1)[:, 0], (pp + 1) & (V - 1))
            z[r] = np.where(act[:, None, :], (zz + C) >> 1, zz)
    return {"yx": X.reshape(N, 128, W).astype(np.float32).astype(BF), "yn": L.reshape(N, 128, W).astype(np.float32)}

@@ -1,0 +1,736 @@
+from concourse.mybir import AluOpType, AxisListType, ActivationFunctionType
+
+A = AluOpType
+F = ActivationFunctionType
+V, M, KK, RO, TH = 2048, 256, 512, 4, 12
+W_ = V + M * RO
+NOSIB = W_
+DUM = W_ + 16
+WC = DUM + M
+SC_ = 1 << 19
+K0 = (TH - 1) * SC_ + (1 << 18)
+OV = (1 << 23) + (1 << 19)
+BIG = 3 * (1 << 22)
+RND = 1.5 * 2.0 ** 23
+RND13 = 1.5 * 2.0 ** 36
+
+P = {'dq': [[56, 0, 0, 0], [56, 16, 0, 0], [56, 16, 0, 0], [56, 16, 0, 0]], 'rsg': 3, 'rsv': 9, 'ynlat': 2000.0, 'bias': {'xpv': -4000, 'ra': 4000, 'KOCg': -3000, 'BBCv': -3000, 'KOEa': 4000, 'mv': -4000, 'xpa': 4000, 'zoutv': -1000, 'Cv': -500, 'puv': -1000, 'Xt': 3000, 'Ka': -500, 'rhoa': 4000, 'TEt': -3000, 'SBCa': -2000, 'srowg': 3000, 'pig': 3000}, 'fb': 3, 'blook': 0.0, 'tse': [1, 1, 1, 0], 'xact': [1, 1, 1, 1], 'cact': [0, 0, 0, 0], 'pefix': 0.0, 'g': 1.56, 'fac': 1.25, 'pe': 0.42, 'rem': 2600.0, 'look': 600.0, 'xo_act': 0, 'tt2': 1.0, 'half': 0.5, 'sig': 1, 'zact': 1, 'ract': [1, 1, 1, 0], 'r0C': [[3, 2], [3, 3], [3, 3], [3, 3]], 'r0E': [[0, 0], [0, 0], [0, 0], [0, 0]], 'bkC': ('TC0', 'X1'), 'bkE': ('TC0', 'X1')}
+
+f32, bf, f16, i32, u16 = "float32", "bfloat16", "float16", "int32", "uint16"
+
+
+def _sb(cols, d):
+    return ("sbuf", [128] + (cols if isinstance(cols, list) else [cols]), d)
+
+
+SCRATCH = {
+    "W": _sb(WC, f32), "L": _sb(WC, f32), "NB": _sb(V, i32), "XC": _sb(V, bf), "XO": _sb(W_, bf),
+    "K1": _sb(KK, bf), "K2": _sb(KK, bf), "wi": _sb(4, i32), "wf": _sb(4, f32),
+    "pin": _sb(16 * RO, i32), "pout": _sb(16 * RO, i32), "zin": _sb(M * RO, bf), "zout": _sb(M * RO, bf),
+    "GA": _sb(16 * M, f32), "GB": _sb(16 * M, bf),
+    "BAC": _sb(16 * M, bf), "BAE": _sb(16 * M, bf), "BBC": _sb(16 * M, bf), "BBE": _sb(16 * M, bf),
+    "SBC": _sb(16 * M, bf), "SBE": _sb(16 * M, bf), "EQ": _sb(16 * M, bf),
+    "Im": _sb(512, bf), "l4": _sb(4, i32), "l4f": _sb(16, f32), "Ih": _sb(128, bf), "If": _sb(128, f32), "n128": _sb(128, bf), "p1k": _sb(128, bf),
+    "zr1": _sb(M, f32), "zr2": _sb(M, f32), "r13a": _sb(M, f32), "KU": _sb(2 * M, bf), "sT": _sb(2 * M, bf), "grp": _sb(8, bf), "I19": _sb(128, bf), "I18": _sb(128, bf), "rho": _sb(2 * M, bf),
+    "ones": _sb(128, bf), "I": _sb(128, bf), "nI": _sb(128, bf), "nIh": _sb(128, bf), "nIq": _sb(128, bf), "nIm": _sb(128, bf),
+    "bigI": _sb(128, bf), "nP": _sb(128, bf), "blk0": _sb(128, bf), "blk": _sb(128, bf), "Bo": _sb(128, bf), "Bw": _sb(128, bf),
+    "S19": _sb(144, bf), "S18": _sb(144, bf), "SW": _sb(144, bf), "SA": _sb(144, bf), "RS": _sb(2048, bf),
+    "sel": _sb(8, f32), "zb": _sb(128, bf), "SWP": _sb(512, f32), "zf": _sb(128, f32), "o16": _sb(128, f32),
+    "sm": _sb(M, bf), "crow": _sb(512, bf), "c22": _sb(M, bf), "thr": _sb(M, bf), "KOC": _sb(M * RO, f32), "fr": _sb(M * RO, f32),
+    "pi": _sb(4, i32), "pa": _sb(4, i32), "lane": _sb(4, f32), "kcol": _sb(4, f32), "srow": _sb(16, f32), "lm": _sb(16, f32),
+    "hf": _sb(16, f32), "zr": _sb(16, f32), "pat": _sb(16, f32), "pm": _sb(16, f32), "pw": _sb(4, f32), "dm0": _sb(16, f32), "dum": _sb(16, f32),
+    "pf16": _sb(32, f16), "pf32": _sb(32, f32), "pu": _sb(32, u16), "prow": _sb(M, u16), "KOE": _sb(2 * M, f32),
+    "act": _sb(2 * M, bf), "junk": _sb(M, bf), "cnt": _sb(8, f32), "of1": _sb(16, f32), "off": _sb(32, u16),
+    "p1a": _sb(16, i32), "p1b": _sb(16, i32), "ovr": _sb(32, f32), "xp": _sb(M, bf), "C": _sb(M, f32), "Cb": _sb(2 * M, bf), "E": _sb(2 * M, bf),
+    "au": _sb(M, u16), "af": _sb(M, f16), "bu": _sb(M, u16), "rT": _sb(M, i32), "fT": _sb(M, f16),
+    "dm": _sb(M, bf), "u1": _sb(16, i32), "u2": _sb(16, i32), "uu": _sb(32, u16),
+    "m1": _sb(M, f32), "m2": _sb(M, f32), "r13": _sb(M, f32), "TT": _sb(M, f32), "SC": _sb(M, f32), "mx": _sb(16, i32),
+    "e1": _sb(M, f32), "e2": _sb(M, i32), "e3": _sb(M, i32), "xt": _sb(1024, f32),
+}
+BANKS = ["TC0", "TC1", "TE0", "TE1", "KC", "KE", "X0", "X1"]
+for _b in BANKS:
+    SCRATCH[_b] = ("psum", [128, 512], f32)
+NDMA = 16
+SEMAPHORES = ["ev", "ea", "et", "eg", "sent"] + ["d%d" % i for i in range(NDMA)] + ["pa%d" % t for t in range(1, RO)] + ["za%d" % t for t in range(1, RO)]
+
+
+def build_ops(g, core, T, topo):
+    rank = T.rank_of(core)
+    nxt = T.cores[(rank + 1) % len(T.cores)]
+    rid, pid, _ = topo.addr(nxt)
+    mask = topo.mask(core, nxt)
+    neng = len(topo.engines(core, nxt))
+    ops = []
+    fac, gc = P["fac"], P["g"]
+    ndma = [0]
+
+    def add(eng, fn, r, w, cost, **kw):
+        ops.append(dict(eng=eng, fn=fn, r=list(r), w=list(w), cost=cost, **kw))
+
+    def vc(n, rate=1.0):
+        return (50 + max(64, n * rate) * 0.83) * fac
+
+    def copy(o, i, r, w, n, rate=1.0):
+        add("v", lambda: g.vector.tensor_copy(o, i), r, w, vc(n, rate))
+
+    def ts(o, i, s1, s2, op0, op1, r, w, n, rate=1.0):
+        if op1 is None:
+            add("v", lambda: g.vector.tensor_scalar(o, i, s1, None, op0), r, w, vc(n, rate))
+        else:
+            add("v", lambda: g.vector.tensor_scalar(o, i, s1, s2, op0, op1), r, w, vc(n, rate))
+
+    def tt(o, a, b, op, r, w, n, rate=1.0):
+        add("v", lambda: g.vector.tensor_tensor(o, a, b, op), r, w, vc(n, rate))
+
+    def mset(o, c, w, n):
+        add("v", lambda: g.vector.memset(o, c), [], w, vc(n, 0.5))
+
+    def act_(o, i, fn, r, w, n, bias=0.0, scale=1.0, rate=1.0, acc=None):
+        if acc is None:
+            add("a", lambda: g.scalar.activation(o, i, fn, bias=bias, scale=scale), r, w, vc(n, rate) + 20)
+        else:
+            add("a", lambda: g.scalar.activation(o, i, fn, bias=bias, scale=scale, accum_out=acc), r, w, vc(n, rate) + 40)
+
+    def mm(o, l, rh, st, sp, r, w, n, wide=False):
+        me = {"start": st, "stop": sp}
+        add("t", lambda: g.tensor.matmul(o, l, rh, st, me["stop"]), r, w, (max(64, n) * (4 if wide else 1) * P["pe"] + P["pefix"]) * fac, flags=me)
+
+    def gp(fn, r, w, n):
+        add("g", fn, r, w, (150 + 2 * n * 0.83) * fac)
+
+    def dma(q, o, i, r, w, nbytes):
+        s = T.sem["d%d" % ndma[0]]
+        ndma[0] += 1
+        e = g.sync if q == "s" else g.scalar
+        add(q, lambda: e.dma_start(o, i), r, w, 60.0, sem=s, inc=16, lat=1800 + nbytes / 250.0, bw=nbytes / 250.0)
+
+    def send(o, i, sem, r, w, slack=0.0):
+        add("g", lambda: g.remote_dma(o, i, sem, T.sem.sent, pid, rid, mask), r, w, 300.0, sem=sem, inc=neng, lat=P["rem"] + slack, remote=True)
+
+    dma("s", T.pin[:, 0:16], T.ps[:], [], ["pin0"], 8192)
+    dma("s", T.XC[:, 0:1024], T.xc[:, 0:1024], [], ["XC0"], 262144)
+    dma("s", T.XC[:, 1024:V], T.xc[:, 1024:V], [], ["XC1"], 262144)
+    dma("s", T.wi[:, 0:1], T.wt[:], [], ["wi"], 512)
+    dma("s", T.zin[:, 0:M], T.zi[:], [], ["zin0"], 65536)
+    dma("s", T.K1[:], T.kc[:], [], ["K1"], 131072)
+    dma("s", T.NB[:], T.nb[:], [], ["NB"], 1048576)
+
+    def spot(o, name, pattern, base, fill, n, zero="zb"):
+        gp(lambda: g.affine_select(o, T[zero][:, 0:n], pattern, A.not_equal, float(fill), base, 1), [zero], [name], n)
+
+    mset(T.ones[:], 1.0, ["ones"], 128)
+    mset(T.zb[:], 0.0, ["zb"], 128)
+    mset(T.zf[:], 0.0, ["zf"], 256)
+    gp(lambda: g.iota(T.pi[:, 0:1], [[0, 1]], 0, 1), [], ["pi"], 1)
+    gp(lambda: g.affine_select(T.blk0[:], T.ones[:], [[-16, 8], [0, 16]], A.is_ge, 0.0, 0, 1), ["ones"], ["blk0"], 128)
+    gp(lambda: g.affine_select(T.blk[:], T.blk0[:], [[16, 8], [0, 16]], A.is_ge, 0.0, 15, -1), ["blk0"], ["blk"], 128)
+    gp(lambda: g.iota(T.srow[:], [[1, 16]], 0, 0, allow_small_or_imprecise_dtypes=True), [], ["srow"], 16)
+    gp(lambda: g.affine_select(T.I[:], T.ones[:], [[-1, 128]], A.is_equal, 0.0, 0, 1), ["ones"], ["I"], 128)
+    gp(lambda: g.iota(T.dm0[:], [[16, 16]], DUM - 1024, 0, allow_small_or_imprecise_dtypes=True), [], ["dm0"], 16)
+    for t in range(RO):
+        gp(lambda t=t: g.iota(T.KOC[:, M * t:M * t + M], [[1, M]], K0 + V + M * t, 0, allow_small_or_imprecise_dtypes=True), [], ["KOC%d" % t], M)
+        if t == 0:
+            gp(lambda: g.iota(T.W[:, V + M:DUM], [[0, DUM - V - M]], -1000, 0, allow_small_or_imprecise_dtypes=True), [], ["Wt"], DUM - V - M)
+        act_(T.fr[:, M * t:M * t + M], T.KOC[:, M * t:M * t + M], F.Identity, ["KOC%d" % t], ["fr%d" % t], M, bias=(K0 + W_) / 4096.0, scale=-1.0 / 4096)
+    ts(T.pa[:, 0:1], T.pi[:, 0:1], 15, None, A.bitwise_and, None, ["pi"], ["pa"], 1)
+    copy(T.lane[:, 0:1], T.pa[:, 0:1], ["pa"], ["lane"], 1)
+    ts(T.lm[:], T.srow[:], T.lane[:, 0:1], None, A.is_equal, None, ["srow", "lane"], ["lm"], 16)
+    for s in range(16):
+        if s < P["rsg"]:
+            spot(T.RS[:, 128 * s:128 * s + 128], "RS%d" % s, [[-16, 8], [0, 16]], -s, 1.0, 128)
+        elif s < P["rsg"] + P["rsv"]:
+            ts(T.RS[:, 128 * s:128 * s + 128], T.blk[:], T.lm[:, s:s + 1], None, A.mult, None, ["blk", "lm"], ["RS%d" % s], 128, 0.5)
+        else:
+            act_(T.RS[:, 128 * s:128 * s + 128], T.blk[:], F.Identity, ["blk", "lm"], ["RS%d" % s], 128, scale=T.lm[:, s:s + 1])
+    mset(T.hf[:], 0.5, ["hf"], 16)
+    mset(T.zr[:], 0.0, ["zr"], 16)
+    add("v", lambda: g.vector.tensor_tensor_scan(T.pat[:], T.hf[:], T.zr[:], 65536.0, A.mult, A.add), ["hf", "zr"], ["pat"], vc(16))
+    tt(T.pm[:], T.pat[:], T.lm[:], A.mult, ["pat", "lm"], ["pm"], 16)
+    add("v", lambda: g.vector.tensor_reduce(T.pw[:, 0:1], T.pm[:], AxisListType.X, A.add), ["pm"], ["pw"], vc(16))
+    ts(T.Bw[:], T.blk[:], T.pw[:, 0:1], None, A.mult, None, ["blk", "pw"], ["Bw"], 128, 0.5)
+    act_(T.Bo[:], T.blk[:], F.Identity, ["blk"], ["Bo"], 128, scale=2.0 ** 17)
+    act_(T.thr[:, 0:16], T.pat[:], F.Identity, ["pat"], ["thr"], 16, scale=2.0)
+    for n in (16, 32, 64, 128):
+        act_(T.thr[:, n:2 * n], T.thr[:, 0:n], F.Identity, ["thr"], ["thr"], n)
+    ts(T.dum[:], T.dm0[:], T.lane[:, 0:1], None, A.add, None, ["dm0", "lane"], ["dum"], 16)
+    copy(T.wf[:, 0:1], T.wi[:, 0:1], ["wi"], ["wf"], 1)
+    for name, sc in (("SW", T.wf[:, 0:1]), ("SA", -BIG / 16.0), ("S19", float(SC_)), ("S18", SC_ / 2.0)):
+        mset(T[name][:], 0.0, [name], 144)
+        act_(T[name][:, 16:144:16], T.blk[:, 0:128:16], F.Identity, ["blk", "wf"], [name], 8, scale=sc)
+    for name, sc in (("nI", -1.0), ("bigI", float(BIG)), ("nIm", -4096.0), ("nIh", -0.5)) + ((("Ih", 0.5), ("n128", -128.0), ("p1k", 1024.0)) if P["zact"] else (("nIq", -0.25),)):
+        spot(T[name][:], name, [[-1, 128]], 0, sc, 128)
+    if P["zact"]:
+        spot(T.If[:], "If", [[-1, 128]], 0, 1.0, 128, "zf")
+    spot(T.nP[:], "nP", [[-2, 64], [1, 2]], -1, -1.0, 128)
+    act_(T.K2[:, 0:KK:2], T.K1[:, 1:KK:2], F.Identity, ["K1"], ["K2"], 256)
+    act_(T.K2[:, 1:KK:2], T.K1[:, 0:KK:2], F.Identity, ["K1"], ["K2"], 256)
+    for h in range(2):
+        act_(T.W[:, 1024 * h:1024 * h + 1024], T.XC[:, 1024 * h:1024 * h + 1024], F.Identity, ["XC%d" % h], ["Wi%d" % h], 1024)
+    spot(T.sel[:], "sel", [[-16, 8]], 0, 1.0, 8, "zf")
+    if max(P["tse"]):
+        act_(T.grp[:], T.blk[:, 0:128:16], F.Identity, ["blk"], ["grp"], 8)
+        spot(T.I19[:], "I19", [[-1, 128]], 0, SC_, 128)
+        spot(T.I18[:], "I18", [[-1, 128]], 0, SC_ // 2, 128)
+    for xh in range(2):
+        for gl in range(2):
+            q = 2 * xh + gl
+            spot(T.SWP[:, 128 * q:128 * q + 128], "SWP%d" % q, [[-32, 4], [1000, 2], [-1, 16]], -16 * xh - 1000 * gl, 1.0, 128, "zf")
+    for r0 in sorted(set(x for y in P["r0C"] for x in y if 0 < x < 4)):
+        for b in range(4):
+            spot(T.Im[:, 128 * r0 + b:128 * r0 + 128:4], "Im%d%d" % (r0, b), [[-4, 32]], -b, 1.0 if b >= r0 else 0.0, 32)
+    mset(T.o16[:], 1.0 / 16, ["o16"], 256)
+    mset(T.sm[:], 1.0, ["sm"], M)
+    ts(T.sm[:, 0:M:16], T.sm[:, 1:M:16], 0.0, None, A.mult, None, ["sm"], ["sm"], 16)
+    ts(T.kcol[:, 0:1], T.lane[:, 0:1], -16384.0, 15 * 16384.0, A.mult, A.add, ["lane"], ["kcol"], 1)
+    mset(T.c22[:], 2.0 ** 22, ["c22"], M)
+    ts(T.crow[:, 0:M], T.c22[:], 9216.0 / 2 ** 22, T.kcol[:, 0:1], A.mult, A.add, ["c22", "kcol"], ["crow0"], M, 0.5)
+    ts(T.crow[:, M:2 * M], T.c22[:], 3072.0 / 2 ** 22, T.kcol[:, 0:1], A.mult, A.add, ["c22", "kcol"], ["crow1"], M, 0.5)
+
+    def sel(name, s):
+        return T[name][:, 16 - s:144 - s]
+
+    def upath(t):
+        pr = t % 2
+        if t:
+            mm(T.X0[:, 32:33], T.o16[:], T.cnt[:, 0:1], True, True, ["o16", "cnt"], ["X0"], 1, True)
+        b = "X0" if t else "X1"
+        for s in range(16):
+            mm(T[b][:, 0:16], sel("SW", s), T.zin[:, M * t + s:M * t + M:16], s == 0, s == 15, ["SW", "zin%d" % t], [b], 16)
+        if t:
+            ts(T.u1[:], T.X0[:, 0:16], T.X0[:, 32:33], float(1 << 18), A.add, A.add, ["X0"], ["u1"], 16)
+        else:
+            ts(T.u1[:], T.X1[:, 0:16], float(1 << 18), None, A.add, None, ["X1"], ["u1"], 16)
+        ts(T.u2[:], T.u1[:], KK - 1, None, A.bitwise_and, None, ["u1"], ["u2"], 16)
+        copy(T.uu[:, 16 * pr:16 * pr + 16], T.u2[:], ["u2"], ["uu%d" % pr], 16)
+
+    def prep(t):
+        pr = t % 2
+        l = slice(16 * pr, 16 * pr + 16)
+        c = slice(M * pr, M * pr + M)
+        pin = T.pin[:, 16 * t:16 * t + 16]
+        pn = "pin%d" % t
+        wr = ["W", "Wn"] + (["Wi0", "Wi1"] if t == 0 else [])
+        lb = "X0"
+        ts(T.pf16[:, l], pin, -1024.0, None, A.add, None, [pn], ["pf16%d" % pr], 16)
+        copy(T.pf32[:, l], pin, [pn], ["pf32%d" % pr], 16)
+        copy(T.pu[:, l], pin, [pn], ["pu%d" % pr], 16)
+        for s in range(16):
+            mm(T.X0[:, s:M:16], T.RS[:, 128 * s:128 * s + 128], T.pf16[:, l], True, True, ["RS%d" % s, "pf16%d" % pr], ["X0"], 16)
+        ts(T.prow[:], T.X0[:, 0:M], 1024.0, None, A.add, None, ["X0"], ["prow"], M)
+        act_(T.KOE[:, c], T.X0[:, 0:M], F.Identity, ["X0"], ["KOE%d" % pr], M, bias=float(K0 + 1024))
+        mm(T.KC[:, 0:M], T.nI[:], T.thr[:], True, False, ["nI", "thr"], ["KC"], M)
+        for cc in range(16):
+            n = M - 16 * cc
+            e0 = M * cc
+            ts(T.EQ[:, e0:e0 + n], T.prow[:, 16 * cc:M], T.pf32[:, 16 * pr + cc:16 * pr + cc + 1], None, A.is_equal, None, ["prow", "pf32%d" % pr], ["EQ%d" % cc], n, P["half"])
+            if cc < 15:
+                mm(T.KC[:, 16 * cc + 16:M], T.Bo[:], T.EQ[:, e0 + 16:e0 + n], False, False, ["Bo", "EQ%d" % cc], ["KC"], n - 16)
+            mm(T.KC[:, 16 * cc:16 * cc + 16], T.Bw[:], T.EQ[:, e0:e0 + 16], False, cc == 15, ["Bw", "EQ%d" % cc], ["KC"], 16)
+        ac = "act%d" % pr
+        if P["sig"]:
+            act_(T.act[:, c], T.KC[:, 0:M], F.Sigmoid, ["KC"], [ac], M, bias=-128.0, scale=-256.0)
+        else:
+            ts(T.act[:, c], T.KC[:, 0:M], 0.0, None, A.is_lt, None, ["KC"], [ac], M)
+        vl = T.X0[:, M:M + 16]
+        mm(vl, T.bigI[:], T.ones[:, 0:16], True, False, ["bigI", "ones"], [lb], 16)
+        mm(vl, T.I[:], T.pf16[:, l], False, False, ["I", "pf16%d" % pr], [lb], 16)
+        for s in range(16):
+            mm(vl, sel("SA", s), T.act[:, M * pr + s:M * pr + M:16], False, s == 15, ["SA", ac], [lb], 16)
+        tt(T.of1[:], vl, T.dum[:], A.min, [lb, "dum"], ["of1"], 16)
+        if t < RO - 1:
+            ts(T.p1a[:], pin, float(OV + 1), None, A.add, None, [pn], ["p1a"], 16)
+            ts(T.p1b[:], T.p1a[:], OV + V - 1, None, A.bitwise_and, None, ["p1a"], ["p1b"], 16)
+            tt(T.ovr[:, l], vl, T.p1b[:], A.min, [lb, "p1b"], ["ovr%d" % pr], 16)
+        ts(T.off[:, l], T.of1[:], 1024.0, None, A.add, None, ["of1"], ["off%d" % pr], 16)
+        hi = V + M * t
+        if P["xact"][t]:
+            act_(T.zr1[:], T.W[:, 0:hi].indirect(T.pu[:, l]), F.Identity, wr + ["pu%d" % pr], ["zr1"], M, bias=RND, rate=gc)
+            act_(T.xp[:], T.zr1[:], F.Identity, ["zr1"], ["xp"], M, bias=-RND)
+        else:
+            ts(T.xp[:], T.W[:, 0:hi].indirect(T.pu[:, l]), RND, RND, A.add, A.subtract, wr + ["pu%d" % pr], ["xp"], M, gc)
+        if P["cact"][t]:
+            act_(T.KU[:, 0:M], T.K1[:].indirect(T.uu[:, l]), F.Copy, ["K1", "uu%d" % pr], ["KU0"], M, rate=gc)
+            act_(T.KU[:, M:2 * M], T.K2[:].indirect(T.uu[:, l]), F.Copy, ["K2", "uu%d" % pr], ["KU1"], M, rate=gc)
+            for src, sn in ((T.KU, ["KU0", "KU1"]), (T.rho, ["rho"])):
+                mm(T.TC1[:], T.nI[:], src[:], True, False, ["nI"] + sn, ["TC1"], 512)
+                for h in range(2):
+                    mm(T.TC1[:, M * h:M * h + M], T.I[:], T.xp[:], False, h == 1, ["I", "xp"], ["TC1"], M)
+                if src is T.KU:
+                    act_(T.rho[:], T.TC1[:], F.Relu, ["TC1"], ["rho"], 512)
+            act_(T.C[:], T.TC1[:, 0:M], F.Identity, ["TC1"], ["C"], M)
+            act_(T.W[:, hi:hi + M], T.TC1[:, M:2 * M], F.Identity, ["TC1"], ["Wn"], M)
+            act_(T.Cb[:, c], T.TC1[:, 0:M], F.Identity, ["TC1"], ["Cb%d" % pr], M)
+            act_(T.E[:, c], T.TC1[:, M:2 * M], F.Identity, ["TC1"], ["E%d" % pr], M)
+        else:
+            tt(T.C[:], T.K1[:].indirect(T.uu[:, l]), T.xp[:], A.min, ["K1", "uu%d" % pr, "xp"], ["C"], M, gc)
+            tt(T.W[:, hi:hi + M], T.K2[:].indirect(T.uu[:, l]), T.xp[:], A.min, ["K2", "uu%d" % pr, "xp"], ["Wn"], M, gc)
+            act_(T.E[:, c], T.W[:, hi:hi + M], F.Identity, ["Wn"], ["E%d" % pr], M)
+            act_(T.Cb[:, c], T.C[:], F.Identity, ["C"], ["Cb%d" % pr], M)
+        tt(T.W[:].indirect(T.off[:, l]), T.C[:], T.fr[:, M * t:M * t + M], A.add, ["C", "fr%d" % t, "off%d" % pr], wr + ["Wt"], M, 3.8)
+
+    def empty(t):
+        pr = t % 2
+        c = slice(M * pr, M * pr + M)
+        hi = V + M * t
+        if t == RO - 1:
+            tt(T.XO[:, hi:hi + M], T.TE1[:, 0:M], T.E[:, c], A.mult, ["E%d" % pr, "TE1"], ["XO6"], M)
+        else:
+            tt(T.W[:, hi:hi + M], T.TE1[:, 0:M], T.E[:, c], A.mult, ["E%d" % pr, "TE1"], ["Wn", "Wt"], M)
+
+    def lists(t):
+        pr = t % 2
+        l = slice(16 * pr, 16 * pr + 16)
+        win = T.NB[:] if t == 0 else T.L[:, 0:V + M * t]
+        copy(T.au[:], win.indirect(T.pu[:, l]), (["NB"] if t == 0 else ["L", "Ln"]) + ["pu%d" % pr], ["au"], M, gc)
+        ts(T.af[:], T.au[:], -1024.0, None, A.add, None, ["au"], ["af"], M, 0.5)
+
+    def zpath(t):
+        pr = t % 2
+        c = slice(M * pr, M * pr + M)
+        z = T.zin[:, M * t:M * t + M]
+        zn, ac = "zin%d" % t, "act%d" % pr
+        act_(T.junk[:], T.act[:, c], F.Identity, [ac], ["junk", "cnt"], M, acc=T.cnt[:, 0:1])
+        if P["zact"]:
+            mm(T.X0[:, 0:M], T.nIh[:], z, True, False, ["nIh", zn], ["X0"], M)
+            mm(T.X0[:, 0:M], T.p1k[:], T.act[:, c], False, False, ["p1k", ac], ["X0"], M)
+            mm(T.X0[:, 0:M], T.Ih[:], T.Cb[:, c], False, True, ["Ih", "Cb%d" % pr], ["X0"], M)
+            act_(T.zr1[:], T.X0[:, 0:M], F.Relu, ["X0"], ["zr1"], M, bias=127.75 - 1024.0)
+            mm(T.X0[:, M:2 * M], T.I[:], z, True, False, ["I", zn], ["X0"], M)
+            mm(T.X0[:, M:2 * M], T.n128[:], T.act[:, c], False, False, ["n128", ac], ["X0"], M)
+            mm(T.X0[:, M:2 * M], T.If[:], T.zr1[:], False, True, ["If", "zr1"], ["X0"], M, True)
+            act_(T.zr2[:], T.X0[:, M:2 * M], F.Identity, ["X0"], ["zr2"], M, bias=RND)
+            act_(T.zout[:, M * t:M * t + M], T.zr2[:], F.Identity, ["zr2"], ["zout%d" % t], M, bias=-RND)
+        else:
+            mm(T.X0[:, 0:M], T.I[:], z, True, False, ["I", zn], ["X0"], M)
+            mm(T.X0[:, 0:M], T.nI[:], T.Cb[:, c], False, True, ["nI", "Cb%d" % pr], ["X0"], M)
+            tt(T.dm[:], T.X0[:, 0:M], T.act[:, c], A.mult, ["X0", ac], ["dm"], M)
+            mm(T.X0[:, M:2 * M], T.I[:], z, True, False, ["I", zn], ["X0"], M)
+            mm(T.X0[:, M:2 * M], T.nIq[:], T.act[:, c], False, False, ["nIq", ac], ["X0"], M)
+            mm(T.X0[:, M:2 * M], T.nIh[:], T.dm[:], False, True, ["nIh", "dm"], ["X0"], M)
+            ts(T.zout[:, M * t:M * t + M], T.X0[:, M:2 * M], RND, RND, A.add, A.subtract, ["X0"], ["zout%d" % t], M)
+        send(T.zin[:, M * (t + 1):M * (t + 2)], T.zout[:, M * t:M * t + M], T.sem["za%d" % (t + 1)], ["zout%d" % t], ["zin%d" % (t + 1)], 6000.0 if t == 0 else 3000.0)
+
+    def compare(src, sn, bank, dst, key, ko, h, last, rs=(0, 1, 2, 3)):
+        o = 2048 * h
+        for r in rs:
+            nm = "%s%d%d" % (dst, h, r)
+            tt(T[dst][:, o + r:o + 2048:4], T[src][:, o + r:o + 2048:4], T[bank][:], A.is_ge, sn + [bank], [nm], 512)
+            for k in range(r, 16, 4):
+                mm(T[key][:, ko + 128 * h:ko + 128 * h + 128], sel("S19", k), T[dst][:, o + k:o + 2048:16], False, last and r == rs[-1] and k >= 12, ["S19", nm], [key], 128)
+
+    nsum = [0]
+
+    def signs(child, cn, dst, key, h, last, rs, banks):
+        o = 2048 * h
+        later = []
+
+        def sums(x):
+            r, d0, nm = x
+            for kk in range(4):
+                mm(T[key][:, M + 128 * h:M + 128 * h + 128], sel("S18", r + 4 * kk), T[dst][:, d0 + 128 * kk:d0 + 128 * kk + 128], False,
+                   last and r == rs[-1] and kk == 3, ["S18", nm], [key], 128)
+        for r in rs:
+            b = banks[nsum[0] % len(banks)]
+            nsum[0] += 1
+            nm = "%s%d%d" % (dst, h, r)
+            for kk in range(4):
+                mm(T[b][:, 128 * kk:128 * kk + 128], T.nP[:], child, True, False, ["nP", cn], [b], 128)
+                mm(T[b][:, 128 * kk:128 * kk + 128], T.nI[:], T.GB[:, o + r + 4 * kk:o + 2048:16], False, True, ["nI", "GB%d" % h, "GV%d" % h], [b], 128)
+            d0 = o + 512 * r
+            act_(T[dst][:, d0:d0 + 512], T[b][:], F.Sign, [b], [nm], 512, bias=0.25, scale=-1.0)
+            sums((r, d0, nm))
+
+    def b_part(t, ch, h, last):
+        pr = t % 2
+        r0 = P["r0" + ch][t][h]
+        src, cn = (T.Cb, "Cb%d" % pr) if ch == "C" else (T.E, "E%d" % pr)
+        if r0 > 0:
+            compare("GB", ["GB%d" % h, "GV%d" % h], "T%s%d" % (ch, h), "BB" + ch, "K" + ch, M, h, last and r0 == 4, tuple(range(r0)))
+        if r0 < 4:
+            signs(src[:, M * pr + 128 * h:M * pr + 128 * h + 128], cn, "SB" + ch, "K" + ch, h, last, tuple(range(r0, 4)), P["bk" + ch])
+
+    def scores(t):
+        pr = t % 2
+        c = slice(M * pr, M * pr + M)
+        hi = V + M * (t + 1)
+        wr = ["W", "Wn"]
+        for h in range(2):
+            b = "TC%d" % h
+            for j in range(4):
+                mm(T[b][:, j:512:4], T.nP[:], T.Cb[:, M * pr + 128 * h:M * pr + 128 * h + 128], True, True, ["nP", "Cb%d" % pr], [b], 128)
+            mm(T.TE0[:, h:512:2], T.nP[:], T.E[:, c], True, True, ["nP", "E%d" % pr], ["TE0"], M)
+        mm(T.TE1[:, 0:M], T.I[:], T.act[:, c], True, True, ["I", "act%d" % pr], ["TE1"], M)
+        mm(T.TE1[:, M:2 * M], T.I[:], T.crow[:, 0:M], True, False, ["I", "crow0"], ["TE1"], M)
+        mm(T.TE1[:, M:2 * M], T.I[:], T.af[:], False, False, ["I", "af"], ["TE1"], M)
+        mm(T.KC[:, M:2 * M], T.I[:], T.crow[:, M:2 * M], True, False, ["I", "crow1"], ["KC"], M)
+        mm(T.KE[:], T.I[:], T.crow[:], True, False, ["I", "crow0", "crow1"], ["KE"], 512)
+        mm(T.KE[:, 0:M], T.I[:], T.af[:], False, False, ["I", "af"], ["KE"], M)
+
+        mm(T.KE[:, M:2 * M], T.I[:], T.c22[:], False, False, ["I", "c22"], ["KE"], M)
+        for h in range(2):
+            r0 = P["r0C"][t][h]
+            if r0 < 4:
+                mm(T.KC[:, M + 128 * h:M + 128 * h + 128], T.Im[:, 128 * r0:128 * r0 + 128] if r0 else T.I[:], T.c22[:, 0:128], False, False,
+                   (["Im%d%d" % (r0, b) for b in range(4)] if r0 else ["I"]) + ["c22"], ["KC"], 128)
+        dq, d1 = P["dq"][t][0:2]
+        ga = [[], []]
+        for i0, i1, e in ((0, dq, "v"), (dq, 128, "a"), (128, 128 + d1, "v"), (128 + d1, M, "a")):
+            if i1 == i0:
+                continue
+            nm = "GA%d" % i0
+            ga[i0 // 128].append(nm)
+            win = T.W[:, 0:hi].indirect(T.au[:, i0:i1])
+            if e == "v":
+                copy(T.GA[:, 16 * i0:16 * i1], win, wr + ["au"], [nm], 16 * (i1 - i0), gc)
+            else:
+                act_(T.GA[:, 16 * i0:16 * i1], win, F.Copy, wr + ["au"], [nm], 16 * (i1 - i0), rate=gc)
+        for h in range(2):
+            hs = slice(128 * h, 128 * h + 128)
+            for k in range(16):
+                mm(T.X1[:, 128 * h + k:128 * h + 128:16], T.GA[:, 2048 * h + k:2048 * h + 2048:16], T.sel[:], True, True, ga[h] + ["sel"], ["X1"], 8, True)
+            copy(T.rT[:, hs], T.X1[:, hs], ["X1"], ["rT%d" % h], 128)
+            tt(T.fT[:, hs], T.X1[:, hs], T.rT[:, hs], A.subtract, ["X1", "rT%d" % h], ["fT%d" % h], 128)
+            mm(T.X1[:, M + 128 * h:M + 128 * h + 128], T.fT[:, hs], T.nIm[:], True, True, ["fT%d" % h, "nIm"], ["X1"], 128)
+            ts(T.bu[:, hs], T.X1[:, M + 128 * h:M + 128 * h + 128], 1024.0, None, A.add, None, ["X1"], ["bu%d" % h], 128)
+            db = P["dq"][t][2 + h]
+            i0 = 128 * h
+            if db:
+                copy(T.GB[:, 16 * i0:16 * (i0 + db)], T.W[:, V:DUM].indirect(T.bu[:, i0:i0 + db]), wr + ["Wt", "bu%d" % h], ["GV%d" % h], 16 * db, gc)
+            act_(T.GB[:, 16 * (i0 + db):16 * i0 + 2048], T.W[:, V:DUM].indirect(T.bu[:, i0 + db:i0 + 128]), F.Copy, wr + ["Wt", "bu%d" % h], ["GB%d" % h], 2048 - 16 * db, rate=gc)
+            compare("GA", ga[h], "TC%d" % h, "BAC", "TE1", M, h, h == 1)
+        for h in range(2):
+            hs = slice(128 * h, 128 * h + 128)
+            for key in ("KC", "KE"):
+                mm(T[key][:, M + 128 * h:M + 128 * h + 128], T.fT[:, hs], T.nIm[:], False, False, ["fT%d" % h, "nIm"], [key], 128)
+            b_part(t, "C", h, h == 1)
+        return ga
+
+    def post_c(t):
+        pr = t % 2
+        l = slice(16 * pr, 16 * pr + 16)
+        tt(T.m1[:], T.TE1[:, M:2 * M], T.KOC[:, M * t:M * t + M], A.max, ["TE1", "KOC%d" % t], ["m1"], M)
+        tt(T.m2[:], T.KC[:, M:2 * M], T.m1[:], A.max, ["KC", "m1"], ["m2"], M)
+        if t < RO - 1:
+            add("v", lambda: g.vector.transpose(T.TT[:], T.m2[:]), ["m2"], ["TT"], vc(M))
+            add("v", lambda: g.vector.tensor_tensor_scan(T.SC[:], T.sm[:], T.TT[:], 0.0, A.mult, A.max), ["sm", "TT"], ["SC"], vc(M))
+            for xh in range(2):
+                for gl in range(2):
+                    q = 2 * xh + gl
+                    mm(T.KC[:, xh:16:2], T.SWP[:, 128 * q:128 * q + 128], T.SC[:, 15 + 16 * gl:M:32], gl == 0, gl == 1, ["SWP%d" % q, "SC"], ["KC"], 8, True)
+            tt(T.mx[:], T.KC[:, 0:16], T.ovr[:, l], A.max, ["KC", "ovr%d" % pr], ["mx"], 16)
+            ts(T.pout[:, 16 * t:16 * t + 16], T.mx[:], 4095, None, A.bitwise_and, None, ["mx"], ["pout%d" % t], 16)
+            send(T.pin[:, 16 * (t + 1):16 * (t + 2)], T.pout[:, 16 * t:16 * t + 16], T.sem["pa%d" % (t + 1)], ["pout%d" % t], ["pin%d" % (t + 1)])
+        if P["ract"][t]:
+            act_(T.r13a[:], T.m2[:], F.Identity, ["m2"], ["r13a"], M, bias=RND13)
+            act_(T.r13[:], T.r13a[:], F.Identity, ["r13a"], ["r13"], M, bias=-RND13)
+        else:
+            ts(T.r13[:], T.m2[:], RND13, RND13, A.add, A.subtract, ["m2"], ["r13"], M)
+        tt(T.L[:].indirect(T.off[:, l]), T.m2[:], T.r13[:], A.subtract, ["m2", "r13", "off%d" % pr],
+           ["L", "Ln"] + (["Li%d" % j for j in range(4)] if t == 0 else []), M, 3.8)
+
+    def part_e(t, ga):
+        pr = t % 2
+        c = slice(M * pr, M * pr + M)
+        tse = P["tse"][t]
+        for r in range(8):
+            tt(T.BAE[:, r:16 * M:8], T.GA[:, r:16 * M:8], T.TE0[:], A.is_ge, ga[0] + ga[1] + ["TE0"], ["BAE%d" % r], 512)
+            for k in (r, r + 8):
+                if tse:
+                    for h in range(2):
+                        mm(T.TC1[:, 128 * h + k:128 * h + 128:16], T.BAE[:, 2048 * h + k:2048 * h + 2048:16], T.grp[:], True, True, ["grp", "BAE%d" % r], ["TC1"], 8)
+                else:
+                    mm(T.KE[:, 0:M], sel("S19", k), T.BAE[:, k:16 * M:16], False, False, ["S19", "BAE%d" % r], ["KE"], M)
+        for j in range(8):
+            b = P["bkE"][j % len(P["bkE"])]
+            for kk in range(2):
+                mm(T[b][:, M * kk:M * kk + M], T.nP[:], T.E[:, c], True, False, ["nP", "E%d" % pr], [b], M)
+                mm(T[b][:, M * kk:M * kk + M], T.nI[:], T.GB[:, 2 * j + kk:16 * M:16], False, True, ["nI", "GB0", "GB1", "GV0", "GV1"], [b], M)
+            act_(T.SBE[:, 512 * j:512 * j + 512], T[b][:], F.Sign, [b], ["SBE%d" % j], 512, bias=0.25, scale=-1.0)
+            for kk in range(2):
+                d0 = 512 * j + M * kk
+                if tse:
+                    for h in range(2):
+                        mm(T.TC1[:, M + 128 * h + 2 * j + kk:M + 128 * h + 128:16], T.SBE[:, d0 + 128 * h:d0 + 128 * h + 128], T.grp[:], True, True, ["grp", "SBE%d" % j], ["TC1"], 8)
+                else:
+                    mm(T.KE[:, M:2 * M], sel("S18", 2 * j + kk), T.SBE[:, d0:d0 + M], False, j == 7 and kk == 1, ["S18", "SBE%d" % j], ["KE"], M)
+        if tse:
+            act_(T.sT[:], T.TC1[:], F.Identity, ["TC1"], ["sT"], 512)
+            for q in range(4):
+                w = ("I19", "I18")[q // 2]
+                mm(T.KE[:, 128 * q:128 * q + 128], T.sT[:, 128 * q:128 * q + 128], T[w][:], False, q == 3, [w, "sT"], ["KE"], 128)
+        tt(T.e1[:], T.KE[:, 0:M], T.KOE[:, c], A.max, ["KE", "KOE%d" % pr], ["e1"], M)
+        tt(T.e2[:], T.KE[:, M:2 * M], T.e1[:], A.max, ["KE", "e1"], ["e2"], M)
+        ts(T.e3[:], T.e2[:], 4095, None, A.bitwise_and, None, ["e2"], ["e3"], M)
+        n0 = V + M * t
+        tt(T.L[:, n0:n0 + M], T.TE1[:, 0:M], T.e3[:], A.mult, ["e3", "TE1"], ["Ln"], M)
+
+    upath(0)
+    prep(0)
+    for t in range(RO):
+        lists(t)
+        if t < RO - 1:
+            zpath(t)
+        ga = scores(t)
+        if t == 0:
+            for j in range(4):
+                copy(T.L[:, 512 * j:512 * j + 512], T.NB[:, 512 * j:512 * j + 512], ["NB"], ["Li%d" % j], 512)
+        empty(t)
+        if t < RO - 1:
+            upath(t + 1)
+        else:
+            for j in range(6):
+                cs = slice(512 * j, min(512 * j + 512, W_ - M))
+                if j < P["xo_act"]:
+                    xs = slice(512 * (j % 2), 512 * (j % 2) + 512)
+                    act_(T.xt[:, xs], T.W[:, cs], F.Identity, ["W", "Wn"], ["xt%d" % (j % 2)], 512, bias=RND)
+                    act_(T.XO[:, cs], T.xt[:, xs], F.Identity, ["xt%d" % (j % 2)], ["XO%d" % j], 512, bias=-RND)
+                else:
+                    ts(T.XO[:, cs], T.W[:, cs], RND, RND, A.add, A.subtract, ["W", "Wn"], ["XO%d" % j], 512)
+                if j % 3 == 2:
+                    cs = slice(512 * j - 1024, 512 * j + 512)
+                    dma("s", T.yx[:, cs], T.XO[:, cs], ["XO%d" % x for x in range(j - 2, j + 1)] + (["XO6"] if j == 5 else []), [], 128 * 1536 * 2)
+        post_c(t)
+        if t == RO - 1:
+            n0 = V + M * t
+            dma("s", T.yn[:, 0:n0], T.L[:, 0:n0], ["L"], [], 128 * n0 * 4)
+            ops[-1]["lat"] += P["ynlat"]
+        part_e(t, ga)
+        if t < RO - 1:
+            prep(t + 1)
+        else:
+            dma("s", T.yn[:, n0:W_], T.L[:, n0:W_], ["Ln"], [], 128 * M * 4)
+    return ops
+
+
+HOP = 90.0
+
+
+def link(ops):
+    lastw, readers, bank, opener = {}, {}, {}, {}
+    for n, o in enumerate(ops):
+        hard, soft = set(), set()
+        if o["eng"] == "s":
+            soft.update(opener.get("s", []))
+            opener["s"] = [n]
+
+        def dep(m, raw):
+            p = ops[m]
+            if p["eng"] == o["eng"] and "sem" not in p and "sem" not in o and o["eng"] == "t":
+                soft.add(m)
+            else:
+                hard.add(m)
+        for x in o["r"]:
+            if x in BANKS:
+                continue
+            if x in lastw:
+                dep(lastw[x], True)
+        for x in o["w"]:
+            if x in BANKS:
+                continue
+            if x in lastw:
+                dep(lastw[x], False)
+            for m in readers.get(x, []):
+                dep(m, False)
+        for x in o["r"]:
+            if x not in BANKS:
+                readers.setdefault(x, []).append(n)
+        for x in o["w"]:
+            if x not in BANKS:
+                lastw[x] = n
+                readers[x] = []
+        for x in set(o["r"] + o["w"]):
+            if x in BANKS:
+                eng, cur, prev = bank.get(x, (None, [], []))
+                if o["eng"] == "t":
+                    if o["flags"]["start"]:
+                        opener[x] = n
+                    o["group"] = opener[x]
+                if eng == o["eng"]:
+                    if eng == "t":
+                        alone = o["flags"]["start"] and o["flags"]["stop"]
+                        soft.update([m for m in cur if not (alone and ops[m]["flags"]["start"] and ops[m]["flags"]["stop"])] if o["flags"]["start"] else [opener[x]])
+                    hard.update(prev)
+                    cur.append(n)
+                else:
+                    hard.update(cur)
+                    bank[x] = (o["eng"], [n], cur)
+        hard.discard(n)
+        soft.discard(n)
+        o["hard"], o["soft"] = hard, soft - hard
+
+
+def schedule(ops):
+    n = len(ops)
+    succ = [[] for _ in range(n)]
+    left = [0] * n
+    for j, o in enumerate(ops):
+        for m in o["hard"] | o["soft"]:
+            succ[m].append(j)
+            left[j] += 1
+    pri = [0.0] * n
+    for j in range(n - 1, -1, -1):
+        o = ops[j]
+        lat = o["cost"] + o.get("lat", 0.0)
+        pri[j] = lat + max([0.0] + [pri[s] + (HOP if j in ops[s]["hard"] else 0.0) - (o.get("lat", 0.0) if j in ops[s]["soft"] else 0.0) for s in succ[j]])
+    bias = [P["bias"].get((o["w"] + ["out"])[0].rstrip("0123456789") + o["eng"], 0.0) for o in ops]
+    best = forward(ops, succ, [pri[j] + bias[j] for j in range(n)])
+    last = best
+    for _ in range(P["fb"]):
+        last = forward(ops, succ, backward(ops, succ, last[2]))
+        if last[0] < best[0]:
+            best = last
+    return best[1]
+
+
+def backward(ops, succ, done):
+    n = len(ops)
+    left = [len(succ[j]) for j in range(n)]
+    fin = [0.0] * n
+    free, ready, rt = {}, {}, {}
+
+    def arm(j):
+        o = ops[j]
+        rt[j] = max([o.get("lat", 0.0)] + [fin[s] + ((HOP + o.get("lat", 0.0)) if j in ops[s]["hard"] else 0.0) for s in succ[j]])
+        ready.setdefault(o["eng"], set()).add(j)
+    for j in range(n):
+        if left[j] == 0:
+            arm(j)
+    for _ in range(n):
+        best = None
+        for e, rs in ready.items():
+            if rs:
+                t0 = max(free.get(e, 0.0), min(rt[j] for j in rs))
+                j = max((x for x in rs if rt[x] <= t0 + P["blook"]), key=lambda x: (done[x], x))
+                st = max(free.get(e, 0.0), rt[j])
+                if best is None or st < best[0]:
+                    best = (st, j, e)
+        st, j, e = best
+        ready[e].discard(j)
+        fin[j] = free[e] = st + ops[j]["cost"]
+        for m in ops[j]["hard"] | ops[j]["soft"]:
+            left[m] -= 1
+            if left[m] == 0:
+                arm(m)
+    return fin
+
+
+def forward(ops, succ, pri):
+    n = len(ops)
+    left = [len(o["hard"] | o["soft"]) for o in ops]
+    free = {}
+    done = [0.0] * n
+    endq = [0.0] * n
+    ready = {}
+    rt = {}
+    dmafree = [0.0]
+
+    def arm(j):
+        o = ops[j]
+        rt[j] = max([0.0] + [done[m] + HOP for m in o["hard"]] + [endq[m] for m in o["soft"]])
+        ready.setdefault(o["eng"], set()).add(j)
+    for j in range(n):
+        if left[j] == 0:
+            arm(j)
+    order = []
+    while len(order) < n:
+        best = None
+        for e, rs in ready.items():
+            if not rs:
+                continue
+            f = free.get(e, 0.0)
+            t0 = max(f, min(rt[j] for j in rs))
+            cand = [j for j in rs if rt[j] <= t0]
+            j = max(cand, key=lambda x: (pri[x], -x))
+            soon = [x for x in rs if t0 < rt[x] <= t0 + min(P["look"], 0.6 * ops[j]["cost"]) and pri[x] > pri[j] + ops[j]["cost"]]
+            if soon:
+                j = max(soon, key=lambda x: (pri[x], -x))
+            st = max(f, rt[j])
+            if best is None or st < best[0]:
+                best = (st, j, e)
+        st, j, e = best
+        o = ops[j]
+        ready[e].discard(j)
+        endq[j] = st + o["cost"]
+        free[e] = endq[j]
+        done[j] = endq[j] + o.get("lat", 0.0)
+        if "bw" in o:
+            dmafree[0] = max(dmafree[0] + o["bw"], done[j])
+            done[j] = dmafree[0]
+        o["at"] = st
+        order.append(j)
+        for s in succ[j]:
+            left[s] -= 1
+            if left[s] == 0:
+                arm(s)
+    return max(done), order, done
+
+
+def rank_program(g, core, T, topo):
+    if T.rank_of(core) is None:
+        return
+    ops = build_ops(g, core, T, topo)
+    link(ops)
+    order = schedule(ops)
+    Q = {"v": g.vector, "a": g.scalar, "t": g.tensor, "g": g, "s": g.sync}
+    esem = {"v": T.sem.ev, "a": T.sem.ea, "t": T.sem.et, "g": T.sem.eg}
+    pos = {j: x for x, j in enumerate(order)}
+    final = {}
+    for j in order:
+        if "group" in ops[j]:
+            final[ops[j]["group"]] = j
+    for j in order:
+        if "group" in ops[j]:
+            ops[j]["flags"]["stop"] = final[ops[j]["group"]] == j
+    known = {e: {} for e in Q}
+    after = {}
+    waits = {}
+    signals = set()
+    for j in order:
+        o = ops[j]
+        kn = known[o["eng"]]
+        need = {}
+        for m in o["hard"]:
+            key = ("own", m) if "sem" in ops[m] else ops[m]["eng"]
+            if kn.get(key, -1) < pos[m] and (key not in need or pos[need[key]] < pos[m]):
+                need[key] = m
+        ws = []
+        for key, m in sorted(need.items(), key=lambda kv: -pos[kv[1]]):
+            if kn.get(key, -1) >= pos[m]:
+                continue
+            ws.append(m)
+            signals.add(m)
+            kn[key] = pos[m]
+            if not ops[m].get("remote"):
+                for k2, v2 in after[m].items():
+                    if kn.get(k2, -1) < v2:
+                        kn[k2] = v2
+        waits[j] = ws
+        after[j] = dict(kn)
+    count = {e: 0 for e in esem}
+    val = {}
+    sent = 0
+    for j in order:
+        o = ops[j]
+        q = Q[o["eng"]]
+        for m in waits[j]:
+            p = ops[m]
+            if "sem" in p:
+                q.wait_ge(p["sem"], p["inc"])
+            else:
+                q.wait_ge(esem[p["eng"]], val[m])
+        ins = o["fn"]()
+        if o.get("remote"):
+            sent += o["inc"]
+        elif "sem" in o:
+            ins.then_inc(o["sem"], 16)
+        elif j in signals:
+            count[o["eng"]] += 1
+            val[j] = count[o["eng"]]
+            ins.then_inc(esem[o["eng"]], 1)
+    g.wait_ge(T.sem.sent, sent)
+    for e in esem:
+        if count[e]:
+            g.wait_ge(esem[e], count[e])
+    for o in ops:
+        if "sem" in o and not o.get("remote") and not o["w"]:
+            g.wait_ge(o["sem"], 16)

@@ -1,51 +1,65 @@
+import math
 from concourse.mybir import AluOpType, AxisListType, ActivationFunctionType
 
 A = AluOpType
 F = ActivationFunctionType
 V, M, KK, RO, TH = 2048, 256, 512, 4, 12
 W_ = V + M * RO
-NOSIB = W_
 DUM = W_ + 16
 WC = DUM + M
+GO = W_
 SC_ = 1 << 19
 K0 = (TH - 1) * SC_ + (1 << 18)
 OV = (1 << 23) + (1 << 19)
 BIG = 3 * (1 << 22)
 RND = 1.5 * 2.0 ** 23
 RND13 = 1.5 * 2.0 ** 36
+LO = 2.0 ** -11
+H1 = 1536.0
+H2 = 768.0
+NONE = 16384.0
 
-P = {'dq': [[56, 0, 0, 0], [56, 16, 0, 0], [56, 16, 0, 0], [56, 16, 0, 0]], 'rsg': 3, 'rsv': 9, 'ynlat': 2000.0, 'bias': {'xpv': -4000, 'ra': 4000, 'KOCg': -3000, 'BBCv': -3000, 'KOEa': 4000, 'mv': -4000, 'xpa': 4000, 'zoutv': -1000, 'Cv': -500, 'puv': -1000, 'Xt': 3000, 'Ka': -500, 'rhoa': 4000, 'TEt': -3000, 'SBCa': -2000, 'srowg': 3000, 'pig': 3000}, 'fb': 3, 'blook': 0.0, 'tse': [1, 1, 1, 0], 'xact': [1, 1, 1, 1], 'cact': [0, 0, 0, 0], 'pefix': 0.0, 'g': 1.56, 'fac': 1.25, 'pe': 0.42, 'rem': 2600.0, 'look': 600.0, 'xo_act': 0, 'tt2': 1.0, 'half': 0.5, 'sig': 1, 'zact': 1, 'ract': [1, 1, 1, 0], 'r0C': [[3, 2], [3, 3], [3, 3], [3, 3]], 'r0E': [[0, 0], [0, 0], [0, 0], [0, 0]], 'bkC': ('TC0', 'X1'), 'bkE': ('TC0', 'X1')}
+P = {'grp': 2, 'ynlat': 1000.0, 'fb': 3, 'blook': 0.0, 'g': 1.56, 'sc': 3.8, 'fac': 1.2, 'pe': 0.42, 'rem': 2200.0, 'dl': 1500.0, 'dr': 250.0,
+     'look': 600.0, 'half': 0.5, 'cap': 500.0, 'tries': 0, 'zs': [5000.0, 2500.0], 'loads': 'pwzkxyn',
+     'SCb': ('TE1', 'KE'), 'LPb': ('X1', 'X0'), 'tra': [[0, 0], [0, 0], [0, 0], [0, 0]], 'lna': [0, 0, 0, 0], 'pee': [0, 0, 0, 0],
+     'dq': [[32, 0, 0, 0], [48, 32, 0, 0], [32, 32, 1, 1], [64, 16, 0, 0]], 'bitsC': ['aaavaavv', 'aaavaavv', 'aaavaavv', 'vvaavvaa'],
+     'bitsE': ['aaaaaaav', 'aavvaavv', 'vvaaaaaa', 'aaaaaaaa'], 'eng': {'pu': 'v', 'zout': 'v', 'prow': 'v'}, 'wi': 'av',
+     'rsg': 3, 'rsv': 6, 'ce': {'SW': 'v', 'nI': 'g', 'Ih': 'g', 'c1k': 'g', 'SA': 'g'}, 'xo': 'aahhvv', 'li': 'aaaa', 'ract': [1, 0, 1, 1]}
+P.update({'grp': 2, 'fb': 2, 'tries': 2500, 'tra': [[0, 0], [0, 0], [1, 0], [0, 0]], 'lna': [0, 0, 0, 0], 'pee': [0, 0, 0, 1], 'dq': [[64, 16, 1, 0], [48, 32, 0, 0], [32, 32, 0, 1], [64, 32, 0, 0]], 'bitsC': ['vvaavvaa', 'aaavaavv', 'vvaaaavv', 'vvaavvaa'], 'bitsE': ['aaaaaaav', 'aaaaaavv', 'vvaaaaaa', 'aaaaavvv'], 'eng': {'pu': 'v', 'zout': 'v', 'uu': 'v'}, 'wi': 'av', 'rsg': 3, 'rsv': 8, 'ce': {'SW': 'g', 'nI': 'g', 'Ih': 'g', 'c1k': 'g', 'SA': 'g', 'blk': 'v', 'Bo': 'v', 'SAb': 'g', 'dum': 'a', 'bigI': 'v', 'o16': 'v', 'In': 'v', 'P11': 'v', 'I20': 'v', 'n8k': 'a'}, 'xo': 'aahhvv', 'li': 'aaaa', 'ract': [1, 0, 1, 1]})
+CASES = [dict(fac=1.0, rem=1900.0, dl=1200.0), dict(fac=1.2, g=1.15, sc=2.2, dr=350.0), dict(fac=1.25, g=1.95, sc=5.4, rem=3300.0, dl=2000.0, dr=200.0),
+         dict(fac=1.45, rem=1600.0)]
 
 f32, bf, f16, i32, u16 = "float32", "bfloat16", "float16", "int32", "uint16"
 
 
 def _sb(cols, d):
-    return ("sbuf", [128] + (cols if isinstance(cols, list) else [cols]), d)
+    return ("sbuf", [128, cols], d)
 
 
+DIAG = {"I": 1.0, "nI": -1.0, "bigI": float(BIG), "Ih": 0.5, "nIh": -0.5, "I2k": 2048.0, "n1280": -1280.0, "I11": LO, "In": NONE,
+        "n8k": -8192.0, "I64": 64.0, "I19": float(SC_), "I20": 2.0 * SC_, "I23": 16.0 * SC_, "IB": 18.0 * SC_}
+MATS = list(DIAG) + ["Pm", "P11", "Dlo", "Dhi", "Kx", "blk", "Bo", "Bw", "zb", "R16"]
 SCRATCH = {
-    "W": _sb(WC, f32), "L": _sb(WC, f32), "NB": _sb(V, i32), "XC": _sb(V, bf), "XO": _sb(W_, bf),
+    "G": _sb(GO + WC, f32), "L": _sb(WC, f32), "MK": _sb(WC, f32), "PAR": _sb(8 + 3 * M, f32),
+    "NB": _sb(V, i32), "XC": _sb(V, bf), "XO": _sb(W_, bf), "XH": _sb(1024, f16),
     "K1": _sb(KK, bf), "K2": _sb(KK, bf), "wi": _sb(4, i32), "wf": _sb(4, f32),
     "pin": _sb(16 * RO, i32), "pout": _sb(16 * RO, i32), "zin": _sb(M * RO, bf), "zout": _sb(M * RO, bf),
-    "GA": _sb(16 * M, f32), "GB": _sb(16 * M, bf),
-    "BAC": _sb(16 * M, bf), "BAE": _sb(16 * M, bf), "BBC": _sb(16 * M, bf), "BBE": _sb(16 * M, bf),
-    "SBC": _sb(16 * M, bf), "SBE": _sb(16 * M, bf), "EQ": _sb(16 * M, bf),
-    "Im": _sb(512, bf), "l4": _sb(4, i32), "l4f": _sb(16, f32), "Ih": _sb(128, bf), "If": _sb(128, f32), "n128": _sb(128, bf), "p1k": _sb(128, bf),
-    "zr1": _sb(M, f32), "zr2": _sb(M, f32), "r13a": _sb(M, f32), "KU": _sb(2 * M, bf), "sT": _sb(2 * M, bf), "grp": _sb(8, bf), "I19": _sb(128, bf), "I18": _sb(128, bf), "rho": _sb(2 * M, bf),
-    "ones": _sb(128, bf), "I": _sb(128, bf), "nI": _sb(128, bf), "nIh": _sb(128, bf), "nIq": _sb(128, bf), "nIm": _sb(128, bf),
-    "bigI": _sb(128, bf), "nP": _sb(128, bf), "blk0": _sb(128, bf), "blk": _sb(128, bf), "Bo": _sb(128, bf), "Bw": _sb(128, bf),
-    "S19": _sb(144, bf), "S18": _sb(144, bf), "SW": _sb(144, bf), "SA": _sb(144, bf), "RS": _sb(2048, bf),
-    "sel": _sb(8, f32), "zb": _sb(128, bf), "SWP": _sb(512, f32), "zf": _sb(128, f32), "o16": _sb(128, f32),
-    "sm": _sb(M, bf), "crow": _sb(512, bf), "c22": _sb(M, bf), "thr": _sb(M, bf), "KOC": _sb(M * RO, f32), "fr": _sb(M * RO, f32),
-    "pi": _sb(4, i32), "pa": _sb(4, i32), "lane": _sb(4, f32), "kcol": _sb(4, f32), "srow": _sb(16, f32), "lm": _sb(16, f32),
-    "hf": _sb(16, f32), "zr": _sb(16, f32), "pat": _sb(16, f32), "pm": _sb(16, f32), "pw": _sb(4, f32), "dm0": _sb(16, f32), "dum": _sb(16, f32),
-    "pf16": _sb(32, f16), "pf32": _sb(32, f32), "pu": _sb(32, u16), "prow": _sb(M, u16), "KOE": _sb(2 * M, f32),
-    "act": _sb(2 * M, bf), "junk": _sb(M, bf), "cnt": _sb(8, f32), "of1": _sb(16, f32), "off": _sb(32, u16),
-    "p1a": _sb(16, i32), "p1b": _sb(16, i32), "ovr": _sb(32, f32), "xp": _sb(M, bf), "C": _sb(M, f32), "Cb": _sb(2 * M, bf), "E": _sb(2 * M, bf),
-    "au": _sb(M, u16), "af": _sb(M, f16), "bu": _sb(M, u16), "rT": _sb(M, i32), "fT": _sb(M, f16),
-    "dm": _sb(M, bf), "u1": _sb(16, i32), "u2": _sb(16, i32), "uu": _sb(32, u16),
-    "m1": _sb(M, f32), "m2": _sb(M, f32), "r13": _sb(M, f32), "TT": _sb(M, f32), "SC": _sb(M, f32), "mx": _sb(16, i32),
-    "e1": _sb(M, f32), "e2": _sb(M, i32), "e3": _sb(M, i32), "xt": _sb(1024, f32),
+    "GA": _sb(16 * M, f32), "RC": _sb(16 * M, f16), "RE": _sb(16 * M, f16), "BC": _sb(16 * M, bf), "BE": _sb(16 * M, bf), "EQ": _sb(16 * M, bf),
+    "MX": _sb(128 * len(MATS), bf), "ones": _sb(512, bf), "zf": _sb(128, f32), "o16": _sb(128, f32), "If": _sb(128, f32),
+    "zn": _sb(256, bf), "grp": _sb(8, bf), "sel": _sb(32, f32), "Kn": _sb(128, bf), "Kt": _sb(128, bf), "c1k": _sb(32, bf),
+    "SW": _sb(144, bf), "SA": _sb(144, bf), "S1": _sb(144, bf), "SM": _sb(144, bf), "RS": _sb(2048, bf),
+    "SWP": _sb(512, f32), "sm": _sb(M, bf), "crow": _sb(512, bf), "thr": _sb(M, bf), "KOC": _sb(M * RO, f32), "lo": _sb(M, bf), "hi": _sb(M * RO, bf),
+    "mkc": _sb(2 * M, f32), "pi": _sb(4, i32), "lane": _sb(4, f32), "srow": _sb(16, f32), "lm": _sb(16, f32),
+    "pat": _sb(16, f32), "pm": _sb(16, f32), "dum": _sb(16, f32), "dug": _sb(16, f32),
+    "pf16": _sb(32, f16), "pf32": _sb(32, f32), "pu": _sb(32, u16), "pv": _sb(16, u16), "prow": _sb(M, f16), "KOE": _sb(2 * M, f32),
+    "act": _sb(2 * M, f16), "cnt": _sb(8, f32), "off": _sb(32, u16), "of2": _sb(16, u16),
+    "pn": _sb(16, i32), "ovr": _sb(32, f32), "xp": _sb(M, f16), "KU": _sb(2 * M, bf), "rho": _sb(2 * M, bf),
+    "CE": _sb(4 * M, f16), "Gn": _sb(M, f32), "PG": _sb(M, f16), "MG": _sb(M, bf), "Gq": _sb(M, f32), "rk": _sb(M, f32),
+    "qu": _sb(16, u16), "qf": _sb(16, f32), "s2": _sb(16, f32), "Ta": _sb(2 * M, f32),
+    "au": _sb(M, u16), "af": _sb(M, f16), "Tr": _sb(2 * M, f16), "Rd": _sb(2 * M, i32), "D": _sb(2 * M, bf),
+    "sC": _sb(2 * M, bf), "sE": _sb(2 * M, bf), "zy": _sb(M, f16), "u1": _sb(16, i32), "uu": _sb(32, u16),
+    "m1": _sb(M, f32), "m2": _sb(M, f32), "r13a": _sb(M, f32), "r13": _sb(M, f32), "TT": _sb(M, f32), "SC": _sb(M, f32), "mx": _sb(16, i32),
+    "e1": _sb(M, f32), "e2": _sb(M, i32), "e3": _sb(M, i32),
 }
 BANKS = ["TC0", "TC1", "TE0", "TE1", "KC", "KE", "X0", "X1"]
 for _b in BANKS:
@@ -54,21 +68,31 @@ NDMA = 16
 SEMAPHORES = ["ev", "ea", "et", "eg", "sent"] + ["d%d" % i for i in range(NDMA)] + ["pa%d" % t for t in range(1, RO)] + ["za%d" % t for t in range(1, RO)]
 
 
-def build_ops(g, core, T, topo):
+def build_ops(g, core, T, topo, case=None):
     rank = T.rank_of(core)
     nxt = T.cores[(rank + 1) % len(T.cores)]
     rid, pid, _ = topo.addr(nxt)
     mask = topo.mask(core, nxt)
     neng = len(topo.engines(core, nxt))
     ops = []
-    fac, gc = P["fac"], P["g"]
+    C = dict(P, **(case or {}))
+    fac, gc, sc = C["fac"], C["g"], C["sc"]
     ndma = [0]
+    rnd = [-1]
 
     def add(eng, fn, r, w, cost, **kw):
-        ops.append(dict(eng=eng, fn=fn, r=list(r), w=list(w), cost=cost, **kw))
+        ops.append(dict(eng=eng, fn=fn, r=list(r), w=list(w), cost=cost, rnd=rnd[0], **kw))
 
     def vc(n, rate=1.0):
         return (50 + max(64, n * rate) * 0.83) * fac
+
+    def mat(name):
+        j = MATS.index(name)
+        return T.MX[:, 128 * j:128 * j + 128]
+
+    def grpcols(name):
+        j = MATS.index(name)
+        return T.MX[:, 128 * j:128 * j + 128:16]
 
     def copy(o, i, r, w, n, rate=1.0):
         add("v", lambda: g.vector.tensor_copy(o, i), r, w, vc(n, rate))
@@ -87,328 +111,421 @@ def build_ops(g, core, T, topo):
 
     def act_(o, i, fn, r, w, n, bias=0.0, scale=1.0, rate=1.0, acc=None):
         if acc is None:
-            add("a", lambda: g.scalar.activation(o, i, fn, bias=bias, scale=scale), r, w, vc(n, rate) + 20)
+            add("a", lambda: g.scalar.activation(o, i, fn, bias=bias, scale=scale), r, w, vc(n, rate) + 15 * fac)
         else:
-            add("a", lambda: g.scalar.activation(o, i, fn, bias=bias, scale=scale, accum_out=acc), r, w, vc(n, rate) + 40)
+            add("a", lambda: g.scalar.activation(o, i, fn, bias=bias, scale=scale, accum_out=acc), r, w, vc(n, rate) + 35 * fac)
+
+    def lin(e, o, i, scale, bias, r, w, n, rate=1.0, vrate=None):
+        e = P["eng"].get(w[0].rstrip("0123456789"), e)
+        if e == "a":
+            act_(o, i, F.Identity, r, w, n, bias=bias, scale=scale, rate=rate)
+        else:
+            ts(o, i, scale, bias, A.mult, A.add, r, w, n, rate if vrate is None else vrate)
 
     def mm(o, l, rh, st, sp, r, w, n, wide=False):
+        r = list(r) + [x for x in (l, rh) if isinstance(x, str)]
+        l = mat(l) if isinstance(l, str) else l
+        rh = mat(rh) if isinstance(rh, str) else rh
         me = {"start": st, "stop": sp}
-        add("t", lambda: g.tensor.matmul(o, l, rh, st, me["stop"]), r, w, (max(64, n) * (4 if wide else 1) * P["pe"] + P["pefix"]) * fac, flags=me)
+        cyc = max(64, n) * (4 if wide else 1)
+        add("t", [lambda: g.tensor.matmul(o, l, rh, st, me["stop"])], r, w, cyc * C["pe"] * fac, flags=dict(me), subs=[me], cyc=cyc)
 
     def gp(fn, r, w, n):
         add("g", fn, r, w, (150 + 2 * n * 0.83) * fac)
 
-    def dma(q, o, i, r, w, nbytes):
+    def dma(o, i, r, w, nbytes, more=0.0):
         s = T.sem["d%d" % ndma[0]]
         ndma[0] += 1
-        e = g.sync if q == "s" else g.scalar
-        add(q, lambda: e.dma_start(o, i), r, w, 60.0, sem=s, inc=16, lat=1800 + nbytes / 250.0, bw=nbytes / 250.0)
+        add("s", lambda: g.sync.dma_start(o, i), r, w, 60.0, sem=s, inc=16, lat=C["dl"] + more + nbytes / C["dr"], bw=nbytes / C["dr"])
 
     def send(o, i, sem, r, w, slack=0.0):
-        add("g", lambda: g.remote_dma(o, i, sem, T.sem.sent, pid, rid, mask), r, w, 300.0, sem=sem, inc=neng, lat=P["rem"] + slack, remote=True)
+        add("g", lambda: g.remote_dma(o, i, sem, T.sem.sent, pid, rid, mask), r, w, 300.0, sem=sem, inc=neng, lat=C["rem"] + slack, remote=True)
 
-    dma("s", T.pin[:, 0:16], T.ps[:], [], ["pin0"], 8192)
-    dma("s", T.XC[:, 0:1024], T.xc[:, 0:1024], [], ["XC0"], 262144)
-    dma("s", T.XC[:, 1024:V], T.xc[:, 1024:V], [], ["XC1"], 262144)
-    dma("s", T.wi[:, 0:1], T.wt[:], [], ["wi"], 512)
-    dma("s", T.zin[:, 0:M], T.zi[:], [], ["zin0"], 65536)
-    dma("s", T.K1[:], T.kc[:], [], ["K1"], 131072)
-    dma("s", T.NB[:], T.nb[:], [], ["NB"], 1048576)
+    loads = {"p": (T.pin[:, 0:16], T.ps[:], "pin0", 8192), "x": (T.XC[:, 0:1024], T.xc[:, 0:1024], "XC0", 262144),
+             "y": (T.XC[:, 1024:V], T.xc[:, 1024:V], "XC1", 262144), "w": (T.wi[:, 0:1], T.wt[:], "wi", 512),
+             "z": (T.zin[:, 0:M], T.zi[:], "zin0", 65536), "k": (T.K1[:], T.kc[:], "K1", 131072), "n": (T.NB[:], T.nb[:], "NB", 1048576)}
+    for x in P["loads"]:
+        dma(loads[x][0], loads[x][1], [], [loads[x][2]], loads[x][3])
 
-    def spot(o, name, pattern, base, fill, n, zero="zb"):
-        gp(lambda: g.affine_select(o, T[zero][:, 0:n], pattern, A.not_equal, float(fill), base, 1), [zero], [name], n)
+    def zero(name, n):
+        j = 128 * MATS.index("zb")
+        return T.MX[:, j:j + n] if name == "zb" else T.zf[:, 0:n]
 
-    mset(T.ones[:], 1.0, ["ones"], 128)
-    mset(T.zb[:], 0.0, ["zb"], 128)
+    def spot(o, name, pattern, base, fill, n, z="zb"):
+        gp(lambda: g.affine_select(o, zero(z, n), pattern, A.not_equal, float(fill), base, 1), [z], [name], n)
+
+    def iota(o, name, pattern, base, n):
+        gp(lambda: g.iota(o, pattern, base, 0, allow_small_or_imprecise_dtypes=True), [], [name], n)
+
+    def band(o, name, lo, hi, fill, z="zb"):
+        gp(lambda: g.affine_select(o, zero(z, 8), [[16, 8]], A.is_gt, float(fill), lo, -1), [z, name], [name], 8)
+        gp(lambda: g.affine_select(o, o, [[16, 8]], A.is_ge, 0.0, hi, -1), [name], [name], 8)
+
+    def ce(name, e):
+        return P["ce"].get(name, e)
+
+    def const(o, name, c, n, e, z="zb"):
+        if ce(name, e) == "v":
+            mset(o, c, [name], n)
+        else:
+            gp(lambda: g.affine_select(o, zero(z, n), [[0, n]], A.is_gt, float(c), 0, 0), [z], [name], n)
+
+    mset(T.ones[:], 1.0, ["ones"], 512)
+    mset(mat("zb"), 0.0, ["zb"], 128)
     mset(T.zf[:], 0.0, ["zf"], 256)
+    iota(mat("R16"), "R16", [[16, 8], [0, 16]], 0, 128)
+    gp(lambda: g.iota(T.wf[:, 2:3], [[0, 1]], 0, 1, allow_small_or_imprecise_dtypes=True), [], ["pcol"], 1)
     gp(lambda: g.iota(T.pi[:, 0:1], [[0, 1]], 0, 1), [], ["pi"], 1)
-    gp(lambda: g.affine_select(T.blk0[:], T.ones[:], [[-16, 8], [0, 16]], A.is_ge, 0.0, 0, 1), ["ones"], ["blk0"], 128)
-    gp(lambda: g.affine_select(T.blk[:], T.blk0[:], [[16, 8], [0, 16]], A.is_ge, 0.0, 15, -1), ["blk0"], ["blk"], 128)
-    gp(lambda: g.iota(T.srow[:], [[1, 16]], 0, 0, allow_small_or_imprecise_dtypes=True), [], ["srow"], 16)
-    gp(lambda: g.affine_select(T.I[:], T.ones[:], [[-1, 128]], A.is_equal, 0.0, 0, 1), ["ones"], ["I"], 128)
-    gp(lambda: g.iota(T.dm0[:], [[16, 16]], DUM - 1024, 0, allow_small_or_imprecise_dtypes=True), [], ["dm0"], 16)
+    ts(T.pi[:, 1:2], T.pi[:, 0:1], 15, None, A.bitwise_and, None, ["pi"], ["pa"], 1)
+    copy(T.lane[:, 0:1], T.pi[:, 1:2], ["pa"], ["lane"], 1)
+    if ce("blk", "g") == "g":
+        gp(lambda: g.affine_select(mat("blk"), T.ones[:, 0:128], [[-16, 8], [0, 16]], A.is_ge, 0.0, 0, 1), ["ones"], ["blk"], 128)
+        gp(lambda: g.affine_select(mat("blk"), mat("blk"), [[16, 8], [0, 16]], A.is_ge, 0.0, 15, -1), ["blk"], ["blk"], 128)
+    else:
+        ts(mat("blk"), mat("R16"), T.lane[:, 0:1], T.wf[:, 2:3], A.add, A.is_equal, ["R16", "lane", "pcol"], ["blk"], 128, 0.5)
+    iota(T.srow[:], "srow", [[1, 16]], 0, 16)
+    spot(mat("I"), "I", [[-1, 128]], 0, 1.0, 128)
+    spot(mat("Pm"), "Pm", [[-2, 64], [1, 2]], -1, 1.0, 128)
+    iota(T.dum[:], "dum", [[16, 16]], DUM, 16)
+    iota(T.lo[:], "lo", [[0, 8], [1, 32]], 0, M)
     for t in range(RO):
-        gp(lambda t=t: g.iota(T.KOC[:, M * t:M * t + M], [[1, M]], K0 + V + M * t, 0, allow_small_or_imprecise_dtypes=True), [], ["KOC%d" % t], M)
-        if t == 0:
-            gp(lambda: g.iota(T.W[:, V + M:DUM], [[0, DUM - V - M]], -1000, 0, allow_small_or_imprecise_dtypes=True), [], ["Wt"], DUM - V - M)
-        act_(T.fr[:, M * t:M * t + M], T.KOC[:, M * t:M * t + M], F.Identity, ["KOC%d" % t], ["fr%d" % t], M, bias=(K0 + W_) / 4096.0, scale=-1.0 / 4096)
-    ts(T.pa[:, 0:1], T.pi[:, 0:1], 15, None, A.bitwise_and, None, ["pi"], ["pa"], 1)
-    copy(T.lane[:, 0:1], T.pa[:, 0:1], ["pa"], ["lane"], 1)
+        iota(T.KOC[:, M * t:M * t + M], "KOC%d" % t, [[1, M]], K0 + V + M * t, M)
+        iota(T.hi[:, M * t:M * t + M], "hi%d" % t, [[1, 8], [0, 32]], 8 * t, M)
     ts(T.lm[:], T.srow[:], T.lane[:, 0:1], None, A.is_equal, None, ["srow", "lane"], ["lm"], 16)
     for s in range(16):
         if s < P["rsg"]:
             spot(T.RS[:, 128 * s:128 * s + 128], "RS%d" % s, [[-16, 8], [0, 16]], -s, 1.0, 128)
         elif s < P["rsg"] + P["rsv"]:
-            ts(T.RS[:, 128 * s:128 * s + 128], T.blk[:], T.lm[:, s:s + 1], None, A.mult, None, ["blk", "lm"], ["RS%d" % s], 128, 0.5)
+            ts(T.RS[:, 128 * s:128 * s + 128], mat("R16"), float(s), T.wf[:, 2:3], A.add, A.is_equal, ["R16", "pcol"], ["RS%d" % s], 128, 0.5)
         else:
-            act_(T.RS[:, 128 * s:128 * s + 128], T.blk[:], F.Identity, ["blk", "lm"], ["RS%d" % s], 128, scale=T.lm[:, s:s + 1])
-    mset(T.hf[:], 0.5, ["hf"], 16)
-    mset(T.zr[:], 0.0, ["zr"], 16)
-    add("v", lambda: g.vector.tensor_tensor_scan(T.pat[:], T.hf[:], T.zr[:], 65536.0, A.mult, A.add), ["hf", "zr"], ["pat"], vc(16))
+            act_(T.RS[:, 128 * s:128 * s + 128], mat("blk"), F.Identity, ["blk", "lm"], ["RS%d" % s], 128, scale=T.lm[:, s:s + 1])
+    mset(T.pm[:], 0.5, ["pm"], 16)
+    add("v", lambda: g.vector.tensor_tensor_scan(T.pat[:], T.pm[:], T.zf[:, 0:16], 65536.0, A.mult, A.add), ["pm", "zf"], ["pat"], vc(16))
     tt(T.pm[:], T.pat[:], T.lm[:], A.mult, ["pat", "lm"], ["pm"], 16)
-    add("v", lambda: g.vector.tensor_reduce(T.pw[:, 0:1], T.pm[:], AxisListType.X, A.add), ["pm"], ["pw"], vc(16))
-    ts(T.Bw[:], T.blk[:], T.pw[:, 0:1], None, A.mult, None, ["blk", "pw"], ["Bw"], 128, 0.5)
-    act_(T.Bo[:], T.blk[:], F.Identity, ["blk"], ["Bo"], 128, scale=2.0 ** 17)
+    add("v", lambda: g.vector.tensor_reduce(T.wf[:, 1:2], T.pm[:], AxisListType.X, A.add), ["pm"], ["pw"], vc(16))
+    lin(ce("Bw", "v"), mat("Bw"), mat("blk"), T.wf[:, 1:2], 0.0, ["blk", "pw"], ["Bw"], 128, vrate=0.5)
+    lin(ce("Bo", "a"), mat("Bo"), mat("blk"), 2.0 ** 17, 0.0, ["blk"], ["Bo"], 128, vrate=0.5)
     act_(T.thr[:, 0:16], T.pat[:], F.Identity, ["pat"], ["thr"], 16, scale=2.0)
     for n in (16, 32, 64, 128):
         act_(T.thr[:, n:2 * n], T.thr[:, 0:n], F.Identity, ["thr"], ["thr"], n)
-    ts(T.dum[:], T.dm0[:], T.lane[:, 0:1], None, A.add, None, ["dm0", "lane"], ["dum"], 16)
-    copy(T.wf[:, 0:1], T.wi[:, 0:1], ["wi"], ["wf"], 1)
-    for name, sc in (("SW", T.wf[:, 0:1]), ("SA", -BIG / 16.0), ("S19", float(SC_)), ("S18", SC_ / 2.0)):
-        mset(T[name][:], 0.0, [name], 144)
-        act_(T[name][:, 16:144:16], T.blk[:, 0:128:16], F.Identity, ["blk", "wf"], [name], 8, scale=sc)
-    for name, sc in (("nI", -1.0), ("bigI", float(BIG)), ("nIm", -4096.0), ("nIh", -0.5)) + ((("Ih", 0.5), ("n128", -128.0), ("p1k", 1024.0)) if P["zact"] else (("nIq", -0.25),)):
-        spot(T[name][:], name, [[-1, 128]], 0, sc, 128)
-    if P["zact"]:
+    lin(ce("dum", "v"), T.dum[:], T.dum[:], 1.0, T.lane[:, 0:1], ["dum", "lane"], ["dum"], 16)
+    lin("a", T.dug[:], T.dum[:], 1.0, float(GO), ["dum"], ["dug"], 16)
+    lin(ce("wf", "v"), T.wf[:, 0:1], T.wi[:, 0:1], 1.0, 0.0, ["wi"], ["wf"], 1)
+    for name, w in (("SW", T.wf[:, 0:1]), ("SA", -BIG / 16.0), ("S1", 1.0 / 16), ("SM", 8192.0 * 2 * M / 16)):
+        if ce(name, "g" if name in ("S1", "SM") else "v") == "v":
+            mset(T[name][:], 0.0, [name], 144)
+        else:
+            iota(T[name][:], name, [[0, 144]], 0, 144)
+        if ce(name + "b", "g" if name in ("S1", "SM") else "a") == "a" or name == "SW":
+            act_(T[name][:, 16:144:16], grpcols("blk"), F.Identity, ["blk"] + (["wf"] if name == "SW" else []), [name], 8, scale=w)
+        else:
+            band(T[name][:, 16:144:16], name, 0, 15, w)
+    for j, name in enumerate(list(DIAG)[1:]):
+        if name in ("I23", "IB") and not max(P["lna"]):
+            continue
+        e = ce(name, "av"[j % 2] if name in ("nI", "bigI", "Ih", "nIh", "I11") else "g")
+        if e == "g":
+            spot(mat(name), name, [[-1, 128]], 0, DIAG[name], 128)
+        else:
+            lin(e, mat(name), mat("I"), DIAG[name], 0.0, ["I"], [name], 128, vrate=0.5)
+    if max(P["lna"]):
+        const(mat("Kx"), "Kx", -18.0 * SC_ / 128, 128, "g")
+    if max(P["pee"]):
         spot(T.If[:], "If", [[-1, 128]], 0, 1.0, 128, "zf")
-    spot(T.nP[:], "nP", [[-2, 64], [1, 2]], -1, -1.0, 128)
-    act_(T.K2[:, 0:KK:2], T.K1[:, 1:KK:2], F.Identity, ["K1"], ["K2"], 256)
-    act_(T.K2[:, 1:KK:2], T.K1[:, 0:KK:2], F.Identity, ["K1"], ["K2"], 256)
+    lin(ce("P11", "a"), mat("P11"), mat("Pm"), LO, 0.0, ["Pm"], ["P11"], 128, vrate=0.5)
+    for j, name in enumerate(("Dlo", "Dhi")):
+        if ce(name, "v") == "v":
+            ts(mat(name), mat("I"), T.lm[:, j:j + 1], LO / 64, A.mult, A.mult, ["I", "lm"], [name], 128, 0.5)
+        else:
+            spot(mat(name), name, [[-16, 8], [1000, 16]], -1001 * j, LO / 64, 128)
+    for name, c0, c1 in (("Kn", -H2 / 64, -H2 * LO / 64), ("Kt", -1.0 / 512, 2.0 ** -19)):
+        mset(T[name][0:64, :], c0, [name + "0"], 128)
+        mset(T[name][64:128, :], c1, [name + "1"], 128)
+    const(T.c1k[:, 0:16], "c1k", 1024.0, 16, "v")
+    const(T.c1k[:, 16:32], "cm1k", -1024.0, 16, "g")
+    const(T.zn[:, 0:128], "zn0", 0.0, 128, "v")
+    lin(ce("zn1", "a"), T.zn[:, 128:256], mat("blk"), -1.0, 0.0, ["blk"], ["zn1"], 128, vrate=0.5)
+    lin(ce("grp", "a"), T.grp[:], grpcols("blk"), 1.0, 0.0, ["blk"], ["grp"], 8)
+    band(T.sel[:, 0:8], "sel0", 0, 7, 1.0, "zf")
+    band(T.sel[:, 8:16], "sel1", 8, 15, 1.0, "zf")
+    for j in range(2):
+        spot(T.sel[:, 16 + 8 * j:24 + 8 * j], "sel%d" % (2 + j), [[-16, 8]], -j, 1 / LO, 8, "zf")
+    lin(ce("K2", "a"), T.K2[:, 0:KK:2], T.K1[:, 1:KK:2], 1.0, 0.0, ["K1"], ["Ka"], 256, vrate=0.5)
+    lin(ce("K2", "a"), T.K2[:, 1:KK:2], T.K1[:, 0:KK:2], 1.0, 0.0, ["K1"], ["Kb"], 256, vrate=0.5)
     for h in range(2):
-        act_(T.W[:, 1024 * h:1024 * h + 1024], T.XC[:, 1024 * h:1024 * h + 1024], F.Identity, ["XC%d" % h], ["Wi%d" % h], 1024)
-    spot(T.sel[:], "sel", [[-16, 8]], 0, 1.0, 8, "zf")
-    if max(P["tse"]):
-        act_(T.grp[:], T.blk[:, 0:128:16], F.Identity, ["blk"], ["grp"], 8)
-        spot(T.I19[:], "I19", [[-1, 128]], 0, SC_, 128)
-        spot(T.I18[:], "I18", [[-1, 128]], 0, SC_ // 2, 128)
+        lin(P["wi"][h], T.G[:, GO + 1024 * h:GO + 1024 * h + 1024], T.XC[:, 1024 * h:1024 * h + 1024], 1 + LO, 0.0, ["XC%d" % h], ["Wi%d" % h], 1024)
     for xh in range(2):
         for gl in range(2):
             q = 2 * xh + gl
             spot(T.SWP[:, 128 * q:128 * q + 128], "SWP%d" % q, [[-32, 4], [1000, 2], [-1, 16]], -16 * xh - 1000 * gl, 1.0, 128, "zf")
-    for r0 in sorted(set(x for y in P["r0C"] for x in y if 0 < x < 4)):
-        for b in range(4):
-            spot(T.Im[:, 128 * r0 + b:128 * r0 + 128:4], "Im%d%d" % (r0, b), [[-4, 32]], -b, 1.0 if b >= r0 else 0.0, 32)
-    mset(T.o16[:], 1.0 / 16, ["o16"], 256)
-    mset(T.sm[:], 1.0, ["sm"], M)
-    ts(T.sm[:, 0:M:16], T.sm[:, 1:M:16], 0.0, None, A.mult, None, ["sm"], ["sm"], 16)
-    ts(T.kcol[:, 0:1], T.lane[:, 0:1], -16384.0, 15 * 16384.0, A.mult, A.add, ["lane"], ["kcol"], 1)
-    mset(T.c22[:], 2.0 ** 22, ["c22"], M)
-    ts(T.crow[:, 0:M], T.c22[:], 9216.0 / 2 ** 22, T.kcol[:, 0:1], A.mult, A.add, ["c22", "kcol"], ["crow0"], M, 0.5)
-    ts(T.crow[:, M:2 * M], T.c22[:], 3072.0 / 2 ** 22, T.kcol[:, 0:1], A.mult, A.add, ["c22", "kcol"], ["crow1"], M, 0.5)
+    const(T.o16[:], "o16", 1.0 / 16, 128, "g", "zf")
+    gp(lambda: g.affine_select(T.sm[:], T.ones[:, 0:M], [[0, 16], [1, 16]], A.is_gt, 0.0, 0, 0), ["ones"], ["sm"], M)
+    lin(ce("kcol", "v"), T.lane[:, 1:2], T.lane[:, 0:1], -16384.0, 15 * 16384.0, ["lane"], ["kcol"], 1)
+    lin(ce("crow", "v"), T.crow[:, 0:M], T.ones[:, 0:M], 9216.0, T.lane[:, 1:2], ["ones", "kcol"], ["crow0"], M, vrate=0.5)
+    lin(ce("crow", "v"), T.crow[:, M:2 * M], T.ones[:, 0:M], float(V), T.lane[:, 1:2], ["ones", "kcol"], ["crow1"], M, vrate=0.5)
+    const(T.PAR[:, 0:8], "PAR", -NONE, 8, "g", "zf")
+    for j in range(11):
+        iota(T.MK[:, M * j:M * j + M], "Mi%d" % j, [[0, M]], 0, M)
+    for t in (1, 2):
+        iota(T.mkc[:, M * (t - 1):M * t], "mkc%d" % t, [[0, M]], 64 * (t - 1), M)
 
     def sel(name, s):
         return T[name][:, 16 - s:144 - s]
 
+    def cells(t):
+        return ["W"] + (["Wn%d" % (t - 1)] if t else ["Wi0", "Wi1"])
+
     def upath(t):
         pr = t % 2
+        l = slice(16 * pr, 16 * pr + 16)
         if t:
-            mm(T.X0[:, 32:33], T.o16[:], T.cnt[:, 0:1], True, True, ["o16", "cnt"], ["X0"], 1, True)
-        b = "X0" if t else "X1"
+            mm(T.X1[:, 32:33], T.o16[:], T.cnt[:, 0:1], True, True, ["o16", "cnt"], ["X1"], 1, True)
         for s in range(16):
-            mm(T[b][:, 0:16], sel("SW", s), T.zin[:, M * t + s:M * t + M:16], s == 0, s == 15, ["SW", "zin%d" % t], [b], 16)
+            mm(T.X1[:, 0:16], sel("SW", s), T.zin[:, M * t + s:M * t + M:16], s == 0, s == 15, ["SW", "zin%d" % t], ["X1"], 16)
         if t:
-            ts(T.u1[:], T.X0[:, 0:16], T.X0[:, 32:33], float(1 << 18), A.add, A.add, ["X0"], ["u1"], 16)
+            ts(T.u1[:], T.X1[:, 0:16], T.X1[:, 32:33], float(1 << 18), A.add, A.add, ["X1"], ["u1"], 16)
         else:
-            ts(T.u1[:], T.X1[:, 0:16], float(1 << 18), None, A.add, None, ["X1"], ["u1"], 16)
-        ts(T.u2[:], T.u1[:], KK - 1, None, A.bitwise_and, None, ["u1"], ["u2"], 16)
-        copy(T.uu[:, 16 * pr:16 * pr + 16], T.u2[:], ["u2"], ["uu%d" % pr], 16)
+            lin("v", T.u1[:], T.X1[:, 0:16], 1.0, float(1 << 18), ["X1"], ["u1"], 16)
+        ts(T.u1[:], T.u1[:], KK - 1, None, A.bitwise_and, None, ["u1"], ["u1"], 16)
+        lin("a", T.uu[:, l], T.u1[:], 1.0, 0.0, ["u1"], ["uu%d" % pr], 16)
+        act_(T.KU[:, 0:M], T.K1[:].indirect(T.uu[:, l]), F.Copy, ["K1", "uu%d" % pr], ["KU0"], M, rate=gc)
+        act_(T.KU[:, M:2 * M], T.K2[:].indirect(T.uu[:, l]), F.Copy, ["Ka", "Kb", "uu%d" % pr], ["KU1"], M, rate=gc)
 
     def prep(t):
         pr = t % 2
         l = slice(16 * pr, 16 * pr + 16)
         c = slice(M * pr, M * pr + M)
         pin = T.pin[:, 16 * t:16 * t + 16]
-        pn = "pin%d" % t
-        wr = ["W", "Wn"] + (["Wi0", "Wi1"] if t == 0 else [])
-        lb = "X0"
-        ts(T.pf16[:, l], pin, -1024.0, None, A.add, None, [pn], ["pf16%d" % pr], 16)
-        copy(T.pf32[:, l], pin, [pn], ["pf32%d" % pr], 16)
-        copy(T.pu[:, l], pin, [pn], ["pu%d" % pr], 16)
+        pn, ac, cn = "pin%d" % t, "act%d" % pr, "CE%d" % pr
+        hi = V + M * t
+        win = T.G[:, GO:GO + hi]
+        wr = cells(t)
+        Cf, Ef = T.CE[:, 2 * M * pr:2 * M * pr + M], T.CE[:, 2 * M * pr + M:2 * M * pr + 2 * M]
+        lin("v", T.pf16[:, l], pin, 1.0, -1024.0, [pn], ["pf%d" % pr], 16)
+        lin("v", T.pf32[:, l], pin, 1.0, -1024.0, [pn], ["pg%d" % pr], 16)
+        lin("a", T.pu[:, l], pin, 1.0, 0.0, [pn], ["pu%d" % pr], 16)
         for s in range(16):
-            mm(T.X0[:, s:M:16], T.RS[:, 128 * s:128 * s + 128], T.pf16[:, l], True, True, ["RS%d" % s, "pf16%d" % pr], ["X0"], 16)
-        ts(T.prow[:], T.X0[:, 0:M], 1024.0, None, A.add, None, ["X0"], ["prow"], M)
-        act_(T.KOE[:, c], T.X0[:, 0:M], F.Identity, ["X0"], ["KOE%d" % pr], M, bias=float(K0 + 1024))
-        mm(T.KC[:, 0:M], T.nI[:], T.thr[:], True, False, ["nI", "thr"], ["KC"], M)
+            mm(T.X0[:, s:M:16], T.RS[:, 128 * s:128 * s + 128], T.pf16[:, l], True, True, ["RS%d" % s, "pf%d" % pr], ["X0"], 16)
+        lin("a", T.prow[:], T.X0[:, 0:M], 1.0, 0.0, ["X0"], ["prow"], M)
+        if not P["lna"][t]:
+            lin("a", T.KOE[:, c], T.X0[:, 0:M], 1.0, float(K0 + 1024), ["X0"], ["KOE%d" % pr], M)
+        mm(T.KC[:, 0:M], "nI", T.thr[:], True, False, ["thr"], ["KC"], M)
         for cc in range(16):
             n = M - 16 * cc
             e0 = M * cc
-            ts(T.EQ[:, e0:e0 + n], T.prow[:, 16 * cc:M], T.pf32[:, 16 * pr + cc:16 * pr + cc + 1], None, A.is_equal, None, ["prow", "pf32%d" % pr], ["EQ%d" % cc], n, P["half"])
+            ts(T.EQ[:, e0:e0 + n], T.prow[:, 16 * cc:M], T.pf32[:, 16 * pr + cc:16 * pr + cc + 1], None, A.is_equal, None, ["prow", "pg%d" % pr], ["EQ%d" % cc], n, P["half"])
             if cc < 15:
-                mm(T.KC[:, 16 * cc + 16:M], T.Bo[:], T.EQ[:, e0 + 16:e0 + n], False, False, ["Bo", "EQ%d" % cc], ["KC"], n - 16)
-            mm(T.KC[:, 16 * cc:16 * cc + 16], T.Bw[:], T.EQ[:, e0:e0 + 16], False, cc == 15, ["Bw", "EQ%d" % cc], ["KC"], 16)
-        ac = "act%d" % pr
-        if P["sig"]:
-            act_(T.act[:, c], T.KC[:, 0:M], F.Sigmoid, ["KC"], [ac], M, bias=-128.0, scale=-256.0)
+                mm(T.KC[:, 16 * cc + 16:M], "Bo", T.EQ[:, e0 + 16:e0 + n], False, False, ["EQ%d" % cc], ["KC"], n - 16)
+            mm(T.KC[:, 16 * cc:16 * cc + 16], "Bw", T.EQ[:, e0:e0 + 16], False, cc == 15, ["EQ%d" % cc], ["KC"], 16)
+        last = t == RO - 1
+        act_(T.act[:, c], T.KC[:, 0:M], F.Sigmoid, ["KC"], [ac] + ([] if last else ["cnt"]), M, bias=-128.0, scale=-256.0, acc=None if last else T.cnt[:, 0:1])
+        if t:
+            act_(T.xp[:], win.indirect(T.pu[:, l]), F.Identity, wr + ["pu%d" % pr], ["xp"], M, bias=H1, rate=gc)
         else:
-            ts(T.act[:, c], T.KC[:, 0:M], 0.0, None, A.is_lt, None, ["KC"], [ac], M)
+            act_(T.xp[:], T.XC[:].indirect(T.pu[:, l]), F.Identity, ["XC0", "XC1", "pu0"], ["xp"], M, bias=H1, rate=gc)
+        for src, sn in ((T.KU, ["KU0", "KU1"]), (T.rho, ["rho"])):
+            mm(T.TC1[:], "nI", src[:], True, False, sn, ["TC1"], 512)
+            for h in range(2):
+                mm(T.TC1[:, M * h:M * h + M], "I", T.xp[:], False, h == 1, ["xp"], ["TC1"], M)
+            if sn[0] == "KU0":
+                act_(T.rho[:], T.TC1[:], F.Relu, ["TC1"], ["rho"], 512, bias=-H1)
+        lin("a", T.CE[:, 2 * M * pr:2 * M * pr + 2 * M], T.TC1[:], 1.0, H2 - H1, ["TC1"], [cn], 512)
+        gn = T.TC0[:, 0:M]
+        mm(gn, T.Kn[:], T.ones[:, 0:M], True, False, ["Kn0", "Kn1", "ones"], ["TC0"], M)
+        mm(gn, "I", Cf, False, False, [cn], ["TC0", "gn0"], M)
+        mm(gn, "I11", Ef, False, False, [cn, "gn0"], ["TC0"], M)
+        mm(gn, "Dlo", T.lo[:], False, False, ["lo", "gn0"], ["TC0"], M)
+        mm(gn, "Dhi", T.hi[:, M * t:M * t + M], False, True, ["hi%d" % t, "gn0"], ["TC0"], M)
+        lin("a", T.Gn[:], gn, 1.0, 0.0, ["TC0"], ["Gn"], M)
+        if t:
+            lin("a", T.pv[:], pin, 1.0, 1.0 - V, [pn], ["pv"], 16)
+            act_(T.PG[:], T.PAR[:, 0:1 + M * t].indirect(T.pv[:]), F.Copy, ["PAR", "pv"], ["PG"], M, rate=gc)
+            ql = T.X1[:, 0:16]
+            mm(ql, "I", T.c1k[:, 0:16], True, False, ["c1k"], ["X1"], 16)
+            for s in range(16):
+                mm(ql, sel("S1", s), T.PG[:, s:M:16], False, s == 15, ["S1", "PG"], ["X1"], 16)
+            lin("a", T.qu[:], ql, 1.0, 0.0, ["X1"], ["qu"], 16)
+            act_(T.qf[:], ql, F.Abs, ["X1"], ["qf"], 16, bias=float(GO))
+            act_(T.Gq[:], win.indirect(T.qu[:]), F.Copy, wr + ["qu"], ["Gq"], M, rate=gc)
+            lin("a", T.rk[:], T.rho[:, 0:M], LO, 0.0, ["rho"], ["rk"], M)
+            if t > 1:
+                act_(T.MG[:], T.MK[:, 0:hi].indirect(T.qu[:]), F.Copy, ["MK", "qu"], ["MG"], M, rate=gc)
+                v2 = T.X1[:, 16:32]
+                mm(v2, "n8k", T.c1k[:, 16:32], True, False, ["cm1k"], ["X1"], 16)
+                mm(v2, "n8k", T.pf16[:, l], False, False, ["pf%d" % pr], ["X1"], 16)
+                for s in range(16):
+                    mm(v2, sel("SM", s), T.MG[:, s:M:16], False, s == 15, ["SM", "MG"], ["X1"], 16)
+                tt(T.qf[:], v2, T.qf[:], A.max, ["X1", "qf"], ["qf"], 16)
         vl = T.X0[:, M:M + 16]
-        mm(vl, T.bigI[:], T.ones[:, 0:16], True, False, ["bigI", "ones"], [lb], 16)
-        mm(vl, T.I[:], T.pf16[:, l], False, False, ["I", "pf16%d" % pr], [lb], 16)
+        mm(vl, "bigI", T.ones[:, 0:16], True, False, ["ones"], ["X0"], 16)
+        mm(vl, "I", T.c1k[:, 0:16], False, False, ["c1k"], ["X0"], 16)
+        mm(vl, "I", T.pf16[:, l], False, False, ["pf%d" % pr], ["X0"], 16)
         for s in range(16):
-            mm(vl, sel("SA", s), T.act[:, M * pr + s:M * pr + M:16], False, s == 15, ["SA", ac], [lb], 16)
-        tt(T.of1[:], vl, T.dum[:], A.min, [lb, "dum"], ["of1"], 16)
-        if t < RO - 1:
-            ts(T.p1a[:], pin, float(OV + 1), None, A.add, None, [pn], ["p1a"], 16)
-            ts(T.p1b[:], T.p1a[:], OV + V - 1, None, A.bitwise_and, None, ["p1a"], ["p1b"], 16)
-            tt(T.ovr[:, l], vl, T.p1b[:], A.min, [lb, "p1b"], ["ovr%d" % pr], 16)
-        ts(T.off[:, l], T.of1[:], 1024.0, None, A.add, None, ["of1"], ["off%d" % pr], 16)
-        hi = V + M * t
-        if P["xact"][t]:
-            act_(T.zr1[:], T.W[:, 0:hi].indirect(T.pu[:, l]), F.Identity, wr + ["pu%d" % pr], ["zr1"], M, bias=RND, rate=gc)
-            act_(T.xp[:], T.zr1[:], F.Identity, ["zr1"], ["xp"], M, bias=-RND)
-        else:
-            ts(T.xp[:], T.W[:, 0:hi].indirect(T.pu[:, l]), RND, RND, A.add, A.subtract, wr + ["pu%d" % pr], ["xp"], M, gc)
-        if P["cact"][t]:
-            act_(T.KU[:, 0:M], T.K1[:].indirect(T.uu[:, l]), F.Copy, ["K1", "uu%d" % pr], ["KU0"], M, rate=gc)
-            act_(T.KU[:, M:2 * M], T.K2[:].indirect(T.uu[:, l]), F.Copy, ["K2", "uu%d" % pr], ["KU1"], M, rate=gc)
-            for src, sn in ((T.KU, ["KU0", "KU1"]), (T.rho, ["rho"])):
-                mm(T.TC1[:], T.nI[:], src[:], True, False, ["nI"] + sn, ["TC1"], 512)
-                for h in range(2):
-                    mm(T.TC1[:, M * h:M * h + M], T.I[:], T.xp[:], False, h == 1, ["I", "xp"], ["TC1"], M)
-                if src is T.KU:
-                    act_(T.rho[:], T.TC1[:], F.Relu, ["TC1"], ["rho"], 512)
-            act_(T.C[:], T.TC1[:, 0:M], F.Identity, ["TC1"], ["C"], M)
-            act_(T.W[:, hi:hi + M], T.TC1[:, M:2 * M], F.Identity, ["TC1"], ["Wn"], M)
-            act_(T.Cb[:, c], T.TC1[:, 0:M], F.Identity, ["TC1"], ["Cb%d" % pr], M)
-            act_(T.E[:, c], T.TC1[:, M:2 * M], F.Identity, ["TC1"], ["E%d" % pr], M)
-        else:
-            tt(T.C[:], T.K1[:].indirect(T.uu[:, l]), T.xp[:], A.min, ["K1", "uu%d" % pr, "xp"], ["C"], M, gc)
-            tt(T.W[:, hi:hi + M], T.K2[:].indirect(T.uu[:, l]), T.xp[:], A.min, ["K2", "uu%d" % pr, "xp"], ["Wn"], M, gc)
-            act_(T.E[:, c], T.W[:, hi:hi + M], F.Identity, ["Wn"], ["E%d" % pr], M)
-            act_(T.Cb[:, c], T.C[:], F.Identity, ["C"], ["Cb%d" % pr], M)
-        tt(T.W[:].indirect(T.off[:, l]), T.C[:], T.fr[:, M * t:M * t + M], A.add, ["C", "fr%d" % t, "off%d" % pr], wr + ["Wt"], M, 3.8)
+            mm(vl, sel("SA", s), T.act[:, M * pr + s:M * pr + M:16], False, s == 15, ["SA", ac], ["X0"], 16)
+        if t:
+            tt(T.s2[:], vl, T.qf[:], A.max, ["X0", "qf"], ["s2"], 16)
+            tt(T.of2[:], T.s2[:], T.dug[:], A.min, ["s2", "dug"], ["of2"], 16)
+        tt(T.off[:, l], vl, T.dum[:], A.min, ["X0", "dum"], ["off%d" % pr], 16)
+        if not last:
+            lin("a", T.pn[:], pin, 1.0, float(OV + 1), [pn], ["pn"], 16)
+            ts(T.pn[:], T.pn[:], OV + V - 1, None, A.bitwise_and, None, ["pn"], ["pn"], 16)
+            tt(T.ovr[:, l], vl, T.pn[:], A.min, ["X0", "pn"], ["ovr%d" % pr], 16)
+        if t:
+            tt(T.G[:].indirect(T.of2[:]), T.Gq[:], T.rk[:], A.subtract, ["Gq", "rk", "of2"], wr, M, sc)
+        copy(T.G[:, GO:GO + WC].indirect(T.off[:, l]), T.Gn[:], ["Gn", "off%d" % pr], wr, M, sc)
 
-    def empty(t):
+    def fresh(t):
         pr = t % 2
+        l = slice(16 * pr, 16 * pr + 16)
         c = slice(M * pr, M * pr + M)
+        ac, cn = "act%d" % pr, "CE%d" % pr
+        Ef = T.CE[:, 2 * M * pr + M:2 * M * pr + 2 * M]
         hi = V + M * t
+        es, pq = T.TE0[:, 0:M], T.TE0[:, M:2 * M]
+        if P["lna"][t]:
+            mm(pq, "I", T.prow[:], True, False, ["prow"], ["TE0"], M)
+            mm(pq, "I23", T.act[:, c], False, True, [ac], ["TE0"], M)
+            act_(T.KOE[:, c], pq, F.Relu, ["TE0"], ["KOE%d" % pr], M, bias=K0 + 1024.0 - DIAG["I23"])
         if t == RO - 1:
-            tt(T.XO[:, hi:hi + M], T.TE1[:, 0:M], T.E[:, c], A.mult, ["E%d" % pr, "TE1"], ["XO6"], M)
-        else:
-            tt(T.W[:, hi:hi + M], T.TE1[:, 0:M], T.E[:, c], A.mult, ["E%d" % pr, "TE1"], ["Wn", "Wt"], M)
+            mm(es, T.Kn[0:64, :], T.ones[0:64, 0:M], True, False, ["Kn0", "ones"], ["TE0"], M)
+            mm(es, "I", Ef, False, True, [cn], ["TE0"], M)
+            tt(T.XO[:, hi:hi + M], es, T.act[:, c], A.mult, ["TE0", ac], ["XO6"], M)
+            return
+        mm(es, T.Kn[:], T.ones[:, 0:M], True, False, ["Kn0", "Kn1", "ones"], ["TE0"], M)
+        mm(es, "I", Ef, False, False, [cn], ["TE0"], M)
+        mm(es, "I11", Ef, False, True, [cn], ["TE0"], M)
+        mm(pq, "I", T.prow[:], True, False, ["prow"], ["TE0"], M)
+        mm(pq, "In", T.act[:, c], False, True, [ac], ["TE0"], M)
+        tt(T.G[:, GO + hi:GO + hi + M], es, T.act[:, c], A.mult, ["TE0", ac, "W"], ["Wn%d" % t], M)
+        lin("a", T.PAR[:, 1 + M * t:1 + M * t + M], pq, 1.0, -NONE, ["TE0"], ["PAR"], M)
+        if t:
+            add("a", lambda: g.scalar.activation(T.MK[:].indirect(T.off[:, l]), T.mkc[:, M * (t - 1):M * t], F.Sigmoid),
+                ["mkc%d" % t, "off%d" % pr], ["MK"] + (["Mi%d" % j for j in range(11)] if t == 1 else []), vc(M, sc) + 15 * fac)
 
     def lists(t):
         pr = t % 2
         l = slice(16 * pr, 16 * pr + 16)
         win = T.NB[:] if t == 0 else T.L[:, 0:V + M * t]
-        copy(T.au[:], win.indirect(T.pu[:, l]), (["NB"] if t == 0 else ["L", "Ln"]) + ["pu%d" % pr], ["au"], M, gc)
-        ts(T.af[:], T.au[:], -1024.0, None, A.add, None, ["au"], ["af"], M, 0.5)
+        lin("a", T.au[:], win.indirect(T.pu[:, l]), 1.0, 0.0, (["NB"] if t == 0 else ["L", "Ln"]) + ["pu%d" % pr], ["au"], M, gc)
+        lin("v", T.af[:], T.au[:], 1.0, -1024.0, ["au"], ["af"], M, vrate=0.5)
 
     def zpath(t):
         pr = t % 2
         c = slice(M * pr, M * pr + M)
         z = T.zin[:, M * t:M * t + M]
-        zn, ac = "zin%d" % t, "act%d" % pr
-        act_(T.junk[:], T.act[:, c], F.Identity, [ac], ["junk", "cnt"], M, acc=T.cnt[:, 0:1])
-        if P["zact"]:
-            mm(T.X0[:, 0:M], T.nIh[:], z, True, False, ["nIh", zn], ["X0"], M)
-            mm(T.X0[:, 0:M], T.p1k[:], T.act[:, c], False, False, ["p1k", ac], ["X0"], M)
-            mm(T.X0[:, 0:M], T.Ih[:], T.Cb[:, c], False, True, ["Ih", "Cb%d" % pr], ["X0"], M)
-            act_(T.zr1[:], T.X0[:, 0:M], F.Relu, ["X0"], ["zr1"], M, bias=127.75 - 1024.0)
-            mm(T.X0[:, M:2 * M], T.I[:], z, True, False, ["I", zn], ["X0"], M)
-            mm(T.X0[:, M:2 * M], T.n128[:], T.act[:, c], False, False, ["n128", ac], ["X0"], M)
-            mm(T.X0[:, M:2 * M], T.If[:], T.zr1[:], False, True, ["If", "zr1"], ["X0"], M, True)
-            act_(T.zr2[:], T.X0[:, M:2 * M], F.Identity, ["X0"], ["zr2"], M, bias=RND)
-            act_(T.zout[:, M * t:M * t + M], T.zr2[:], F.Identity, ["zr2"], ["zout%d" % t], M, bias=-RND)
-        else:
-            mm(T.X0[:, 0:M], T.I[:], z, True, False, ["I", zn], ["X0"], M)
-            mm(T.X0[:, 0:M], T.nI[:], T.Cb[:, c], False, True, ["nI", "Cb%d" % pr], ["X0"], M)
-            tt(T.dm[:], T.X0[:, 0:M], T.act[:, c], A.mult, ["X0", ac], ["dm"], M)
-            mm(T.X0[:, M:2 * M], T.I[:], z, True, False, ["I", zn], ["X0"], M)
-            mm(T.X0[:, M:2 * M], T.nIq[:], T.act[:, c], False, False, ["nIq", ac], ["X0"], M)
-            mm(T.X0[:, M:2 * M], T.nIh[:], T.dm[:], False, True, ["nIh", "dm"], ["X0"], M)
-            ts(T.zout[:, M * t:M * t + M], T.X0[:, M:2 * M], RND, RND, A.add, A.subtract, ["X0"], ["zout%d" % t], M)
-        send(T.zin[:, M * (t + 1):M * (t + 2)], T.zout[:, M * t:M * t + M], T.sem["za%d" % (t + 1)], ["zout%d" % t], ["zin%d" % (t + 1)], 6000.0 if t == 0 else 3000.0)
+        zn, ac, cn = "zin%d" % t, "act%d" % pr, "CE%d" % pr
+        y0, y1 = T.KE[:, 0:M], T.KE[:, M:2 * M]
+        mm(y0, "nIh", z, True, False, [zn], ["KE"], M)
+        mm(y0, "I2k", T.act[:, c], False, False, [ac], ["KE"], M)
+        mm(y0, "Ih", T.CE[:, 2 * M * pr:2 * M * pr + M], False, True, [cn], ["KE"], M)
+        act_(T.zy[:], y0, F.Relu, ["KE"], ["zy"], M, bias=1279.75 - 2048.0 - H2 / 2)
+        mm(y1, "I", z, True, False, [zn], ["KE"], M)
+        mm(y1, "n1280", T.act[:, c], False, False, [ac], ["KE"], M)
+        mm(y1, "I", T.zy[:], False, True, ["zy"], ["KE"], M)
+        lin("a", T.zout[:, M * t:M * t + M], y1, 1.0, 0.0, ["KE"], ["zout%d" % t], M)
+        send(T.zin[:, M * (t + 1):M * (t + 2)], T.zout[:, M * t:M * t + M], T.sem["za%d" % (t + 1)], ["zout%d" % t], ["zin%d" % (t + 1)], P["zs"][min(t, 1)])
 
-    def compare(src, sn, bank, dst, key, ko, h, last, rs=(0, 1, 2, 3)):
-        o = 2048 * h
-        for r in rs:
-            nm = "%s%d%d" % (dst, h, r)
-            tt(T[dst][:, o + r:o + 2048:4], T[src][:, o + r:o + 2048:4], T[bank][:], A.is_ge, sn + [bank], [nm], 512)
-            for k in range(r, 16, 4):
-                mm(T[key][:, ko + 128 * h:ko + 128 * h + 128], sel("S19", k), T[dst][:, o + k:o + 2048:16], False, last and r == rs[-1] and k >= 12, ["S19", nm], [key], 128)
+    def limits(bank, child, cn, rep, more=None):
+        n = 512 // rep
+        mm(T[bank][:], T.Kt[:], T.ones[:], True, False, ["Kt0", "Kt1", "ones"], [bank], 512)
+        for j in range(rep):
+            for w in ("Pm", "P11"):
+                mm(T[bank][:, j:512:rep], w, child, False, j == rep - 1 and w == "P11", [cn], [bank] + ([more] if more else []), n)
 
-    nsum = [0]
+    def bits(R, B, plan, c0, c1, then):
+        j = c0
+        while j < c1:
+            e = j + 1
+            while e < c1 and plan[e] == plan[j] and e - j < P["grp"]:
+                e += 1
+            cs = slice(512 * j, 512 * e)
+            rn = sum([then["rn"](x) for x in range(j, e)], [])
+            bn = ["%s%d" % (B, x) for x in range(j, e)]
+            if plan[j] == "v":
+                ts(T[B][:, cs], T[R][:, cs], H2, None, A.is_ge, None, rn, bn, 512 * (e - j), 0.5)
+            else:
+                act_(T[B][:, cs], T[R][:, cs], F.Sigmoid, rn, bn, 512 * (e - j), bias=-512.0 * (H2 - 0.25), scale=512.0)
+            for x in range(j, e):
+                then["sum"](x)
+            j = e
 
-    def signs(child, cn, dst, key, h, last, rs, banks):
-        o = 2048 * h
-        later = []
+    def key_open(key):
+        mm(T[key][:], "I", T.crow[:], True, False, ["crow0", "crow1"], [key], 512)
+        mm(T[key][:, 0:M], "I", T.af[:], False, False, ["af"], [key], M)
+        for h in range(2):
+            for d, w in enumerate(("I64", "I2k")):
+                mm(T[key][:, M + 128 * h:M + 128 * h + 128], T.D[:, M * h + 128 * d:M * h + 128 * d + 128], w, False, False, ["D%d" % h], [key], 128)
 
-        def sums(x):
-            r, d0, nm = x
-            for kk in range(4):
-                mm(T[key][:, M + 128 * h:M + 128 * h + 128], sel("S18", r + 4 * kk), T[dst][:, d0 + 128 * kk:d0 + 128 * kk + 128], False,
-                   last and r == rs[-1] and kk == 3, ["S18", nm], [key], 128)
-        for r in rs:
-            b = banks[nsum[0] % len(banks)]
-            nsum[0] += 1
-            nm = "%s%d%d" % (dst, h, r)
-            for kk in range(4):
-                mm(T[b][:, 128 * kk:128 * kk + 128], T.nP[:], child, True, False, ["nP", cn], [b], 128)
-                mm(T[b][:, 128 * kk:128 * kk + 128], T.nI[:], T.GB[:, o + r + 4 * kk:o + 2048:16], False, True, ["nI", "GB%d" % h, "GV%d" % h], [b], 128)
-            d0 = o + 512 * r
-            act_(T[dst][:, d0:d0 + 512], T[b][:], F.Sign, [b], [nm], 512, bias=0.25, scale=-1.0)
-            sums((r, d0, nm))
+    def key_scores(key, s, h):
+        for x, w in enumerate(("I19", "I20")):
+            mm(T[key][:, M * x + 128 * h:M * x + 128 * h + 128], T[s][:, M * h + 128 * x:M * h + 128 * x + 128], w, False, h == 1 and x == 1, ["%s%d" % (s, h)], [key], 128)
 
-    def b_part(t, ch, h, last):
-        pr = t % 2
-        r0 = P["r0" + ch][t][h]
-        src, cn = (T.Cb, "Cb%d" % pr) if ch == "C" else (T.E, "E%d" % pr)
-        if r0 > 0:
-            compare("GB", ["GB%d" % h, "GV%d" % h], "T%s%d" % (ch, h), "BB" + ch, "K" + ch, M, h, last and r0 == 4, tuple(range(r0)))
-        if r0 < 4:
-            signs(src[:, M * pr + 128 * h:M * pr + 128 * h + 128], cn, "SB" + ch, "K" + ch, h, last, tuple(range(r0, 4)), P["bk" + ch])
+    def less_sums(bank, o, h):
+        for x in range(2):
+            mm(T[bank][:, o + 128:o + 256], "nI", T.Tr[:, M * h + 128 * x:M * h + 128 * x + 128], False, False, ["Tr%d" % h], [bank], 128)
 
     def scores(t):
         pr = t % 2
-        c = slice(M * pr, M * pr + M)
-        hi = V + M * (t + 1)
-        wr = ["W", "Wn"]
+        cn = "CE%d" % pr
+        hi = V + M * t
+        wr = ["W"] + (["Wn%d" % (t - 1)] if t else [])
         for h in range(2):
-            b = "TC%d" % h
-            for j in range(4):
-                mm(T[b][:, j:512:4], T.nP[:], T.Cb[:, M * pr + 128 * h:M * pr + 128 * h + 128], True, True, ["nP", "Cb%d" % pr], [b], 128)
-            mm(T.TE0[:, h:512:2], T.nP[:], T.E[:, c], True, True, ["nP", "E%d" % pr], ["TE0"], M)
-        mm(T.TE1[:, 0:M], T.I[:], T.act[:, c], True, True, ["I", "act%d" % pr], ["TE1"], M)
-        mm(T.TE1[:, M:2 * M], T.I[:], T.crow[:, 0:M], True, False, ["I", "crow0"], ["TE1"], M)
-        mm(T.TE1[:, M:2 * M], T.I[:], T.af[:], False, False, ["I", "af"], ["TE1"], M)
-        mm(T.KC[:, M:2 * M], T.I[:], T.crow[:, M:2 * M], True, False, ["I", "crow1"], ["KC"], M)
-        mm(T.KE[:], T.I[:], T.crow[:], True, False, ["I", "crow0", "crow1"], ["KE"], 512)
-        mm(T.KE[:, 0:M], T.I[:], T.af[:], False, False, ["I", "af"], ["KE"], M)
-
-        mm(T.KE[:, M:2 * M], T.I[:], T.c22[:], False, False, ["I", "c22"], ["KE"], M)
-        for h in range(2):
-            r0 = P["r0C"][t][h]
-            if r0 < 4:
-                mm(T.KC[:, M + 128 * h:M + 128 * h + 128], T.Im[:, 128 * r0:128 * r0 + 128] if r0 else T.I[:], T.c22[:, 0:128], False, False,
-                   (["Im%d%d" % (r0, b) for b in range(4)] if r0 else ["I"]) + ["c22"], ["KC"], 128)
-        dq, d1 = P["dq"][t][0:2]
-        ga = [[], []]
-        for i0, i1, e in ((0, dq, "v"), (dq, 128, "a"), (128, 128 + d1, "v"), (128 + d1, M, "a")):
-            if i1 == i0:
-                continue
+            limits("TC%d" % h, T.CE[:, 2 * M * pr + 128 * h:2 * M * pr + 128 * h + 128], cn, 4)
+        dq, d1, s0, s1 = P["dq"][t]
+        gq = [[], [], [], []]
+        cuts = sorted(set([0, dq, 128, 128 + d1, M] + ([64] if s0 else []) + ([192] if s1 else [])))
+        for i0, i1 in zip(cuts, cuts[1:]):
+            e = "v" if i1 <= dq or 128 < i1 <= 128 + d1 else "a"
             nm = "GA%d" % i0
-            ga[i0 // 128].append(nm)
-            win = T.W[:, 0:hi].indirect(T.au[:, i0:i1])
+            for q in range(i0 // 64, (i1 + 63) // 64):
+                gq[q].append(nm)
+            win = T.G[:, GO:GO + hi].indirect(T.au[:, i0:i1])
             if e == "v":
                 copy(T.GA[:, 16 * i0:16 * i1], win, wr + ["au"], [nm], 16 * (i1 - i0), gc)
             else:
                 act_(T.GA[:, 16 * i0:16 * i1], win, F.Copy, wr + ["au"], [nm], 16 * (i1 - i0), rate=gc)
+        ga = [gq[0] + gq[1], gq[2] + gq[3]]
         for h in range(2):
-            hs = slice(128 * h, 128 * h + 128)
+            lp = P["LPb"][h]
+            hs = slice(M * h, M * h + M)
             for k in range(16):
-                mm(T.X1[:, 128 * h + k:128 * h + 128:16], T.GA[:, 2048 * h + k:2048 * h + 2048:16], T.sel[:], True, True, ga[h] + ["sel"], ["X1"], 8, True)
-            copy(T.rT[:, hs], T.X1[:, hs], ["X1"], ["rT%d" % h], 128)
-            tt(T.fT[:, hs], T.X1[:, hs], T.rT[:, hs], A.subtract, ["X1", "rT%d" % h], ["fT%d" % h], 128)
-            mm(T.X1[:, M + 128 * h:M + 128 * h + 128], T.fT[:, hs], T.nIm[:], True, True, ["fT%d" % h, "nIm"], ["X1"], 128)
-            ts(T.bu[:, hs], T.X1[:, M + 128 * h:M + 128 * h + 128], 1024.0, None, A.add, None, ["X1"], ["bu%d" % h], 128)
-            db = P["dq"][t][2 + h]
-            i0 = 128 * h
-            if db:
-                copy(T.GB[:, 16 * i0:16 * (i0 + db)], T.W[:, V:DUM].indirect(T.bu[:, i0:i0 + db]), wr + ["Wt", "bu%d" % h], ["GV%d" % h], 16 * db, gc)
-            act_(T.GB[:, 16 * (i0 + db):16 * i0 + 2048], T.W[:, V:DUM].indirect(T.bu[:, i0 + db:i0 + 128]), F.Copy, wr + ["Wt", "bu%d" % h], ["GB%d" % h], 2048 - 16 * db, rate=gc)
-            compare("GA", ga[h], "TC%d" % h, "BAC", "TE1", M, h, h == 1)
+                mm(T[lp][:, k:512:16], T.GA[:, 2048 * h + k:2048 * h + 2048:16], T.sel[:], True, True, ga[h] + ["sel%d" % o for o in range(4)], [lp], 32, True)
+            lin("a", T.Rd[:, hs], T[lp][:, M:2 * M], 1.0, 0.0, [lp], ["Rd%d" % h], M)
+            if P["tra"][t][h]:
+                act_(T.Ta[:, hs], T[lp][:, 0:M], F.Identity, [lp], ["Ta%d" % h], M, bias=RND)
+                act_(T.Tr[:, hs], T.Ta[:, hs], F.Identity, ["Ta%d" % h], ["Tr%d" % h], M, bias=-RND)
+            else:
+                ts(T.Tr[:, hs], T[lp][:, 0:M], RND, RND, A.add, A.subtract, [lp], ["Tr%d" % h], M)
+            tt(T.D[:, hs], T[lp][:, M:2 * M], T.Rd[:, hs], A.subtract, [lp, "Rd%d" % h], ["D%d" % h], M)
+        key_open("KC")
         for h in range(2):
-            hs = slice(128 * h, 128 * h + 128)
-            for key in ("KC", "KE"):
-                mm(T[key][:, M + 128 * h:M + 128 * h + 128], T.fT[:, hs], T.nIm[:], False, False, ["fT%d" % h, "nIm"], [key], 128)
-            b_part(t, "C", h, h == 1)
+            sb = P["SCb"][h]
+            mm(T[sb][:, 0:M], T.CE[:, 2 * M * pr + 128 * h:2 * M * pr + 128 * h + 128], T.zn[:], True, False, [cn, "zn0", "zn1"], [sb], M)
+            for r in range(4):
+                x = 4 * h + r
+                if (s0, s1)[h]:
+                    for q in range(2):
+                        o = 2048 * h + 1024 * q
+                        tt(T.RC[:, 512 * x + M * q:512 * x + M * q + M], T.GA[:, o + r:o + 1024:4], T["TC%d" % h][:, M * q:M * q + M], A.add,
+                           gq[2 * h + q] + ["TC%d" % h], [("RC%d", "RD%d")[q] % x], M)
+                else:
+                    tt(T.RC[:, 512 * x:512 * x + 512], T.GA[:, 2048 * h + r:2048 * h + 2048:4], T["TC%d" % h][:], A.add, ga[h] + ["TC%d" % h], ["RC%d" % x, "RD%d" % x], 512)
+                for j in range(4):
+                    mm(T[sb][:, 128 + r + 4 * j:M:16], T.RC[:, 512 * x + j:512 * x + 512:4], T.grp[:], False, False, ["grp", "RC%d" % x, "RD%d" % x], [sb], 8)
+
+            def sums(x, sb=sb):
+                for j in range(4):
+                    mm(T[sb][:, x % 4 + 4 * j:128:16], T.BC[:, 512 * x + j:512 * x + 512:4], T.grp[:], False, False, ["grp", "BC%d" % x], [sb], 8)
+            bits("RC", "BC", P["bitsC"][t], 4 * h, 4 * h + 4, {"rn": lambda x: ["RC%d" % x, "RD%d" % x], "sum": sums})
+            less_sums(sb, 0, h)
+            lin("a", T.sC[:, M * h:M * h + M], T[sb][:, 0:M], 1.0, 0.0, [sb], ["sC%d" % h], M)
+            key_scores("KC", "sC", h)
         return ga
 
     def post_c(t):
         pr = t % 2
         l = slice(16 * pr, 16 * pr + 16)
-        tt(T.m1[:], T.TE1[:, M:2 * M], T.KOC[:, M * t:M * t + M], A.max, ["TE1", "KOC%d" % t], ["m1"], M)
+        tt(T.m1[:], T.KC[:, 0:M], T.KOC[:, M * t:M * t + M], A.max, ["KC", "KOC%d" % t], ["m1"], M)
         tt(T.m2[:], T.KC[:, M:2 * M], T.m1[:], A.max, ["KC", "m1"], ["m2"], M)
         if t < RO - 1:
             add("v", lambda: g.vector.transpose(T.TT[:], T.m2[:]), ["m2"], ["TT"], vc(M))
@@ -426,80 +543,113 @@ def build_ops(g, core, T, topo):
         else:
             ts(T.r13[:], T.m2[:], RND13, RND13, A.add, A.subtract, ["m2"], ["r13"], M)
         tt(T.L[:].indirect(T.off[:, l]), T.m2[:], T.r13[:], A.subtract, ["m2", "r13", "off%d" % pr],
-           ["L", "Ln"] + (["Li%d" % j for j in range(4)] if t == 0 else []), M, 3.8)
+           ["L", "Ln"] + (["Li%d" % j for j in range(4)] if t == 0 else []), M, sc)
 
     def part_e(t, ga):
         pr = t % 2
         c = slice(M * pr, M * pr + M)
-        tse = P["tse"][t]
-        for r in range(8):
-            tt(T.BAE[:, r:16 * M:8], T.GA[:, r:16 * M:8], T.TE0[:], A.is_ge, ga[0] + ga[1] + ["TE0"], ["BAE%d" % r], 512)
-            for k in (r, r + 8):
-                if tse:
-                    for h in range(2):
-                        mm(T.TC1[:, 128 * h + k:128 * h + 128:16], T.BAE[:, 2048 * h + k:2048 * h + 2048:16], T.grp[:], True, True, ["grp", "BAE%d" % r], ["TC1"], 8)
-                else:
-                    mm(T.KE[:, 0:M], sel("S19", k), T.BAE[:, k:16 * M:16], False, False, ["S19", "BAE%d" % r], ["KE"], M)
-        for j in range(8):
-            b = P["bkE"][j % len(P["bkE"])]
-            for kk in range(2):
-                mm(T[b][:, M * kk:M * kk + M], T.nP[:], T.E[:, c], True, False, ["nP", "E%d" % pr], [b], M)
-                mm(T[b][:, M * kk:M * kk + M], T.nI[:], T.GB[:, 2 * j + kk:16 * M:16], False, True, ["nI", "GB0", "GB1", "GV0", "GV1"], [b], M)
-            act_(T.SBE[:, 512 * j:512 * j + 512], T[b][:], F.Sign, [b], ["SBE%d" % j], 512, bias=0.25, scale=-1.0)
-            for kk in range(2):
-                d0 = 512 * j + M * kk
-                if tse:
-                    for h in range(2):
-                        mm(T.TC1[:, M + 128 * h + 2 * j + kk:M + 128 * h + 128:16], T.SBE[:, d0 + 128 * h:d0 + 128 * h + 128], T.grp[:], True, True, ["grp", "SBE%d" % j], ["TC1"], 8)
-                else:
-                    mm(T.KE[:, M:2 * M], sel("S18", 2 * j + kk), T.SBE[:, d0:d0 + M], False, j == 7 and kk == 1, ["S18", "SBE%d" % j], ["KE"], M)
-        if tse:
-            act_(T.sT[:], T.TC1[:], F.Identity, ["TC1"], ["sT"], 512)
-            for q in range(4):
-                w = ("I19", "I18")[q // 2]
-                mm(T.KE[:, 128 * q:128 * q + 128], T.sT[:, 128 * q:128 * q + 128], T[w][:], False, q == 3, [w, "sT"], ["KE"], 128)
+        cn, ac = "CE%d" % pr, "act%d" % pr
+        e0 = 2 * M * pr + M
+        limits("TE0", T.CE[:, e0:e0 + M], cn, 2)
+        mm(T.TE1[:], "zb", T.ones[:], True, False, ["ones"], ["TE1"], 512)
+        for h in range(2):
+            mm(T.TE1[:, M * h + 128:M * h + M], T.CE[:, e0 + 128 * h:e0 + 128 * h + 128], T.zn[:, 128:256], False, False, [cn, "zn1"], ["TE1"], 128)
+            less_sums("TE1", M * h, h)
+
+        def sums(x, buf="BE", o=0):
+            for j in range(2):
+                for h in range(2):
+                    mm(T.TE1[:, M * h + o + x + 8 * j:M * h + o + 128:16], T[buf][:, 512 * x + M * h + j:512 * x + M * h + M:2], T.grp[:], False, False, ["grp", "%s%d" % (buf, x)], ["TE1"], 8)
+        for x in range(8):
+            if x >= 8 - P["pee"][t]:
+                b = "TC%d" % (x % 2)
+                limits(b, T.CE[:, e0:e0 + M], cn, 2, "lim")
+                for q in range(4):
+                    mm(T[b][:, 128 * q:128 * q + 128], T.If[:], T.GA[:, 1024 * q + x:1024 * q + 1024:8], False, q == 3, ga[q // 2] + ["If", "lim"], [b], 128, True)
+                act_(T.RE[:, 512 * x:512 * x + 512], T[b][:], F.Identity, [b], ["RE%d" % x], 512)
+            else:
+                tt(T.RE[:, 512 * x:512 * x + 512], T.GA[:, x:16 * M:8], T.TE0[:], A.add, ga[0] + ga[1] + ["TE0"], ["RE%d" % x], 512)
+            sums(x, "RE", 128)
+        bits("RE", "BE", P["bitsE"][t], 0, 8, {"rn": lambda x: ["RE%d" % x], "sum": sums})
+        lin("a", T.sE[:], T.TE1[:], 1.0, 0.0, ["TE1"], ["sE0", "sE1"], 512)
+        key_open("KE")
+        if P["lna"][t]:
+            mm(T.KE[:], "Kx", T.ones[:], False, False, ["ones"], ["KE"], 512)
+            for x in range(2):
+                mm(T.KE[:, M * x:M * x + M], "IB", T.act[:, c], False, False, [ac], ["KE"], M)
+        else:
+            mm(T.TE0[:, 0:M], "I", T.act[:, c], True, True, [ac], ["TE0"], M)
+        for h in range(2):
+            key_scores("KE", "sE", h)
         tt(T.e1[:], T.KE[:, 0:M], T.KOE[:, c], A.max, ["KE", "KOE%d" % pr], ["e1"], M)
         tt(T.e2[:], T.KE[:, M:2 * M], T.e1[:], A.max, ["KE", "e1"], ["e2"], M)
         ts(T.e3[:], T.e2[:], 4095, None, A.bitwise_and, None, ["e2"], ["e3"], M)
         n0 = V + M * t
-        tt(T.L[:, n0:n0 + M], T.TE1[:, 0:M], T.e3[:], A.mult, ["e3", "TE1"], ["Ln"], M)
+        if P["lna"][t]:
+            lin("a", T.L[:, n0:n0 + M], T.e3[:], 1.0, 0.0, ["e3"], ["Ln"], M)
+        else:
+            tt(T.L[:, n0:n0 + M], T.TE0[:, 0:M], T.e3[:], A.mult, ["e3", "TE0"], ["Ln"], M)
 
+    rnd[0] = 0
     upath(0)
     prep(0)
     for t in range(RO):
         lists(t)
         if t < RO - 1:
             zpath(t)
+        fresh(t)
         ga = scores(t)
         if t == 0:
             for j in range(4):
-                copy(T.L[:, 512 * j:512 * j + 512], T.NB[:, 512 * j:512 * j + 512], ["NB"], ["Li%d" % j], 512)
-        empty(t)
+                cs = slice(512 * j, 512 * j + 512)
+                lin(P["li"][j], T.L[:, cs], T.NB[:, cs], 1.0, 0.0, ["NB"], ["Li%d" % j], 512)
         if t < RO - 1:
             upath(t + 1)
         else:
             for j in range(6):
                 cs = slice(512 * j, min(512 * j + 512, W_ - M))
-                if j < P["xo_act"]:
-                    xs = slice(512 * (j % 2), 512 * (j % 2) + 512)
-                    act_(T.xt[:, xs], T.W[:, cs], F.Identity, ["W", "Wn"], ["xt%d" % (j % 2)], 512, bias=RND)
-                    act_(T.XO[:, cs], T.xt[:, xs], F.Identity, ["xt%d" % (j % 2)], ["XO%d" % j], 512, bias=-RND)
+                n = cs.stop - cs.start
+                src = T.G[:, GO + cs.start:GO + cs.stop]
+                rd = ["W", "Wn%d" % (t - 1)]
+                if P["xo"][j] == "v":
+                    ts(T.XO[:, cs], src, RND, RND, A.add, A.subtract, rd, ["XO%d" % j], n)
                 else:
-                    ts(T.XO[:, cs], T.W[:, cs], RND, RND, A.add, A.subtract, ["W", "Wn"], ["XO%d" % j], 512)
+                    xs = slice(512 * (j % 2), 512 * (j % 2) + n)
+                    act_(T.XH[:, xs], src, F.Identity, rd, ["XH%d" % (j % 2)], n, bias=H1)
+                    lin("a" if P["xo"][j] == "a" else "v", T.XO[:, cs], T.XH[:, xs], 1.0, -H1, ["XH%d" % (j % 2)], ["XO%d" % j], n, vrate=0.5)
                 if j % 3 == 2:
                     cs = slice(512 * j - 1024, 512 * j + 512)
-                    dma("s", T.yx[:, cs], T.XO[:, cs], ["XO%d" % x for x in range(j - 2, j + 1)] + (["XO6"] if j == 5 else []), [], 128 * 1536 * 2)
+                    dma(T.yx[:, cs], T.XO[:, cs], ["XO%d" % x for x in range(j - 2, j + 1)] + (["XO6"] if j == 5 else []), [], 128 * 1536 * 2)
         post_c(t)
         if t == RO - 1:
             n0 = V + M * t
-            dma("s", T.yn[:, 0:n0], T.L[:, 0:n0], ["L"], [], 128 * n0 * 4)
-            ops[-1]["lat"] += P["ynlat"]
+            dma(T.yn[:, 0:n0], T.L[:, 0:n0], ["L"], [], 128 * n0 * 4, P["ynlat"])
         part_e(t, ga)
         if t < RO - 1:
+            rnd[0] = t + 1
             prep(t + 1)
         else:
-            dma("s", T.yn[:, n0:W_], T.L[:, n0:W_], ["Ln"], [], 128 * M * 4)
-    return ops
+            dma(T.yn[:, n0:W_], T.L[:, n0:W_], ["Ln"], [], 128 * M * 4)
+    return fuse(ops)
+
+
+def fuse(ops):
+    fixed = set(x for o in ops if o["rnd"] < 0 and "sem" not in o for x in o["w"])
+    out = []
+    for o in ops:
+        p = out[-1] if out else None
+        if (o["eng"] == "t" and p and p["eng"] == "t" and p["w"] == o["w"] and set(p["r"]) - fixed == set(o["r"]) - fixed
+                and (p["cyc"] + o["cyc"]) * P["pe"] <= P["cap"]
+                and (not o["flags"]["start"] or (o["flags"]["stop"] and p["flags"]["start"] and p["flags"]["stop"]))
+                and (o["flags"]["start"] or not (p["flags"]["start"] and p["flags"]["stop"]))):
+            p["fn"] += o["fn"]
+            p["subs"] += o["subs"]
+            p["r"] += [x for x in o["r"] if x not in p["r"]]
+            p["cost"] += o["cost"]
+            p["cyc"] += o["cyc"]
+        else:
+            out.append(o)
+    return out
 
 
 HOP = 90.0
@@ -513,7 +663,7 @@ def link(ops):
             soft.update(opener.get("s", []))
             opener["s"] = [n]
 
-        def dep(m, raw):
+        def dep(m):
             p = ops[m]
             if p["eng"] == o["eng"] and "sem" not in p and "sem" not in o and o["eng"] == "t":
                 soft.add(m)
@@ -523,14 +673,14 @@ def link(ops):
             if x in BANKS:
                 continue
             if x in lastw:
-                dep(lastw[x], True)
+                dep(lastw[x])
         for x in o["w"]:
             if x in BANKS:
                 continue
             if x in lastw:
-                dep(lastw[x], False)
+                dep(lastw[x])
             for m in readers.get(x, []):
-                dep(m, False)
+                dep(m)
         for x in o["r"]:
             if x not in BANKS:
                 readers.setdefault(x, []).append(n)
@@ -556,30 +706,67 @@ def link(ops):
                     bank[x] = (o["eng"], [n], cur)
         hard.discard(n)
         soft.discard(n)
-        o["hard"], o["soft"] = hard, soft - hard
+        o["hard"], o["soft"] = sorted(hard), sorted(soft - hard)
 
 
-def schedule(ops):
+def replay(ops, order, costs):
+    n = len(ops)
+    done, endq, free, dmafree = [0.0] * n, [0.0] * n, {}, 0.0
+    for j in order:
+        o = ops[j]
+        cost, lat, bw = costs[j]
+        st = free.get(o["eng"], 0.0)
+        for m in o["hard"]:
+            if done[m] + HOP > st:
+                st = done[m] + HOP
+        for m in o["soft"]:
+            if endq[m] > st:
+                st = endq[m]
+        endq[j] = free[o["eng"]] = st + cost
+        done[j] = st + cost + lat
+        if bw:
+            dmafree = done[j] = max(dmafree + bw, done[j])
+    return max(done)
+
+
+def schedule(ops, cases):
     n = len(ops)
     succ = [[] for _ in range(n)]
-    left = [0] * n
     for j, o in enumerate(ops):
-        for m in o["hard"] | o["soft"]:
+        for m in o["hard"] + o["soft"]:
             succ[m].append(j)
-            left[j] += 1
     pri = [0.0] * n
     for j in range(n - 1, -1, -1):
         o = ops[j]
         lat = o["cost"] + o.get("lat", 0.0)
-        pri[j] = lat + max([0.0] + [pri[s] + (HOP if j in ops[s]["hard"] else 0.0) - (o.get("lat", 0.0) if j in ops[s]["soft"] else 0.0) for s in succ[j]])
-    bias = [P["bias"].get((o["w"] + ["out"])[0].rstrip("0123456789") + o["eng"], 0.0) for o in ops]
-    best = forward(ops, succ, [pri[j] + bias[j] for j in range(n)])
-    last = best
+        pri[j] = lat + max([0.0] + [pri[s] + (HOP if j in ops[s]["hard"] else -o.get("lat", 0.0)) for s in succ[j]])
+
+    def judge(p):
+        end, order, done = forward(ops, succ, p)
+        return sum(math.log(replay(ops, order, c)) for c in cases) / len(cases), order, done, p
+    best = last = judge(pri)
     for _ in range(P["fb"]):
-        last = forward(ops, succ, backward(ops, succ, last[2]))
+        last = judge(backward(ops, succ, last[2]))
         if last[0] < best[0]:
             best = last
-    return best[1]
+    kinds = {}
+    for j, o in enumerate(ops):
+        kinds.setdefault(((o["w"] + ["out"])[0].rstrip("0123456789"), o["eng"], o["rnd"]), []).append(j)
+    keys = sorted(kinds)
+    seed = 12345
+    for it in range(P["tries"]):
+        seed = (seed * 1103515245 + 12345) % (1 << 31)
+        if it % 40 == 39:
+            p = backward(ops, succ, best[2])
+        else:
+            p = list(best[3])
+            d = (-3000.0, -1200.0, -400.0, 400.0, 1200.0, 3000.0)[(seed >> 8) % 6]
+            for j in kinds[keys[(seed >> 12) % len(keys)]]:
+                p[j] += d
+        now = judge(p)
+        if now[0] <= best[0]:
+            best = now
+    return best
 
 
 def backward(ops, succ, done):
@@ -607,7 +794,7 @@ def backward(ops, succ, done):
         st, j, e = best
         ready[e].discard(j)
         fin[j] = free[e] = st + ops[j]["cost"]
-        for m in ops[j]["hard"] | ops[j]["soft"]:
+        for m in ops[j]["hard"] + ops[j]["soft"]:
             left[m] -= 1
             if left[m] == 0:
                 arm(m)
@@ -616,18 +803,26 @@ def backward(ops, succ, done):
 
 def forward(ops, succ, pri):
     n = len(ops)
-    left = [len(o["hard"] | o["soft"]) for o in ops]
-    free = {}
-    done = [0.0] * n
-    endq = [0.0] * n
-    ready = {}
-    rt = {}
-    dmafree = [0.0]
+    left = [len(o["hard"]) + len(o["soft"]) for o in ops]
+    free = {e: 0.0 for e in "vatgs"}
+    ready = {e: [] for e in "vatgs"}
+    pick = {}
+    done, endq, rt = [0.0] * n, [0.0] * n, [0.0] * n
+    dmafree = 0.0
+    look = P["look"]
 
     def arm(j):
         o = ops[j]
-        rt[j] = max([0.0] + [done[m] + HOP for m in o["hard"]] + [endq[m] for m in o["soft"]])
-        ready.setdefault(o["eng"], set()).add(j)
+        r = 0.0
+        for m in o["hard"]:
+            if done[m] + HOP > r:
+                r = done[m] + HOP
+        for m in o["soft"]:
+            if endq[m] > r:
+                r = endq[m]
+        rt[j] = r
+        ready[o["eng"]].append(j)
+        pick.pop(o["eng"], None)
     for j in range(n):
         if left[j] == 0:
             arm(j)
@@ -637,26 +832,27 @@ def forward(ops, succ, pri):
         for e, rs in ready.items():
             if not rs:
                 continue
-            f = free.get(e, 0.0)
-            t0 = max(f, min(rt[j] for j in rs))
-            cand = [j for j in rs if rt[j] <= t0]
-            j = max(cand, key=lambda x: (pri[x], -x))
-            soon = [x for x in rs if t0 < rt[x] <= t0 + min(P["look"], 0.6 * ops[j]["cost"]) and pri[x] > pri[j] + ops[j]["cost"]]
-            if soon:
-                j = max(soon, key=lambda x: (pri[x], -x))
-            st = max(f, rt[j])
-            if best is None or st < best[0]:
-                best = (st, j, e)
+            if e not in pick:
+                f = free[e]
+                t0 = max(f, min([rt[j] for j in rs]))
+                j = max([(pri[x], -x) for x in rs if rt[x] <= t0])
+                j = -j[1]
+                c = ops[j]["cost"]
+                t1, p1 = t0 + min(look, 0.6 * c), pri[j] + c
+                soon = [(pri[x], -x) for x in rs if t0 < rt[x] <= t1 and pri[x] > p1]
+                if soon:
+                    j = -max(soon)[1]
+                pick[e] = (max(f, rt[j]), j, e)
+            if best is None or pick[e][0] < best[0]:
+                best = pick[e]
         st, j, e = best
         o = ops[j]
-        ready[e].discard(j)
-        endq[j] = st + o["cost"]
-        free[e] = endq[j]
+        ready[e].remove(j)
+        del pick[e]
+        endq[j] = free[e] = st + o["cost"]
         done[j] = endq[j] + o.get("lat", 0.0)
         if "bw" in o:
-            dmafree[0] = max(dmafree[0] + o["bw"], done[j])
-            done[j] = dmafree[0]
-        o["at"] = st
+            dmafree = done[j] = max(dmafree + o["bw"], done[j])
         order.append(j)
         for s in succ[j]:
             left[s] -= 1
@@ -665,12 +861,23 @@ def forward(ops, succ, pri):
     return max(done), order, done
 
 
+ORDER = {}
+
+
+def plan(g, core, T, topo):
+    ops = build_ops(g, core, T, topo)
+    link(ops)
+    if "order" not in ORDER:
+        cases = [[(o["cost"], o.get("lat", 0.0), o.get("bw", 0.0)) for o in build_ops(g, core, T, topo, c)] for c in CASES]
+        ORDER["order"] = schedule(ops, cases)
+    return ops, ORDER["order"]
+
+
 def rank_program(g, core, T, topo):
     if T.rank_of(core) is None:
         return
-    ops = build_ops(g, core, T, topo)
-    link(ops)
-    order = schedule(ops)
+    ops, best = plan(g, core, T, topo)
+    order = best[1]
     Q = {"v": g.vector, "a": g.scalar, "t": g.tensor, "g": g, "s": g.sync}
     esem = {"v": T.sem.ev, "a": T.sem.ea, "t": T.sem.et, "g": T.sem.eg}
     pos = {j: x for x, j in enumerate(order)}
@@ -679,8 +886,11 @@ def rank_program(g, core, T, topo):
         if "group" in ops[j]:
             final[ops[j]["group"]] = j
     for j in order:
-        if "group" in ops[j]:
-            ops[j]["flags"]["stop"] = final[ops[j]["group"]] == j
+        o = ops[j]
+        if "group" in o and not (o["flags"]["start"] and o["flags"]["stop"]):
+            for s in o["subs"]:
+                s["stop"] = False
+            o["subs"][-1]["stop"] = final[o["group"]] == j
     known = {e: {} for e in Q}
     after = {}
     waits = {}
@@ -718,7 +928,7 @@ def rank_program(g, core, T, topo):
                 q.wait_ge(p["sem"], p["inc"])
             else:
                 q.wait_ge(esem[p["eng"]], val[m])
-        ins = o["fn"]()
+        ins = [f() for f in o["fn"]][-1] if o["eng"] == "t" else o["fn"]()
         if o.get("remote"):
             sent += o["inc"]
         elif "sem" in o:

@@ -26,8 +26,42 @@ P = {'grp': 2, 'ynlat': 1000.0, 'fb': 3, 'blook': 0.0, 'g': 1.56, 'sc': 3.8, 'fa
      'bitsE': ['aaaaaaav', 'aavvaavv', 'vvaaaaaa', 'aaaaaaaa'], 'eng': {'pu': 'v', 'zout': 'v', 'prow': 'v'}, 'wi': 'av',
      'rsg': 3, 'rsv': 6, 'ce': {'SW': 'v', 'nI': 'g', 'Ih': 'g', 'c1k': 'g', 'SA': 'g'}, 'xo': 'aahhvv', 'li': 'aaaa', 'ract': [1, 0, 1, 1]}
 P.update({'grp': 2, 'fb': 2, 'tries': 2500, 'tra': [[0, 0], [0, 0], [1, 0], [0, 0]], 'lna': [0, 0, 0, 0], 'pee': [0, 0, 0, 1], 'dq': [[64, 16, 1, 0], [48, 32, 0, 0], [32, 32, 0, 1], [64, 32, 0, 0]], 'bitsC': ['vvaavvaa', 'aaavaavv', 'vvaaaavv', 'vvaavvaa'], 'bitsE': ['aaaaaaav', 'aaaaaavv', 'vvaaaaaa', 'aaaaavvv'], 'eng': {'pu': 'v', 'zout': 'v', 'uu': 'v'}, 'wi': 'av', 'rsg': 3, 'rsv': 8, 'ce': {'SW': 'g', 'nI': 'g', 'Ih': 'g', 'c1k': 'g', 'SA': 'g', 'blk': 'v', 'Bo': 'v', 'SAb': 'g', 'dum': 'a', 'bigI': 'v', 'o16': 'v', 'In': 'v', 'P11': 'v', 'I20': 'v', 'n8k': 'a'}, 'xo': 'aahhvv', 'li': 'aaaa', 'ract': [1, 0, 1, 1]})
-CASES = [dict(fac=1.0, rem=1900.0, dl=1200.0), dict(fac=1.2, g=1.15, sc=2.2, dr=350.0), dict(fac=1.25, g=1.95, sc=5.4, rem=3300.0, dl=2000.0, dr=200.0),
-         dict(fac=1.45, rem=1600.0)]
+P.update({'rep2': [0, 0, 0, 0], 'fix': 40.0, 'pe': 0.44, 'tries': 0, 'dr': 220.0, 'ynlat': 500.0, 'fac': 1.1})
+P.update({'bitsC': ['vvaaaavv', 'aaavaavv', 'vvaaaavv', 'vvvvaaav'], 'ract': [1, 1, 1, 1], 'esp': 1, 'rep2': [0, 0, 0, 0], 'grp': 2, 'tries': 500,
+          'gnx': 1, 'eh': 2, 'fix': 45.0, 'swaps': 0, 'heat': 0.001})
+P.update({'turn': 22000.0, 'warm': 0.0, 'tries': 350, 'fb': 2, 'zs': [5000., 1500.], 'xo': 'vvvhhh', 'dq': [[64, 0, 0, 0], [64, 0, 0, 0], [64, 0, 0, 0], [0, 0, 0, 0]],
+          'bitsC': ['aavvaavv'] * 3 + ['vvvvaavv'], 'bitsE': ['aaaaaavv'] * 4, 'tra': [[0, 0], [0, 0], [0, 0], [0, 0]], 'pee': [0] * 4,
+          'eng': {'zout': 'v', 'PAR': 'v', 'prow': 'v'}, 'pgf': 0, 'loads': 'pwzkxn'})
+P.update({'warm': 0.001, 'tries': 1200, 'eng': {'zout': 'v', 'prow': 'v', 'af': 'a'}, 'tra': [[1, 0]] * 4})
+TURN = {"v": "av GA zout PAR Wn ovr XO RC*4 RD*4 af RC*2 BC*1 Tr*1 D*1 RC RD BC u+ Tr D RE*1 m r TT SC RE*1 mx pout RE*4 pf+ pg+ pu+ prow+ RE BE EQ+ L e*2 qf+ s+ of+ off+ e W*1+ Ln Lm W+",
+        "a": "GA zy zout Ta*1 Rd*1 BC*1 Tr*1 PAR af BC*1 Ta Tr Rd sC*1 BC sC cnu+ u+ uu+ KU+ RE BE*1 r13a r XH XO MK KOE Li BE*1 pu+ pv+ prow+ PG+ xp+ BE*1 qu+ qf+ rho+ MG+ BE act+ sE Gq+ rk+ Gn+ CE+ au+ pn+ zy+"}
+P['eng'].update({'prow': 'a', 'PAR': 'v'})
+P.update({'frl': [0, 0, 0, 0], 'frb': 'KC', 'zs': [4000., 1500.], 'afl': 2, 'zl': [0, 0, 0], 'ua': 1, 'aus': [1, 0, 0, 0], 'pgf': 1, 'fix': 50.0, 'pe': 0.42, 'ynlat': 0.0, 'xo': 'vvvvvv', 'ract': [1, 1, 1, 0]})
+P['eng']['PAR'] = 'a'
+P.update({'ul': [1, 1, 1], 'lna': [1, 1, 1, 0], 'tries': 1300, 'swaps': 1000, 'heat': 0.0002, 'seed': 12345, 'frl': [1, 1, 1, 0], 'dq': [[64, 16, 0, 0]] * 3 + [[0, 32, 0, 0]], 'tra': [[0, 0]] * 4, 'bitsC': ['aavvaavv'] * 4})
+CASES = [dict(fac=1.0, rem=1900.0, dl=1500.0, dr=220.0), dict(fac=1.1, g=1.15, sc=2.2, dr=300.0, rem=2600.0),
+         dict(fac=1.2, g=1.95, sc=5.4, rem=3000.0, dl=2000.0, dr=190.0), dict(fac=1.35, g=1.4, sc=4.5, rem=1600.0, dr=250.0),
+         dict(fac=1.1, g=1.3, sc=3.0, rem=3000.0, zs=[7000.0, 2500.0], dl=2000.0, dr=220.0, wake=90.0)]
+P.update({'ul': [1, 0, 0], 'ua': 0, 'xof': 0, 'xon': 2, 'zf': 0, 'bitsC': ['aavvaavv'] * 3 + ['aaaaaavv'], 'tries': 2200, 'swaps': 800})
+P['ce'].update({'K2': 'v'})
+P['zq'] = ['', '', '']
+CASES[4] = dict(fac=1.3, g=1.04, sc=1.7, rem=2200.0, zs=[6000.0, 2000.0], dl=1800.0, wake=30.0)
+P.update({'tries': 900, 'swaps': 500, 'heat': 0.0001, 'rsg': 1, 'rsv': 15, 'ul': [0, 0, 0], 'ua': 1, 'zl': [0, 0, 0], 'xon': 4, 'xok': 2, 'bitsC': ['aavvaavv'] * 4, 'dr': 250.0})
+P.update({'tries': 4200, 'swaps': 1500, 'warm': 0.0007, 'seed': 64, 'dq': [[64, 32, 0, 0]] * 3 + [[0, 48, 0, 0]], 'tra': [[1, 0]] * 4, 'bitsC': ['aaavaavv'] * 4})
+P.update({'afix': 22.0, 'cv': 1})
+CASES[3] = dict(fac=1.4, g=1.25, sc=3.0, rem=1800.0)
+TURN['v'] = TURN['v'].replace('BE EQ+', 'BE EQ*8+ Cc+ CE+ EQ+')
+TURN['a'] = TURN['a'].replace('prow+ PG+ xp+', 'prow+ xp+ PG+').replace('pn+ zy+', 'pn+ zy+ zout+')
+P['eng']['zout'] = 'a'
+P.update({'bitsE': ['aaaaaaaa'] * 3 + ['aaaaaavv'], 'zq': ['', 'a', 'a'], 'tries': 4000, 'swaps': 1200, 'afl': 0, 'ua': 0, 'zf': 1})
+P['ce'].update({'In': 'g', 'I20': 'g', 'o16': 'g', 'n8k': 'g'})
+TURN['a'] = TURN['a'].replace(' af ', ' ').replace('au+', 'au+ af+')
+CASES.append(dict(fac=1.15, g=1.08, sc=1.8, rem=2000.0, dr=260.0))
+P.update({'tries': 3200, 'swaps': 1000, 'seed': 11, 'warm': 0.001, 'pee': [1, 1, 1, 0], 'bitsE': ['aaaaaaav'] * 3 + ['aaaaaavv']})
+CASES[1] = dict(fac=1.45, g=1.06, sc=1.8, rem=2400.0)
+P.update({'bitsC': ['aaavaavv'] * 3 + ['aaaaaavv'], 'tries': 850, 'swaps': 3000, 'xoa': 3, 'pee': [0] * 4, 'bitsE': ['aaaaaaaa'] * 3 + ['aaaaaavv'], 'seed': 64, 'dq': [[64, 16, 0, 0]] * 3 + [[0, 48, 0, 0]]})
+for _c, _r in zip(CASES, (250.0, 320.0, 210.0, 280.0, 250.0)):
+    _c["dr"] = _r
 
 f32, bf, f16, i32, u16 = "float32", "bfloat16", "float16", "int32", "uint16"
 
@@ -36,24 +70,24 @@ def _sb(cols, d):
     return ("sbuf", [128, cols], d)
 
 
-DIAG = {"I": 1.0, "nI": -1.0, "bigI": float(BIG), "Ih": 0.5, "nIh": -0.5, "I2k": 2048.0, "n1280": -1280.0, "I11": LO, "In": NONE,
-        "n8k": -8192.0, "I64": 64.0, "I19": float(SC_), "I20": 2.0 * SC_, "I23": 16.0 * SC_, "IB": 18.0 * SC_}
-MATS = list(DIAG) + ["Pm", "P11", "Dlo", "Dhi", "Kx", "blk", "Bo", "Bw", "zb", "R16"]
+DIAG = {"I": 1.0, "nI": -1.0, "bigI": float(BIG), "Ih": 0.5, "nIh": -0.5, "I2k": 2048.0, "n1280": -1280.0, "I11": LO, "nI11": -LO, "In": NONE,
+        "n8k": -8192.0, "I64": 64.0, "I19": float(SC_), "I20": 2.0 * SC_, "I23": 16.0 * SC_}
+MATS = list(DIAG) + ["Pm", "P11", "Dlo", "Dhi", "blk", "Bo", "Bw", "zb", "R16"]
 SCRATCH = {
-    "G": _sb(GO + WC, f32), "L": _sb(WC, f32), "MK": _sb(WC, f32), "PAR": _sb(8 + 3 * M, f32),
-    "NB": _sb(V, i32), "XC": _sb(V, bf), "XO": _sb(W_, bf), "XH": _sb(1024, f16),
-    "K1": _sb(KK, bf), "K2": _sb(KK, bf), "wi": _sb(4, i32), "wf": _sb(4, f32),
+    "G": _sb(GO + WC, f32), "L": _sb(WC, f32), "MK": _sb(WC, f32), "PAR": _sb(W_ - M, f32),
+    "NB": _sb(V, i32), "XC": _sb(V, bf), "XO": _sb(W_, bf), "XH": _sb(1408, f16),
+    "K1": _sb(KK, bf), "K2": _sb(KK, bf), "KF": _sb(2 * KK, f32), "wi": _sb(4, i32), "wf": _sb(4, f32),
     "pin": _sb(16 * RO, i32), "pout": _sb(16 * RO, i32), "zin": _sb(M * RO, bf), "zout": _sb(M * RO, bf),
-    "GA": _sb(16 * M, f32), "RC": _sb(16 * M, f16), "RE": _sb(16 * M, f16), "BC": _sb(16 * M, bf), "BE": _sb(16 * M, bf), "EQ": _sb(16 * M, bf),
+    "GA": _sb(16 * M, f32), "RC": _sb(16 * M, f16), "RE": _sb(16 * M, f16), "BC": _sb(16 * M, bf), "BE": _sb(16 * M, bf), "EQ": ("sbuf", [128, 16, M], bf),
     "MX": _sb(128 * len(MATS), bf), "ones": _sb(512, bf), "zf": _sb(128, f32), "o16": _sb(128, f32), "If": _sb(128, f32),
-    "zn": _sb(256, bf), "grp": _sb(8, bf), "sel": _sb(32, f32), "Kn": _sb(128, bf), "Kt": _sb(128, bf), "c1k": _sb(32, bf),
+    "zn": _sb(128, bf), "grp": _sb(8, bf), "sel": _sb(32, f32), "Kn": _sb(128, bf), "Kt": _sb(128, bf), "c1k": _sb(32, bf),
     "SW": _sb(144, bf), "SA": _sb(144, bf), "S1": _sb(144, bf), "SM": _sb(144, bf), "RS": _sb(2048, bf),
     "SWP": _sb(512, f32), "sm": _sb(M, bf), "crow": _sb(512, bf), "thr": _sb(M, bf), "KOC": _sb(M * RO, f32), "lo": _sb(M, bf), "hi": _sb(M * RO, bf),
     "mkc": _sb(2 * M, f32), "pi": _sb(4, i32), "lane": _sb(4, f32), "srow": _sb(16, f32), "lm": _sb(16, f32),
     "pat": _sb(16, f32), "pm": _sb(16, f32), "dum": _sb(16, f32), "dug": _sb(16, f32),
-    "pf16": _sb(32, f16), "pf32": _sb(32, f32), "pu": _sb(32, u16), "pv": _sb(16, u16), "prow": _sb(M, f16), "KOE": _sb(2 * M, f32),
+    "pf16": _sb(32, f16), "pf32": _sb(32, f32), "pu": _sb(32, u16), "pv": _sb(16, u16), "prow": _sb(2 * M, f16), "two": _sb(M, bf), "pb": _sb(M, bf), "KOE": _sb(2 * M, f32),
     "act": _sb(2 * M, f16), "cnt": _sb(8, f32), "off": _sb(32, u16), "of2": _sb(16, u16),
-    "pn": _sb(16, i32), "ovr": _sb(32, f32), "xp": _sb(M, f16), "KU": _sb(2 * M, bf), "rho": _sb(2 * M, bf),
+    "pw": _sb(16, f32), "ovr": _sb(32, f32), "xp": _sb(M, f16), "KU": _sb(2 * M, bf), "rho": _sb(2 * M, bf),
     "CE": _sb(4 * M, f16), "Gn": _sb(M, f32), "PG": _sb(M, f16), "MG": _sb(M, bf), "Gq": _sb(M, f32), "rk": _sb(M, f32),
     "qu": _sb(16, u16), "qf": _sb(16, f32), "s2": _sb(16, f32), "Ta": _sb(2 * M, f32),
     "au": _sb(M, u16), "af": _sb(M, f16), "Tr": _sb(2 * M, f16), "Rd": _sb(2 * M, i32), "D": _sb(2 * M, bf),
@@ -84,7 +118,7 @@ def build_ops(g, core, T, topo, case=None):
         ops.append(dict(eng=eng, fn=fn, r=list(r), w=list(w), cost=cost, rnd=rnd[0], **kw))
 
     def vc(n, rate=1.0):
-        return (50 + max(64, n * rate) * 0.83) * fac
+        return (C["fix"] + max(64, n * rate) * 0.83) * fac
 
     def mat(name):
         j = MATS.index(name)
@@ -111,7 +145,7 @@ def build_ops(g, core, T, topo, case=None):
 
     def act_(o, i, fn, r, w, n, bias=0.0, scale=1.0, rate=1.0, acc=None):
         if acc is None:
-            add("a", lambda: g.scalar.activation(o, i, fn, bias=bias, scale=scale), r, w, vc(n, rate) + 15 * fac)
+            add("a", lambda: g.scalar.activation(o, i, fn, bias=bias, scale=scale), r, w, vc(n, rate) + C["afix"] * fac)
         else:
             add("a", lambda: g.scalar.activation(o, i, fn, bias=bias, scale=scale, accum_out=acc), r, w, vc(n, rate) + 35 * fac)
 
@@ -141,8 +175,7 @@ def build_ops(g, core, T, topo, case=None):
     def send(o, i, sem, r, w, slack=0.0):
         add("g", lambda: g.remote_dma(o, i, sem, T.sem.sent, pid, rid, mask), r, w, 300.0, sem=sem, inc=neng, lat=C["rem"] + slack, remote=True)
 
-    loads = {"p": (T.pin[:, 0:16], T.ps[:], "pin0", 8192), "x": (T.XC[:, 0:1024], T.xc[:, 0:1024], "XC0", 262144),
-             "y": (T.XC[:, 1024:V], T.xc[:, 1024:V], "XC1", 262144), "w": (T.wi[:, 0:1], T.wt[:], "wi", 512),
+    loads = {"p": (T.pin[:, 0:16], T.ps[:], "pin0", 8192), "x": (T.XC[:], T.xc[:], "XC", 524288), "w": (T.wi[:, 0:1], T.wt[:], "wi", 512),
              "z": (T.zin[:, 0:M], T.zi[:], "zin0", 65536), "k": (T.K1[:], T.kc[:], "K1", 131072), "n": (T.NB[:], T.nb[:], "NB", 1048576)}
     for x in P["loads"]:
         dma(loads[x][0], loads[x][1], [], [loads[x][2]], loads[x][3])
@@ -188,8 +221,8 @@ def build_ops(g, core, T, topo, case=None):
     spot(mat("Pm"), "Pm", [[-2, 64], [1, 2]], -1, 1.0, 128)
     iota(T.dum[:], "dum", [[16, 16]], DUM, 16)
     iota(T.lo[:], "lo", [[0, 8], [1, 32]], 0, M)
-    for t in range(RO):
-        iota(T.KOC[:, M * t:M * t + M], "KOC%d" % t, [[1, M]], K0 + V + M * t, M)
+    iota(T.KOC[:, 0:M], "KOC0", [[1, M]], K0 + V, M)
+    for t in range(2):
         iota(T.hi[:, M * t:M * t + M], "hi%d" % t, [[1, 8], [0, 32]], 8 * t, M)
     ts(T.lm[:], T.srow[:], T.lane[:, 0:1], None, A.is_equal, None, ["srow", "lane"], ["lm"], 16)
     for s in range(16):
@@ -229,7 +262,8 @@ def build_ops(g, core, T, topo, case=None):
         else:
             lin(e, mat(name), mat("I"), DIAG[name], 0.0, ["I"], [name], 128, vrate=0.5)
     if max(P["lna"]):
-        const(mat("Kx"), "Kx", -18.0 * SC_ / 128, 128, "g")
+        for h in range(2):
+            lin(ce("pb", "a"), T.pb[:, 128 * h:128 * h + 128], mat("blk"), 2.0, 0.0, ["blk"], ["pb%d" % h], 128, vrate=0.5)
     if max(P["pee"]):
         spot(T.If[:], "If", [[-1, 128]], 0, 1.0, 128, "zf")
     lin(ce("P11", "a"), mat("P11"), mat("Pm"), LO, 0.0, ["Pm"], ["P11"], 128, vrate=0.5)
@@ -241,19 +275,30 @@ def build_ops(g, core, T, topo, case=None):
     for name, c0, c1 in (("Kn", -H2 / 64, -H2 * LO / 64), ("Kt", -1.0 / 512, 2.0 ** -19)):
         mset(T[name][0:64, :], c0, [name + "0"], 128)
         mset(T[name][64:128, :], c1, [name + "1"], 128)
+    if P["cv"]:
+        pass
+    elif ce("two", "v") == "v":
+        mset(T.two[:], 2.0, ["two"], M)
+    else:
+        iota(T.two[:], "two", [[0, M]], 2, M)
     const(T.c1k[:, 0:16], "c1k", 1024.0, 16, "v")
     const(T.c1k[:, 16:32], "cm1k", -1024.0, 16, "g")
-    const(T.zn[:, 0:128], "zn0", 0.0, 128, "v")
-    lin(ce("zn1", "a"), T.zn[:, 128:256], mat("blk"), -1.0, 0.0, ["blk"], ["zn1"], 128, vrate=0.5)
-    lin(ce("grp", "a"), T.grp[:], grpcols("blk"), 1.0, 0.0, ["blk"], ["grp"], 8)
+    lin(ce("zn1", "a"), T.zn[:], mat("blk"), -1.0, 0.0, ["blk"], ["zn1"], 128, vrate=0.5)
+    act_(T.grp[:], grpcols("blk"), F.Sigmoid, ["blk"], ["grp"], 8, bias=-128.0, scale=256.0)
+    ops[-1]["cost"] += 1300.0 * fac
     band(T.sel[:, 0:8], "sel0", 0, 7, 1.0, "zf")
     band(T.sel[:, 8:16], "sel1", 8, 15, 1.0, "zf")
     for j in range(2):
         spot(T.sel[:, 16 + 8 * j:24 + 8 * j], "sel%d" % (2 + j), [[-16, 8]], -j, 1 / LO, 8, "zf")
-    lin(ce("K2", "a"), T.K2[:, 0:KK:2], T.K1[:, 1:KK:2], 1.0, 0.0, ["K1"], ["Ka"], 256, vrate=0.5)
-    lin(ce("K2", "a"), T.K2[:, 1:KK:2], T.K1[:, 0:KK:2], 1.0, 0.0, ["K1"], ["Kb"], 256, vrate=0.5)
+    if P["cv"]:
+        lin(ce("Kc", "a"), T.KF[:, 0:KK], T.K1[:], 1.0, H2, ["K1"], ["Kc"], KK)
+        lin(ce("K2", "a"), T.KF[:, KK:2 * KK:2], T.K1[:, 1:KK:2], 1.0, H2, ["K1"], ["Ka"], 256)
+        lin(ce("K2", "a"), T.KF[:, KK + 1:2 * KK:2], T.K1[:, 0:KK:2], 1.0, H2, ["K1"], ["Kb"], 256)
+    else:
+        lin(ce("K2", "a"), T.K2[:, 0:KK:2], T.K1[:, 1:KK:2], 1.0, 0.0, ["K1"], ["Ka"], 256, vrate=0.5)
+        lin(ce("K2", "a"), T.K2[:, 1:KK:2], T.K1[:, 0:KK:2], 1.0, 0.0, ["K1"], ["Kb"], 256, vrate=0.5)
     for h in range(2):
-        lin(P["wi"][h], T.G[:, GO + 1024 * h:GO + 1024 * h + 1024], T.XC[:, 1024 * h:1024 * h + 1024], 1 + LO, 0.0, ["XC%d" % h], ["Wi%d" % h], 1024)
+        lin(P["wi"][h], T.G[:, GO + 1024 * h:GO + 1024 * h + 1024], T.XC[:, 1024 * h:1024 * h + 1024], 1 + LO, 0.0, ["XC"], ["Wi%d" % h], 1024)
     for xh in range(2):
         for gl in range(2):
             q = 2 * xh + gl
@@ -263,11 +308,18 @@ def build_ops(g, core, T, topo, case=None):
     lin(ce("kcol", "v"), T.lane[:, 1:2], T.lane[:, 0:1], -16384.0, 15 * 16384.0, ["lane"], ["kcol"], 1)
     lin(ce("crow", "v"), T.crow[:, 0:M], T.ones[:, 0:M], 9216.0, T.lane[:, 1:2], ["ones", "kcol"], ["crow0"], M, vrate=0.5)
     lin(ce("crow", "v"), T.crow[:, M:2 * M], T.ones[:, 0:M], float(V), T.lane[:, 1:2], ["ones", "kcol"], ["crow1"], M, vrate=0.5)
-    const(T.PAR[:, 0:8], "PAR", -NONE, 8, "g", "zf")
-    for j in range(11):
-        iota(T.MK[:, M * j:M * j + M], "Mi%d" % j, [[0, M]], 0, M)
-    for t in (1, 2):
-        iota(T.mkc[:, M * (t - 1):M * t], "mkc%d" % t, [[0, M]], 64 * (t - 1), M)
+    iota(T.PAR[:, 0:8], "PAR", [[0, 8]], -int(NONE), 8)
+
+    def later(t):
+        def fill(o, name, pattern, base):
+            gp(lambda: g.iota(o, pattern, base, 0, allow_small_or_imprecise_dtypes=True), ["pout%d" % t], [name], M)
+        fill(T.KOC[:, M * (t + 1):M * (t + 2)], "KOC%d" % (t + 1), [[1, M]], K0 + V + M * (t + 1))
+        if t < 2:
+            fill(T.hi[:, M * (t + 2):M * (t + 3)], "hi%d" % (t + 2), [[1, 8], [0, 32]], 8 * (t + 2))
+            fill(T.mkc[:, M * t:M * t + M], "mkc%d" % (t + 1), [[0, M]], 64 * t)
+        if t == 0:
+            for j in range(11):
+                fill(T.MK[:, M * j:M * j + M], "Mi%d" % j, [[0, M]], 0)
 
     def sel(name, s):
         return T[name][:, 16 - s:144 - s]
@@ -275,19 +327,24 @@ def build_ops(g, core, T, topo, case=None):
     def cells(t):
         return ["W"] + (["Wn%d" % (t - 1)] if t else ["Wi0", "Wi1"])
 
-    def upath(t):
+    def upath(t, after=()):
         pr = t % 2
         l = slice(16 * pr, 16 * pr + 16)
         if t:
             mm(T.X1[:, 32:33], T.o16[:], T.cnt[:, 0:1], True, True, ["o16", "cnt"], ["X1"], 1, True)
         for s in range(16):
-            mm(T.X1[:, 0:16], sel("SW", s), T.zin[:, M * t + s:M * t + M:16], s == 0, s == 15, ["SW", "zin%d" % t], ["X1"], 16)
-        if t:
+            mm(T.X1[:, 0:16], sel("SW", s), T.zin[:, M * t + s:M * t + M:16], s == 0, s == 15, ["SW", "zin%d" % t] + list(after), ["X1"], 16)
+        if t and P["ua"]:
+            act_(T.cnt[:, 1:2], T.X1[:, 32:33], F.Identity, ["X1"], ["cnu"], 1, bias=float(1 << 18))
+            act_(T.u1[:], T.X1[:, 0:16], F.Identity, ["X1", "cnu"], ["u1"], 16, bias=T.cnt[:, 1:2])
+        elif t:
             ts(T.u1[:], T.X1[:, 0:16], T.X1[:, 32:33], float(1 << 18), A.add, A.add, ["X1"], ["u1"], 16)
         else:
             lin("v", T.u1[:], T.X1[:, 0:16], 1.0, float(1 << 18), ["X1"], ["u1"], 16)
         ts(T.u1[:], T.u1[:], KK - 1, None, A.bitwise_and, None, ["u1"], ["u1"], 16)
         lin("a", T.uu[:, l], T.u1[:], 1.0, 0.0, ["u1"], ["uu%d" % pr], 16)
+        if P["cv"]:
+            return
         act_(T.KU[:, 0:M], T.K1[:].indirect(T.uu[:, l]), F.Copy, ["K1", "uu%d" % pr], ["KU0"], M, rate=gc)
         act_(T.KU[:, M:2 * M], T.K2[:].indirect(T.uu[:, l]), F.Copy, ["Ka", "Kb", "uu%d" % pr], ["KU1"], M, rate=gc)
 
@@ -302,38 +359,49 @@ def build_ops(g, core, T, topo, case=None):
         wr = cells(t)
         Cf, Ef = T.CE[:, 2 * M * pr:2 * M * pr + M], T.CE[:, 2 * M * pr + M:2 * M * pr + 2 * M]
         lin("v", T.pf16[:, l], pin, 1.0, -1024.0, [pn], ["pf%d" % pr], 16)
-        lin("v", T.pf32[:, l], pin, 1.0, -1024.0, [pn], ["pg%d" % pr], 16)
+        if not P["pgf"]:
+            lin("v", T.pf32[:, l], pin, 1.0, -1024.0, [pn], ["pg%d" % pr], 16)
         lin("a", T.pu[:, l], pin, 1.0, 0.0, [pn], ["pu%d" % pr], 16)
         for s in range(16):
             mm(T.X0[:, s:M:16], T.RS[:, 128 * s:128 * s + 128], T.pf16[:, l], True, True, ["RS%d" % s, "pf%d" % pr], ["X0"], 16)
-        lin("a", T.prow[:], T.X0[:, 0:M], 1.0, 0.0, ["X0"], ["prow"], M)
-        if not P["lna"][t]:
-            lin("a", T.KOE[:, c], T.X0[:, 0:M], 1.0, float(K0 + 1024), ["X0"], ["KOE%d" % pr], M)
+        lin("a", T.prow[:, c], T.X0[:, 0:M], 1.0, 0.0, ["X0"], ["prow%d" % pr], M)
         mm(T.KC[:, 0:M], "nI", T.thr[:], True, False, ["thr"], ["KC"], M)
         for cc in range(16):
             n = M - 16 * cc
-            e0 = M * cc
-            ts(T.EQ[:, e0:e0 + n], T.prow[:, 16 * cc:M], T.pf32[:, 16 * pr + cc:16 * pr + cc + 1], None, A.is_equal, None, ["prow", "pg%d" % pr], ["EQ%d" % cc], n, P["half"])
+            ts(T.EQ[:, cc, 0:n], T.prow[:, M * pr + 16 * cc:M * pr + M], T["pf16" if P["pgf"] else "pf32"][:, 16 * pr + cc:16 * pr + cc + 1], None, A.is_equal, None, ["prow%d" % pr, ("pf%d" if P["pgf"] else "pg%d") % pr], ["EQ%d" % cc], n, P["half"])
             if cc < 15:
-                mm(T.KC[:, 16 * cc + 16:M], "Bo", T.EQ[:, e0 + 16:e0 + n], False, False, ["EQ%d" % cc], ["KC"], n - 16)
-            mm(T.KC[:, 16 * cc:16 * cc + 16], "Bw", T.EQ[:, e0:e0 + 16], False, cc == 15, ["EQ%d" % cc], ["KC"], 16)
+                mm(T.KC[:, 16 * cc + 16:M], "Bo", T.EQ[:, cc, 16:n], False, False, ["EQ%d" % cc], ["KC"], n - 16)
+            if cc % 4 == 3:
+                mm(T.KC[:, 16 * cc - 48:16 * cc + 16], "Bw", T.EQ[:, cc - 3:cc + 1, 0:16], False, cc == 15, ["EQ%d" % x for x in range(cc - 3, cc + 1)], ["KC"], 64)
         last = t == RO - 1
-        act_(T.act[:, c], T.KC[:, 0:M], F.Sigmoid, ["KC"], [ac] + ([] if last else ["cnt"]), M, bias=-128.0, scale=-256.0, acc=None if last else T.cnt[:, 0:1])
+        act_(T.act[:, c], T.KC[:, 0:M], F.Sigmoid, ["KC", "grp"], [ac] + ([] if last else ["cnt"]), M, bias=-128.0, scale=-256.0, acc=None if last else T.cnt[:, 0:1])
+        hx = H2 if P["cv"] else H1
         if t:
-            act_(T.xp[:], win.indirect(T.pu[:, l]), F.Identity, wr + ["pu%d" % pr], ["xp"], M, bias=H1, rate=gc)
+            act_(T.xp[:], win.indirect(T.pu[:, l]), F.Identity, wr + ["pu%d" % pr], ["xp"], M, bias=hx, rate=gc)
         else:
-            act_(T.xp[:], T.XC[:].indirect(T.pu[:, l]), F.Identity, ["XC0", "XC1", "pu0"], ["xp"], M, bias=H1, rate=gc)
-        for src, sn in ((T.KU, ["KU0", "KU1"]), (T.rho, ["rho"])):
+            act_(T.xp[:], T.XC[:].indirect(T.pu[:, l]), F.Identity, ["XC", "pu0"], ["xp"], M, bias=hx, rate=gc)
+        if P["cv"]:
+            tt(Cf, T.KF[:, 0:KK].indirect(T.uu[:, l]), T.xp[:], A.min, ["Kc", "uu%d" % pr, "xp"], ["Cc%d" % pr, cn], M, gc)
+            tt(Ef, T.KF[:, KK:2 * KK].indirect(T.uu[:, l]), T.xp[:], A.min, ["Ka", "Kb", "uu%d" % pr, "xp"], [cn], M, gc)
+        for src, sn in ((T.KU, ["KU0", "KU1"]), (T.rho, ["rho"])) * (not P["cv"]):
             mm(T.TC1[:], "nI", src[:], True, False, sn, ["TC1"], 512)
             for h in range(2):
                 mm(T.TC1[:, M * h:M * h + M], "I", T.xp[:], False, h == 1, ["xp"], ["TC1"], M)
             if sn[0] == "KU0":
                 act_(T.rho[:], T.TC1[:], F.Relu, ["TC1"], ["rho"], 512, bias=-H1)
-        lin("a", T.CE[:, 2 * M * pr:2 * M * pr + 2 * M], T.TC1[:], 1.0, H2 - H1, ["TC1"], [cn], 512)
+        if not P["cv"]:
+            lin("a", T.CE[:, 2 * M * pr:2 * M * pr + 2 * M], T.TC1[:], 1.0, H2 - H1, ["TC1"], [cn], 512)
         gn = T.TC0[:, 0:M]
-        mm(gn, T.Kn[:], T.ones[:, 0:M], True, False, ["Kn0", "Kn1", "ones"], ["TC0"], M)
-        mm(gn, "I", Cf, False, False, [cn], ["TC0", "gn0"], M)
-        mm(gn, "I11", Ef, False, False, [cn, "gn0"], ["TC0"], M)
+        if P["gnx"] and not P["cv"]:
+            mm(gn, T.Kn[:], T.two[:], True, False, ["Kn0", "Kn1", "two"], ["TC0"], M)
+            mm(gn, "I", T.xp[:], False, False, ["xp"], ["TC0", "gn0"], M)
+            mm(gn, "I11", T.xp[:], False, False, ["xp", "gn0"], ["TC0"], M)
+            mm(gn, "nI", T.rho[:, 0:M], False, False, ["rho", "gn0"], ["TC0"], M)
+            mm(gn, "nI11", T.rho[:, M:2 * M], False, False, ["rho", "gn0"], ["TC0"], M)
+        else:
+            mm(gn, T.Kn[:], T.ones[:, 0:M], True, False, ["Kn0", "Kn1", "ones"], ["TC0"], M)
+            mm(gn, "I", Cf, False, False, [cn], ["TC0", "gn0"], M)
+            mm(gn, "I11", Ef, False, False, [cn, "gn0"], ["TC0"], M)
         mm(gn, "Dlo", T.lo[:], False, False, ["lo", "gn0"], ["TC0"], M)
         mm(gn, "Dhi", T.hi[:, M * t:M * t + M], False, True, ["hi%d" % t, "gn0"], ["TC0"], M)
         lin("a", T.Gn[:], gn, 1.0, 0.0, ["TC0"], ["Gn"], M)
@@ -347,7 +415,12 @@ def build_ops(g, core, T, topo, case=None):
             lin("a", T.qu[:], ql, 1.0, 0.0, ["X1"], ["qu"], 16)
             act_(T.qf[:], ql, F.Abs, ["X1"], ["qf"], 16, bias=float(GO))
             act_(T.Gq[:], win.indirect(T.qu[:]), F.Copy, wr + ["qu"], ["Gq"], M, rate=gc)
-            lin("a", T.rk[:], T.rho[:, 0:M], LO, 0.0, ["rho"], ["rk"], M)
+            if P["cv"]:
+                mm(T.TC1[:, 0:M], "I11", T.xp[:], True, False, ["xp"], ["TC1"], M)
+                mm(T.TC1[:, 0:M], "nI11", Cf, False, True, ["Cc%d" % pr], ["TC1"], M)
+                lin("a", T.rk[:], T.TC1[:, 0:M], 1.0, 0.0, ["TC1"], ["rk"], M)
+            else:
+                lin("a", T.rk[:], T.rho[:, 0:M], LO, 0.0, ["rho"], ["rk"], M)
             if t > 1:
                 act_(T.MG[:], T.MK[:, 0:hi].indirect(T.qu[:]), F.Copy, ["MK", "qu"], ["MG"], M, rate=gc)
                 v2 = T.X1[:, 16:32]
@@ -367,9 +440,9 @@ def build_ops(g, core, T, topo, case=None):
             tt(T.of2[:], T.s2[:], T.dug[:], A.min, ["s2", "dug"], ["of2"], 16)
         tt(T.off[:, l], vl, T.dum[:], A.min, ["X0", "dum"], ["off%d" % pr], 16)
         if not last:
-            lin("a", T.pn[:], pin, 1.0, float(OV + 1), [pn], ["pn"], 16)
-            ts(T.pn[:], T.pn[:], OV + V - 1, None, A.bitwise_and, None, ["pn"], ["pn"], 16)
-            tt(T.ovr[:, l], vl, T.pn[:], A.min, ["X0", "pn"], ["ovr%d" % pr], 16)
+            act_(T.pw[:], pin, F.Sign, [pn], ["pn"], 16, bias=1.5 - V)
+            act_(T.pw[:], T.pw[:], F.Identity, ["pn"], ["pn"], 16, bias=OV - BIG + 1.0 - V / 2, scale=-V / 2)
+            tt(T.ovr[:, l], vl, T.pw[:], A.add, ["X0", "pn"], ["ovr%d" % pr], 16)
         if t:
             tt(T.G[:].indirect(T.of2[:]), T.Gq[:], T.rk[:], A.subtract, ["Gq", "rk", "of2"], wr, M, sc)
         copy(T.G[:, GO:GO + WC].indirect(T.off[:, l]), T.Gn[:], ["Gn", "off%d" % pr], wr, M, sc)
@@ -381,35 +454,47 @@ def build_ops(g, core, T, topo, case=None):
         ac, cn = "act%d" % pr, "CE%d" % pr
         Ef = T.CE[:, 2 * M * pr + M:2 * M * pr + 2 * M]
         hi = V + M * t
-        es, pq = T.TE0[:, 0:M], T.TE0[:, M:2 * M]
+        fb = P["frb"]
+        es, pq = T[fb][:, 0:M], T[fb][:, M:2 * M]
         if P["lna"][t]:
-            mm(pq, "I", T.prow[:], True, False, ["prow"], ["TE0"], M)
-            mm(pq, "I23", T.act[:, c], False, True, [ac], ["TE0"], M)
-            act_(T.KOE[:, c], pq, F.Relu, ["TE0"], ["KOE%d" % pr], M, bias=K0 + 1024.0 - DIAG["I23"])
+            mm(pq, "I", T.prow[:, c], True, False, ["prow%d" % pr], [fb], M)
+            mm(pq, "I23", T.act[:, c], False, True, [ac], [fb], M)
+            act_(T.KOE[:, c], pq, F.Relu, [fb], ["KOE%d" % pr], M, bias=K0 + 1024.0 - DIAG["I23"])
         if t == RO - 1:
-            mm(es, T.Kn[0:64, :], T.ones[0:64, 0:M], True, False, ["Kn0", "ones"], ["TE0"], M)
-            mm(es, "I", Ef, False, True, [cn], ["TE0"], M)
-            tt(T.XO[:, hi:hi + M], es, T.act[:, c], A.mult, ["TE0", ac], ["XO6"], M)
+            mm(es, T.Kn[0:64, :], T.ones[0:64, 0:M], True, False, ["Kn0", "ones"], [fb], M)
+            mm(es, "I", Ef, False, True, [cn], [fb], M)
+            tt(T.XO[:, hi:hi + M], es, T.act[:, c], A.mult, [fb, ac], ["XO6"], M)
             return
-        mm(es, T.Kn[:], T.ones[:, 0:M], True, False, ["Kn0", "Kn1", "ones"], ["TE0"], M)
-        mm(es, "I", Ef, False, False, [cn], ["TE0"], M)
-        mm(es, "I11", Ef, False, True, [cn], ["TE0"], M)
-        mm(pq, "I", T.prow[:], True, False, ["prow"], ["TE0"], M)
-        mm(pq, "In", T.act[:, c], False, True, [ac], ["TE0"], M)
-        tt(T.G[:, GO + hi:GO + hi + M], es, T.act[:, c], A.mult, ["TE0", ac, "W"], ["Wn%d" % t], M)
-        lin("a", T.PAR[:, 1 + M * t:1 + M * t + M], pq, 1.0, -NONE, ["TE0"], ["PAR"], M)
-        if t:
+        mm(es, T.Kn[:], T.ones[:, 0:M], True, False, ["Kn0", "Kn1", "ones"], [fb], M)
+        mm(es, "I", Ef, False, False, [cn], [fb], M)
+        mm(es, "I11", Ef, False, True, [cn], [fb], M)
+        mm(pq, "I", T.prow[:, c], True, False, ["prow%d" % pr], [fb], M)
+        mm(pq, "In", T.act[:, c], False, True, [ac], [fb], M)
+        tt(T.G[:, GO + hi:GO + hi + M], es, T.act[:, c], A.mult, [fb, ac, "W"], ["Wn%d" % t], M)
+        lin("a", T.PAR[:, 1 + M * t:1 + M * t + M], pq, 1.0, -NONE, [fb], ["PAR"], M)
+
+    def marks(t):
+        pr = t % 2
+        l = slice(16 * pr, 16 * pr + 16)
+        c = slice(M * pr, M * pr + M)
+        if not P["lna"][t]:
+            lin("a", T.KOE[:, c], T.prow[:, c], 1.0, float(K0 + 1024), ["prow%d" % pr, "sC0", "sC1"], ["KOE%d" % pr], M)
+        if 0 < t < RO - 1:
             add("a", lambda: g.scalar.activation(T.MK[:].indirect(T.off[:, l]), T.mkc[:, M * (t - 1):M * t], F.Sigmoid),
-                ["mkc%d" % t, "off%d" % pr], ["MK"] + (["Mi%d" % j for j in range(11)] if t == 1 else []), vc(M, sc) + 15 * fac)
+                ["mkc%d" % t, "off%d" % pr, "sC0", "sC1"], ["MK"] + (["Mi%d" % j for j in range(11)] if t == 1 else []), vc(M, sc) + 15 * fac)
 
     def lists(t):
         pr = t % 2
         l = slice(16 * pr, 16 * pr + 16)
         win = T.NB[:] if t == 0 else T.L[:, 0:V + M * t]
-        lin("a", T.au[:], win.indirect(T.pu[:, l]), 1.0, 0.0, (["NB"] if t == 0 else ["L", "Ln"]) + ["pu%d" % pr], ["au"], M, gc)
-        lin("v", T.af[:], T.au[:], 1.0, -1024.0, ["au"], ["af"], M, vrate=0.5)
+        rd = (["NB"] if t == 0 else ["L", "Ln"]) + ["pu%d" % pr]
+        if P["aus"][t]:
+            copy(T.au[:, 0:64], win.indirect(T.pu[:, 16 * pr:16 * pr + 4]), rd + ["zout0"] * P["zf"], ["av"], 64, gc)
+            lin("a", T.au[:, 64:M], win.indirect(T.pu[:, 16 * pr + 4:16 * pr + 16]), 1.0, 0.0, rd, ["au"], M - 64, gc)
+        else:
+            lin("a", T.au[:], win.indirect(T.pu[:, l]), 1.0, 0.0, rd, ["au", "av"], M, gc)
 
-    def zpath(t):
+    def zpath(t, after=()):
         pr = t % 2
         c = slice(M * pr, M * pr + M)
         z = T.zin[:, M * t:M * t + M]
@@ -418,12 +503,12 @@ def build_ops(g, core, T, topo, case=None):
         mm(y0, "nIh", z, True, False, [zn], ["KE"], M)
         mm(y0, "I2k", T.act[:, c], False, False, [ac], ["KE"], M)
         mm(y0, "Ih", T.CE[:, 2 * M * pr:2 * M * pr + M], False, True, [cn], ["KE"], M)
-        act_(T.zy[:], y0, F.Relu, ["KE"], ["zy"], M, bias=1279.75 - 2048.0 - H2 / 2)
+        act_(T.zy[:], y0, F.Relu, ["KE"] + list(after), ["zy"], M, bias=1279.75 - 2048.0 - H2 / 2)
         mm(y1, "I", z, True, False, [zn], ["KE"], M)
         mm(y1, "n1280", T.act[:, c], False, False, [ac], ["KE"], M)
         mm(y1, "I", T.zy[:], False, True, ["zy"], ["KE"], M)
         lin("a", T.zout[:, M * t:M * t + M], y1, 1.0, 0.0, ["KE"], ["zout%d" % t], M)
-        send(T.zin[:, M * (t + 1):M * (t + 2)], T.zout[:, M * t:M * t + M], T.sem["za%d" % (t + 1)], ["zout%d" % t], ["zin%d" % (t + 1)], P["zs"][min(t, 1)])
+        send(T.zin[:, M * (t + 1):M * (t + 2)], T.zout[:, M * t:M * t + M], T.sem["za%d" % (t + 1)], ["zout%d" % t], ["zin%d" % (t + 1)], C["zs"][min(t, 1)])
 
     def limits(bank, child, cn, rep, more=None):
         n = 512 // rep
@@ -464,14 +549,35 @@ def build_ops(g, core, T, topo, case=None):
         for x in range(2):
             mm(T[bank][:, o + 128:o + 256], "nI", T.Tr[:, M * h + 128 * x:M * h + 128 * x + 128], False, False, ["Tr%d" % h], [bank], 128)
 
+    def extents(t):
+        n = (W_ - M) // P["xon"]
+        for j in range(P["xon"]):
+            if j >= P["xoa"]:
+                xs = slice(n * (j % 2), n * (j % 2) + n)
+                act_(T.XH[:, xs], T.G[:, GO + n * j:GO + n * j + n], F.Identity, ["W", "Wn%d" % (t - 1)], ["XH%d" % (j % 2)], n, bias=H1)
+                act_(T.XO[:, n * j:n * j + n], T.XH[:, xs], F.Identity, ["XH%d" % (j % 2)], ["XO%d" % j], n, bias=-H1)
+                continue
+            ts(T.XO[:, n * j:n * j + n], T.G[:, GO + n * j:GO + n * j + n], RND, RND, A.add, A.subtract, ["W", "Wn%d" % (t - 1)], ["XO%d" % j], n)
+        names = ["XO%d" % j for j in range(P["xon"])] + ["XO6"]
+        k = P["xon"] // 2
+        dma(T.yx[:, 0:n * k], T.XO[:, 0:n * k], names[:k], [], 128 * n * k * 2)
+        dma(T.yx[:, n * k:W_], T.XO[:, n * k:W_], names[k:], [], 128 * (W_ - n * k) * 2)
+        return names[:P["xok"]]
+
     def scores(t):
         pr = t % 2
         cn = "CE%d" % pr
         hi = V + M * t
         wr = ["W"] + (["Wn%d" % (t - 1)] if t else [])
-        for h in range(2):
-            limits("TC%d" % h, T.CE[:, 2 * M * pr + 128 * h:2 * M * pr + 128 * h + 128], cn, 4)
+        rep2 = P["rep2"][t]
+        if rep2:
+            limits("TC1", T.CE[:, 2 * M * pr:2 * M * pr + M], cn, 2)
+        else:
+            for h in range(2):
+                limits("TC%d" % h, T.CE[:, 2 * M * pr + 128 * h:2 * M * pr + 128 * h + 128], cn, 4)
         dq, d1, s0, s1 = P["dq"][t]
+        if rep2:
+            s0 = s1 = 0
         gq = [[], [], [], []]
         cuts = sorted(set([0, dq, 128, 128 + d1, M] + ([64] if s0 else []) + ([192] if s1 else [])))
         for i0, i1 in zip(cuts, cuts[1:]):
@@ -480,11 +586,16 @@ def build_ops(g, core, T, topo, case=None):
             for q in range(i0 // 64, (i1 + 63) // 64):
                 gq[q].append(nm)
             win = T.G[:, GO:GO + hi].indirect(T.au[:, i0:i1])
+            if t < RO - 1 and e in P["zq"][t]:
+                wr = wr + ["zout%d" % t]
             if e == "v":
-                copy(T.GA[:, 16 * i0:16 * i1], win, wr + ["au"], [nm], 16 * (i1 - i0), gc)
+                copy(T.GA[:, 16 * i0:16 * i1], win, wr + ["av"] + ["au"] * (i1 > 64), [nm], 16 * (i1 - i0), gc)
             else:
-                act_(T.GA[:, 16 * i0:16 * i1], win, F.Copy, wr + ["au"], [nm], 16 * (i1 - i0), rate=gc)
+                act_(T.GA[:, 16 * i0:16 * i1], win, F.Copy, wr + ["au", "av"], [nm], 16 * (i1 - i0), rate=gc)
         ga = [gq[0] + gq[1], gq[2] + gq[3]]
+        lin("v", T.af[:], T.au[:], 1.0, -1024.0, ["au", "av"] + ga[P["afl"] - 1] * (P["afl"] > 0), ["af"], M, vrate=0.5)
+        if t < RO - 1 and P["zl"][t]:
+            zpath(t, ga[P["zl"][t] - 1])
         for h in range(2):
             lp = P["LPb"][h]
             hs = slice(M * h, M * h + M)
@@ -498,24 +609,36 @@ def build_ops(g, core, T, topo, case=None):
                 ts(T.Tr[:, hs], T[lp][:, 0:M], RND, RND, A.add, A.subtract, [lp], ["Tr%d" % h], M)
             tt(T.D[:, hs], T[lp][:, M:2 * M], T.Rd[:, hs], A.subtract, [lp, "Rd%d" % h], ["D%d" % h], M)
         key_open("KC")
+        stored = extents(t) if t == RO - 1 else []
+
+        def cols(x, j):
+            if rep2:
+                o = 512 * x + M * (j % 2)
+                return slice(o + j // 2, o + M, 2)
+            return slice(512 * x + j, 512 * x + 512, 4)
         for h in range(2):
             sb = P["SCb"][h]
-            mm(T[sb][:, 0:M], T.CE[:, 2 * M * pr + 128 * h:2 * M * pr + 128 * h + 128], T.zn[:], True, False, [cn, "zn0", "zn1"], [sb], M)
+            mm(T[sb][:, 128:M], T.CE[:, 2 * M * pr + 128 * h:2 * M * pr + 128 * h + 128], T.zn[:], True, False, [cn, "zn1"], [sb], 128)
             for r in range(4):
                 x = 4 * h + r
-                if (s0, s1)[h]:
+                if rep2:
+                    for q in range(2):
+                        tt(T.RC[:, 512 * x + M * q:512 * x + M * q + M], T.GA[:, 2048 * h + r + 4 * q:2048 * h + 2048:8], T.TC1[:, M * h:M * h + M], A.add,
+                           ga[h] + ["TC1"], [("RC%d", "RD%d")[q] % x], M)
+                elif (s0, s1)[h]:
                     for q in range(2):
                         o = 2048 * h + 1024 * q
                         tt(T.RC[:, 512 * x + M * q:512 * x + M * q + M], T.GA[:, o + r:o + 1024:4], T["TC%d" % h][:, M * q:M * q + M], A.add,
                            gq[2 * h + q] + ["TC%d" % h], [("RC%d", "RD%d")[q] % x], M)
                 else:
-                    tt(T.RC[:, 512 * x:512 * x + 512], T.GA[:, 2048 * h + r:2048 * h + 2048:4], T["TC%d" % h][:], A.add, ga[h] + ["TC%d" % h], ["RC%d" % x, "RD%d" % x], 512)
+                    tt(T.RC[:, 512 * x:512 * x + 512], T.GA[:, 2048 * h + r:2048 * h + 2048:4], T["TC%d" % h][:], A.add,
+                       ga[h] + ["TC%d" % h] + (stored if h >= P["xof"] else []), ["RC%d" % x, "RD%d" % x], 512)
                 for j in range(4):
-                    mm(T[sb][:, 128 + r + 4 * j:M:16], T.RC[:, 512 * x + j:512 * x + 512:4], T.grp[:], False, False, ["grp", "RC%d" % x, "RD%d" % x], [sb], 8)
+                    mm(T[sb][:, 128 + r + 4 * j:M:16], T.RC[:, cols(x, j)], T.grp[:], False, False, ["grp", "RC%d" % x, "RD%d" % x], [sb], 8)
 
             def sums(x, sb=sb):
                 for j in range(4):
-                    mm(T[sb][:, x % 4 + 4 * j:128:16], T.BC[:, 512 * x + j:512 * x + 512:4], T.grp[:], False, False, ["grp", "BC%d" % x], [sb], 8)
+                    mm(T[sb][:, x % 4 + 4 * j:128:16], T.BC[:, cols(x, j)], T.grp[:], False, False, ["grp", "BC%d" % x], [sb], 8)
             bits("RC", "BC", P["bitsC"][t], 4 * h, 4 * h + 4, {"rn": lambda x: ["RC%d" % x, "RD%d" % x], "sum": sums})
             less_sums(sb, 0, h)
             lin("a", T.sC[:, M * h:M * h + M], T[sb][:, 0:M], 1.0, 0.0, [sb], ["sC%d" % h], M)
@@ -551,33 +674,38 @@ def build_ops(g, core, T, topo, case=None):
         cn, ac = "CE%d" % pr, "act%d" % pr
         e0 = 2 * M * pr + M
         limits("TE0", T.CE[:, e0:e0 + M], cn, 2)
-        mm(T.TE1[:], "zb", T.ones[:], True, False, ["ones"], ["TE1"], 512)
+        if P["lna"][t]:
+            for h in range(2):
+                mm(T.TE1[:, M * h:M * h + M], T.act[:, M * pr + 128 * h:M * pr + 128 * h + 128], T.pb[:], h == 0, False, [ac, "pb0", "pb1"], ["TE1"], M)
         for h in range(2):
-            mm(T.TE1[:, M * h + 128:M * h + M], T.CE[:, e0 + 128 * h:e0 + 128 * h + 128], T.zn[:, 128:256], False, False, [cn, "zn1"], ["TE1"], 128)
+            mm(T.TE1[:, M * h + 128:M * h + M], T.CE[:, e0 + 128 * h:e0 + 128 * h + 128], T.zn[:], h == 0 and not P["lna"][t], False, [cn, "zn1"], ["TE1"], 128)
+        for h in range(2):
             less_sums("TE1", M * h, h)
 
         def sums(x, buf="BE", o=0):
             for j in range(2):
                 for h in range(2):
-                    mm(T.TE1[:, M * h + o + x + 8 * j:M * h + o + 128:16], T[buf][:, 512 * x + M * h + j:512 * x + M * h + M:2], T.grp[:], False, False, ["grp", "%s%d" % (buf, x)], ["TE1"], 8)
+                    mm(T.TE1[:, M * h + o + x + 8 * j:M * h + o + 128:16], T[buf][:, 512 * x + M * h + j:512 * x + M * h + M:2], T.grp[:], False, False, ["grp"] + (re(x) if o else ["BE%d" % x]), ["TE1"], 8)
+
+        def re(x):
+            return ["RE%d" % (10 * q + x) for q in range(P["esp"])]
         for x in range(8):
-            if x >= 8 - P["pee"][t]:
-                b = "TC%d" % (x % 2)
+            if x < P["pee"][t]:
+                b = "TC%d" % ((x + 1) % 2)
                 limits(b, T.CE[:, e0:e0 + M], cn, 2, "lim")
                 for q in range(4):
                     mm(T[b][:, 128 * q:128 * q + 128], T.If[:], T.GA[:, 1024 * q + x:1024 * q + 1024:8], False, q == 3, ga[q // 2] + ["If", "lim"], [b], 128, True)
-                act_(T.RE[:, 512 * x:512 * x + 512], T[b][:], F.Identity, [b], ["RE%d" % x], 512)
+                act_(T.RE[:, 512 * x:512 * x + 512], T[b][:], F.Identity, [b], re(x), 512)
             else:
-                tt(T.RE[:, 512 * x:512 * x + 512], T.GA[:, x:16 * M:8], T.TE0[:], A.add, ga[0] + ga[1] + ["TE0"], ["RE%d" % x], 512)
+                n = 512 // P["esp"]
+                for q in range(P["esp"]):
+                    tt(T.RE[:, 512 * x + n * q:512 * x + n * q + n], T.GA[:, 8 * n * q + x:8 * n * q + 8 * n:8], T.TE0[:, n * q:n * q + n], A.add,
+                       ga[0] + ga[1] + ["TE0"], [re(x)[q]], n)
             sums(x, "RE", 128)
-        bits("RE", "BE", P["bitsE"][t], 0, 8, {"rn": lambda x: ["RE%d" % x], "sum": sums})
-        lin("a", T.sE[:], T.TE1[:], 1.0, 0.0, ["TE1"], ["sE0", "sE1"], 512)
+        bits("RE", "BE", P["bitsE"][t], 0, 8, {"rn": re, "sum": sums})
+        lin("a", T.sE[:], T.TE1[:], 1.0, -32.0 * P["lna"][t], ["TE1"], ["sE0", "sE1"], 512)
         key_open("KE")
-        if P["lna"][t]:
-            mm(T.KE[:], "Kx", T.ones[:], False, False, ["ones"], ["KE"], 512)
-            for x in range(2):
-                mm(T.KE[:, M * x:M * x + M], "IB", T.act[:, c], False, False, [ac], ["KE"], M)
-        else:
+        if not P["lna"][t]:
             mm(T.TE0[:, 0:M], "I", T.act[:, c], True, True, [ac], ["TE0"], M)
         for h in range(2):
             key_scores("KE", "sE", h)
@@ -590,40 +718,79 @@ def build_ops(g, core, T, topo, case=None):
         else:
             tt(T.L[:, n0:n0 + M], T.TE0[:, 0:M], T.e3[:], A.mult, ["e3", "TE0"], ["Ln"], M)
 
+    def last_e(t, ga):
+        pr = t % 2
+        cn, ac = "CE%d" % pr, "act%d" % pr
+        e0, n0 = 2 * M * pr + M, V + M * t
+        for h in range(2):
+            lim, sb, key, row = "TC%d" % h, ("TE1", "TE0")[h], ("KE", "KC")[h], ("X0", "X1")[h]
+            hs = slice(128 * h, 128 * h + 128)
+            child = T.CE[:, e0 + 128 * h:e0 + 128 * h + 128]
+            limits(lim, child, cn, 4)
+            mm(T[sb][:, 128:M], child, T.zn[:], True, False, [cn, "zn1"], [sb], 128)
+            less_sums(sb, 0, h)
+
+            def sums(x, buf="BE", o=0, sb=sb):
+                for j in range(4):
+                    mm(T[sb][:, o + x % 4 + 4 * j:o + 128:16], T[buf][:, 512 * x + j:512 * x + 512:4], T.grp[:], False, False, ["grp", "%s%d" % (buf, x)], [sb], 8)
+            for x in range(4 * h, 4 * h + 4):
+                tt(T.RE[:, 512 * x:512 * x + 512], T.GA[:, 2048 * h + x % 4:2048 * h + 2048:4], T[lim][:], A.add, ga[h] + [lim], ["RE%d" % x], 512)
+                sums(x, "RE", 128)
+            bits("RE", "BE", P["bitsE"][t], 4 * h, 4 * h + 4, {"rn": lambda x: ["RE%d" % x], "sum": sums})
+            lin("a", T.sE[:, M * h:M * h + M], T[sb][:, 0:M], 1.0, 0.0, [sb], ["sE%d" % h], M)
+            mm(T[key][:, 0:M], "I", T.crow[:, 128:384], True, False, ["crow0", "crow1"], [key], M)
+            mm(T[key][:, 0:128], "I", T.af[:, hs], False, False, ["af"], [key], 128)
+            for d, w in enumerate(("I64", "I2k")):
+                mm(T[key][:, 128:M], T.D[:, M * h + 128 * d:M * h + 128 * d + 128], w, False, False, ["D%d" % h], [key], 128)
+            for x, w in enumerate(("I19", "I20")):
+                mm(T[key][:, 128 * x:128 * x + 128], T.sE[:, M * h + 128 * x:M * h + 128 * x + 128], w, False, x == 1, ["sE%d" % h], [key], 128)
+            mm(T[row][:, 0:128], "I", T.act[:, M * pr + 128 * h:M * pr + 128 * h + 128], True, True, [ac], [row], 128)
+            tt(T.e1[:, hs], T[key][:, 0:128], T.KOE[:, M * pr + 128 * h:M * pr + 128 * h + 128], A.max, [key, "KOE%d" % pr], ["e1%d" % h], 128)
+            tt(T.e2[:, hs], T[key][:, 128:M], T.e1[:, hs], A.max, [key, "e1%d" % h], ["e2%d" % h], 128)
+            ts(T.e3[:, hs], T.e2[:, hs], 4095, None, A.bitwise_and, None, ["e2%d" % h], ["e3%d" % h], 128)
+            cs = slice(n0 + 128 * h, n0 + 128 * h + 128)
+            tt(T.L[:, cs], T[row][:, 0:128], T.e3[:, hs], A.mult, ["e3%d" % h, row, "Ln"], ["Lm%d" % h], 128)
+            if P["eh"] == 2:
+                dma(T.yn[:, cs], T.L[:, cs], ["Lm%d" % h], [], 128 * 128 * 4)
+        if P["eh"] == 1:
+            dma(T.yn[:, n0:W_], T.L[:, n0:W_], ["Lm0", "Lm1"], [], 128 * M * 4)
+
     rnd[0] = 0
     upath(0)
     prep(0)
+    if P["zf"]:
+        zpath(0)
     for t in range(RO):
         lists(t)
-        if t < RO - 1:
+        if t < RO - 1 and not P["zl"][t] and not (t == 0 and P["zf"]):
             zpath(t)
-        fresh(t)
+        if not P["frl"][t]:
+            fresh(t)
         ga = scores(t)
+        marks(t)
         if t == 0:
             for j in range(4):
                 cs = slice(512 * j, 512 * j + 512)
                 lin(P["li"][j], T.L[:, cs], T.NB[:, cs], 1.0, 0.0, ["NB"], ["Li%d" % j], 512)
-        if t < RO - 1:
+        if t < RO - 1 and not P["ul"][t]:
+            rnd[0] = t + 1
             upath(t + 1)
-        else:
-            for j in range(6):
-                cs = slice(512 * j, min(512 * j + 512, W_ - M))
-                n = cs.stop - cs.start
-                src = T.G[:, GO + cs.start:GO + cs.stop]
-                rd = ["W", "Wn%d" % (t - 1)]
-                if P["xo"][j] == "v":
-                    ts(T.XO[:, cs], src, RND, RND, A.add, A.subtract, rd, ["XO%d" % j], n)
-                else:
-                    xs = slice(512 * (j % 2), 512 * (j % 2) + n)
-                    act_(T.XH[:, xs], src, F.Identity, rd, ["XH%d" % (j % 2)], n, bias=H1)
-                    lin("a" if P["xo"][j] == "a" else "v", T.XO[:, cs], T.XH[:, xs], 1.0, -H1, ["XH%d" % (j % 2)], ["XO%d" % j], n, vrate=0.5)
-                if j % 3 == 2:
-                    cs = slice(512 * j - 1024, 512 * j + 512)
-                    dma(T.yx[:, cs], T.XO[:, cs], ["XO%d" % x for x in range(j - 2, j + 1)] + (["XO6"] if j == 5 else []), [], 128 * 1536 * 2)
+            rnd[0] = t
         post_c(t)
+        if t < RO - 1:
+            later(t)
+            if P["ul"][t]:
+                rnd[0] = t + 1
+                upath(t + 1, ["mx"])
+                rnd[0] = t
+            if P["frl"][t]:
+                fresh(t)
         if t == RO - 1:
             n0 = V + M * t
             dma(T.yn[:, 0:n0], T.L[:, 0:n0], ["L"], [], 128 * n0 * 4, P["ynlat"])
+            if P["eh"]:
+                last_e(t, ga)
+                break
         part_e(t, ga)
         if t < RO - 1:
             rnd[0] = t + 1
@@ -707,6 +874,17 @@ def link(ops):
         hard.discard(n)
         soft.discard(n)
         o["hard"], o["soft"] = sorted(hard), sorted(soft - hard)
+    done, issued = [], []
+    for o in ops:
+        d = i = 0
+        for m in o["hard"] + o["soft"]:
+            if not ops[m].get("remote"):
+                d |= done[m]
+                i |= issued[m]
+        o["hard"] = [m for m in o["hard"] if not d >> m & 1]
+        o["soft"] = [m for m in o["soft"] if not (d | i) >> m & 1]
+        done.append(d | sum(1 << m for m in o["hard"]))
+        issued.append(i | sum(1 << m for m in o["soft"]))
 
 
 def replay(ops, order, costs):
@@ -729,6 +907,69 @@ def replay(ops, order, costs):
     return max(done)
 
 
+def blocked(ops, order, costs):
+    n = len(ops)
+    done, endq, free, dmafree = [0.0] * n, [0.0] * n, {}, 0.0
+    why, ready, before, last = [None] * n, [0.0] * n, [None] * n, {}
+    for j in order:
+        o = ops[j]
+        cost, lat, bw = costs[j]
+        st = 0.0
+        for m in o["hard"]:
+            if done[m] + HOP > st:
+                st, why[j] = done[m] + HOP, m
+        for m in o["soft"]:
+            if endq[m] > st:
+                st, why[j] = endq[m], m
+        ready[j], before[j] = st, last.get(o["eng"])
+        if free.get(o["eng"], 0.0) > st:
+            st, why[j] = free[o["eng"]], before[j]
+        last[o["eng"]] = j
+        endq[j] = free[o["eng"]] = st + cost
+        done[j] = st + cost + lat
+        if bw:
+            dmafree = done[j] = max(dmafree + bw, done[j])
+    j = max(range(n), key=lambda x: done[x])
+    pairs = []
+    while j is not None:
+        b = before[j]
+        for _ in range(4):
+            if b is None or endq[b] <= ready[j]:
+                break
+            if b not in ops[j]["hard"] and b not in ops[j]["soft"]:
+                pairs.append((b, j))
+            b = before[b]
+        j = why[j]
+    return pairs
+
+
+def turns(ops, succ):
+    n = len(ops)
+    left = {}
+    for j, o in enumerate(ops):
+        left.setdefault((o["eng"], (o["w"] + ["out"])[0].rstrip("0123456789"), o["rnd"]), []).append(j)
+    due = {}
+    for t in range(-1, RO):
+        for e, plan_ in TURN.items():
+            row = []
+            for item in plan_.split():
+                name, _, cnt = item.rstrip("+").partition("*")
+                have = left.get((e, name, t + item.endswith("+")), [])
+                k = int(cnt) if cnt else len(have)
+                row += have[:k]
+                del have[:k]
+            at = P["turn"] * (t + 1) - sum(ops[j]["cost"] for j in row) if t < 0 else P["turn"] * t
+            step = 1.0 if t < 0 or t == RO - 1 else P["turn"] / sum(ops[j]["cost"] for j in row)
+            for j in row:
+                due[j] = at
+                at += ops[j]["cost"] * step
+    pri = [0.0] * n
+    for j in range(n - 1, -1, -1):
+        o = ops[j]
+        pri[j] = -due[j] if j in due else max([-P["turn"] * (RO + 1)] + [pri[s] for s in succ[j]]) + o["cost"] + o.get("lat", 0.0) + HOP
+    return pri
+
+
 def schedule(ops, cases):
     n = len(ops)
     succ = [[] for _ in range(n)]
@@ -745,6 +986,8 @@ def schedule(ops, cases):
         end, order, done = forward(ops, succ, p)
         return sum(math.log(replay(ops, order, c)) for c in cases) / len(cases), order, done, p
     best = last = judge(pri)
+    if P["turn"]:
+        best = last = judge(turns(ops, succ))
     for _ in range(P["fb"]):
         last = judge(backward(ops, succ, last[2]))
         if last[0] < best[0]:
@@ -752,21 +995,83 @@ def schedule(ops, cases):
     kinds = {}
     for j, o in enumerate(ops):
         kinds.setdefault(((o["w"] + ["out"])[0].rstrip("0123456789"), o["eng"], o["rnd"]), []).append(j)
+    for k in list(kinds):
+        if k[2] >= 0:
+            kinds.setdefault((k[0], k[1], RO), []).extend(kinds[k])
     keys = sorted(kinds)
-    seed = 12345
+    keys += [k for k in keys if k[2] == RO and k[1] != "g"] * 3
+    seed = P["seed"]
+    held = [None, None]
+    first = best
     for it in range(P["tries"]):
         seed = (seed * 1103515245 + 12345) % (1 << 31)
         if it % 40 == 39:
             p = backward(ops, succ, best[2])
+        elif it % 3:
+            if held[0] is not best:
+                held[:] = [best, {}]
+            c = (seed >> 6) % len(cases)
+            if c not in held[1]:
+                held[1][c] = blocked(ops, best[1], cases[c])
+            pairs = held[1][c]
+            if not pairs:
+                continue
+            b, j = pairs[(seed >> 10) % len(pairs)]
+            p = list(best[3])
+            d = max(p[b] - p[j], 0.0) + (50.0, ops[b]["cost"] + 50.0, 1500.0)[(seed >> 20) % 3]
+            if (seed >> 8) % 2:
+                p[b] -= d
+            else:
+                p[j] += d
+                for m in ops[j]["hard"] + ops[j]["soft"]:
+                    p[m] = max(p[m], p[j] + 1.0)
         else:
             p = list(best[3])
             d = (-3000.0, -1200.0, -400.0, 400.0, 1200.0, 3000.0)[(seed >> 8) % 6]
             for j in kinds[keys[(seed >> 12) % len(keys)]]:
                 p[j] += d
         now = judge(p)
-        if now[0] <= best[0]:
+        if now[0] <= best[0] + P["warm"] * (1.0 - it / P["tries"]) * ((seed >> 3) % 32) / 32.0:
             best = now
-    return best
+            if now[0] < first[0]:
+                first = now
+    best = first
+
+    def mark(order):
+        return sum(math.log(replay(ops, order, c)) for c in cases) / len(cases)
+    cur, order = best[0], best[1]
+    top = (cur, order)
+    pairs = None
+    for it in range(P["swaps"]):
+        if pairs is None:
+            pairs = blocked(ops, order, cases[it % len(cases)]) + blocked(ops, order, cases[(it + 2) % len(cases)])
+            pos = {j: x for x, j in enumerate(order)}
+        seed = (seed * 1103515245 + 12345) % (1 << 31)
+        b, j = pairs[(seed >> 8) % len(pairs)]
+        seg = order[pos[b]:pos[j] + 1]
+        if (seed >> 5) % 2:
+            move = {j}
+            for x in reversed(seg):
+                if x in move:
+                    move.update(ops[x]["hard"] + ops[x]["soft"])
+            if b in move:
+                continue
+            seg = [x for x in seg if x in move] + [x for x in seg if x not in move]
+        else:
+            move = {b}
+            for x in seg:
+                if x in move:
+                    move.update(succ[x])
+            if j in move:
+                continue
+            seg = [x for x in seg if x not in move] + [x for x in seg if x in move]
+        new = order[:pos[b]] + seg + order[pos[j] + 1:]
+        now = mark(new)
+        if now <= cur + P["heat"] * (1.0 - it / P["swaps"]) * ((seed >> 12) % 64) / 64.0:
+            cur, order, pairs = now, new, None
+            if cur < top[0]:
+                top = (cur, order)
+    return top
 
 
 def backward(ops, succ, done):
@@ -868,7 +1173,7 @@ def plan(g, core, T, topo):
     ops = build_ops(g, core, T, topo)
     link(ops)
     if "order" not in ORDER:
-        cases = [[(o["cost"], o.get("lat", 0.0), o.get("bw", 0.0)) for o in build_ops(g, core, T, topo, c)] for c in CASES]
+        cases = [[(o["cost"], o.get("lat", 0.0) + c.get("wake", 0.0), o.get("bw", 0.0)) for o in build_ops(g, core, T, topo, c)] for c in CASES]
         ORDER["order"] = schedule(ops, cases)
     return ops, ORDER["order"]
 

@@ -5,63 +5,36 @@ A = AluOpType
 F = ActivationFunctionType
 V, M, KK, RO, TH = 2048, 256, 512, 4, 12
 W_ = V + M * RO
+NO = W_ - M
 DUM = W_ + 16
 WC = DUM + M
 GO = W_
 SC_ = 1 << 19
-K0 = (TH - 1) * SC_ + (1 << 18)
-OV = (1 << 23) + (1 << 19)
+K0 = 1 << 15
+OV = 1 << 23
 BIG = 3 * (1 << 22)
 RND = 1.5 * 2.0 ** 23
 RND13 = 1.5 * 2.0 ** 36
 LO = 2.0 ** -11
 H1 = 1536.0
 H2 = 768.0
-NONE = 16384.0
+SG = 2.0 ** -9
+Y0 = 128
 
-P = {'grp': 2, 'ynlat': 1000.0, 'fb': 3, 'blook': 0.0, 'g': 1.56, 'sc': 3.8, 'fac': 1.2, 'pe': 0.42, 'rem': 2200.0, 'dl': 1500.0, 'dr': 250.0,
-     'look': 600.0, 'half': 0.5, 'cap': 500.0, 'tries': 0, 'zs': [5000.0, 2500.0], 'loads': 'pwzkxyn',
-     'SCb': ('TE1', 'KE'), 'LPb': ('X1', 'X0'), 'tra': [[0, 0], [0, 0], [0, 0], [0, 0]], 'lna': [0, 0, 0, 0], 'pee': [0, 0, 0, 0],
-     'dq': [[32, 0, 0, 0], [48, 32, 0, 0], [32, 32, 1, 1], [64, 16, 0, 0]], 'bitsC': ['aaavaavv', 'aaavaavv', 'aaavaavv', 'vvaavvaa'],
-     'bitsE': ['aaaaaaav', 'aavvaavv', 'vvaaaaaa', 'aaaaaaaa'], 'eng': {'pu': 'v', 'zout': 'v', 'prow': 'v'}, 'wi': 'av',
-     'rsg': 3, 'rsv': 6, 'ce': {'SW': 'v', 'nI': 'g', 'Ih': 'g', 'c1k': 'g', 'SA': 'g'}, 'xo': 'aahhvv', 'li': 'aaaa', 'ract': [1, 0, 1, 1]}
-P.update({'grp': 2, 'fb': 2, 'tries': 2500, 'tra': [[0, 0], [0, 0], [1, 0], [0, 0]], 'lna': [0, 0, 0, 0], 'pee': [0, 0, 0, 1], 'dq': [[64, 16, 1, 0], [48, 32, 0, 0], [32, 32, 0, 1], [64, 32, 0, 0]], 'bitsC': ['vvaavvaa', 'aaavaavv', 'vvaaaavv', 'vvaavvaa'], 'bitsE': ['aaaaaaav', 'aaaaaavv', 'vvaaaaaa', 'aaaaavvv'], 'eng': {'pu': 'v', 'zout': 'v', 'uu': 'v'}, 'wi': 'av', 'rsg': 3, 'rsv': 8, 'ce': {'SW': 'g', 'nI': 'g', 'Ih': 'g', 'c1k': 'g', 'SA': 'g', 'blk': 'v', 'Bo': 'v', 'SAb': 'g', 'dum': 'a', 'bigI': 'v', 'o16': 'v', 'In': 'v', 'P11': 'v', 'I20': 'v', 'n8k': 'a'}, 'xo': 'aahhvv', 'li': 'aaaa', 'ract': [1, 0, 1, 1]})
-P.update({'rep2': [0, 0, 0, 0], 'fix': 40.0, 'pe': 0.44, 'tries': 0, 'dr': 220.0, 'ynlat': 500.0, 'fac': 1.1})
-P.update({'bitsC': ['vvaaaavv', 'aaavaavv', 'vvaaaavv', 'vvvvaaav'], 'ract': [1, 1, 1, 1], 'esp': 1, 'rep2': [0, 0, 0, 0], 'grp': 2, 'tries': 500,
-          'gnx': 1, 'eh': 2, 'fix': 45.0, 'swaps': 0, 'heat': 0.001})
-P.update({'turn': 22000.0, 'warm': 0.0, 'tries': 350, 'fb': 2, 'zs': [5000., 1500.], 'xo': 'vvvhhh', 'dq': [[64, 0, 0, 0], [64, 0, 0, 0], [64, 0, 0, 0], [0, 0, 0, 0]],
-          'bitsC': ['aavvaavv'] * 3 + ['vvvvaavv'], 'bitsE': ['aaaaaavv'] * 4, 'tra': [[0, 0], [0, 0], [0, 0], [0, 0]], 'pee': [0] * 4,
-          'eng': {'zout': 'v', 'PAR': 'v', 'prow': 'v'}, 'pgf': 0, 'loads': 'pwzkxn'})
-P.update({'warm': 0.001, 'tries': 1200, 'eng': {'zout': 'v', 'prow': 'v', 'af': 'a'}, 'tra': [[1, 0]] * 4})
-TURN = {"v": "av GA zout PAR Wn ovr XO RC*4 RD*4 af RC*2 BC*1 Tr*1 D*1 RC RD BC u+ Tr D RE*1 m r TT SC RE*1 mx pout RE*4 pf+ pg+ pu+ prow+ RE BE EQ+ L e*2 qf+ s+ of+ off+ e W*1+ Ln Lm W+",
-        "a": "GA zy zout Ta*1 Rd*1 BC*1 Tr*1 PAR af BC*1 Ta Tr Rd sC*1 BC sC cnu+ u+ uu+ KU+ RE BE*1 r13a r XH XO MK KOE Li BE*1 pu+ pv+ prow+ PG+ xp+ BE*1 qu+ qf+ rho+ MG+ BE act+ sE Gq+ rk+ Gn+ CE+ au+ pn+ zy+"}
-P['eng'].update({'prow': 'a', 'PAR': 'v'})
-P.update({'frl': [0, 0, 0, 0], 'frb': 'KC', 'zs': [4000., 1500.], 'afl': 2, 'zl': [0, 0, 0], 'ua': 1, 'aus': [1, 0, 0, 0], 'pgf': 1, 'fix': 50.0, 'pe': 0.42, 'ynlat': 0.0, 'xo': 'vvvvvv', 'ract': [1, 1, 1, 0]})
-P['eng']['PAR'] = 'a'
-P.update({'ul': [1, 1, 1], 'lna': [1, 1, 1, 0], 'tries': 1300, 'swaps': 1000, 'heat': 0.0002, 'seed': 12345, 'frl': [1, 1, 1, 0], 'dq': [[64, 16, 0, 0]] * 3 + [[0, 32, 0, 0]], 'tra': [[0, 0]] * 4, 'bitsC': ['aavvaavv'] * 4})
-CASES = [dict(fac=1.0, rem=1900.0, dl=1500.0, dr=220.0), dict(fac=1.1, g=1.15, sc=2.2, dr=300.0, rem=2600.0),
-         dict(fac=1.2, g=1.95, sc=5.4, rem=3000.0, dl=2000.0, dr=190.0), dict(fac=1.35, g=1.4, sc=4.5, rem=1600.0, dr=250.0),
-         dict(fac=1.1, g=1.3, sc=3.0, rem=3000.0, zs=[7000.0, 2500.0], dl=2000.0, dr=220.0, wake=90.0)]
-P.update({'ul': [1, 0, 0], 'ua': 0, 'xof': 0, 'xon': 2, 'zf': 0, 'bitsC': ['aavvaavv'] * 3 + ['aaaaaavv'], 'tries': 2200, 'swaps': 800})
-P['ce'].update({'K2': 'v'})
-P['zq'] = ['', '', '']
-CASES[4] = dict(fac=1.3, g=1.04, sc=1.7, rem=2200.0, zs=[6000.0, 2000.0], dl=1800.0, wake=30.0)
-P.update({'tries': 900, 'swaps': 500, 'heat': 0.0001, 'rsg': 1, 'rsv': 15, 'ul': [0, 0, 0], 'ua': 1, 'zl': [0, 0, 0], 'xon': 4, 'xok': 2, 'bitsC': ['aavvaavv'] * 4, 'dr': 250.0})
-P.update({'tries': 4200, 'swaps': 1500, 'warm': 0.0007, 'seed': 64, 'dq': [[64, 32, 0, 0]] * 3 + [[0, 48, 0, 0]], 'tra': [[1, 0]] * 4, 'bitsC': ['aaavaavv'] * 4})
-P.update({'afix': 22.0, 'cv': 1})
-CASES[3] = dict(fac=1.4, g=1.25, sc=3.0, rem=1800.0)
-TURN['v'] = TURN['v'].replace('BE EQ+', 'BE EQ*8+ Cc+ CE+ EQ+')
-TURN['a'] = TURN['a'].replace('prow+ PG+ xp+', 'prow+ xp+ PG+').replace('pn+ zy+', 'pn+ zy+ zout+')
-P['eng']['zout'] = 'a'
-P.update({'bitsE': ['aaaaaaaa'] * 3 + ['aaaaaavv'], 'zq': ['', 'a', 'a'], 'tries': 4000, 'swaps': 1200, 'afl': 0, 'ua': 0, 'zf': 1})
-P['ce'].update({'In': 'g', 'I20': 'g', 'o16': 'g', 'n8k': 'g'})
-TURN['a'] = TURN['a'].replace(' af ', ' ').replace('au+', 'au+ af+')
-CASES.append(dict(fac=1.15, g=1.08, sc=1.8, rem=2000.0, dr=260.0))
-P.update({'tries': 3200, 'swaps': 1000, 'seed': 11, 'warm': 0.001, 'pee': [1, 1, 1, 0], 'bitsE': ['aaaaaaav'] * 3 + ['aaaaaavv']})
-CASES[1] = dict(fac=1.45, g=1.06, sc=1.8, rem=2400.0)
-P.update({'bitsC': ['aaavaavv'] * 3 + ['aaaaaavv'], 'tries': 850, 'swaps': 3000, 'xoa': 3, 'pee': [0] * 4, 'bitsE': ['aaaaaaaa'] * 3 + ['aaaaaavv'], 'seed': 64, 'dq': [[64, 16, 0, 0]] * 3 + [[0, 48, 0, 0]]})
-for _c, _r in zip(CASES, (250.0, 320.0, 210.0, 280.0, 250.0)):
-    _c["dr"] = _r
+P = {"ga": ["vVVVaAAAaAAAAAvV"] * 4, "bitsC": ["aAavaAvV"] * 4, "bitsE": ["aAaAaAaA"] * 3 + ["aAaAaAvV"],
+     "tra": [[1, 0]] * 4, "ract": [1, 1, 1, 0], "xo": "ggga", "xs": ((0, 1), (1, 2), (3, 5), (2, 3)), "li": "gggg", "early": "sel0 sel1 sel2 sel3 grp", "frl": [1, 1, 1, 0], "zq": ["", "a", "a"], "pnv": 0, "mv": 1,
+     "eng": {"Ln": "g"}, "wi": "vavg", "rsg": 0, "rsv": 13, "loads": "pwzkxn", "frb": "TC1", "LPb": ("X1", "X0"),
+     "sb": [(("KE", "TE1"), ("KE", "TE1"))] * 4, "kb": ["TC0"] * 4,
+     "eb": [(("TE0",), (("TE1", "TE1"), ("TE1", "TE1")))] * 3 + [(("TE0", "TC1"), (("TE1", "TE1"), ("X1", "X1")))],
+     "ce": {"Bo": "v", "dum": "a", "Ka": "v", "Kb": "a", "Kn": "v", "Dhi": "v", "I11": "a", "crow": "a", "kcol": "a", "zn1": "v", "nI2": "v", "grp": "g", "Bw": "a"},
+     "fac": 1.1, "g": 1.56, "sc": 3.8, "pe": 0.42, "fix": 50.0, "afix": 22.0, "rem": 2200.0, "dl": 1500.0, "dr": 250.0, "zs": [4000.0, 1500.0], "acc": 1.5,
+     "look": 600.0, "cap": 500.0, "turn": 21000.0, "fb": 2, "tries": 1000, "steps": 350, "far": 100, "gain": -0.001, "stall": 100, "kick": 10, "wild": 2e-5, "warm": 0.001, "seed": 1}
+TURN = {"v": "av GA Wn ovr XO RC*6 BC*1 Tr*1 D*1 RC BC u+ Tr D RE*1 m r TT SC RE*1 mx pout RE*4 pf+ RE BE EQ*8+ Cc+ CE+ EQ+ L pn+ e*2 qf+ s+ off+ e W*1+ Lm W+",
+        "a": "GA Ta*1 Rd*1 BC*1 Tr*1 BC*1 Ta Tr Rd sC*1 BC sC u+ uu+ BE*1 r13a r XH XO MK KOE Li BE*1 pf+ pu+ pv+ prow+ xp+ PG+ BE*1 qu+ qf+ MG+ BE act+ sE Gq+ rk+ Gn+ Ln aw+ au+ af+ pn+ zy+ zout+"}
+CASES = [dict(fac=1.0, fix=30.0, afix=15.0, rem=2500.0, dl=1800.0, dr=220.0, wake=110.0), dict(fac=1.45, fix=40.0, g=1.06, sc=1.8, rem=2400.0, dr=320.0, wake=60.0),
+         dict(fac=1.2, fix=40.0, g=1.95, sc=5.4, rem=3000.0, dl=2000.0, dr=210.0, wake=80.0),
+         dict(fac=1.25, fix=30.0, afix=15.0, g=1.3, sc=3.0, rem=3000.0, zs=[6000.0, 2000.0], dl=1800.0, wake=130.0, dr=250.0),
+         dict(fac=1.05, fix=40.0, g=1.1, sc=2.0, rem=2400.0, dr=300.0, wake=80.0)]
 
 f32, bf, f16, i32, u16 = "float32", "bfloat16", "float16", "int32", "uint16"
 
@@ -70,26 +43,25 @@ def _sb(cols, d):
     return ("sbuf", [128, cols], d)
 
 
-DIAG = {"I": 1.0, "nI": -1.0, "bigI": float(BIG), "Ih": 0.5, "nIh": -0.5, "I2k": 2048.0, "n1280": -1280.0, "I11": LO, "nI11": -LO, "In": NONE,
-        "n8k": -8192.0, "I64": 64.0, "I19": float(SC_), "I20": 2.0 * SC_, "I23": 16.0 * SC_}
+DIAG = {"I": 1.0, "nI": -1.0, "I2k": 2048.0, "n1280": -1280.0, "I11": LO, "n24k": -BIG / 512.0, "I64": 64.0, "I19": float(SC_), "nI2": -2.0}
 MATS = list(DIAG) + ["Pm", "P11", "Dlo", "Dhi", "blk", "Bo", "Bw", "zb", "R16"]
 SCRATCH = {
-    "G": _sb(GO + WC, f32), "L": _sb(WC, f32), "MK": _sb(WC, f32), "PAR": _sb(W_ - M, f32),
+    "G": _sb(GO + WC, f32), "L": _sb(WC, f32), "MK": _sb(WC, f32), "PAR": _sb(W_, f32),
     "NB": _sb(V, i32), "XC": _sb(V, bf), "XO": _sb(W_, bf), "XH": _sb(1408, f16),
-    "K1": _sb(KK, bf), "K2": _sb(KK, bf), "KF": _sb(2 * KK, f32), "wi": _sb(4, i32), "wf": _sb(4, f32),
+    "K1": _sb(KK, bf), "KF": _sb(2 * KK, f32), "wi": _sb(4, i32), "wf": _sb(4, f32),
     "pin": _sb(16 * RO, i32), "pout": _sb(16 * RO, i32), "zin": _sb(M * RO, bf), "zout": _sb(M * RO, bf),
     "GA": _sb(16 * M, f32), "RC": _sb(16 * M, f16), "RE": _sb(16 * M, f16), "BC": _sb(16 * M, bf), "BE": _sb(16 * M, bf), "EQ": ("sbuf", [128, 16, M], bf),
-    "MX": _sb(128 * len(MATS), bf), "ones": _sb(512, bf), "zf": _sb(128, f32), "o16": _sb(128, f32), "If": _sb(128, f32),
-    "zn": _sb(128, bf), "grp": _sb(8, bf), "sel": _sb(32, f32), "Kn": _sb(128, bf), "Kt": _sb(128, bf), "c1k": _sb(32, bf),
-    "SW": _sb(144, bf), "SA": _sb(144, bf), "S1": _sb(144, bf), "SM": _sb(144, bf), "RS": _sb(2048, bf),
-    "SWP": _sb(512, f32), "sm": _sb(M, bf), "crow": _sb(512, bf), "thr": _sb(M, bf), "KOC": _sb(M * RO, f32), "lo": _sb(M, bf), "hi": _sb(M * RO, bf),
+    "MX": _sb(128 * len(MATS), bf), "ones": _sb(512, bf), "zf": _sb(128, f32), "o16": _sb(128, f32),
+    "zn": _sb(128, bf), "grp": _sb(8, bf), "grq": _sb(8, bf), "BI": _sb(NO // 4, i32), "sel": _sb(32, f32), "Kn": _sb(128, bf), "Kt": _sb(128, bf), "c1k": _sb(64, f16),
+    "SW": _sb(144, bf), "SA": _sb(144, bf), "S1": _sb(144, bf), "RS": _sb(2048, bf),
+    "SWP": _sb(512, f32), "sm": _sb(M, bf), "crow": _sb(512, f16), "thr": _sb(M, bf), "KOC": _sb(M * RO, f32), "lo": _sb(M, bf), "hi": _sb(M * RO, bf),
     "mkc": _sb(2 * M, f32), "pi": _sb(4, i32), "lane": _sb(4, f32), "srow": _sb(16, f32), "lm": _sb(16, f32),
-    "pat": _sb(16, f32), "pm": _sb(16, f32), "dum": _sb(16, f32), "dug": _sb(16, f32),
-    "pf16": _sb(32, f16), "pf32": _sb(32, f32), "pu": _sb(32, u16), "pv": _sb(16, u16), "prow": _sb(2 * M, f16), "two": _sb(M, bf), "pb": _sb(M, bf), "KOE": _sb(2 * M, f32),
-    "act": _sb(2 * M, f16), "cnt": _sb(8, f32), "off": _sb(32, u16), "of2": _sb(16, u16),
-    "pw": _sb(16, f32), "ovr": _sb(32, f32), "xp": _sb(M, f16), "KU": _sb(2 * M, bf), "rho": _sb(2 * M, bf),
-    "CE": _sb(4 * M, f16), "Gn": _sb(M, f32), "PG": _sb(M, f16), "MG": _sb(M, bf), "Gq": _sb(M, f32), "rk": _sb(M, f32),
-    "qu": _sb(16, u16), "qf": _sb(16, f32), "s2": _sb(16, f32), "Ta": _sb(2 * M, f32),
+    "pat": _sb(16, f32), "pm": _sb(16, f32), "dum": _sb(32, f32),
+    "pf16": _sb(16 * RO, f16), "pu": _sb(32, u16), "prow": _sb(2 * M, f16), "pb": _sb(128, bf),
+    "act": _sb(4 * M, f16), "cnt": _sb(8, f32), "off": _sb(64, u16),
+    "pw": _sb(16, f32), "ovr": _sb(32, f32), "xp": _sb(M, f16),
+    "CE": _sb(4 * M, f16), "Gn": _sb(M, f32), "PG": _sb(M, f16), "Gq": _sb(M, f32), "rk": _sb(M, f32),
+    "qu": _sb(16, u16), "qf": _sb(16, f32), "Ta": _sb(2 * M, f32),
     "au": _sb(M, u16), "af": _sb(M, f16), "Tr": _sb(2 * M, f16), "Rd": _sb(2 * M, i32), "D": _sb(2 * M, bf),
     "sC": _sb(2 * M, bf), "sE": _sb(2 * M, bf), "zy": _sb(M, f16), "u1": _sb(16, i32), "uu": _sb(32, u16),
     "m1": _sb(M, f32), "m2": _sb(M, f32), "r13a": _sb(M, f32), "r13": _sb(M, f32), "TT": _sb(M, f32), "SC": _sb(M, f32), "mx": _sb(16, i32),
@@ -98,7 +70,7 @@ SCRATCH = {
 BANKS = ["TC0", "TC1", "TE0", "TE1", "KC", "KE", "X0", "X1"]
 for _b in BANKS:
     SCRATCH[_b] = ("psum", [128, 512], f32)
-NDMA = 16
+NDMA = 14
 SEMAPHORES = ["ev", "ea", "et", "eg", "sent"] + ["d%d" % i for i in range(NDMA)] + ["pa%d" % t for t in range(1, RO)] + ["za%d" % t for t in range(1, RO)]
 
 
@@ -115,7 +87,7 @@ def build_ops(g, core, T, topo, case=None):
     rnd = [-1]
 
     def add(eng, fn, r, w, cost, **kw):
-        ops.append(dict(eng=eng, fn=fn, r=list(r), w=list(w), cost=cost, rnd=rnd[0], **kw))
+        ops.append(dict(eng=eng, fn=fn, r=list(r) + ["ones1"] * ("ones" in r), w=list(w), cost=cost, rnd=rnd[0], **kw))
 
     def vc(n, rate=1.0):
         return (C["fix"] + max(64, n * rate) * 0.83) * fac
@@ -149,10 +121,15 @@ def build_ops(g, core, T, topo, case=None):
         else:
             add("a", lambda: g.scalar.activation(o, i, fn, bias=bias, scale=scale, accum_out=acc), r, w, vc(n, rate) + 35 * fac)
 
+    def gp(fn, r, w, n):
+        add("g", fn, r, w, (150 + 2 * n * 0.83) * fac)
+
     def lin(e, o, i, scale, bias, r, w, n, rate=1.0, vrate=None):
         e = P["eng"].get(w[0].rstrip("0123456789"), e)
         if e == "a":
             act_(o, i, F.Identity, r, w, n, bias=bias, scale=scale, rate=rate)
+        elif e == "g":
+            gp(lambda: g.affine_select(o, i, [[0, n]], A.is_ge, 0.0, 0, 0), r, w, n)
         else:
             ts(o, i, scale, bias, A.mult, A.add, r, w, n, rate if vrate is None else vrate)
 
@@ -164,16 +141,17 @@ def build_ops(g, core, T, topo, case=None):
         cyc = max(64, n) * (4 if wide else 1)
         add("t", [lambda: g.tensor.matmul(o, l, rh, st, me["stop"])], r, w, cyc * C["pe"] * fac, flags=dict(me), subs=[me], cyc=cyc)
 
-    def gp(fn, r, w, n):
-        add("g", fn, r, w, (150 + 2 * n * 0.83) * fac)
-
-    def dma(o, i, r, w, nbytes, more=0.0):
+    def dma(o, i, r, w, nbytes):
         s = T.sem["d%d" % ndma[0]]
         ndma[0] += 1
-        add("s", lambda: g.sync.dma_start(o, i), r, w, 60.0, sem=s, inc=16, lat=C["dl"] + more + nbytes / C["dr"], bw=nbytes / C["dr"])
+        add("s", lambda: g.sync.dma_start(o, i), r, w, 60.0, sem=s, inc=16, lat=C["dl"] + nbytes / C["dr"], bw=nbytes / C["dr"])
 
     def send(o, i, sem, r, w, slack=0.0):
         add("g", lambda: g.remote_dma(o, i, sem, T.sem.sent, pid, rid, mask), r, w, 300.0, sem=sem, inc=neng, lat=C["rem"] + slack, remote=True)
+
+    def runs(plan):
+        cut = [j for j, x in enumerate(plan) if x.islower()] + [len(plan)]
+        return [(plan[a], a, b) for a, b in zip(cut, cut[1:])]
 
     loads = {"p": (T.pin[:, 0:16], T.ps[:], "pin0", 8192), "x": (T.XC[:], T.xc[:], "XC", 524288), "w": (T.wi[:, 0:1], T.wt[:], "wi", 512),
              "z": (T.zin[:, 0:M], T.zi[:], "zin0", 65536), "k": (T.K1[:], T.kc[:], "K1", 131072), "n": (T.NB[:], T.nb[:], "NB", 1048576)}
@@ -187,8 +165,8 @@ def build_ops(g, core, T, topo, case=None):
     def spot(o, name, pattern, base, fill, n, z="zb"):
         gp(lambda: g.affine_select(o, zero(z, n), pattern, A.not_equal, float(fill), base, 1), [z], [name], n)
 
-    def iota(o, name, pattern, base, n):
-        gp(lambda: g.iota(o, pattern, base, 0, allow_small_or_imprecise_dtypes=True), [], [name], n)
+    def iota(o, name, pattern, base, n, r=()):
+        gp(lambda: g.iota(o, pattern, base, 0, allow_small_or_imprecise_dtypes=True), r, [name], n)
 
     def band(o, name, lo, hi, fill, z="zb"):
         gp(lambda: g.affine_select(o, zero(z, 8), [[16, 8]], A.is_gt, float(fill), lo, -1), [z, name], [name], 8)
@@ -203,23 +181,19 @@ def build_ops(g, core, T, topo, case=None):
         else:
             gp(lambda: g.affine_select(o, zero(z, n), [[0, n]], A.is_gt, float(c), 0, 0), [z], [name], n)
 
-    mset(T.ones[:], 1.0, ["ones"], 512)
     mset(mat("zb"), 0.0, ["zb"], 128)
+    mset(T.ones[:, 128:512], 1.0, ["ones1"], 384)
     mset(T.zf[:], 0.0, ["zf"], 256)
     iota(mat("R16"), "R16", [[16, 8], [0, 16]], 0, 128)
     gp(lambda: g.iota(T.wf[:, 2:3], [[0, 1]], 0, 1, allow_small_or_imprecise_dtypes=True), [], ["pcol"], 1)
     gp(lambda: g.iota(T.pi[:, 0:1], [[0, 1]], 0, 1), [], ["pi"], 1)
     ts(T.pi[:, 1:2], T.pi[:, 0:1], 15, None, A.bitwise_and, None, ["pi"], ["pa"], 1)
     copy(T.lane[:, 0:1], T.pi[:, 1:2], ["pa"], ["lane"], 1)
-    if ce("blk", "g") == "g":
-        gp(lambda: g.affine_select(mat("blk"), T.ones[:, 0:128], [[-16, 8], [0, 16]], A.is_ge, 0.0, 0, 1), ["ones"], ["blk"], 128)
-        gp(lambda: g.affine_select(mat("blk"), mat("blk"), [[16, 8], [0, 16]], A.is_ge, 0.0, 15, -1), ["blk"], ["blk"], 128)
-    else:
-        ts(mat("blk"), mat("R16"), T.lane[:, 0:1], T.wf[:, 2:3], A.add, A.is_equal, ["R16", "lane", "pcol"], ["blk"], 128, 0.5)
+    ts(mat("blk"), mat("R16"), T.lane[:, 0:1], T.wf[:, 2:3], A.add, A.is_equal, ["R16", "lane", "pcol"], ["blk"], 128, 0.5)
     iota(T.srow[:], "srow", [[1, 16]], 0, 16)
     spot(mat("I"), "I", [[-1, 128]], 0, 1.0, 128)
     spot(mat("Pm"), "Pm", [[-2, 64], [1, 2]], -1, 1.0, 128)
-    iota(T.dum[:], "dum", [[16, 16]], DUM, 16)
+    iota(T.dum[:], "dum", [[GO, 2], [16, 16]], DUM, 32)
     iota(T.lo[:], "lo", [[0, 8], [1, 32]], 0, M)
     iota(T.KOC[:, 0:M], "KOC0", [[1, M]], K0 + V, M)
     for t in range(2):
@@ -238,176 +212,151 @@ def build_ops(g, core, T, topo, case=None):
     add("v", lambda: g.vector.tensor_reduce(T.wf[:, 1:2], T.pm[:], AxisListType.X, A.add), ["pm"], ["pw"], vc(16))
     lin(ce("Bw", "v"), mat("Bw"), mat("blk"), T.wf[:, 1:2], 0.0, ["blk", "pw"], ["Bw"], 128, vrate=0.5)
     lin(ce("Bo", "a"), mat("Bo"), mat("blk"), 2.0 ** 17, 0.0, ["blk"], ["Bo"], 128, vrate=0.5)
-    act_(T.thr[:, 0:16], T.pat[:], F.Identity, ["pat"], ["thr"], 16, scale=2.0)
+    lin("a", T.thr[:, 0:16], T.pat[:], 2.0, 0.0, ["pat"], ["thr"], 16)
     for n in (16, 32, 64, 128):
-        act_(T.thr[:, n:2 * n], T.thr[:, 0:n], F.Identity, ["thr"], ["thr"], n)
-    lin(ce("dum", "v"), T.dum[:], T.dum[:], 1.0, T.lane[:, 0:1], ["dum", "lane"], ["dum"], 16)
-    lin("a", T.dug[:], T.dum[:], 1.0, float(GO), ["dum"], ["dug"], 16)
+        lin(ce("thr", "a"), T.thr[:, n:2 * n], T.thr[:, 0:n], 1.0, 0.0, ["thr"], ["thr"], n, vrate=0.5)
+    lin(ce("dum", "v"), T.dum[:], T.dum[:], 1.0, T.lane[:, 0:1], ["dum", "lane"], ["dum", "dug"], 32)
     lin(ce("wf", "v"), T.wf[:, 0:1], T.wi[:, 0:1], 1.0, 0.0, ["wi"], ["wf"], 1)
-    for name, w in (("SW", T.wf[:, 0:1]), ("SA", -BIG / 16.0), ("S1", 1.0 / 16), ("SM", 8192.0 * 2 * M / 16)):
-        if ce(name, "g" if name in ("S1", "SM") else "v") == "v":
-            mset(T[name][:], 0.0, [name], 144)
-        else:
-            iota(T[name][:], name, [[0, 144]], 0, 144)
-        if ce(name + "b", "g" if name in ("S1", "SM") else "a") == "a" or name == "SW":
-            act_(T[name][:, 16:144:16], grpcols("blk"), F.Identity, ["blk"] + (["wf"] if name == "SW" else []), [name], 8, scale=w)
-        else:
-            band(T[name][:, 16:144:16], name, 0, 15, w)
+    for name in ("SW", "SA", "S1"):
+        iota(T[name][:], name, [[0, 144]], 0, 144)
+    act_(T.SW[:, 16:144:16], grpcols("blk"), F.Identity, ["blk", "wf"], ["SW"], 8, scale=T.wf[:, 0:1])
+    spot(T.SA[:, 16:144:16], "SA", [[-16, 8]], 0, -BIG, 8)
+    gp(lambda: g.affine_select(T.SA[:, 16:144:16], T.SA[:, 16:144:16], [[-16, 8]], A.not_equal, -1.0, -1, 1), ["SA"], ["SA"], 8)
+    spot(T.S1[:, 16:144:16], "S1", [[-16, 8]], 0, 1.0, 8)
     for j, name in enumerate(list(DIAG)[1:]):
-        if name in ("I23", "IB") and not max(P["lna"]):
-            continue
-        e = ce(name, "av"[j % 2] if name in ("nI", "bigI", "Ih", "nIh", "I11") else "g")
+        e = ce(name, "g")
         if e == "g":
             spot(mat(name), name, [[-1, 128]], 0, DIAG[name], 128)
         else:
             lin(e, mat(name), mat("I"), DIAG[name], 0.0, ["I"], [name], 128, vrate=0.5)
-    if max(P["lna"]):
-        for h in range(2):
-            lin(ce("pb", "a"), T.pb[:, 128 * h:128 * h + 128], mat("blk"), 2.0, 0.0, ["blk"], ["pb%d" % h], 128, vrate=0.5)
-    if max(P["pee"]):
-        spot(T.If[:], "If", [[-1, 128]], 0, 1.0, 128, "zf")
-    lin(ce("P11", "a"), mat("P11"), mat("Pm"), LO, 0.0, ["Pm"], ["P11"], 128, vrate=0.5)
-    for j, name in enumerate(("Dlo", "Dhi")):
-        if ce(name, "v") == "v":
-            ts(mat(name), mat("I"), T.lm[:, j:j + 1], LO / 64, A.mult, A.mult, ["I", "lm"], [name], 128, 0.5)
-        else:
-            spot(mat(name), name, [[-16, 8], [1000, 16]], -1001 * j, LO / 64, 128)
-    for name, c0, c1 in (("Kn", -H2 / 64, -H2 * LO / 64), ("Kt", -1.0 / 512, 2.0 ** -19)):
-        mset(T[name][0:64, :], c0, [name + "0"], 128)
-        mset(T[name][64:128, :], c1, [name + "1"], 128)
-    if P["cv"]:
-        pass
-    elif ce("two", "v") == "v":
-        mset(T.two[:], 2.0, ["two"], M)
+    lin(ce("pb", "a"), T.pb[:], mat("blk"), 2.0, 0.0, ["blk"], ["pb"], 128, vrate=0.5)
+    if ce("P11", "g") == "g":
+        spot(mat("P11"), "P11", [[-2, 64], [1, 2]], -1, LO, 128)
     else:
-        iota(T.two[:], "two", [[0, M]], 2, M)
-    const(T.c1k[:, 0:16], "c1k", 1024.0, 16, "v")
+        lin(ce("P11", "g"), mat("P11"), mat("Pm"), LO, 0.0, ["Pm"], ["P11"], 128, vrate=0.5)
+    for j, name in enumerate(("Dlo", "Dhi")):
+        if ce(name, "g") == "g":
+            spot(mat(name), name, [[-16, 8], [1000, 16]], -1001 * j, LO / 64, 128)
+        else:
+            ts(mat(name), mat("I"), T.lm[:, j:j + 1], LO / 64, A.mult, A.mult, ["I", "lm"], [name], 128, 0.5)
+    for name, c0, c1 in (("Kn", -H2 / 64, (Y0 - H2) * LO / 64), ("Kt", -1.0 / 512, 2.0 ** -19)):
+        if ce(name, "g") == "g":
+            const(T[name][:], name + "0", c0, 128, "g")
+            gp(lambda o=T[name][:], c=c1: g.affine_select(o, o, [[0, 128]], A.is_gt, c, 64, -1), [], [name + "0", name + "1"], 128)
+        else:
+            mset(T[name][0:64, :], c0, [name + "0"], 128)
+            mset(T[name][64:128, :], c1, [name + "1"], 128)
+    const(T.c1k[:, 0:16], "c1k", 1024.0, 16, "g")
+    const(T.c1k[:, 48:64], "c6k", BIG / 2048, 16, "g")
     const(T.c1k[:, 16:32], "cm1k", -1024.0, 16, "g")
-    lin(ce("zn1", "a"), T.zn[:], mat("blk"), -1.0, 0.0, ["blk"], ["zn1"], 128, vrate=0.5)
-    act_(T.grp[:], grpcols("blk"), F.Sigmoid, ["blk"], ["grp"], 8, bias=-128.0, scale=256.0)
+    const(T.c1k[:, 32:48], "c1k1", 1025.0, 16, "g")
+    lin(ce("zn1", "a"), T.zn[:], mat("blk"), -2.0, 0.0, ["blk"], ["zn1"], 128, vrate=0.5)
+    act_(T.ones[:, 0:128], mat("zb"), F.Sigmoid, ["zb"], ["ones"], 128, bias=64.0)
     ops[-1]["cost"] += 1300.0 * fac
+    lin(ce("grp", "a"), T.grp[:], grpcols("blk"), 1.0, 0.0, ["blk"], ["grp"], 8)
+    lin(ce("grq", "a"), T.grq[:], grpcols("blk"), 2.0, 0.0, ["blk"], ["grq"], 8)
     band(T.sel[:, 0:8], "sel0", 0, 7, 1.0, "zf")
     band(T.sel[:, 8:16], "sel1", 8, 15, 1.0, "zf")
     for j in range(2):
         spot(T.sel[:, 16 + 8 * j:24 + 8 * j], "sel%d" % (2 + j), [[-16, 8]], -j, 1 / LO, 8, "zf")
-    if P["cv"]:
-        lin(ce("Kc", "a"), T.KF[:, 0:KK], T.K1[:], 1.0, H2, ["K1"], ["Kc"], KK)
-        lin(ce("K2", "a"), T.KF[:, KK:2 * KK:2], T.K1[:, 1:KK:2], 1.0, H2, ["K1"], ["Ka"], 256)
-        lin(ce("K2", "a"), T.KF[:, KK + 1:2 * KK:2], T.K1[:, 0:KK:2], 1.0, H2, ["K1"], ["Kb"], 256)
-    else:
-        lin(ce("K2", "a"), T.K2[:, 0:KK:2], T.K1[:, 1:KK:2], 1.0, 0.0, ["K1"], ["Ka"], 256, vrate=0.5)
-        lin(ce("K2", "a"), T.K2[:, 1:KK:2], T.K1[:, 0:KK:2], 1.0, 0.0, ["K1"], ["Kb"], 256, vrate=0.5)
-    for h in range(2):
-        lin(P["wi"][h], T.G[:, GO + 1024 * h:GO + 1024 * h + 1024], T.XC[:, 1024 * h:1024 * h + 1024], 1 + LO, 0.0, ["XC"], ["Wi%d" % h], 1024)
+    lin(ce("Kc", "a"), T.KF[:, 0:KK], T.K1[:], 1.0, H2, ["K1"], ["Kc"], KK)
+    for j, name in enumerate(("Ka", "Kb")):
+        if ce(name, "g") == "g":
+            lin("g", T.KF[:, KK + j:2 * KK:2], T.KF[:, 1 - j:KK:2], 1.0, 0.0, ["Kc"], [name], 256)
+        else:
+            lin(ce(name, "g"), T.KF[:, KK + j:2 * KK:2], T.K1[:, 1 - j:KK:2], 1.0, H2, ["K1"], [name], 256)
+    for h in range(4):
+        lin(P["wi"][h], T.G[:, GO + 512 * h:GO + 512 * h + 512], T.XC[:, 512 * h:512 * h + 512], 1.0, 0.0, ["XC"], ["Wi%d" % h], 512)
     for xh in range(2):
         for gl in range(2):
             q = 2 * xh + gl
             spot(T.SWP[:, 128 * q:128 * q + 128], "SWP%d" % q, [[-32, 4], [1000, 2], [-1, 16]], -16 * xh - 1000 * gl, 1.0, 128, "zf")
     const(T.o16[:], "o16", 1.0 / 16, 128, "g", "zf")
     gp(lambda: g.affine_select(T.sm[:], T.ones[:, 0:M], [[0, 16], [1, 16]], A.is_gt, 0.0, 0, 0), ["ones"], ["sm"], M)
-    lin(ce("kcol", "v"), T.lane[:, 1:2], T.lane[:, 0:1], -16384.0, 15 * 16384.0, ["lane"], ["kcol"], 1)
-    lin(ce("crow", "v"), T.crow[:, 0:M], T.ones[:, 0:M], 9216.0, T.lane[:, 1:2], ["ones", "kcol"], ["crow0"], M, vrate=0.5)
-    lin(ce("crow", "v"), T.crow[:, M:2 * M], T.ones[:, 0:M], float(V), T.lane[:, 1:2], ["ones", "kcol"], ["crow1"], M, vrate=0.5)
-    iota(T.PAR[:, 0:8], "PAR", [[0, 8]], -int(NONE), 8)
+    lin(ce("kcol", "v"), T.lane[:, 1:2], T.lane[:, 0:1], -8.0, 15 * 8.0 + (SC_ / 2 + K0) / 2048, ["lane"], ["kcol"], 1)
+    lin(ce("crow", "v"), T.crow[:, 0:M], T.ones[:, 0:M], 4.5, T.lane[:, 1:2], ["ones", "kcol"], ["crow0"], M, vrate=0.5)
+    lin(ce("crow", "v"), T.crow[:, M:2 * M], T.ones[:, 0:M], 1.0, T.lane[:, 1:2], ["ones", "kcol"], ["crow1"], M, vrate=0.5)
+    for j in range(4):
+        iota(T.PAR[:, 512 * j:512 * j + 512], "PAR%d" % j, [[0, 512]], 0, 512)
 
     def later(t):
-        def fill(o, name, pattern, base):
-            gp(lambda: g.iota(o, pattern, base, 0, allow_small_or_imprecise_dtypes=True), ["pout%d" % t], [name], M)
+        def fill(o, name, pattern, base, n=M):
+            iota(o, name, pattern, base, n)
+            ops[-1]["behind"] = ["pin%d" % (t + 1)]
         fill(T.KOC[:, M * (t + 1):M * (t + 2)], "KOC%d" % (t + 1), [[1, M]], K0 + V + M * (t + 1))
         if t < 2:
             fill(T.hi[:, M * (t + 2):M * (t + 3)], "hi%d" % (t + 2), [[1, 8], [0, 32]], 8 * (t + 2))
             fill(T.mkc[:, M * t:M * t + M], "mkc%d" % (t + 1), [[0, M]], 64 * t)
         if t == 0:
-            for j in range(11):
-                fill(T.MK[:, M * j:M * j + M], "Mi%d" % j, [[0, M]], 0)
+            for j in range(4):
+                cs = slice(512 * j, 512 * j + 512)
+                lin(P["li"][j], T.L[:, cs], T.NB[:, cs], 1.0, 0.0, ["NB"], ["Li%d" % j], 512)
+                ops[-1]["behind"] = ["pin1"]
 
     def sel(name, s):
         return T[name][:, 16 - s:144 - s]
 
-    def cells(t):
-        return ["W"] + (["Wn%d" % (t - 1)] if t else ["Wi0", "Wi1"])
+    def acts(t, a=0, b=M):
+        return T.act[:, 2 * M * (t % 2) + a:2 * M * (t % 2) + b]
 
-    def upath(t, after=()):
+    def cells(t):
+        return ["W"] + (["Wn%d" % (t - 1)] if t else ["Wi0", "Wi1", "Wi2", "Wi3"])
+
+    def upath(t):
         pr = t % 2
         l = slice(16 * pr, 16 * pr + 16)
         if t:
             mm(T.X1[:, 32:33], T.o16[:], T.cnt[:, 0:1], True, True, ["o16", "cnt"], ["X1"], 1, True)
         for s in range(16):
-            mm(T.X1[:, 0:16], sel("SW", s), T.zin[:, M * t + s:M * t + M:16], s == 0, s == 15, ["SW", "zin%d" % t] + list(after), ["X1"], 16)
-        if t and P["ua"]:
-            act_(T.cnt[:, 1:2], T.X1[:, 32:33], F.Identity, ["X1"], ["cnu"], 1, bias=float(1 << 18))
-            act_(T.u1[:], T.X1[:, 0:16], F.Identity, ["X1", "cnu"], ["u1"], 16, bias=T.cnt[:, 1:2])
-        elif t:
+            mm(T.X1[:, 0:16], sel("SW", s), T.zin[:, M * t + s:M * t + M:16], s == 0, s == 15, ["SW", "zin%d" % t], ["X1"], 16)
+        if t:
             ts(T.u1[:], T.X1[:, 0:16], T.X1[:, 32:33], float(1 << 18), A.add, A.add, ["X1"], ["u1"], 16)
         else:
             lin("v", T.u1[:], T.X1[:, 0:16], 1.0, float(1 << 18), ["X1"], ["u1"], 16)
         ts(T.u1[:], T.u1[:], KK - 1, None, A.bitwise_and, None, ["u1"], ["u1"], 16)
         lin("a", T.uu[:, l], T.u1[:], 1.0, 0.0, ["u1"], ["uu%d" % pr], 16)
-        if P["cv"]:
-            return
-        act_(T.KU[:, 0:M], T.K1[:].indirect(T.uu[:, l]), F.Copy, ["K1", "uu%d" % pr], ["KU0"], M, rate=gc)
-        act_(T.KU[:, M:2 * M], T.K2[:].indirect(T.uu[:, l]), F.Copy, ["Ka", "Kb", "uu%d" % pr], ["KU1"], M, rate=gc)
 
     def prep(t):
         pr = t % 2
         l = slice(16 * pr, 16 * pr + 16)
         c = slice(M * pr, M * pr + M)
-        pin = T.pin[:, 16 * t:16 * t + 16]
-        pn, ac, cn = "pin%d" % t, "act%d" % pr, "CE%d" % pr
+        pf = T.pf16[:, 16 * t:16 * t + 16]
+        pn, ac, cn = "pf%d" % t, "act%d" % pr, "CE%d" % pr
         hi = V + M * t
         win = T.G[:, GO:GO + hi]
         wr = cells(t)
         Cf, Ef = T.CE[:, 2 * M * pr:2 * M * pr + M], T.CE[:, 2 * M * pr + M:2 * M * pr + 2 * M]
-        lin("v", T.pf16[:, l], pin, 1.0, -1024.0, [pn], ["pf%d" % pr], 16)
-        if not P["pgf"]:
-            lin("v", T.pf32[:, l], pin, 1.0, -1024.0, [pn], ["pg%d" % pr], 16)
-        lin("a", T.pu[:, l], pin, 1.0, 0.0, [pn], ["pu%d" % pr], 16)
+        pin = T.pin[:, 16 * t:16 * t + 16]
+        lin("v", pf, pin, 1.0, -1024.0, ["pin%d" % t], [pn], 16)
+        lin("a", T.pu[:, l], pin, 1.0, 0.0, ["pin%d" % t], ["pu%d" % pr], 16)
         for s in range(16):
-            mm(T.X0[:, s:M:16], T.RS[:, 128 * s:128 * s + 128], T.pf16[:, l], True, True, ["RS%d" % s, "pf%d" % pr], ["X0"], 16)
+            mm(T.X0[:, s:M:16], T.RS[:, 128 * s:128 * s + 128], pf, True, True, ["RS%d" % s, pn], ["X0"], 16)
         lin("a", T.prow[:, c], T.X0[:, 0:M], 1.0, 0.0, ["X0"], ["prow%d" % pr], M)
         mm(T.KC[:, 0:M], "nI", T.thr[:], True, False, ["thr"], ["KC"], M)
         for cc in range(16):
             n = M - 16 * cc
-            ts(T.EQ[:, cc, 0:n], T.prow[:, M * pr + 16 * cc:M * pr + M], T["pf16" if P["pgf"] else "pf32"][:, 16 * pr + cc:16 * pr + cc + 1], None, A.is_equal, None, ["prow%d" % pr, ("pf%d" if P["pgf"] else "pg%d") % pr], ["EQ%d" % cc], n, P["half"])
+            ts(T.EQ[:, cc, 0:n], T.prow[:, M * pr + 16 * cc:M * pr + M], T.pf16[:, 16 * t + cc:16 * t + cc + 1], None, A.is_equal, None, ["prow%d" % pr, pn], ["EQ%d" % cc], n, 0.5)
             if cc < 15:
                 mm(T.KC[:, 16 * cc + 16:M], "Bo", T.EQ[:, cc, 16:n], False, False, ["EQ%d" % cc], ["KC"], n - 16)
             if cc % 4 == 3:
                 mm(T.KC[:, 16 * cc - 48:16 * cc + 16], "Bw", T.EQ[:, cc - 3:cc + 1, 0:16], False, cc == 15, ["EQ%d" % x for x in range(cc - 3, cc + 1)], ["KC"], 64)
         last = t == RO - 1
-        act_(T.act[:, c], T.KC[:, 0:M], F.Sigmoid, ["KC", "grp"], [ac] + ([] if last else ["cnt"]), M, bias=-128.0, scale=-256.0, acc=None if last else T.cnt[:, 0:1])
-        hx = H2 if P["cv"] else H1
+        act_(acts(t), T.KC[:, 0:M], F.Sigmoid, ["KC", "ones"], [ac] + ([] if last else ["cnt"]), M, bias=-128.0, scale=-256.0, acc=None if last else T.cnt[:, 0:1])
         if t:
-            act_(T.xp[:], win.indirect(T.pu[:, l]), F.Identity, wr + ["pu%d" % pr], ["xp"], M, bias=hx, rate=gc)
+            act_(T.xp[:], win.indirect(T.pu[:, l]), F.Identity, wr + ["pu%d" % pr], ["xp"], M, bias=H2, rate=gc)
         else:
-            act_(T.xp[:], T.XC[:].indirect(T.pu[:, l]), F.Identity, ["XC", "pu0"], ["xp"], M, bias=hx, rate=gc)
-        if P["cv"]:
-            tt(Cf, T.KF[:, 0:KK].indirect(T.uu[:, l]), T.xp[:], A.min, ["Kc", "uu%d" % pr, "xp"], ["Cc%d" % pr, cn], M, gc)
-            tt(Ef, T.KF[:, KK:2 * KK].indirect(T.uu[:, l]), T.xp[:], A.min, ["Ka", "Kb", "uu%d" % pr, "xp"], [cn], M, gc)
-        for src, sn in ((T.KU, ["KU0", "KU1"]), (T.rho, ["rho"])) * (not P["cv"]):
-            mm(T.TC1[:], "nI", src[:], True, False, sn, ["TC1"], 512)
-            for h in range(2):
-                mm(T.TC1[:, M * h:M * h + M], "I", T.xp[:], False, h == 1, ["xp"], ["TC1"], M)
-            if sn[0] == "KU0":
-                act_(T.rho[:], T.TC1[:], F.Relu, ["TC1"], ["rho"], 512, bias=-H1)
-        if not P["cv"]:
-            lin("a", T.CE[:, 2 * M * pr:2 * M * pr + 2 * M], T.TC1[:], 1.0, H2 - H1, ["TC1"], [cn], 512)
+            act_(T.xp[:], T.XC[:].indirect(T.pu[:, l]), F.Identity, ["XC", "pu0"], ["xp"], M, bias=H2, rate=gc)
+        tt(Cf, T.KF[:, 0:KK].indirect(T.uu[:, l]), T.xp[:], A.min, ["Kc", "uu%d" % pr, "xp"], ["Cc%d" % pr, cn], M, gc)
+        tt(Ef, T.KF[:, KK:2 * KK].indirect(T.uu[:, l]), T.xp[:], A.min, ["Ka", "Kb", "uu%d" % pr, "xp"], [cn], M, gc)
         gn = T.TC0[:, 0:M]
-        if P["gnx"] and not P["cv"]:
-            mm(gn, T.Kn[:], T.two[:], True, False, ["Kn0", "Kn1", "two"], ["TC0"], M)
-            mm(gn, "I", T.xp[:], False, False, ["xp"], ["TC0", "gn0"], M)
-            mm(gn, "I11", T.xp[:], False, False, ["xp", "gn0"], ["TC0"], M)
-            mm(gn, "nI", T.rho[:, 0:M], False, False, ["rho", "gn0"], ["TC0"], M)
-            mm(gn, "nI11", T.rho[:, M:2 * M], False, False, ["rho", "gn0"], ["TC0"], M)
-        else:
-            mm(gn, T.Kn[:], T.ones[:, 0:M], True, False, ["Kn0", "Kn1", "ones"], ["TC0"], M)
-            mm(gn, "I", Cf, False, False, [cn], ["TC0", "gn0"], M)
-            mm(gn, "I11", Ef, False, False, [cn, "gn0"], ["TC0"], M)
+        mm(gn, T.Kn[:], T.ones[:, 0:M], True, False, ["Kn0", "Kn1", "ones"], ["TC0"], M)
+        mm(gn, "I", Cf, False, False, [cn], ["TC0", "gn0"], M)
+        mm(gn, "I11", Ef, False, False, [cn, "gn0"], ["TC0"], M)
         mm(gn, "Dlo", T.lo[:], False, False, ["lo", "gn0"], ["TC0"], M)
         mm(gn, "Dhi", T.hi[:, M * t:M * t + M], False, True, ["hi%d" % t, "gn0"], ["TC0"], M)
         lin("a", T.Gn[:], gn, 1.0, 0.0, ["TC0"], ["Gn"], M)
         if t:
-            lin("a", T.pv[:], pin, 1.0, 1.0 - V, [pn], ["pv"], 16)
-            act_(T.PG[:], T.PAR[:, 0:1 + M * t].indirect(T.pv[:]), F.Copy, ["PAR", "pv"], ["PG"], M, rate=gc)
+            act_(T.PG[:], T.PAR[:, 0:hi].indirect(T.pu[:, l]), F.Identity, ["PAR0", "PAR1", "PAR2", "PAR3", "KOE%d" % (t - 1), "pu%d" % pr], ["PG"], M, bias=-K0 - 1024.0, rate=gc)
             ql = T.X1[:, 0:16]
             mm(ql, "I", T.c1k[:, 0:16], True, False, ["c1k"], ["X1"], 16)
             for s in range(16):
@@ -415,192 +364,131 @@ def build_ops(g, core, T, topo, case=None):
             lin("a", T.qu[:], ql, 1.0, 0.0, ["X1"], ["qu"], 16)
             act_(T.qf[:], ql, F.Abs, ["X1"], ["qf"], 16, bias=float(GO))
             act_(T.Gq[:], win.indirect(T.qu[:]), F.Copy, wr + ["qu"], ["Gq"], M, rate=gc)
-            if P["cv"]:
-                mm(T.TC1[:, 0:M], "I11", T.xp[:], True, False, ["xp"], ["TC1"], M)
-                mm(T.TC1[:, 0:M], "nI11", Cf, False, True, ["Cc%d" % pr], ["TC1"], M)
-                lin("a", T.rk[:], T.TC1[:, 0:M], 1.0, 0.0, ["TC1"], ["rk"], M)
-            else:
-                lin("a", T.rk[:], T.rho[:, 0:M], LO, 0.0, ["rho"], ["rk"], M)
+            mm(T.TC1[:, 0:M], "I", T.xp[:], True, False, ["xp"], ["TC1"], M)
+            mm(T.TC1[:, 0:M], "nI", Cf, False, True, ["Cc%d" % pr], ["TC1"], M)
+            lin("a", T.rk[:], T.TC1[:, 0:M], LO, 0.0, ["TC1"], ["rk"], M)
             if t > 1:
-                act_(T.MG[:], T.MK[:, 0:hi].indirect(T.qu[:]), F.Copy, ["MK", "qu"], ["MG"], M, rate=gc)
-                v2 = T.X1[:, 16:32]
-                mm(v2, "n8k", T.c1k[:, 16:32], True, False, ["cm1k"], ["X1"], 16)
-                mm(v2, "n8k", T.pf16[:, l], False, False, ["pf%d" % pr], ["X1"], 16)
-                for s in range(16):
-                    mm(v2, sel("SM", s), T.MG[:, s:M:16], False, s == 15, ["SM", "MG"], ["X1"], 16)
-                tt(T.qf[:], v2, T.qf[:], A.max, ["X1", "qf"], ["qf"], 16)
-        vl = T.X0[:, M:M + 16]
-        mm(vl, "bigI", T.ones[:, 0:16], True, False, ["ones"], ["X0"], 16)
-        mm(vl, "I", T.c1k[:, 0:16], False, False, ["c1k"], ["X0"], 16)
-        mm(vl, "I", T.pf16[:, l], False, False, ["pf%d" % pr], ["X0"], 16)
+                act_(acts(t, M, 2 * M), T.MK[:, 0:hi].indirect(T.qu[:]), F.Identity, ["MK", "qu"], ["MG"], M, scale=-1.0, rate=gc)
+        vl, v2, two = T.X0[:, M:M + 16], T.X0[:, M + 16:M + 32], t > 1
+        mm(vl, "I2k", T.c1k[:, 48:64], True, False, ["c6k"], ["X0"], 16)
+        mm(vl, "I", T.c1k[:, 32:48], False, False, ["c1k1"], ["X0"], 16)
+        mm(vl, "I", pf, False, False, [pn], ["X0"], 16)
+        if two:
+            mm(v2, "n24k", T.c1k[:, 16:32], False, False, ["cm1k"], ["X0", "v2"], 16)
+            mm(v2, "n24k", pf, False, False, [pn], ["X0"], 16)
         for s in range(16):
-            mm(vl, sel("SA", s), T.act[:, M * pr + s:M * pr + M:16], False, s == 15, ["SA", ac], ["X0"], 16)
+            mm(T.X0[:, M:M + 16 + 16 * two], sel("SA", s), T.act[:, 2 * M * pr + s:2 * M * pr + M + M * two:16], False, s == 15, ["SA", ac] + ["MG", "v2"] * two, ["X0"], 16)
+        off, of2 = T.off[:, 32 * pr:32 * pr + 16], T.off[:, 32 * pr + 16:32 * pr + 32]
+        if two:
+            tt(T.qf[:], v2, T.qf[:], A.max, ["X0", "qf"], ["qf"], 16)
         if t:
-            tt(T.s2[:], vl, T.qf[:], A.max, ["X0", "qf"], ["s2"], 16)
-            tt(T.of2[:], T.s2[:], T.dug[:], A.min, ["s2", "dug"], ["of2"], 16)
-        tt(T.off[:, l], vl, T.dum[:], A.min, ["X0", "dum"], ["off%d" % pr], 16)
+            tt(T.X0[:, M + 16:M + 32], vl, T.qf[:], A.max, ["X0", "qf"], ["s2"], 16)
+            tt(T.off[:, 32 * pr:32 * pr + 32], T.X0[:, M:M + 32], T.dum[:], A.min, ["X0", "s2", "dum", "dug"], ["off%d" % pr], 32)
+        else:
+            tt(off, vl, T.dum[:, 0:16], A.min, ["X0", "dum"], ["off%d" % pr], 16)
         if not last:
-            act_(T.pw[:], pin, F.Sign, [pn], ["pn"], 16, bias=1.5 - V)
-            act_(T.pw[:], T.pw[:], F.Identity, ["pn"], ["pn"], 16, bias=OV - BIG + 1.0 - V / 2, scale=-V / 2)
+            if P["pnv"]:
+                ts(T.pw[:], pin, V - 1.5, -float(V), A.is_ge, A.mult, ["pin%d" % t], ["pn"], 16)
+            else:
+                act_(T.pw[:], pin, F.Sign, ["pin%d" % t], ["pn"], 16, bias=1.5 - V)
+                act_(T.pw[:], T.pw[:], F.Identity, ["pn"], ["pn"], 16, bias=-V / 2, scale=-V / 2)
             tt(T.ovr[:, l], vl, T.pw[:], A.add, ["X0", "pn"], ["ovr%d" % pr], 16)
         if t:
-            tt(T.G[:].indirect(T.of2[:]), T.Gq[:], T.rk[:], A.subtract, ["Gq", "rk", "of2"], wr, M, sc)
-        copy(T.G[:, GO:GO + WC].indirect(T.off[:, l]), T.Gn[:], ["Gn", "off%d" % pr], wr, M, sc)
+            tt(T.G[:].indirect(of2), T.Gq[:], T.rk[:], A.subtract, ["Gq", "rk", "off%d" % pr], wr, M, sc)
+        copy(T.G[:, GO:GO + WC].indirect(off), T.Gn[:], ["Gn", "off%d" % pr], wr, M, sc)
+
+    def koe(t, a=0, b=M):
+        return T.PAR[:, V + M * t + a:V + M * t + b]
 
     def fresh(t):
         pr = t % 2
-        l = slice(16 * pr, 16 * pr + 16)
         c = slice(M * pr, M * pr + M)
         ac, cn = "act%d" % pr, "CE%d" % pr
         Ef = T.CE[:, 2 * M * pr + M:2 * M * pr + 2 * M]
         hi = V + M * t
         fb = P["frb"]
         es, pq = T[fb][:, 0:M], T[fb][:, M:2 * M]
-        if P["lna"][t]:
-            mm(pq, "I", T.prow[:, c], True, False, ["prow%d" % pr], [fb], M)
-            mm(pq, "I23", T.act[:, c], False, True, [ac], [fb], M)
-            act_(T.KOE[:, c], pq, F.Relu, [fb], ["KOE%d" % pr], M, bias=K0 + 1024.0 - DIAG["I23"])
-        if t == RO - 1:
-            mm(es, T.Kn[0:64, :], T.ones[0:64, 0:M], True, False, ["Kn0", "ones"], [fb], M)
-            mm(es, "I", Ef, False, True, [cn], [fb], M)
-            tt(T.XO[:, hi:hi + M], es, T.act[:, c], A.mult, [fb, ac], ["XO6"], M)
-            return
-        mm(es, T.Kn[:], T.ones[:, 0:M], True, False, ["Kn0", "Kn1", "ones"], [fb], M)
-        mm(es, "I", Ef, False, False, [cn], [fb], M)
-        mm(es, "I11", Ef, False, True, [cn], [fb], M)
         mm(pq, "I", T.prow[:, c], True, False, ["prow%d" % pr], [fb], M)
-        mm(pq, "In", T.act[:, c], False, True, [ac], [fb], M)
-        tt(T.G[:, GO + hi:GO + hi + M], es, T.act[:, c], A.mult, [fb, ac, "W"], ["Wn%d" % t], M)
-        lin("a", T.PAR[:, 1 + M * t:1 + M * t + M], pq, 1.0, -NONE, [fb], ["PAR"], M)
+        mm(pq, "I19", acts(t), False, True, [ac], [fb], M)
+        act_(koe(t), pq, F.Relu, [fb], ["KOE%d" % t], M, bias=K0 + 1024.0 - SC_)
+        mm(es, T.Kn[0:64, :], T.ones[0:64, 0:M], True, False, ["Kn0", "Kn1", "ones"], [fb], M)
+        mm(es, "I", Ef, False, True, [cn], [fb], M)
+        if t == RO - 1:
+            tt(T.XO[:, hi:hi + M], es, acts(t), A.mult, [fb, ac], ["XO4"], M)
+        else:
+            tt(T.G[:, GO + hi:GO + hi + M], es, acts(t), A.mult, [fb, ac, "W"], ["Wn%d" % t], M)
 
     def marks(t):
         pr = t % 2
-        l = slice(16 * pr, 16 * pr + 16)
-        c = slice(M * pr, M * pr + M)
-        if not P["lna"][t]:
-            lin("a", T.KOE[:, c], T.prow[:, c], 1.0, float(K0 + 1024), ["prow%d" % pr, "sC0", "sC1"], ["KOE%d" % pr], M)
         if 0 < t < RO - 1:
-            add("a", lambda: g.scalar.activation(T.MK[:].indirect(T.off[:, l]), T.mkc[:, M * (t - 1):M * t], F.Sigmoid),
-                ["mkc%d" % t, "off%d" % pr, "sC0", "sC1"], ["MK"] + (["Mi%d" % j for j in range(11)] if t == 1 else []), vc(M, sc) + 15 * fac)
+            add("a", lambda: g.scalar.activation(T.MK[:].indirect(T.off[:, 32 * pr:32 * pr + 16]), T.mkc[:, M * (t - 1):M * t], F.Sigmoid),
+                ["mkc%d" % t, "off%d" % pr, "sC0", "sC1", "sC2", "sC3"], ["MK"] + (["Mi%d" % j for j in range(4)] if t == 1 else []), vc(M, sc) + 15 * fac)
 
     def lists(t):
         pr = t % 2
-        l = slice(16 * pr, 16 * pr + 16)
         win = T.NB[:] if t == 0 else T.L[:, 0:V + M * t]
         rd = (["NB"] if t == 0 else ["L", "Ln"]) + ["pu%d" % pr]
-        if P["aus"][t]:
-            copy(T.au[:, 0:64], win.indirect(T.pu[:, 16 * pr:16 * pr + 4]), rd + ["zout0"] * P["zf"], ["av"], 64, gc)
-            lin("a", T.au[:, 64:M], win.indirect(T.pu[:, 16 * pr + 4:16 * pr + 16]), 1.0, 0.0, rd, ["au"], M - 64, gc)
+        if t == 0:
+            for e, a, b, name in (("v", 0, 4, "av"), ("a", 4, 8, "aw"), ("a", 8, 16, "au")):
+                lin(e, T.au[:, 16 * a:16 * b], win.indirect(T.pu[:, a:b]), 1.0, 0.0, rd, [name], 16 * (b - a), gc)
         else:
-            lin("a", T.au[:], win.indirect(T.pu[:, l]), 1.0, 0.0, rd, ["au", "av"], M, gc)
+            lin("a", T.au[:], win.indirect(T.pu[:, 16 * pr:16 * pr + 16]), 1.0, 0.0, rd, ["au", "av", "aw"], M, gc)
+        lin("a", T.af[:], T.au[:], 1.0, -1024.0, ["au", "av", "aw"], ["af"], M, vrate=0.5)
 
-    def zpath(t, after=()):
+    def zpath(t):
         pr = t % 2
         c = slice(M * pr, M * pr + M)
         z = T.zin[:, M * t:M * t + M]
         zn, ac, cn = "zin%d" % t, "act%d" % pr, "CE%d" % pr
         y0, y1 = T.KE[:, 0:M], T.KE[:, M:2 * M]
-        mm(y0, "nIh", z, True, False, [zn], ["KE"], M)
-        mm(y0, "I2k", T.act[:, c], False, False, [ac], ["KE"], M)
-        mm(y0, "Ih", T.CE[:, 2 * M * pr:2 * M * pr + M], False, True, [cn], ["KE"], M)
-        act_(T.zy[:], y0, F.Relu, ["KE"] + list(after), ["zy"], M, bias=1279.75 - 2048.0 - H2 / 2)
+        mm(y0, "nI", z, True, False, [zn], ["KE"], M)
+        mm(y0, "I19", acts(t), False, False, [ac], ["KE"], M)
+        mm(y0, "I", T.CE[:, 2 * M * pr:2 * M * pr + M], False, True, [cn], ["KE"], M)
+        act_(T.zy[:], y0, F.Relu, ["KE"], ["zy"], M, bias=1279.75 - SC_ / 2 - H2 / 2, scale=0.5)
         mm(y1, "I", z, True, False, [zn], ["KE"], M)
-        mm(y1, "n1280", T.act[:, c], False, False, [ac], ["KE"], M)
+        mm(y1, "n1280", acts(t), False, False, [ac], ["KE"], M)
         mm(y1, "I", T.zy[:], False, True, ["zy"], ["KE"], M)
         lin("a", T.zout[:, M * t:M * t + M], y1, 1.0, 0.0, ["KE"], ["zout%d" % t], M)
         send(T.zin[:, M * (t + 1):M * (t + 2)], T.zout[:, M * t:M * t + M], T.sem["za%d" % (t + 1)], ["zout%d" % t], ["zin%d" % (t + 1)], C["zs"][min(t, 1)])
-
-    def limits(bank, child, cn, rep, more=None):
-        n = 512 // rep
-        mm(T[bank][:], T.Kt[:], T.ones[:], True, False, ["Kt0", "Kt1", "ones"], [bank], 512)
-        for j in range(rep):
-            for w in ("Pm", "P11"):
-                mm(T[bank][:, j:512:rep], w, child, False, j == rep - 1 and w == "P11", [cn], [bank] + ([more] if more else []), n)
-
-    def bits(R, B, plan, c0, c1, then):
-        j = c0
-        while j < c1:
-            e = j + 1
-            while e < c1 and plan[e] == plan[j] and e - j < P["grp"]:
-                e += 1
-            cs = slice(512 * j, 512 * e)
-            rn = sum([then["rn"](x) for x in range(j, e)], [])
-            bn = ["%s%d" % (B, x) for x in range(j, e)]
-            if plan[j] == "v":
-                ts(T[B][:, cs], T[R][:, cs], H2, None, A.is_ge, None, rn, bn, 512 * (e - j), 0.5)
-            else:
-                act_(T[B][:, cs], T[R][:, cs], F.Sigmoid, rn, bn, 512 * (e - j), bias=-512.0 * (H2 - 0.25), scale=512.0)
-            for x in range(j, e):
-                then["sum"](x)
-            j = e
-
-    def key_open(key):
-        mm(T[key][:], "I", T.crow[:], True, False, ["crow0", "crow1"], [key], 512)
-        mm(T[key][:, 0:M], "I", T.af[:], False, False, ["af"], [key], M)
-        for h in range(2):
-            for d, w in enumerate(("I64", "I2k")):
-                mm(T[key][:, M + 128 * h:M + 128 * h + 128], T.D[:, M * h + 128 * d:M * h + 128 * d + 128], w, False, False, ["D%d" % h], [key], 128)
-
-    def key_scores(key, s, h):
-        for x, w in enumerate(("I19", "I20")):
-            mm(T[key][:, M * x + 128 * h:M * x + 128 * h + 128], T[s][:, M * h + 128 * x:M * h + 128 * x + 128], w, False, h == 1 and x == 1, ["%s%d" % (s, h)], [key], 128)
-
-    def less_sums(bank, o, h):
-        for x in range(2):
-            mm(T[bank][:, o + 128:o + 256], "nI", T.Tr[:, M * h + 128 * x:M * h + 128 * x + 128], False, False, ["Tr%d" % h], [bank], 128)
+        if t == 0:
+            ops[-1]["behind"] = P["early"].split()
+        if t == 1:
+            n = NO // 4
+            for j in range(4):
+                iota(T.MK[:, n * j:n * j + n], "Mi%d" % j, [[0, n]], 0, n)
+                ops[-1]["behind"] = ["zin2"]
 
     def extents(t):
-        n = (W_ - M) // P["xon"]
-        for j in range(P["xon"]):
-            if j >= P["xoa"]:
+        wr = ["W", "Wn%d" % (t - 1)]
+        n = NO // 4
+        for j in range(4):
+            if P["xo"][j] == "g":
+                lin("g", T.BI[:, 0:n], T.G[:, GO + n * j:GO + n * j + n], 1.0, 0.0, wr, ["BI"], n)
+                lin("g", T.XO[:, n * j:n * j + n], T.BI[:, 0:n], 1.0, 0.0, ["BI"], ["XO%d" % j], n)
+                continue
+            if P["xo"][j] == "a":
                 xs = slice(n * (j % 2), n * (j % 2) + n)
-                act_(T.XH[:, xs], T.G[:, GO + n * j:GO + n * j + n], F.Identity, ["W", "Wn%d" % (t - 1)], ["XH%d" % (j % 2)], n, bias=H1)
+                act_(T.XH[:, xs], T.G[:, GO + n * j:GO + n * j + n], F.Identity, wr, ["XH%d" % (j % 2)], n, bias=H1)
                 act_(T.XO[:, n * j:n * j + n], T.XH[:, xs], F.Identity, ["XH%d" % (j % 2)], ["XO%d" % j], n, bias=-H1)
                 continue
-            ts(T.XO[:, n * j:n * j + n], T.G[:, GO + n * j:GO + n * j + n], RND, RND, A.add, A.subtract, ["W", "Wn%d" % (t - 1)], ["XO%d" % j], n)
-        names = ["XO%d" % j for j in range(P["xon"])] + ["XO6"]
-        k = P["xon"] // 2
-        dma(T.yx[:, 0:n * k], T.XO[:, 0:n * k], names[:k], [], 128 * n * k * 2)
-        dma(T.yx[:, n * k:W_], T.XO[:, n * k:W_], names[k:], [], 128 * (W_ - n * k) * 2)
-        return names[:P["xok"]]
+            ts(T.XO[:, n * j:n * j + n], T.G[:, GO + n * j:GO + n * j + n], RND, RND, A.add, A.subtract, wr, ["XO%d" % j], n)
+        for a, b in P["xs"]:
+            lo, hi = n * a, min(n * b, W_)
+            dma(T.yx[:, lo:hi], T.XO[:, lo:hi], ["XO%d" % j for j in range(a, b)], [], 128 * (hi - lo) * 2)
 
-    def scores(t):
-        pr = t % 2
-        cn = "CE%d" % pr
-        hi = V + M * t
+    def gather(t):
         wr = ["W"] + (["Wn%d" % (t - 1)] if t else [])
-        rep2 = P["rep2"][t]
-        if rep2:
-            limits("TC1", T.CE[:, 2 * M * pr:2 * M * pr + M], cn, 2)
-        else:
-            for h in range(2):
-                limits("TC%d" % h, T.CE[:, 2 * M * pr + 128 * h:2 * M * pr + 128 * h + 128], cn, 4)
-        dq, d1, s0, s1 = P["dq"][t]
-        if rep2:
-            s0 = s1 = 0
-        gq = [[], [], [], []]
-        cuts = sorted(set([0, dq, 128, 128 + d1, M] + ([64] if s0 else []) + ([192] if s1 else [])))
-        for i0, i1 in zip(cuts, cuts[1:]):
-            e = "v" if i1 <= dq or 128 < i1 <= 128 + d1 else "a"
-            nm = "GA%d" % i0
-            for q in range(i0 // 64, (i1 + 63) // 64):
-                gq[q].append(nm)
-            win = T.G[:, GO:GO + hi].indirect(T.au[:, i0:i1])
-            if t < RO - 1 and e in P["zq"][t]:
-                wr = wr + ["zout%d" % t]
-            if e == "v":
-                copy(T.GA[:, 16 * i0:16 * i1], win, wr + ["av"] + ["au"] * (i1 > 64), [nm], 16 * (i1 - i0), gc)
-            else:
-                act_(T.GA[:, 16 * i0:16 * i1], win, F.Copy, wr + ["au", "av"], [nm], 16 * (i1 - i0), rate=gc)
-        ga = [gq[0] + gq[1], gq[2] + gq[3]]
-        lin("v", T.af[:], T.au[:], 1.0, -1024.0, ["au", "av"] + ga[P["afl"] - 1] * (P["afl"] > 0), ["af"], M, vrate=0.5)
-        if t < RO - 1 and P["zl"][t]:
-            zpath(t, ga[P["zl"][t] - 1])
+        for e, a, b in runs(P["ga"][t]):
+            win = T.G[:, GO:GO + V + M * t].indirect(T.au[:, 16 * a:16 * b])
+            rd = wr + ["av"] * (a < 4) + ["aw"] * (a < 8 and b > 4) + ["au"] * (b > 8) + (["zout%d" % t] if t < RO - 1 and e in P["zq"][t] else [])
+            nm = ["GA%d" % x for x in range(a, b)]
+            lin(e, T.GA[:, M * a:M * b], win, 1.0, -Y0 * LO, rd, nm, M * (b - a), gc)
         for h in range(2):
             lp = P["LPb"][h]
             hs = slice(M * h, M * h + M)
             for k in range(16):
-                mm(T[lp][:, k:512:16], T.GA[:, 2048 * h + k:2048 * h + 2048:16], T.sel[:], True, True, ga[h] + ["sel%d" % o for o in range(4)], [lp], 32, True)
+                mm(T[lp][:, k:512:16], T.GA[:, 2048 * h + k:2048 * h + 2048:16], T.sel[:], True, True,
+                   ["GA%d" % (8 * h + j) for j in range(8)] + ["sel%d" % o for o in range(4)], [lp], 32, True)
             lin("a", T.Rd[:, hs], T[lp][:, M:2 * M], 1.0, 0.0, [lp], ["Rd%d" % h], M)
             if P["tra"][t][h]:
                 act_(T.Ta[:, hs], T[lp][:, 0:M], F.Identity, [lp], ["Ta%d" % h], M, bias=RND)
@@ -608,48 +496,90 @@ def build_ops(g, core, T, topo, case=None):
             else:
                 ts(T.Tr[:, hs], T[lp][:, 0:M], RND, RND, A.add, A.subtract, [lp], ["Tr%d" % h], M)
             tt(T.D[:, hs], T[lp][:, M:2 * M], T.Rd[:, hs], A.subtract, [lp, "Rd%d" % h], ["D%d" % h], M)
-        key_open("KC")
-        stored = extents(t) if t == RO - 1 else []
 
-        def cols(x, j):
-            if rep2:
-                o = 512 * x + M * (j % 2)
-                return slice(o + j // 2, o + M, 2)
-            return slice(512 * x + j, 512 * x + 512, 4)
+    def scores(t, x, lims, banks):
+        pr = t % 2
+        cn, ac = "CE%d" % pr, "act%d" % pr
+        R, B, s = "R" + x, "B" + x, "s" + x
+        c0 = 2 * M * pr + M * (x == "E")
+        blocks = sorted([(h, p) for h in range(2) for p in range(2)], key=lambda b: (banks[b[0]][b[1]], b[1], b[0]))
+        at = {b: 128 * j for j, b in enumerate(blocks)}
+        held = {k: [b for b in blocks if banks[b[0]][b[1]] == k] for k in set(banks[0] + banks[1])}
+        opened = set()
+
+        def into(h, p, lhs, rhs, r, n, k=0, step=1):
+            bank = banks[h][p]
+            o = at[h, p] - at[held[bank][0]]
+            mm(T[bank][:, o + k:o + 128:step], lhs, rhs, bank not in opened, False, r, [bank], n)
+            opened.add(bank)
+
+        def piece(j):
+            if len(lims) == 2:
+                h, r = divmod(j, 4)
+                return T.GA[:, 2048 * h + r:2048 * h + 2048:4], range(8 * h, 8 * h + 8), [(h, r + 4 * q, slice(q, 512, 4)) for q in range(4)]
+            return T.GA[:, j:4096:8], range(16), [(h, j + 8 * q, slice(M * h + q, M * h + M, 2)) for q in range(2) for h in range(2)]
+
+        def sums(j, buf, p, w):
+            for h, k, cs in piece(j)[2]:
+                into(h, p, T[buf][:, 512 * j + cs.start:512 * j + cs.stop:cs.step], T[w][:], [w, "%s%d" % (buf, j)], 8, k, 16)
+        for h, p in blocks:
+            if x == "E":
+                into(h, p, acts(t, 128 * h, 128 * h + 128), T.pb[:], [ac, "pb"], 128)
+            elif p == 0 and banks[h][0] not in opened | {banks[h][1]}:
+                into(h, p, "zb", T.ones[:, 0:8], ["ones"], 8, 0, 16)
         for h in range(2):
-            sb = P["SCb"][h]
-            mm(T[sb][:, 128:M], T.CE[:, 2 * M * pr + 128 * h:2 * M * pr + 128 * h + 128], T.zn[:], True, False, [cn, "zn1"], [sb], 128)
-            for r in range(4):
-                x = 4 * h + r
-                if rep2:
-                    for q in range(2):
-                        tt(T.RC[:, 512 * x + M * q:512 * x + M * q + M], T.GA[:, 2048 * h + r + 4 * q:2048 * h + 2048:8], T.TC1[:, M * h:M * h + M], A.add,
-                           ga[h] + ["TC1"], [("RC%d", "RD%d")[q] % x], M)
-                elif (s0, s1)[h]:
-                    for q in range(2):
-                        o = 2048 * h + 1024 * q
-                        tt(T.RC[:, 512 * x + M * q:512 * x + M * q + M], T.GA[:, o + r:o + 1024:4], T["TC%d" % h][:, M * q:M * q + M], A.add,
-                           gq[2 * h + q] + ["TC%d" % h], [("RC%d", "RD%d")[q] % x], M)
-                else:
-                    tt(T.RC[:, 512 * x:512 * x + 512], T.GA[:, 2048 * h + r:2048 * h + 2048:4], T["TC%d" % h][:], A.add,
-                       ga[h] + ["TC%d" % h] + (stored if h >= P["xof"] else []), ["RC%d" % x, "RD%d" % x], 512)
-                for j in range(4):
-                    mm(T[sb][:, 128 + r + 4 * j:M:16], T.RC[:, cols(x, j)], T.grp[:], False, False, ["grp", "RC%d" % x, "RD%d" % x], [sb], 8)
+            into(h, 1, T.CE[:, c0 + 128 * h:c0 + 128 * h + 128], T.zn[:], [cn, "zn1"], 128)
+        for h, lim in enumerate(lims):
+            rep, n = 2 * len(lims), M // len(lims)
+            mm(T[lim][:], T.Kt[:], T.ones[:], True, False, ["Kt0", "Kt1", "ones"], [lim], 512)
+            for j in range(rep):
+                for w in ("Pm", "P11"):
+                    mm(T[lim][:, j:512:rep], w, T.CE[:, c0 + n * h:c0 + n * h + n], False, j == rep - 1 and w == "P11", [cn], [lim], n)
+            for j in range(8 // len(lims) * h, 8 // len(lims) * (h + 1)):
+                src, need, _ = piece(j)
+                tt(T[R][:, 512 * j:512 * j + 512], src, T[lim][:], A.add, ["GA%d" % q for q in need] + [lim], ["%s%d" % (R, j)], 512)
+                sums(j, R, 1, "grq")
+        for e, a, b in runs(P["bits" + x][t]):
+            cs = slice(512 * a, 512 * b)
+            rn, bn = ["%s%d" % (R, j) for j in range(a, b)], ["%s%d" % (B, j) for j in range(a, b)]
+            if e == "v":
+                ts(T[B][:, cs], T[R][:, cs], H2, None, A.is_ge, None, rn, bn, 512 * (b - a), 0.5)
+            else:
+                act_(T[B][:, cs], T[R][:, cs], F.Sigmoid, rn, bn, 512 * (b - a), bias=-512.0 * (H2 - 0.25), scale=512.0)
+            for j in range(a, b):
+                sums(j, B, 0, "grp")
+        for h in range(2):
+            for j in range(2):
+                into(h, 1, "nI2", T.Tr[:, M * h + 128 * j:M * h + 128 * j + 128], ["Tr%d" % h], 128)
+        for bank in sorted(held):
+            o, n = at[held[bank][0]], 128 * len(held[bank])
+            lin("a", T[s][:, o:o + n], T[bank][:, 0:n], 1.0, -TH - 32.0 * (x == "E"), [bank], ["%s%d" % (s, 2 * h + p) for h, p in held[bank]], n)
+        return at
 
-            def sums(x, sb=sb):
-                for j in range(4):
-                    mm(T[sb][:, x % 4 + 4 * j:128:16], T.BC[:, cols(x, j)], T.grp[:], False, False, ["grp", "BC%d" % x], [sb], 8)
-            bits("RC", "BC", P["bitsC"][t], 4 * h, 4 * h + 4, {"rn": lambda x: ["RC%d" % x, "RD%d" % x], "sum": sums})
-            less_sums(sb, 0, h)
-            lin("a", T.sC[:, M * h:M * h + M], T[sb][:, 0:M], 1.0, 0.0, [sb], ["sC%d" % h], M)
-            key_scores("KC", "sC", h)
-        return ga
+    def keys(s, at, ka, kb, halves):
+        n = 128 * len(halves)
+        o = n * (ka == kb)
+        if o:
+            mm(T[ka][:, 0:2 * n], "I2k", T.crow[:, M - n:M + n], True, False, ["crow0", "crow1"], [ka], 2 * n)
+        else:
+            mm(T[ka][:, 0:n], "I2k", T.crow[:, 0:n], True, False, ["crow0"], [ka], n)
+            mm(T[kb][:, 0:n], "I2k", T.crow[:, M:M + n], True, False, ["crow1"], [kb], n)
+        mm(T[ka][:, 0:n], "I", T.af[:, 128 * halves[0]:128 * halves[0] + n], False, False, ["af"], [ka], n)
+        for j, h in enumerate(halves):
+            for d, w in enumerate(("I64", "I2k")):
+                mm(T[kb][:, o + 128 * j:o + 128 * j + 128], T.D[:, M * h + 128 * d:M * h + 128 * d + 128], w, False, False, ["D%d" % h], [kb], 128)
+        for j, h in enumerate(halves):
+            for p, (bank, q) in enumerate(((ka, 128 * j), (kb, o + 128 * j))):
+                mm(T[bank][:, q:q + 128], T[s][:, at[h, p]:at[h, p] + 128], "I19", False, False, ["%s%d" % (s, 2 * h + p)], [bank], 128)
+        return T[ka][:, 0:n], T[kb][:, o:o + n]
 
-    def post_c(t):
+    def post_c(t, at):
         pr = t % 2
         l = slice(16 * pr, 16 * pr + 16)
-        tt(T.m1[:], T.KC[:, 0:M], T.KOC[:, M * t:M * t + M], A.max, ["KC", "KOC%d" % t], ["m1"], M)
-        tt(T.m2[:], T.KC[:, M:2 * M], T.m1[:], A.max, ["KC", "m1"], ["m2"], M)
+        kb = P["kb"][t]
+        ya, yb = keys("sC", at, "KC", kb, (0, 1))
+        tt(T.m1[:], yb, T.KOC[:, M * t:M * t + M], A.max, [kb, "KOC%d" % t], ["m1"], M)
+        tt(T.m2[:], ya, T.m1[:], A.max, ["KC", "m1"], ["m2"], M)
         if t < RO - 1:
             add("v", lambda: g.vector.transpose(T.TT[:], T.m2[:]), ["m2"], ["TT"], vc(M))
             add("v", lambda: g.vector.tensor_tensor_scan(T.SC[:], T.sm[:], T.TT[:], 0.0, A.mult, A.max), ["sm", "TT"], ["SC"], vc(M))
@@ -660,143 +590,59 @@ def build_ops(g, core, T, topo, case=None):
             tt(T.mx[:], T.KC[:, 0:16], T.ovr[:, l], A.max, ["KC", "ovr%d" % pr], ["mx"], 16)
             ts(T.pout[:, 16 * t:16 * t + 16], T.mx[:], 4095, None, A.bitwise_and, None, ["mx"], ["pout%d" % t], 16)
             send(T.pin[:, 16 * (t + 1):16 * (t + 2)], T.pout[:, 16 * t:16 * t + 16], T.sem["pa%d" % (t + 1)], ["pout%d" % t], ["pin%d" % (t + 1)])
+            later(t)
         if P["ract"][t]:
             act_(T.r13a[:], T.m2[:], F.Identity, ["m2"], ["r13a"], M, bias=RND13)
             act_(T.r13[:], T.r13a[:], F.Identity, ["r13a"], ["r13"], M, bias=-RND13)
         else:
             ts(T.r13[:], T.m2[:], RND13, RND13, A.add, A.subtract, ["m2"], ["r13"], M)
-        tt(T.L[:].indirect(T.off[:, l]), T.m2[:], T.r13[:], A.subtract, ["m2", "r13", "off%d" % pr],
+        tt(T.L[:].indirect(T.off[:, 32 * pr:32 * pr + 16]), T.m2[:], T.r13[:], A.subtract, ["m2", "r13", "off%d" % pr],
            ["L", "Ln"] + (["Li%d" % j for j in range(4)] if t == 0 else []), M, sc)
 
-    def part_e(t, ga):
-        pr = t % 2
-        c = slice(M * pr, M * pr + M)
-        cn, ac = "CE%d" % pr, "act%d" % pr
-        e0 = 2 * M * pr + M
-        limits("TE0", T.CE[:, e0:e0 + M], cn, 2)
-        if P["lna"][t]:
-            for h in range(2):
-                mm(T.TE1[:, M * h:M * h + M], T.act[:, M * pr + 128 * h:M * pr + 128 * h + 128], T.pb[:], h == 0, False, [ac, "pb0", "pb1"], ["TE1"], M)
-        for h in range(2):
-            mm(T.TE1[:, M * h + 128:M * h + M], T.CE[:, e0 + 128 * h:e0 + 128 * h + 128], T.zn[:], h == 0 and not P["lna"][t], False, [cn, "zn1"], ["TE1"], 128)
-        for h in range(2):
-            less_sums("TE1", M * h, h)
-
-        def sums(x, buf="BE", o=0):
-            for j in range(2):
-                for h in range(2):
-                    mm(T.TE1[:, M * h + o + x + 8 * j:M * h + o + 128:16], T[buf][:, 512 * x + M * h + j:512 * x + M * h + M:2], T.grp[:], False, False, ["grp"] + (re(x) if o else ["BE%d" % x]), ["TE1"], 8)
-
-        def re(x):
-            return ["RE%d" % (10 * q + x) for q in range(P["esp"])]
-        for x in range(8):
-            if x < P["pee"][t]:
-                b = "TC%d" % ((x + 1) % 2)
-                limits(b, T.CE[:, e0:e0 + M], cn, 2, "lim")
-                for q in range(4):
-                    mm(T[b][:, 128 * q:128 * q + 128], T.If[:], T.GA[:, 1024 * q + x:1024 * q + 1024:8], False, q == 3, ga[q // 2] + ["If", "lim"], [b], 128, True)
-                act_(T.RE[:, 512 * x:512 * x + 512], T[b][:], F.Identity, [b], re(x), 512)
+    def post_e(t, at):
+        n0, parts = V + M * t, 1 + (t == RO - 1)
+        n = M // parts
+        for h in range(parts):
+            key = ("KE", "KC")[h]
+            ya, yb = keys("sE", at, key, key, (h,) if parts == 2 else (0, 1))
+            hs, x = slice(n * h, n * h + n), "%d" % h
+            cs = slice(n0 + n * h, n0 + n * h + n)
+            tt(T.e1[:, hs], ya, koe(t, n * h, n * h + n), A.max, [key, "KOE%d" % t], ["e1" + x], n)
+            tt(T.e2[:, hs], yb, T.e1[:, hs], A.max, [key, "e1" + x], ["e2" + x], n)
+            ts(T.e3[:, hs], T.e2[:, hs], 4095, None, A.bitwise_and, None, ["e2" + x], ["e3" + x], n)
+            if t < RO - 1:
+                lin("a", T.L[:, cs], T.e3[:, hs], 1.0, 0.0, ["e3" + x], ["Ln"], n)
             else:
-                n = 512 // P["esp"]
-                for q in range(P["esp"]):
-                    tt(T.RE[:, 512 * x + n * q:512 * x + n * q + n], T.GA[:, 8 * n * q + x:8 * n * q + 8 * n:8], T.TE0[:, n * q:n * q + n], A.add,
-                       ga[0] + ga[1] + ["TE0"], [re(x)[q]], n)
-            sums(x, "RE", 128)
-        bits("RE", "BE", P["bitsE"][t], 0, 8, {"rn": re, "sum": sums})
-        lin("a", T.sE[:], T.TE1[:], 1.0, -32.0 * P["lna"][t], ["TE1"], ["sE0", "sE1"], 512)
-        key_open("KE")
-        if not P["lna"][t]:
-            mm(T.TE0[:, 0:M], "I", T.act[:, c], True, True, [ac], ["TE0"], M)
-        for h in range(2):
-            key_scores("KE", "sE", h)
-        tt(T.e1[:], T.KE[:, 0:M], T.KOE[:, c], A.max, ["KE", "KOE%d" % pr], ["e1"], M)
-        tt(T.e2[:], T.KE[:, M:2 * M], T.e1[:], A.max, ["KE", "e1"], ["e2"], M)
-        ts(T.e3[:], T.e2[:], 4095, None, A.bitwise_and, None, ["e2"], ["e3"], M)
-        n0 = V + M * t
-        if P["lna"][t]:
-            lin("a", T.L[:, n0:n0 + M], T.e3[:], 1.0, 0.0, ["e3"], ["Ln"], M)
-        else:
-            tt(T.L[:, n0:n0 + M], T.TE0[:, 0:M], T.e3[:], A.mult, ["e3", "TE0"], ["Ln"], M)
-
-    def last_e(t, ga):
-        pr = t % 2
-        cn, ac = "CE%d" % pr, "act%d" % pr
-        e0, n0 = 2 * M * pr + M, V + M * t
-        for h in range(2):
-            lim, sb, key, row = "TC%d" % h, ("TE1", "TE0")[h], ("KE", "KC")[h], ("X0", "X1")[h]
-            hs = slice(128 * h, 128 * h + 128)
-            child = T.CE[:, e0 + 128 * h:e0 + 128 * h + 128]
-            limits(lim, child, cn, 4)
-            mm(T[sb][:, 128:M], child, T.zn[:], True, False, [cn, "zn1"], [sb], 128)
-            less_sums(sb, 0, h)
-
-            def sums(x, buf="BE", o=0, sb=sb):
-                for j in range(4):
-                    mm(T[sb][:, o + x % 4 + 4 * j:o + 128:16], T[buf][:, 512 * x + j:512 * x + 512:4], T.grp[:], False, False, ["grp", "%s%d" % (buf, x)], [sb], 8)
-            for x in range(4 * h, 4 * h + 4):
-                tt(T.RE[:, 512 * x:512 * x + 512], T.GA[:, 2048 * h + x % 4:2048 * h + 2048:4], T[lim][:], A.add, ga[h] + [lim], ["RE%d" % x], 512)
-                sums(x, "RE", 128)
-            bits("RE", "BE", P["bitsE"][t], 4 * h, 4 * h + 4, {"rn": lambda x: ["RE%d" % x], "sum": sums})
-            lin("a", T.sE[:, M * h:M * h + M], T[sb][:, 0:M], 1.0, 0.0, [sb], ["sE%d" % h], M)
-            mm(T[key][:, 0:M], "I", T.crow[:, 128:384], True, False, ["crow0", "crow1"], [key], M)
-            mm(T[key][:, 0:128], "I", T.af[:, hs], False, False, ["af"], [key], 128)
-            for d, w in enumerate(("I64", "I2k")):
-                mm(T[key][:, 128:M], T.D[:, M * h + 128 * d:M * h + 128 * d + 128], w, False, False, ["D%d" % h], [key], 128)
-            for x, w in enumerate(("I19", "I20")):
-                mm(T[key][:, 128 * x:128 * x + 128], T.sE[:, M * h + 128 * x:M * h + 128 * x + 128], w, False, x == 1, ["sE%d" % h], [key], 128)
-            mm(T[row][:, 0:128], "I", T.act[:, M * pr + 128 * h:M * pr + 128 * h + 128], True, True, [ac], [row], 128)
-            tt(T.e1[:, hs], T[key][:, 0:128], T.KOE[:, M * pr + 128 * h:M * pr + 128 * h + 128], A.max, [key, "KOE%d" % pr], ["e1%d" % h], 128)
-            tt(T.e2[:, hs], T[key][:, 128:M], T.e1[:, hs], A.max, [key, "e1%d" % h], ["e2%d" % h], 128)
-            ts(T.e3[:, hs], T.e2[:, hs], 4095, None, A.bitwise_and, None, ["e2%d" % h], ["e3%d" % h], 128)
-            cs = slice(n0 + 128 * h, n0 + 128 * h + 128)
-            tt(T.L[:, cs], T[row][:, 0:128], T.e3[:, hs], A.mult, ["e3%d" % h, row, "Ln"], ["Lm%d" % h], 128)
-            if P["eh"] == 2:
-                dma(T.yn[:, cs], T.L[:, cs], ["Lm%d" % h], [], 128 * 128 * 4)
-        if P["eh"] == 1:
-            dma(T.yn[:, n0:W_], T.L[:, n0:W_], ["Lm0", "Lm1"], [], 128 * M * 4)
+                lin("a", T.L[:, cs], T.e3[:, hs], 1.0, 0.0, ["e3" + x, "Ln"], ["Lm" + x], n)
+                dma(T.yn[:, cs], T.L[:, cs], ["Lm" + x], [], 128 * n * 4)
 
     rnd[0] = 0
     upath(0)
     prep(0)
-    if P["zf"]:
-        zpath(0)
     for t in range(RO):
         lists(t)
-        if t < RO - 1 and not P["zl"][t] and not (t == 0 and P["zf"]):
+        if t < RO - 1:
             zpath(t)
         if not P["frl"][t]:
             fresh(t)
-        ga = scores(t)
+        gather(t)
+        if t == RO - 1:
+            extents(t)
+        at = scores(t, "C", ("TC0", "TC1"), P["sb"][t])
         marks(t)
-        if t == 0:
-            for j in range(4):
-                cs = slice(512 * j, 512 * j + 512)
-                lin(P["li"][j], T.L[:, cs], T.NB[:, cs], 1.0, 0.0, ["NB"], ["Li%d" % j], 512)
-        if t < RO - 1 and not P["ul"][t]:
+        if t < RO - 1:
             rnd[0] = t + 1
             upath(t + 1)
             rnd[0] = t
-        post_c(t)
-        if t < RO - 1:
-            later(t)
-            if P["ul"][t]:
-                rnd[0] = t + 1
-                upath(t + 1, ["mx"])
-                rnd[0] = t
-            if P["frl"][t]:
-                fresh(t)
+        post_c(t, at)
+        if P["frl"][t]:
+            fresh(t)
         if t == RO - 1:
-            n0 = V + M * t
-            dma(T.yn[:, 0:n0], T.L[:, 0:n0], ["L"], [], 128 * n0 * 4, P["ynlat"])
-            if P["eh"]:
-                last_e(t, ga)
-                break
-        part_e(t, ga)
+            dma(T.yn[:, 0:NO], T.L[:, 0:NO], ["L"], [], 128 * NO * 4)
+        post_e(t, scores(t, "E", *P["eb"][t]))
         if t < RO - 1:
             rnd[0] = t + 1
             prep(t + 1)
-        else:
-            dma(T.yn[:, n0:W_], T.L[:, n0:W_], ["Ln"], [], 128 * M * 4)
     return fuse(ops)
 
 
@@ -829,6 +675,7 @@ def link(ops):
         if o["eng"] == "s":
             soft.update(opener.get("s", []))
             opener["s"] = [n]
+        soft.update(lastw[x] for x in o.get("behind", []) if x in lastw)
 
         def dep(m):
             p = ops[m]
@@ -859,7 +706,7 @@ def link(ops):
             if x in BANKS:
                 eng, cur, prev = bank.get(x, (None, [], []))
                 if o["eng"] == "t":
-                    if o["flags"]["start"]:
+                    if o["flags"]["start"] or o.get("again"):
                         opener[x] = n
                     o["group"] = opener[x]
                 if eng == o["eng"]:
@@ -1037,41 +884,170 @@ def schedule(ops, cases):
                 first = now
     best = first
 
-    def mark(order):
-        return sum(math.log(replay(ops, order, c)) for c in cases) / len(cases)
-    cur, order = best[0], best[1]
-    top = (cur, order)
-    pairs = None
-    for it in range(P["swaps"]):
-        if pairs is None:
-            pairs = blocked(ops, order, cases[it % len(cases)]) + blocked(ops, order, cases[(it + 2) % len(cases)])
-            pos = {j: x for x, j in enumerate(order)}
+    return shift(ops, best[1], cases, P["steps"], P["seed"]) if P["steps"] else best
+
+
+def shift(ops, order, cases, steps, seed, span=6, keep=20):
+    n, nc = len(ops), len(cases)
+    eng = ["vatgs".index(o["eng"]) for o in ops]
+    hard, soft = [o["hard"] for o in ops], [o["soft"] for o in ops]
+    hs, ss = [[] for _ in ops], [[] for _ in ops]
+    for j in range(n):
+        for m in hard[j]:
+            hs[m].append(j)
+        for m in soft[j]:
+            ss[m].append(j)
+    cost = [[c[j][0] for j in range(n)] for c in cases]
+    lat = [[c[j][1] for j in range(n)] for c in cases]
+    bws = [[c[j][2] for j in range(n)] for c in cases]
+
+    def times(order, c):
+        co, la, bw = cost[c], lat[c], bws[c]
+        ready, st, done, endq, free, dm = [0.0] * n, [0.0] * n, [0.0] * n, [0.0] * n, [0.0] * 5, 0.0
+        for j in order:
+            r = 0.0
+            for m in hard[j]:
+                if done[m] + HOP > r:
+                    r = done[m] + HOP
+            for m in soft[j]:
+                if endq[m] > r:
+                    r = endq[m]
+            ready[j] = r
+            e = eng[j]
+            if free[e] > r:
+                r = free[e]
+            st[j] = r
+            endq[j] = free[e] = r = r + co[j]
+            r += la[j]
+            if bw[j]:
+                dm = r = max(dm + bw[j], r)
+            done[j] = r
+        own, tail, nxt, dm = [0.0] * n, [0.0] * n, [0.0] * 5, 0.0
+        for j in reversed(order):
+            q = 0.0
+            for m in hs[j]:
+                if tail[m] + HOP > q:
+                    q = tail[m] + HOP
+            if bw[j]:
+                q = max(q, dm)
+                dm = q + bw[j]
+            q += la[j]
+            for m in ss[j]:
+                if tail[m] > q:
+                    q = tail[m]
+            own[j] = q
+            e = eng[j]
+            if nxt[e] > q:
+                q = nxt[e]
+            tail[j] = nxt[e] = q + co[j]
+        return ready, st, own, tail, max(done)
+
+    def moved(order, pos, a, b, forth):
+        seg = order[pos[a]:pos[b] + 1]
+        e0 = eng[a]
+        move, touched = {b if forth else a}, set()
+        for x in (reversed(seg) if forth else seg):
+            if x in move or eng[x] in touched:
+                if eng[x] == e0:
+                    if x != (b if forth else a):
+                        return None
+                else:
+                    touched.add(eng[x])
+                move.add(x)
+                move.update(hard[x] + soft[x] if forth else hs[x] + ss[x])
+        one, two = [x for x in seg if x in move], [x for x in seg if x not in move]
+        return order[:pos[a]] + (one + two if forth else two + one) + order[pos[b] + 1:]
+    best = None
+    ban = {}
+    since = kick = 0
+    for it in range(steps):
+        tm = [times(order, c) for c in range(nc)]
+        now = sum(math.log(t[4]) for t in tm) / nc
+        if best is None or now < best[0] - 1e-9:
+            best, since = (now, order), 0
+        since += 1
+        if since > P["stall"]:
+            order, since, ban, kick = best[1], 0, {}, P["kick"]
+            continue
+        pos = {j: x for x, j in enumerate(order)}
+        rows = [[] for _ in range(5)]
+        for j in order:
+            rows[eng[j]].append(j)
         seed = (seed * 1103515245 + 12345) % (1 << 31)
-        b, j = pairs[(seed >> 8) % len(pairs)]
-        seg = order[pos[b]:pos[j] + 1]
-        if (seed >> 5) % 2:
-            move = {j}
-            for x in reversed(seg):
-                if x in move:
-                    move.update(ops[x]["hard"] + ops[x]["soft"])
-            if b in move:
+        c0 = (seed >> 16) % nc
+        ready, st, own, tail, end = tm[c0]
+        co = cost[c0]
+        cand = []
+        for e in range(4):
+            row = rows[e]
+            for x in range(1, len(row)):
+                j, p = row[x], row[x - 1]
+                if st[j] + tail[j] > end - 1.0 and st[p] + tail[p] > end - 1.0 and st[j] > ready[j] + 0.5:
+                    y = x - 1
+                    while y >= 0 and x - y <= span and st[row[y]] + co[row[y]] > ready[j]:
+                        if row[y] in hard[j] or row[y] in soft[j]:
+                            break
+                        cand.append((e, y, x, True))
+                        y -= 1
+                    y = x
+                    while y < len(row) and y - x < span:
+                        if p in hard[row[y]] or p in soft[row[y]]:
+                            break
+                        if y > x:
+                            cand.append((e, x - 1, y, False))
+                        if own[p] + co[p] >= tail[row[y]]:
+                            break
+                        y += 1
+        marks = []
+        for e, y, x, forth in cand:
+            row = rows[e]
+            seq = [row[x]] + row[y:x] if forth else row[y + 1:x + 1] + [row[y]]
+            val = 0.0
+            for c in range(nc):
+                ready, st, own, tail, end = tm[c]
+                co = cost[c]
+                r = st[row[y - 1]] + co[row[y - 1]] if y else 0.0
+                heads = []
+                crit = False
+                for j in seq:
+                    if ready[j] > r:
+                        r = ready[j]
+                    heads.append(r)
+                    r += co[j]
+                    if st[j] + tail[j] > end - 1.0:
+                        crit = True
+                q = tail[row[x + 1]] if x + 1 < len(row) else 0.0
+                top = 0.0
+                for k in range(len(seq) - 1, -1, -1):
+                    j = seq[k]
+                    if own[j] > q:
+                        q = own[j]
+                    q += co[j]
+                    if heads[k] + q > top:
+                        top = heads[k] + q
+                val += math.log(max(top, end - 300.0) if crit else max(top, end))
+            val /= nc
+            a, b = row[y], row[x]
+            pairs = [(b, z) for z in row[y:x]] if forth else [(z, a) for z in row[y + 1:x + 1]]
+            if any(ban.get(p, -1) > it for p in pairs) and val >= best[0]:
                 continue
-            seg = [x for x in seg if x in move] + [x for x in seg if x not in move]
-        else:
-            move = {b}
-            for x in seg:
-                if x in move:
-                    move.update(succ[x])
-            if j in move:
+            seed = (seed * 1103515245 + 12345) % (1 << 31)
+            marks.append((val + (P["wild"] if kick else 1e-7) * (seed >> 20), a, b, forth, pairs))
+        kick = max(kick - 1, 0)
+        marks.sort(key=lambda m: m[0])
+        spots = []
+        for val, a, b, forth, pairs in marks:
+            if spots and (val > now - P["gain"] or any(pos[a] < y + P["far"] and x < pos[b] + P["far"] for x, y in spots)):
                 continue
-            seg = [x for x in seg if x not in move] + [x for x in seg if x in move]
-        new = order[:pos[b]] + seg + order[pos[j] + 1:]
-        now = mark(new)
-        if now <= cur + P["heat"] * (1.0 - it / P["swaps"]) * ((seed >> 12) % 64) / 64.0:
-            cur, order, pairs = now, new, None
-            if cur < top[0]:
-                top = (cur, order)
-    return top
+            new = moved(order, pos, a, b, forth)
+            if new is not None:
+                order = new
+                spots.append((pos[a], pos[b]))
+                for u, v in pairs:
+                    ban[v, u] = it + keep + (seed >> 12) % keep
+        if not spots:
+            ban = {}
+    return best
 
 
 def backward(ops, succ, done):
@@ -1092,7 +1068,7 @@ def backward(ops, succ, done):
         for e, rs in ready.items():
             if rs:
                 t0 = max(free.get(e, 0.0), min(rt[j] for j in rs))
-                j = max((x for x in rs if rt[x] <= t0 + P["blook"]), key=lambda x: (done[x], x))
+                j = max((x for x in rs if rt[x] <= t0), key=lambda x: (done[x], x))
                 st = max(free.get(e, 0.0), rt[j])
                 if best is None or st < best[0]:
                     best = (st, j, e)
@@ -1247,5 +1223,5 @@ def rank_program(g, core, T, topo):
         if count[e]:
             g.wait_ge(esem[e], count[e])
     for o in ops:
-        if "sem" in o and not o.get("remote") and not o["w"]:
+        if "sem" in o and (o["w"] + ["out"])[0][:3] == "out":
             g.wait_ge(o["sem"], 16)

import math
from concourse.mybir import AluOpType, AxisListType, ActivationFunctionType

A = AluOpType
F = ActivationFunctionType
V, M, KK, RO, TH = 2048, 256, 512, 4, 12
W_ = V + M * RO
NO = W_ - M
DUM = W_ + 16
WC = DUM + M
GO = W_
SC_ = 1 << 19
K0 = 1 << 15
OV = 1 << 23
BIG = 3 * (1 << 22)
RND = 1.5 * 2.0 ** 23
RND13 = 1.5 * 2.0 ** 36
LO = 2.0 ** -11
H1 = 1536.0
H2 = 768.0
SG = 2.0 ** -9
Y0 = 128

P = {"ga": ["vVVVaAAAaAAAAAvV"] * 4, "bitsC": ["aAavaAvV"] * 4, "bitsE": ["aAaAaAaA"] * 3 + ["aAaAaAvV"],
     "tra": [[1, 0]] * 4, "ract": [1, 1, 1, 0], "xo": "ggga", "xs": ((0, 1), (1, 2), (3, 5), (2, 3)), "li": "gggg", "early": "sel0 sel1 sel2 sel3 grp", "frl": [1, 1, 1, 0], "zq": ["", "a", "a"], "pnv": 0, "mv": 1,
     "eng": {"Ln": "g"}, "wi": "vavg", "rsg": 0, "rsv": 13, "loads": "pwzkxn", "frb": "TC1", "LPb": ("X1", "X0"),
     "sb": [(("KE", "TE1"), ("KE", "TE1"))] * 4, "kb": ["TC0"] * 4,
     "eb": [(("TE0",), (("TE1", "TE1"), ("TE1", "TE1")))] * 3 + [(("TE0", "TC1"), (("TE1", "TE1"), ("X1", "X1")))],
     "ce": {"Bo": "v", "dum": "a", "Ka": "v", "Kb": "a", "Kn": "v", "Dhi": "v", "I11": "a", "crow": "a", "kcol": "a", "zn1": "v", "nI2": "v", "grp": "g", "Bw": "a"},
     "fac": 1.1, "g": 1.56, "sc": 3.8, "pe": 0.42, "fix": 50.0, "afix": 22.0, "rem": 2200.0, "dl": 1500.0, "dr": 250.0, "zs": [4000.0, 1500.0], "acc": 1.5,
     "look": 600.0, "cap": 500.0, "turn": 21000.0, "fb": 2, "tries": 1000, "steps": 350, "far": 100, "gain": -0.001, "stall": 100, "kick": 10, "wild": 2e-5, "warm": 0.001, "seed": 1}
TURN = {"v": "av GA Wn ovr XO RC*6 BC*1 Tr*1 D*1 RC BC u+ Tr D RE*1 m r TT SC RE*1 mx pout RE*4 pf+ RE BE EQ*8+ Cc+ CE+ EQ+ L pn+ e*2 qf+ s+ off+ e W*1+ Lm W+",
        "a": "GA Ta*1 Rd*1 BC*1 Tr*1 BC*1 Ta Tr Rd sC*1 BC sC u+ uu+ BE*1 r13a r XH XO MK KOE Li BE*1 pf+ pu+ pv+ prow+ xp+ PG+ BE*1 qu+ qf+ MG+ BE act+ sE Gq+ rk+ Gn+ Ln aw+ au+ af+ pn+ zy+ zout+"}
CASES = [dict(fac=1.0, fix=30.0, afix=15.0, rem=2500.0, dl=1800.0, dr=220.0, wake=110.0), dict(fac=1.45, fix=40.0, g=1.06, sc=1.8, rem=2400.0, dr=320.0, wake=60.0),
         dict(fac=1.2, fix=40.0, g=1.95, sc=5.4, rem=3000.0, dl=2000.0, dr=210.0, wake=80.0),
         dict(fac=1.25, fix=30.0, afix=15.0, g=1.3, sc=3.0, rem=3000.0, zs=[6000.0, 2000.0], dl=1800.0, wake=130.0, dr=250.0),
         dict(fac=1.05, fix=40.0, g=1.1, sc=2.0, rem=2400.0, dr=300.0, wake=80.0)]

f32, bf, f16, i32, u16 = "float32", "bfloat16", "float16", "int32", "uint16"


def _sb(cols, d):
    return ("sbuf", [128, cols], d)


DIAG = {"I": 1.0, "nI": -1.0, "I2k": 2048.0, "n1280": -1280.0, "I11": LO, "n24k": -BIG / 512.0, "I64": 64.0, "I19": float(SC_), "nI2": -2.0}
MATS = list(DIAG) + ["Pm", "P11", "Dlo", "Dhi", "blk", "Bo", "Bw", "zb", "R16"]
SCRATCH = {
    "G": _sb(GO + WC, f32), "L": _sb(WC, f32), "MK": _sb(WC, f32), "PAR": _sb(W_, f32),
    "NB": _sb(V, i32), "XC": _sb(V, bf), "XO": _sb(W_, bf), "XH": _sb(1408, f16),
    "K1": _sb(KK, bf), "KF": _sb(2 * KK, f32), "wi": _sb(4, i32), "wf": _sb(4, f32),
    "pin": _sb(16 * RO, i32), "pout": _sb(16 * RO, i32), "zin": _sb(M * RO, bf), "zout": _sb(M * RO, bf),
    "GA": _sb(16 * M, f32), "RC": _sb(16 * M, f16), "RE": _sb(16 * M, f16), "BC": _sb(16 * M, bf), "BE": _sb(16 * M, bf), "EQ": ("sbuf", [128, 16, M], bf),
    "MX": _sb(128 * len(MATS), bf), "ones": _sb(512, bf), "zf": _sb(128, f32), "o16": _sb(128, f32),
    "zn": _sb(128, bf), "grp": _sb(8, bf), "grq": _sb(8, bf), "BI": _sb(NO // 4, i32), "sel": _sb(32, f32), "Kn": _sb(128, bf), "Kt": _sb(128, bf), "c1k": _sb(64, f16),
    "SW": _sb(144, bf), "SA": _sb(144, bf), "S1": _sb(144, bf), "RS": _sb(2048, bf),
    "SWP": _sb(512, f32), "sm": _sb(M, bf), "crow": _sb(512, f16), "thr": _sb(M, bf), "KOC": _sb(M * RO, f32), "lo": _sb(M, bf), "hi": _sb(M * RO, bf),
    "mkc": _sb(2 * M, f32), "pi": _sb(4, i32), "lane": _sb(4, f32), "srow": _sb(16, f32), "lm": _sb(16, f32),
    "pat": _sb(16, f32), "pm": _sb(16, f32), "dum": _sb(32, f32),
    "pf16": _sb(16 * RO, f16), "pu": _sb(32, u16), "prow": _sb(2 * M, f16), "pb": _sb(128, bf),
    "act": _sb(4 * M, f16), "cnt": _sb(8, f32), "off": _sb(64, u16),
    "pw": _sb(16, f32), "ovr": _sb(32, f32), "xp": _sb(M, f16),
    "CE": _sb(4 * M, f16), "Gn": _sb(M, f32), "PG": _sb(M, f16), "Gq": _sb(M, f32), "rk": _sb(M, f32),
    "qu": _sb(16, u16), "qf": _sb(16, f32), "Ta": _sb(2 * M, f32),
    "au": _sb(M, u16), "af": _sb(M, f16), "Tr": _sb(2 * M, f16), "Rd": _sb(2 * M, i32), "D": _sb(2 * M, bf),
    "sC": _sb(2 * M, bf), "sE": _sb(2 * M, bf), "zy": _sb(M, f16), "u1": _sb(16, i32), "uu": _sb(32, u16),
    "m1": _sb(M, f32), "m2": _sb(M, f32), "r13a": _sb(M, f32), "r13": _sb(M, f32), "TT": _sb(M, f32), "SC": _sb(M, f32), "mx": _sb(16, i32),
    "e1": _sb(M, f32), "e2": _sb(M, i32), "e3": _sb(M, i32),
}
BANKS = ["TC0", "TC1", "TE0", "TE1", "KC", "KE", "X0", "X1"]
for _b in BANKS:
    SCRATCH[_b] = ("psum", [128, 512], f32)
NDMA = 14
SEMAPHORES = ["ev", "ea", "et", "eg", "sent"] + ["d%d" % i for i in range(NDMA)] + ["pa%d" % t for t in range(1, RO)] + ["za%d" % t for t in range(1, RO)]


def build_ops(g, core, T, topo, case=None):
    rank = T.rank_of(core)
    nxt = T.cores[(rank + 1) % len(T.cores)]
    rid, pid, _ = topo.addr(nxt)
    mask = topo.mask(core, nxt)
    neng = len(topo.engines(core, nxt))
    ops = []
    C = dict(P, **(case or {}))
    fac, gc, sc = C["fac"], C["g"], C["sc"]
    ndma = [0]
    rnd = [-1]

    def add(eng, fn, r, w, cost, **kw):
        ops.append(dict(eng=eng, fn=fn, r=list(r) + ["ones1"] * ("ones" in r), w=list(w), cost=cost, rnd=rnd[0], **kw))

    def vc(n, rate=1.0):
        return (C["fix"] + max(64, n * rate) * 0.83) * fac

    def mat(name):
        j = MATS.index(name)
        return T.MX[:, 128 * j:128 * j + 128]

    def grpcols(name):
        j = MATS.index(name)
        return T.MX[:, 128 * j:128 * j + 128:16]

    def copy(o, i, r, w, n, rate=1.0):
        add("v", lambda: g.vector.tensor_copy(o, i), r, w, vc(n, rate))

    def ts(o, i, s1, s2, op0, op1, r, w, n, rate=1.0):
        if op1 is None:
            add("v", lambda: g.vector.tensor_scalar(o, i, s1, None, op0), r, w, vc(n, rate))
        else:
            add("v", lambda: g.vector.tensor_scalar(o, i, s1, s2, op0, op1), r, w, vc(n, rate))

    def tt(o, a, b, op, r, w, n, rate=1.0):
        add("v", lambda: g.vector.tensor_tensor(o, a, b, op), r, w, vc(n, rate))

    def mset(o, c, w, n):
        add("v", lambda: g.vector.memset(o, c), [], w, vc(n, 0.5))

    def act_(o, i, fn, r, w, n, bias=0.0, scale=1.0, rate=1.0, acc=None):
        if acc is None:
            add("a", lambda: g.scalar.activation(o, i, fn, bias=bias, scale=scale), r, w, vc(n, rate) + C["afix"] * fac)
        else:
            add("a", lambda: g.scalar.activation(o, i, fn, bias=bias, scale=scale, accum_out=acc), r, w, vc(n, rate) + 35 * fac)

    def gp(fn, r, w, n):
        add("g", fn, r, w, (150 + 2 * n * 0.83) * fac)

    def lin(e, o, i, scale, bias, r, w, n, rate=1.0, vrate=None):
        e = P["eng"].get(w[0].rstrip("0123456789"), e)
        if e == "a":
            act_(o, i, F.Identity, r, w, n, bias=bias, scale=scale, rate=rate)
        elif e == "g":
            gp(lambda: g.affine_select(o, i, [[0, n]], A.is_ge, 0.0, 0, 0), r, w, n)
        else:
            ts(o, i, scale, bias, A.mult, A.add, r, w, n, rate if vrate is None else vrate)

    def mm(o, l, rh, st, sp, r, w, n, wide=False):
        r = list(r) + [x for x in (l, rh) if isinstance(x, str)]
        l = mat(l) if isinstance(l, str) else l
        rh = mat(rh) if isinstance(rh, str) else rh
        me = {"start": st, "stop": sp}
        cyc = max(64, n) * (4 if wide else 1)
        add("t", [lambda: g.tensor.matmul(o, l, rh, st, me["stop"])], r, w, cyc * C["pe"] * fac, flags=dict(me), subs=[me], cyc=cyc)

    def dma(o, i, r, w, nbytes):
        s = T.sem["d%d" % ndma[0]]
        ndma[0] += 1
        add("s", lambda: g.sync.dma_start(o, i), r, w, 60.0, sem=s, inc=16, lat=C["dl"] + nbytes / C["dr"], bw=nbytes / C["dr"])

    def send(o, i, sem, r, w, slack=0.0):
        add("g", lambda: g.remote_dma(o, i, sem, T.sem.sent, pid, rid, mask), r, w, 300.0, sem=sem, inc=neng, lat=C["rem"] + slack, remote=True)

    def runs(plan):
        cut = [j for j, x in enumerate(plan) if x.islower()] + [len(plan)]
        return [(plan[a], a, b) for a, b in zip(cut, cut[1:])]

    loads = {"p": (T.pin[:, 0:16], T.ps[:], "pin0", 8192), "x": (T.XC[:], T.xc[:], "XC", 524288), "w": (T.wi[:, 0:1], T.wt[:], "wi", 512),
             "z": (T.zin[:, 0:M], T.zi[:], "zin0", 65536), "k": (T.K1[:], T.kc[:], "K1", 131072), "n": (T.NB[:], T.nb[:], "NB", 1048576)}
    for x in P["loads"]:
        dma(loads[x][0], loads[x][1], [], [loads[x][2]], loads[x][3])

    def zero(name, n):
        j = 128 * MATS.index("zb")
        return T.MX[:, j:j + n] if name == "zb" else T.zf[:, 0:n]

    def spot(o, name, pattern, base, fill, n, z="zb"):
        gp(lambda: g.affine_select(o, zero(z, n), pattern, A.not_equal, float(fill), base, 1), [z], [name], n)

    def iota(o, name, pattern, base, n, r=()):
        gp(lambda: g.iota(o, pattern, base, 0, allow_small_or_imprecise_dtypes=True), r, [name], n)

    def band(o, name, lo, hi, fill, z="zb"):
        gp(lambda: g.affine_select(o, zero(z, 8), [[16, 8]], A.is_gt, float(fill), lo, -1), [z, name], [name], 8)
        gp(lambda: g.affine_select(o, o, [[16, 8]], A.is_ge, 0.0, hi, -1), [name], [name], 8)

    def ce(name, e):
        return P["ce"].get(name, e)

    def const(o, name, c, n, e, z="zb"):
        if ce(name, e) == "v":
            mset(o, c, [name], n)
        else:
            gp(lambda: g.affine_select(o, zero(z, n), [[0, n]], A.is_gt, float(c), 0, 0), [z], [name], n)

    mset(mat("zb"), 0.0, ["zb"], 128)
    mset(T.ones[:, 128:512], 1.0, ["ones1"], 384)
    mset(T.zf[:], 0.0, ["zf"], 256)
    iota(mat("R16"), "R16", [[16, 8], [0, 16]], 0, 128)
    gp(lambda: g.iota(T.wf[:, 2:3], [[0, 1]], 0, 1, allow_small_or_imprecise_dtypes=True), [], ["pcol"], 1)
    gp(lambda: g.iota(T.pi[:, 0:1], [[0, 1]], 0, 1), [], ["pi"], 1)
    ts(T.pi[:, 1:2], T.pi[:, 0:1], 15, None, A.bitwise_and, None, ["pi"], ["pa"], 1)
    copy(T.lane[:, 0:1], T.pi[:, 1:2], ["pa"], ["lane"], 1)
    ts(mat("blk"), mat("R16"), T.lane[:, 0:1], T.wf[:, 2:3], A.add, A.is_equal, ["R16", "lane", "pcol"], ["blk"], 128, 0.5)
    iota(T.srow[:], "srow", [[1, 16]], 0, 16)
    spot(mat("I"), "I", [[-1, 128]], 0, 1.0, 128)
    spot(mat("Pm"), "Pm", [[-2, 64], [1, 2]], -1, 1.0, 128)
    iota(T.dum[:], "dum", [[GO, 2], [16, 16]], DUM, 32)
    iota(T.lo[:], "lo", [[0, 8], [1, 32]], 0, M)
    iota(T.KOC[:, 0:M], "KOC0", [[1, M]], K0 + V, M)
    for t in range(2):
        iota(T.hi[:, M * t:M * t + M], "hi%d" % t, [[1, 8], [0, 32]], 8 * t, M)
    ts(T.lm[:], T.srow[:], T.lane[:, 0:1], None, A.is_equal, None, ["srow", "lane"], ["lm"], 16)
    for s in range(16):
        if s < P["rsg"]:
            spot(T.RS[:, 128 * s:128 * s + 128], "RS%d" % s, [[-16, 8], [0, 16]], -s, 1.0, 128)
        elif s < P["rsg"] + P["rsv"]:
            ts(T.RS[:, 128 * s:128 * s + 128], mat("R16"), float(s), T.wf[:, 2:3], A.add, A.is_equal, ["R16", "pcol"], ["RS%d" % s], 128, 0.5)
        else:
            act_(T.RS[:, 128 * s:128 * s + 128], mat("blk"), F.Identity, ["blk", "lm"], ["RS%d" % s], 128, scale=T.lm[:, s:s + 1])
    mset(T.pm[:], 0.5, ["pm"], 16)
    add("v", lambda: g.vector.tensor_tensor_scan(T.pat[:], T.pm[:], T.zf[:, 0:16], 65536.0, A.mult, A.add), ["pm", "zf"], ["pat"], vc(16))
    tt(T.pm[:], T.pat[:], T.lm[:], A.mult, ["pat", "lm"], ["pm"], 16)
    add("v", lambda: g.vector.tensor_reduce(T.wf[:, 1:2], T.pm[:], AxisListType.X, A.add), ["pm"], ["pw"], vc(16))
    lin(ce("Bw", "v"), mat("Bw"), mat("blk"), T.wf[:, 1:2], 0.0, ["blk", "pw"], ["Bw"], 128, vrate=0.5)
    lin(ce("Bo", "a"), mat("Bo"), mat("blk"), 2.0 ** 17, 0.0, ["blk"], ["Bo"], 128, vrate=0.5)
    lin("a", T.thr[:, 0:16], T.pat[:], 2.0, 0.0, ["pat"], ["thr"], 16)
    for n in (16, 32, 64, 128):
        lin(ce("thr", "a"), T.thr[:, n:2 * n], T.thr[:, 0:n], 1.0, 0.0, ["thr"], ["thr"], n, vrate=0.5)
    lin(ce("dum", "v"), T.dum[:], T.dum[:], 1.0, T.lane[:, 0:1], ["dum", "lane"], ["dum", "dug"], 32)
    lin(ce("wf", "v"), T.wf[:, 0:1], T.wi[:, 0:1], 1.0, 0.0, ["wi"], ["wf"], 1)
    for name in ("SW", "SA", "S1"):
        iota(T[name][:], name, [[0, 144]], 0, 144)
    act_(T.SW[:, 16:144:16], grpcols("blk"), F.Identity, ["blk", "wf"], ["SW"], 8, scale=T.wf[:, 0:1])
    spot(T.SA[:, 16:144:16], "SA", [[-16, 8]], 0, -BIG, 8)
    gp(lambda: g.affine_select(T.SA[:, 16:144:16], T.SA[:, 16:144:16], [[-16, 8]], A.not_equal, -1.0, -1, 1), ["SA"], ["SA"], 8)
    spot(T.S1[:, 16:144:16], "S1", [[-16, 8]], 0, 1.0, 8)
    for j, name in enumerate(list(DIAG)[1:]):
        e = ce(name, "g")
        if e == "g":
            spot(mat(name), name, [[-1, 128]], 0, DIAG[name], 128)
        else:
            lin(e, mat(name), mat("I"), DIAG[name], 0.0, ["I"], [name], 128, vrate=0.5)
    lin(ce("pb", "a"), T.pb[:], mat("blk"), 2.0, 0.0, ["blk"], ["pb"], 128, vrate=0.5)
    if ce("P11", "g") == "g":
        spot(mat("P11"), "P11", [[-2, 64], [1, 2]], -1, LO, 128)
    else:
        lin(ce("P11", "g"), mat("P11"), mat("Pm"), LO, 0.0, ["Pm"], ["P11"], 128, vrate=0.5)
    for j, name in enumerate(("Dlo", "Dhi")):
        if ce(name, "g") == "g":
            spot(mat(name), name, [[-16, 8], [1000, 16]], -1001 * j, LO / 64, 128)
        else:
            ts(mat(name), mat("I"), T.lm[:, j:j + 1], LO / 64, A.mult, A.mult, ["I", "lm"], [name], 128, 0.5)
    for name, c0, c1 in (("Kn", -H2 / 64, (Y0 - H2) * LO / 64), ("Kt", -1.0 / 512, 2.0 ** -19)):
        if ce(name, "g") == "g":
            const(T[name][:], name + "0", c0, 128, "g")
            gp(lambda o=T[name][:], c=c1: g.affine_select(o, o, [[0, 128]], A.is_gt, c, 64, -1), [], [name + "0", name + "1"], 128)
        else:
            mset(T[name][0:64, :], c0, [name + "0"], 128)
            mset(T[name][64:128, :], c1, [name + "1"], 128)
    const(T.c1k[:, 0:16], "c1k", 1024.0, 16, "g")
    const(T.c1k[:, 48:64], "c6k", BIG / 2048, 16, "g")
    const(T.c1k[:, 16:32], "cm1k", -1024.0, 16, "g")
    const(T.c1k[:, 32:48], "c1k1", 1025.0, 16, "g")
    lin(ce("zn1", "a"), T.zn[:], mat("blk"), -2.0, 0.0, ["blk"], ["zn1"], 128, vrate=0.5)
    act_(T.ones[:, 0:128], mat("zb"), F.Sigmoid, ["zb"], ["ones"], 128, bias=64.0)
    ops[-1]["cost"] += 1300.0 * fac
    lin(ce("grp", "a"), T.grp[:], grpcols("blk"), 1.0, 0.0, ["blk"], ["grp"], 8)
    lin(ce("grq", "a"), T.grq[:], grpcols("blk"), 2.0, 0.0, ["blk"], ["grq"], 8)
    band(T.sel[:, 0:8], "sel0", 0, 7, 1.0, "zf")
    band(T.sel[:, 8:16], "sel1", 8, 15, 1.0, "zf")
    for j in range(2):
        spot(T.sel[:, 16 + 8 * j:24 + 8 * j], "sel%d" % (2 + j), [[-16, 8]], -j, 1 / LO, 8, "zf")
    lin(ce("Kc", "a"), T.KF[:, 0:KK], T.K1[:], 1.0, H2, ["K1"], ["Kc"], KK)
    for j, name in enumerate(("Ka", "Kb")):
        if ce(name, "g") == "g":
            lin("g", T.KF[:, KK + j:2 * KK:2], T.KF[:, 1 - j:KK:2], 1.0, 0.0, ["Kc"], [name], 256)
        else:
            lin(ce(name, "g"), T.KF[:, KK + j:2 * KK:2], T.K1[:, 1 - j:KK:2], 1.0, H2, ["K1"], [name], 256)
    for h in range(4):
        lin(P["wi"][h], T.G[:, GO + 512 * h:GO + 512 * h + 512], T.XC[:, 512 * h:512 * h + 512], 1.0, 0.0, ["XC"], ["Wi%d" % h], 512)
    for xh in range(2):
        for gl in range(2):
            q = 2 * xh + gl
            spot(T.SWP[:, 128 * q:128 * q + 128], "SWP%d" % q, [[-32, 4], [1000, 2], [-1, 16]], -16 * xh - 1000 * gl, 1.0, 128, "zf")
    const(T.o16[:], "o16", 1.0 / 16, 128, "g", "zf")
    gp(lambda: g.affine_select(T.sm[:], T.ones[:, 0:M], [[0, 16], [1, 16]], A.is_gt, 0.0, 0, 0), ["ones"], ["sm"], M)
    lin(ce("kcol", "v"), T.lane[:, 1:2], T.lane[:, 0:1], -8.0, 15 * 8.0 + (SC_ / 2 + K0) / 2048, ["lane"], ["kcol"], 1)
    lin(ce("crow", "v"), T.crow[:, 0:M], T.ones[:, 0:M], 4.5, T.lane[:, 1:2], ["ones", "kcol"], ["crow0"], M, vrate=0.5)
    lin(ce("crow", "v"), T.crow[:, M:2 * M], T.ones[:, 0:M], 1.0, T.lane[:, 1:2], ["ones", "kcol"], ["crow1"], M, vrate=0.5)
    for j in range(4):
        iota(T.PAR[:, 512 * j:512 * j + 512], "PAR%d" % j, [[0, 512]], 0, 512)

    def later(t):
        def fill(o, name, pattern, base, n=M):
            iota(o, name, pattern, base, n)
            ops[-1]["behind"] = ["pin%d" % (t + 1)]
        fill(T.KOC[:, M * (t + 1):M * (t + 2)], "KOC%d" % (t + 1), [[1, M]], K0 + V + M * (t + 1))
        if t < 2:
            fill(T.hi[:, M * (t + 2):M * (t + 3)], "hi%d" % (t + 2), [[1, 8], [0, 32]], 8 * (t + 2))
            fill(T.mkc[:, M * t:M * t + M], "mkc%d" % (t + 1), [[0, M]], 64 * t)
        if t == 0:
            for j in range(4):
                cs = slice(512 * j, 512 * j + 512)
                lin(P["li"][j], T.L[:, cs], T.NB[:, cs], 1.0, 0.0, ["NB"], ["Li%d" % j], 512)
                ops[-1]["behind"] = ["pin1"]

    def sel(name, s):
        return T[name][:, 16 - s:144 - s]

    def acts(t, a=0, b=M):
        return T.act[:, 2 * M * (t % 2) + a:2 * M * (t % 2) + b]

    def cells(t):
        return ["W"] + (["Wn%d" % (t - 1)] if t else ["Wi0", "Wi1", "Wi2", "Wi3"])

    def upath(t):
        pr = t % 2
        l = slice(16 * pr, 16 * pr + 16)
        if t:
            mm(T.X1[:, 32:33], T.o16[:], T.cnt[:, 0:1], True, True, ["o16", "cnt"], ["X1"], 1, True)
        for s in range(16):
            mm(T.X1[:, 0:16], sel("SW", s), T.zin[:, M * t + s:M * t + M:16], s == 0, s == 15, ["SW", "zin%d" % t], ["X1"], 16)
        if t:
            ts(T.u1[:], T.X1[:, 0:16], T.X1[:, 32:33], float(1 << 18), A.add, A.add, ["X1"], ["u1"], 16)
        else:
            lin("v", T.u1[:], T.X1[:, 0:16], 1.0, float(1 << 18), ["X1"], ["u1"], 16)
        ts(T.u1[:], T.u1[:], KK - 1, None, A.bitwise_and, None, ["u1"], ["u1"], 16)
        lin("a", T.uu[:, l], T.u1[:], 1.0, 0.0, ["u1"], ["uu%d" % pr], 16)

    def prep(t):
        pr = t % 2
        l = slice(16 * pr, 16 * pr + 16)
        c = slice(M * pr, M * pr + M)
        pf = T.pf16[:, 16 * t:16 * t + 16]
        pn, ac, cn = "pf%d" % t, "act%d" % pr, "CE%d" % pr
        hi = V + M * t
        win = T.G[:, GO:GO + hi]
        wr = cells(t)
        Cf, Ef = T.CE[:, 2 * M * pr:2 * M * pr + M], T.CE[:, 2 * M * pr + M:2 * M * pr + 2 * M]
        pin = T.pin[:, 16 * t:16 * t + 16]
        lin("v", pf, pin, 1.0, -1024.0, ["pin%d" % t], [pn], 16)
        lin("a", T.pu[:, l], pin, 1.0, 0.0, ["pin%d" % t], ["pu%d" % pr], 16)
        for s in range(16):
            mm(T.X0[:, s:M:16], T.RS[:, 128 * s:128 * s + 128], pf, True, True, ["RS%d" % s, pn], ["X0"], 16)
        lin("a", T.prow[:, c], T.X0[:, 0:M], 1.0, 0.0, ["X0"], ["prow%d" % pr], M)
        mm(T.KC[:, 0:M], "nI", T.thr[:], True, False, ["thr"], ["KC"], M)
        for cc in range(16):
            n = M - 16 * cc
            ts(T.EQ[:, cc, 0:n], T.prow[:, M * pr + 16 * cc:M * pr + M], T.pf16[:, 16 * t + cc:16 * t + cc + 1], None, A.is_equal, None, ["prow%d" % pr, pn], ["EQ%d" % cc], n, 0.5)
            if cc < 15:
                mm(T.KC[:, 16 * cc + 16:M], "Bo", T.EQ[:, cc, 16:n], False, False, ["EQ%d" % cc], ["KC"], n - 16)
            if cc % 4 == 3:
                mm(T.KC[:, 16 * cc - 48:16 * cc + 16], "Bw", T.EQ[:, cc - 3:cc + 1, 0:16], False, cc == 15, ["EQ%d" % x for x in range(cc - 3, cc + 1)], ["KC"], 64)
        last = t == RO - 1
        act_(acts(t), T.KC[:, 0:M], F.Sigmoid, ["KC", "ones"], [ac] + ([] if last else ["cnt"]), M, bias=-128.0, scale=-256.0, acc=None if last else T.cnt[:, 0:1])
        if t:
            act_(T.xp[:], win.indirect(T.pu[:, l]), F.Identity, wr + ["pu%d" % pr], ["xp"], M, bias=H2, rate=gc)
        else:
            act_(T.xp[:], T.XC[:].indirect(T.pu[:, l]), F.Identity, ["XC", "pu0"], ["xp"], M, bias=H2, rate=gc)
        tt(Cf, T.KF[:, 0:KK].indirect(T.uu[:, l]), T.xp[:], A.min, ["Kc", "uu%d" % pr, "xp"], ["Cc%d" % pr, cn], M, gc)
        tt(Ef, T.KF[:, KK:2 * KK].indirect(T.uu[:, l]), T.xp[:], A.min, ["Ka", "Kb", "uu%d" % pr, "xp"], [cn], M, gc)
        gn = T.TC0[:, 0:M]
        mm(gn, T.Kn[:], T.ones[:, 0:M], True, False, ["Kn0", "Kn1", "ones"], ["TC0"], M)
        mm(gn, "I", Cf, False, False, [cn], ["TC0", "gn0"], M)
        mm(gn, "I11", Ef, False, False, [cn, "gn0"], ["TC0"], M)
        mm(gn, "Dlo", T.lo[:], False, False, ["lo", "gn0"], ["TC0"], M)
        mm(gn, "Dhi", T.hi[:, M * t:M * t + M], False, True, ["hi%d" % t, "gn0"], ["TC0"], M)
        lin("a", T.Gn[:], gn, 1.0, 0.0, ["TC0"], ["Gn"], M)
        if t:
            act_(T.PG[:], T.PAR[:, 0:hi].indirect(T.pu[:, l]), F.Identity, ["PAR0", "PAR1", "PAR2", "PAR3", "KOE%d" % (t - 1), "pu%d" % pr], ["PG"], M, bias=-K0 - 1024.0, rate=gc)
            ql = T.X1[:, 0:16]
            mm(ql, "I", T.c1k[:, 0:16], True, False, ["c1k"], ["X1"], 16)
            for s in range(16):
                mm(ql, sel("S1", s), T.PG[:, s:M:16], False, s == 15, ["S1", "PG"], ["X1"], 16)
            lin("a", T.qu[:], ql, 1.0, 0.0, ["X1"], ["qu"], 16)
            act_(T.qf[:], ql, F.Abs, ["X1"], ["qf"], 16, bias=float(GO))
            act_(T.Gq[:], win.indirect(T.qu[:]), F.Copy, wr + ["qu"], ["Gq"], M, rate=gc)
            mm(T.TC1[:, 0:M], "I", T.xp[:], True, False, ["xp"], ["TC1"], M)
            mm(T.TC1[:, 0:M], "nI", Cf, False, True, ["Cc%d" % pr], ["TC1"], M)
            lin("a", T.rk[:], T.TC1[:, 0:M], LO, 0.0, ["TC1"], ["rk"], M)
            if t > 1:
                act_(acts(t, M, 2 * M), T.MK[:, 0:hi].indirect(T.qu[:]), F.Identity, ["MK", "qu"], ["MG"], M, scale=-1.0, rate=gc)
        vl, v2, two = T.X0[:, M:M + 16], T.X0[:, M + 16:M + 32], t > 1
        mm(vl, "I2k", T.c1k[:, 48:64], True, False, ["c6k"], ["X0"], 16)
        mm(vl, "I", T.c1k[:, 32:48], False, False, ["c1k1"], ["X0"], 16)
        mm(vl, "I", pf, False, False, [pn], ["X0"], 16)
        if two:
            mm(v2, "n24k", T.c1k[:, 16:32], False, False, ["cm1k"], ["X0", "v2"], 16)
            mm(v2, "n24k", pf, False, False, [pn], ["X0"], 16)
        for s in range(16):
            mm(T.X0[:, M:M + 16 + 16 * two], sel("SA", s), T.act[:, 2 * M * pr + s:2 * M * pr + M + M * two:16], False, s == 15, ["SA", ac] + ["MG", "v2"] * two, ["X0"], 16)
        off, of2 = T.off[:, 32 * pr:32 * pr + 16], T.off[:, 32 * pr + 16:32 * pr + 32]
        if two:
            tt(T.qf[:], v2, T.qf[:], A.max, ["X0", "qf"], ["qf"], 16)
        if t:
            tt(T.X0[:, M + 16:M + 32], vl, T.qf[:], A.max, ["X0", "qf"], ["s2"], 16)
            tt(T.off[:, 32 * pr:32 * pr + 32], T.X0[:, M:M + 32], T.dum[:], A.min, ["X0", "s2", "dum", "dug"], ["off%d" % pr], 32)
        else:
            tt(off, vl, T.dum[:, 0:16], A.min, ["X0", "dum"], ["off%d" % pr], 16)
        if not last:
            if P["pnv"]:
                ts(T.pw[:], pin, V - 1.5, -float(V), A.is_ge, A.mult, ["pin%d" % t], ["pn"], 16)
            else:
                act_(T.pw[:], pin, F.Sign, ["pin%d" % t], ["pn"], 16, bias=1.5 - V)
                act_(T.pw[:], T.pw[:], F.Identity, ["pn"], ["pn"], 16, bias=-V / 2, scale=-V / 2)
            tt(T.ovr[:, l], vl, T.pw[:], A.add, ["X0", "pn"], ["ovr%d" % pr], 16)
        if t:
            tt(T.G[:].indirect(of2), T.Gq[:], T.rk[:], A.subtract, ["Gq", "rk", "off%d" % pr], wr, M, sc)
        copy(T.G[:, GO:GO + WC].indirect(off), T.Gn[:], ["Gn", "off%d" % pr], wr, M, sc)

    def koe(t, a=0, b=M):
        return T.PAR[:, V + M * t + a:V + M * t + b]

    def fresh(t):
        pr = t % 2
        c = slice(M * pr, M * pr + M)
        ac, cn = "act%d" % pr, "CE%d" % pr
        Ef = T.CE[:, 2 * M * pr + M:2 * M * pr + 2 * M]
        hi = V + M * t
        fb = P["frb"]
        es, pq = T[fb][:, 0:M], T[fb][:, M:2 * M]
        mm(pq, "I", T.prow[:, c], True, False, ["prow%d" % pr], [fb], M)
        mm(pq, "I19", acts(t), False, True, [ac], [fb], M)
        act_(koe(t), pq, F.Relu, [fb], ["KOE%d" % t], M, bias=K0 + 1024.0 - SC_)
        mm(es, T.Kn[0:64, :], T.ones[0:64, 0:M], True, False, ["Kn0", "Kn1", "ones"], [fb], M)
        mm(es, "I", Ef, False, True, [cn], [fb], M)
        if t == RO - 1:
            tt(T.XO[:, hi:hi + M], es, acts(t), A.mult, [fb, ac], ["XO4"], M)
        else:
            tt(T.G[:, GO + hi:GO + hi + M], es, acts(t), A.mult, [fb, ac, "W"], ["Wn%d" % t], M)

    def marks(t):
        pr = t % 2
        if 0 < t < RO - 1:
            add("a", lambda: g.scalar.activation(T.MK[:].indirect(T.off[:, 32 * pr:32 * pr + 16]), T.mkc[:, M * (t - 1):M * t], F.Sigmoid),
                ["mkc%d" % t, "off%d" % pr, "sC0", "sC1", "sC2", "sC3"], ["MK"] + (["Mi%d" % j for j in range(4)] if t == 1 else []), vc(M, sc) + 15 * fac)

    def lists(t):
        pr = t % 2
        win = T.NB[:] if t == 0 else T.L[:, 0:V + M * t]
        rd = (["NB"] if t == 0 else ["L", "Ln"]) + ["pu%d" % pr]
        if t == 0:
            for e, a, b, name in (("v", 0, 4, "av"), ("a", 4, 8, "aw"), ("a", 8, 16, "au")):
                lin(e, T.au[:, 16 * a:16 * b], win.indirect(T.pu[:, a:b]), 1.0, 0.0, rd, [name], 16 * (b - a), gc)
        else:
            lin("a", T.au[:], win.indirect(T.pu[:, 16 * pr:16 * pr + 16]), 1.0, 0.0, rd, ["au", "av", "aw"], M, gc)
        lin("a", T.af[:], T.au[:], 1.0, -1024.0, ["au", "av", "aw"], ["af"], M, vrate=0.5)

    def zpath(t):
        pr = t % 2
        c = slice(M * pr, M * pr + M)
        z = T.zin[:, M * t:M * t + M]
        zn, ac, cn = "zin%d" % t, "act%d" % pr, "CE%d" % pr
        y0, y1 = T.KE[:, 0:M], T.KE[:, M:2 * M]
        mm(y0, "nI", z, True, False, [zn], ["KE"], M)
        mm(y0, "I19", acts(t), False, False, [ac], ["KE"], M)
        mm(y0, "I", T.CE[:, 2 * M * pr:2 * M * pr + M], False, True, [cn], ["KE"], M)
        act_(T.zy[:], y0, F.Relu, ["KE"], ["zy"], M, bias=1279.75 - SC_ / 2 - H2 / 2, scale=0.5)
        mm(y1, "I", z, True, False, [zn], ["KE"], M)
        mm(y1, "n1280", acts(t), False, False, [ac], ["KE"], M)
        mm(y1, "I", T.zy[:], False, True, ["zy"], ["KE"], M)
        lin("a", T.zout[:, M * t:M * t + M], y1, 1.0, 0.0, ["KE"], ["zout%d" % t], M)
        send(T.zin[:, M * (t + 1):M * (t + 2)], T.zout[:, M * t:M * t + M], T.sem["za%d" % (t + 1)], ["zout%d" % t], ["zin%d" % (t + 1)], C["zs"][min(t, 1)])
        if t == 0:
            ops[-1]["behind"] = P["early"].split()
        if t == 1:
            n = NO // 4
            for j in range(4):
                iota(T.MK[:, n * j:n * j + n], "Mi%d" % j, [[0, n]], 0, n)
                ops[-1]["behind"] = ["zin2"]

    def extents(t):
        wr = ["W", "Wn%d" % (t - 1)]
        n = NO // 4
        for j in range(4):
            if P["xo"][j] == "g":
                lin("g", T.BI[:, 0:n], T.G[:, GO + n * j:GO + n * j + n], 1.0, 0.0, wr, ["BI"], n)
                lin("g", T.XO[:, n * j:n * j + n], T.BI[:, 0:n], 1.0, 0.0, ["BI"], ["XO%d" % j], n)
                continue
            if P["xo"][j] == "a":
                xs = slice(n * (j % 2), n * (j % 2) + n)
                act_(T.XH[:, xs], T.G[:, GO + n * j:GO + n * j + n], F.Identity, wr, ["XH%d" % (j % 2)], n, bias=H1)
                act_(T.XO[:, n * j:n * j + n], T.XH[:, xs], F.Identity, ["XH%d" % (j % 2)], ["XO%d" % j], n, bias=-H1)
                continue
            ts(T.XO[:, n * j:n * j + n], T.G[:, GO + n * j:GO + n * j + n], RND, RND, A.add, A.subtract, wr, ["XO%d" % j], n)
        for a, b in P["xs"]:
            lo, hi = n * a, min(n * b, W_)
            dma(T.yx[:, lo:hi], T.XO[:, lo:hi], ["XO%d" % j for j in range(a, b)], [], 128 * (hi - lo) * 2)

    def gather(t):
        wr = ["W"] + (["Wn%d" % (t - 1)] if t else [])
        for e, a, b in runs(P["ga"][t]):
            win = T.G[:, GO:GO + V + M * t].indirect(T.au[:, 16 * a:16 * b])
            rd = wr + ["av"] * (a < 4) + ["aw"] * (a < 8 and b > 4) + ["au"] * (b > 8) + (["zout%d" % t] if t < RO - 1 and e in P["zq"][t] else [])
            nm = ["GA%d" % x for x in range(a, b)]
            lin(e, T.GA[:, M * a:M * b], win, 1.0, -Y0 * LO, rd, nm, M * (b - a), gc)
        for h in range(2):
            lp = P["LPb"][h]
            hs = slice(M * h, M * h + M)
            for k in range(16):
                mm(T[lp][:, k:512:16], T.GA[:, 2048 * h + k:2048 * h + 2048:16], T.sel[:], True, True,
                   ["GA%d" % (8 * h + j) for j in range(8)] + ["sel%d" % o for o in range(4)], [lp], 32, True)
            lin("a", T.Rd[:, hs], T[lp][:, M:2 * M], 1.0, 0.0, [lp], ["Rd%d" % h], M)
            if P["tra"][t][h]:
                act_(T.Ta[:, hs], T[lp][:, 0:M], F.Identity, [lp], ["Ta%d" % h], M, bias=RND)
                act_(T.Tr[:, hs], T.Ta[:, hs], F.Identity, ["Ta%d" % h], ["Tr%d" % h], M, bias=-RND)
            else:
                ts(T.Tr[:, hs], T[lp][:, 0:M], RND, RND, A.add, A.subtract, [lp], ["Tr%d" % h], M)
            tt(T.D[:, hs], T[lp][:, M:2 * M], T.Rd[:, hs], A.subtract, [lp, "Rd%d" % h], ["D%d" % h], M)

    def scores(t, x, lims, banks):
        pr = t % 2
        cn, ac = "CE%d" % pr, "act%d" % pr
        R, B, s = "R" + x, "B" + x, "s" + x
        c0 = 2 * M * pr + M * (x == "E")
        blocks = sorted([(h, p) for h in range(2) for p in range(2)], key=lambda b: (banks[b[0]][b[1]], b[1], b[0]))
        at = {b: 128 * j for j, b in enumerate(blocks)}
        held = {k: [b for b in blocks if banks[b[0]][b[1]] == k] for k in set(banks[0] + banks[1])}
        opened = set()

        def into(h, p, lhs, rhs, r, n, k=0, step=1):
            bank = banks[h][p]
            o = at[h, p] - at[held[bank][0]]
            mm(T[bank][:, o + k:o + 128:step], lhs, rhs, bank not in opened, False, r, [bank], n)
            opened.add(bank)

        def piece(j):
            if len(lims) == 2:
                h, r = divmod(j, 4)
                return T.GA[:, 2048 * h + r:2048 * h + 2048:4], range(8 * h, 8 * h + 8), [(h, r + 4 * q, slice(q, 512, 4)) for q in range(4)]
            return T.GA[:, j:4096:8], range(16), [(h, j + 8 * q, slice(M * h + q, M * h + M, 2)) for q in range(2) for h in range(2)]

        def sums(j, buf, p, w):
            for h, k, cs in piece(j)[2]:
                into(h, p, T[buf][:, 512 * j + cs.start:512 * j + cs.stop:cs.step], T[w][:], [w, "%s%d" % (buf, j)], 8, k, 16)
        for h, p in blocks:
            if x == "E":
                into(h, p, acts(t, 128 * h, 128 * h + 128), T.pb[:], [ac, "pb"], 128)
            elif p == 0 and banks[h][0] not in opened | {banks[h][1]}:
                into(h, p, "zb", T.ones[:, 0:8], ["ones"], 8, 0, 16)
        for h in range(2):
            into(h, 1, T.CE[:, c0 + 128 * h:c0 + 128 * h + 128], T.zn[:], [cn, "zn1"], 128)
        for h, lim in enumerate(lims):
            rep, n = 2 * len(lims), M // len(lims)
            mm(T[lim][:], T.Kt[:], T.ones[:], True, False, ["Kt0", "Kt1", "ones"], [lim], 512)
            for j in range(rep):
                for w in ("Pm", "P11"):
                    mm(T[lim][:, j:512:rep], w, T.CE[:, c0 + n * h:c0 + n * h + n], False, j == rep - 1 and w == "P11", [cn], [lim], n)
            for j in range(8 // len(lims) * h, 8 // len(lims) * (h + 1)):
                src, need, _ = piece(j)
                tt(T[R][:, 512 * j:512 * j + 512], src, T[lim][:], A.add, ["GA%d" % q for q in need] + [lim], ["%s%d" % (R, j)], 512)
                sums(j, R, 1, "grq")
        for e, a, b in runs(P["bits" + x][t]):
            cs = slice(512 * a, 512 * b)
            rn, bn = ["%s%d" % (R, j) for j in range(a, b)], ["%s%d" % (B, j) for j in range(a, b)]
            if e == "v":
                ts(T[B][:, cs], T[R][:, cs], H2, None, A.is_ge, None, rn, bn, 512 * (b - a), 0.5)
            else:
                act_(T[B][:, cs], T[R][:, cs], F.Sigmoid, rn, bn, 512 * (b - a), bias=-512.0 * (H2 - 0.25), scale=512.0)
            for j in range(a, b):
                sums(j, B, 0, "grp")
        for h in range(2):
            for j in range(2):
                into(h, 1, "nI2", T.Tr[:, M * h + 128 * j:M * h + 128 * j + 128], ["Tr%d" % h], 128)
        for bank in sorted(held):
            o, n = at[held[bank][0]], 128 * len(held[bank])
            lin("a", T[s][:, o:o + n], T[bank][:, 0:n], 1.0, -TH - 32.0 * (x == "E"), [bank], ["%s%d" % (s, 2 * h + p) for h, p in held[bank]], n)
        return at

    def keys(s, at, ka, kb, halves):
        n = 128 * len(halves)
        o = n * (ka == kb)
        if o:
            mm(T[ka][:, 0:2 * n], "I2k", T.crow[:, M - n:M + n], True, False, ["crow0", "crow1"], [ka], 2 * n)
        else:
            mm(T[ka][:, 0:n], "I2k", T.crow[:, 0:n], True, False, ["crow0"], [ka], n)
            mm(T[kb][:, 0:n], "I2k", T.crow[:, M:M + n], True, False, ["crow1"], [kb], n)
        mm(T[ka][:, 0:n], "I", T.af[:, 128 * halves[0]:128 * halves[0] + n], False, False, ["af"], [ka], n)
        for j, h in enumerate(halves):
            for d, w in enumerate(("I64", "I2k")):
                mm(T[kb][:, o + 128 * j:o + 128 * j + 128], T.D[:, M * h + 128 * d:M * h + 128 * d + 128], w, False, False, ["D%d" % h], [kb], 128)
        for j, h in enumerate(halves):
            for p, (bank, q) in enumerate(((ka, 128 * j), (kb, o + 128 * j))):
                mm(T[bank][:, q:q + 128], T[s][:, at[h, p]:at[h, p] + 128], "I19", False, False, ["%s%d" % (s, 2 * h + p)], [bank], 128)
        return T[ka][:, 0:n], T[kb][:, o:o + n]

    def post_c(t, at):
        pr = t % 2
        l = slice(16 * pr, 16 * pr + 16)
        kb = P["kb"][t]
        ya, yb = keys("sC", at, "KC", kb, (0, 1))
        tt(T.m1[:], yb, T.KOC[:, M * t:M * t + M], A.max, [kb, "KOC%d" % t], ["m1"], M)
        tt(T.m2[:], ya, T.m1[:], A.max, ["KC", "m1"], ["m2"], M)
        if t < RO - 1:
            add("v", lambda: g.vector.transpose(T.TT[:], T.m2[:]), ["m2"], ["TT"], vc(M))
            add("v", lambda: g.vector.tensor_tensor_scan(T.SC[:], T.sm[:], T.TT[:], 0.0, A.mult, A.max), ["sm", "TT"], ["SC"], vc(M))
            for xh in range(2):
                for gl in range(2):
                    q = 2 * xh + gl
                    mm(T.KC[:, xh:16:2], T.SWP[:, 128 * q:128 * q + 128], T.SC[:, 15 + 16 * gl:M:32], gl == 0, gl == 1, ["SWP%d" % q, "SC"], ["KC"], 8, True)
            tt(T.mx[:], T.KC[:, 0:16], T.ovr[:, l], A.max, ["KC", "ovr%d" % pr], ["mx"], 16)
            ts(T.pout[:, 16 * t:16 * t + 16], T.mx[:], 4095, None, A.bitwise_and, None, ["mx"], ["pout%d" % t], 16)
            send(T.pin[:, 16 * (t + 1):16 * (t + 2)], T.pout[:, 16 * t:16 * t + 16], T.sem["pa%d" % (t + 1)], ["pout%d" % t], ["pin%d" % (t + 1)])
            later(t)
        if P["ract"][t]:
            act_(T.r13a[:], T.m2[:], F.Identity, ["m2"], ["r13a"], M, bias=RND13)
            act_(T.r13[:], T.r13a[:], F.Identity, ["r13a"], ["r13"], M, bias=-RND13)
        else:
            ts(T.r13[:], T.m2[:], RND13, RND13, A.add, A.subtract, ["m2"], ["r13"], M)
        tt(T.L[:].indirect(T.off[:, 32 * pr:32 * pr + 16]), T.m2[:], T.r13[:], A.subtract, ["m2", "r13", "off%d" % pr],
           ["L", "Ln"] + (["Li%d" % j for j in range(4)] if t == 0 else []), M, sc)

    def post_e(t, at):
        n0, parts = V + M * t, 1 + (t == RO - 1)
        n = M // parts
        for h in range(parts):
            key = ("KE", "KC")[h]
            ya, yb = keys("sE", at, key, key, (h,) if parts == 2 else (0, 1))
            hs, x = slice(n * h, n * h + n), "%d" % h
            cs = slice(n0 + n * h, n0 + n * h + n)
            tt(T.e1[:, hs], ya, koe(t, n * h, n * h + n), A.max, [key, "KOE%d" % t], ["e1" + x], n)
            tt(T.e2[:, hs], yb, T.e1[:, hs], A.max, [key, "e1" + x], ["e2" + x], n)
            ts(T.e3[:, hs], T.e2[:, hs], 4095, None, A.bitwise_and, None, ["e2" + x], ["e3" + x], n)
            if t < RO - 1:
                lin("a", T.L[:, cs], T.e3[:, hs], 1.0, 0.0, ["e3" + x], ["Ln"], n)
            else:
                lin("a", T.L[:, cs], T.e3[:, hs], 1.0, 0.0, ["e3" + x, "Ln"], ["Lm" + x], n)
                dma(T.yn[:, cs], T.L[:, cs], ["Lm" + x], [], 128 * n * 4)

    rnd[0] = 0
    upath(0)
    prep(0)
    for t in range(RO):
        lists(t)
        if t < RO - 1:
            zpath(t)
        if not P["frl"][t]:
            fresh(t)
        gather(t)
        if t == RO - 1:
            extents(t)
        at = scores(t, "C", ("TC0", "TC1"), P["sb"][t])
        marks(t)
        if t < RO - 1:
            rnd[0] = t + 1
            upath(t + 1)
            rnd[0] = t
        post_c(t, at)
        if P["frl"][t]:
            fresh(t)
        if t == RO - 1:
            dma(T.yn[:, 0:NO], T.L[:, 0:NO], ["L"], [], 128 * NO * 4)
        post_e(t, scores(t, "E", *P["eb"][t]))
        if t < RO - 1:
            rnd[0] = t + 1
            prep(t + 1)
    return fuse(ops)


def fuse(ops):
    fixed = set(x for o in ops if o["rnd"] < 0 and "sem" not in o for x in o["w"])
    out = []
    for o in ops:
        p = out[-1] if out else None
        if (o["eng"] == "t" and p and p["eng"] == "t" and p["w"] == o["w"] and set(p["r"]) - fixed == set(o["r"]) - fixed
                and (p["cyc"] + o["cyc"]) * P["pe"] <= P["cap"]
                and (not o["flags"]["start"] or (o["flags"]["stop"] and p["flags"]["start"] and p["flags"]["stop"]))
                and (o["flags"]["start"] or not (p["flags"]["start"] and p["flags"]["stop"]))):
            p["fn"] += o["fn"]
            p["subs"] += o["subs"]
            p["r"] += [x for x in o["r"] if x not in p["r"]]
            p["cost"] += o["cost"]
            p["cyc"] += o["cyc"]
        else:
            out.append(o)
    return out


HOP = 90.0


def link(ops):
    lastw, readers, bank, opener = {}, {}, {}, {}
    for n, o in enumerate(ops):
        hard, soft = set(), set()
        if o["eng"] == "s":
            soft.update(opener.get("s", []))
            opener["s"] = [n]
        soft.update(lastw[x] for x in o.get("behind", []) if x in lastw)

        def dep(m):
            p = ops[m]
            if p["eng"] == o["eng"] and "sem" not in p and "sem" not in o and o["eng"] == "t":
                soft.add(m)
            else:
                hard.add(m)
        for x in o["r"]:
            if x in BANKS:
                continue
            if x in lastw:
                dep(lastw[x])
        for x in o["w"]:
            if x in BANKS:
                continue
            if x in lastw:
                dep(lastw[x])
            for m in readers.get(x, []):
                dep(m)
        for x in o["r"]:
            if x not in BANKS:
                readers.setdefault(x, []).append(n)
        for x in o["w"]:
            if x not in BANKS:
                lastw[x] = n
                readers[x] = []
        for x in set(o["r"] + o["w"]):
            if x in BANKS:
                eng, cur, prev = bank.get(x, (None, [], []))
                if o["eng"] == "t":
                    if o["flags"]["start"] or o.get("again"):
                        opener[x] = n
                    o["group"] = opener[x]
                if eng == o["eng"]:
                    if eng == "t":
                        alone = o["flags"]["start"] and o["flags"]["stop"]
                        soft.update([m for m in cur if not (alone and ops[m]["flags"]["start"] and ops[m]["flags"]["stop"])] if o["flags"]["start"] else [opener[x]])
                    hard.update(prev)
                    cur.append(n)
                else:
                    hard.update(cur)
                    bank[x] = (o["eng"], [n], cur)
        hard.discard(n)
        soft.discard(n)
        o["hard"], o["soft"] = sorted(hard), sorted(soft - hard)
    done, issued = [], []
    for o in ops:
        d = i = 0
        for m in o["hard"] + o["soft"]:
            if not ops[m].get("remote"):
                d |= done[m]
                i |= issued[m]
        o["hard"] = [m for m in o["hard"] if not d >> m & 1]
        o["soft"] = [m for m in o["soft"] if not (d | i) >> m & 1]
        done.append(d | sum(1 << m for m in o["hard"]))
        issued.append(i | sum(1 << m for m in o["soft"]))


def replay(ops, order, costs):
    n = len(ops)
    done, endq, free, dmafree = [0.0] * n, [0.0] * n, {}, 0.0
    for j in order:
        o = ops[j]
        cost, lat, bw = costs[j]
        st = free.get(o["eng"], 0.0)
        for m in o["hard"]:
            if done[m] + HOP > st:
                st = done[m] + HOP
        for m in o["soft"]:
            if endq[m] > st:
                st = endq[m]
        endq[j] = free[o["eng"]] = st + cost
        done[j] = st + cost + lat
        if bw:
            dmafree = done[j] = max(dmafree + bw, done[j])
    return max(done)


def blocked(ops, order, costs):
    n = len(ops)
    done, endq, free, dmafree = [0.0] * n, [0.0] * n, {}, 0.0
    why, ready, before, last = [None] * n, [0.0] * n, [None] * n, {}
    for j in order:
        o = ops[j]
        cost, lat, bw = costs[j]
        st = 0.0
        for m in o["hard"]:
            if done[m] + HOP > st:
                st, why[j] = done[m] + HOP, m
        for m in o["soft"]:
            if endq[m] > st:
                st, why[j] = endq[m], m
        ready[j], before[j] = st, last.get(o["eng"])
        if free.get(o["eng"], 0.0) > st:
            st, why[j] = free[o["eng"]], before[j]
        last[o["eng"]] = j
        endq[j] = free[o["eng"]] = st + cost
        done[j] = st + cost + lat
        if bw:
            dmafree = done[j] = max(dmafree + bw, done[j])
    j = max(range(n), key=lambda x: done[x])
    pairs = []
    while j is not None:
        b = before[j]
        for _ in range(4):
            if b is None or endq[b] <= ready[j]:
                break
            if b not in ops[j]["hard"] and b not in ops[j]["soft"]:
                pairs.append((b, j))
            b = before[b]
        j = why[j]
    return pairs


def turns(ops, succ):
    n = len(ops)
    left = {}
    for j, o in enumerate(ops):
        left.setdefault((o["eng"], (o["w"] + ["out"])[0].rstrip("0123456789"), o["rnd"]), []).append(j)
    due = {}
    for t in range(-1, RO):
        for e, plan_ in TURN.items():
            row = []
            for item in plan_.split():
                name, _, cnt = item.rstrip("+").partition("*")
                have = left.get((e, name, t + item.endswith("+")), [])
                k = int(cnt) if cnt else len(have)
                row += have[:k]
                del have[:k]
            at = P["turn"] * (t + 1) - sum(ops[j]["cost"] for j in row) if t < 0 else P["turn"] * t
            step = 1.0 if t < 0 or t == RO - 1 else P["turn"] / sum(ops[j]["cost"] for j in row)
            for j in row:
                due[j] = at
                at += ops[j]["cost"] * step
    pri = [0.0] * n
    for j in range(n - 1, -1, -1):
        o = ops[j]
        pri[j] = -due[j] if j in due else max([-P["turn"] * (RO + 1)] + [pri[s] for s in succ[j]]) + o["cost"] + o.get("lat", 0.0) + HOP
    return pri


def schedule(ops, cases):
    n = len(ops)
    succ = [[] for _ in range(n)]
    for j, o in enumerate(ops):
        for m in o["hard"] + o["soft"]:
            succ[m].append(j)
    pri = [0.0] * n
    for j in range(n - 1, -1, -1):
        o = ops[j]
        lat = o["cost"] + o.get("lat", 0.0)
        pri[j] = lat + max([0.0] + [pri[s] + (HOP if j in ops[s]["hard"] else -o.get("lat", 0.0)) for s in succ[j]])

    def judge(p):
        end, order, done = forward(ops, succ, p)
        return sum(math.log(replay(ops, order, c)) for c in cases) / len(cases), order, done, p
    best = last = judge(pri)
    if P["turn"]:
        best = last = judge(turns(ops, succ))
    for _ in range(P["fb"]):
        last = judge(backward(ops, succ, last[2]))
        if last[0] < best[0]:
            best = last
    kinds = {}
    for j, o in enumerate(ops):
        kinds.setdefault(((o["w"] + ["out"])[0].rstrip("0123456789"), o["eng"], o["rnd"]), []).append(j)
    for k in list(kinds):
        if k[2] >= 0:
            kinds.setdefault((k[0], k[1], RO), []).extend(kinds[k])
    keys = sorted(kinds)
    keys += [k for k in keys if k[2] == RO and k[1] != "g"] * 3
    seed = P["seed"]
    held = [None, None]
    first = best
    for it in range(P["tries"]):
        seed = (seed * 1103515245 + 12345) % (1 << 31)
        if it % 40 == 39:
            p = backward(ops, succ, best[2])
        elif it % 3:
            if held[0] is not best:
                held[:] = [best, {}]
            c = (seed >> 6) % len(cases)
            if c not in held[1]:
                held[1][c] = blocked(ops, best[1], cases[c])
            pairs = held[1][c]
            if not pairs:
                continue
            b, j = pairs[(seed >> 10) % len(pairs)]
            p = list(best[3])
            d = max(p[b] - p[j], 0.0) + (50.0, ops[b]["cost"] + 50.0, 1500.0)[(seed >> 20) % 3]
            if (seed >> 8) % 2:
                p[b] -= d
            else:
                p[j] += d
                for m in ops[j]["hard"] + ops[j]["soft"]:
                    p[m] = max(p[m], p[j] + 1.0)
        else:
            p = list(best[3])
            d = (-3000.0, -1200.0, -400.0, 400.0, 1200.0, 3000.0)[(seed >> 8) % 6]
            for j in kinds[keys[(seed >> 12) % len(keys)]]:
                p[j] += d
        now = judge(p)
        if now[0] <= best[0] + P["warm"] * (1.0 - it / P["tries"]) * ((seed >> 3) % 32) / 32.0:
            best = now
            if now[0] < first[0]:
                first = now
    best = first

    return shift(ops, best[1], cases, P["steps"], P["seed"]) if P["steps"] else best


def shift(ops, order, cases, steps, seed, span=6, keep=20):
    n, nc = len(ops), len(cases)
    eng = ["vatgs".index(o["eng"]) for o in ops]
    hard, soft = [o["hard"] for o in ops], [o["soft"] for o in ops]
    hs, ss = [[] for _ in ops], [[] for _ in ops]
    for j in range(n):
        for m in hard[j]:
            hs[m].append(j)
        for m in soft[j]:
            ss[m].append(j)
    cost = [[c[j][0] for j in range(n)] for c in cases]
    lat = [[c[j][1] for j in range(n)] for c in cases]
    bws = [[c[j][2] for j in range(n)] for c in cases]

    def times(order, c):
        co, la, bw = cost[c], lat[c], bws[c]
        ready, st, done, endq, free, dm = [0.0] * n, [0.0] * n, [0.0] * n, [0.0] * n, [0.0] * 5, 0.0
        for j in order:
            r = 0.0
            for m in hard[j]:
                if done[m] + HOP > r:
                    r = done[m] + HOP
            for m in soft[j]:
                if endq[m] > r:
                    r = endq[m]
            ready[j] = r
            e = eng[j]
            if free[e] > r:
                r = free[e]
            st[j] = r
            endq[j] = free[e] = r = r + co[j]
            r += la[j]
            if bw[j]:
                dm = r = max(dm + bw[j], r)
            done[j] = r
        own, tail, nxt, dm = [0.0] * n, [0.0] * n, [0.0] * 5, 0.0
        for j in reversed(order):
            q = 0.0
            for m in hs[j]:
                if tail[m] + HOP > q:
                    q = tail[m] + HOP
            if bw[j]:
                q = max(q, dm)
                dm = q + bw[j]
            q += la[j]
            for m in ss[j]:
                if tail[m] > q:
                    q = tail[m]
            own[j] = q
            e = eng[j]
            if nxt[e] > q:
                q = nxt[e]
            tail[j] = nxt[e] = q + co[j]
        return ready, st, own, tail, max(done)

    def moved(order, pos, a, b, forth):
        seg = order[pos[a]:pos[b] + 1]
        e0 = eng[a]
        move, touched = {b if forth else a}, set()
        for x in (reversed(seg) if forth else seg):
            if x in move or eng[x] in touched:
                if eng[x] == e0:
                    if x != (b if forth else a):
                        return None
                else:
                    touched.add(eng[x])
                move.add(x)
                move.update(hard[x] + soft[x] if forth else hs[x] + ss[x])
        one, two = [x for x in seg if x in move], [x for x in seg if x not in move]
        return order[:pos[a]] + (one + two if forth else two + one) + order[pos[b] + 1:]
    best = None
    ban = {}
    since = kick = 0
    for it in range(steps):
        tm = [times(order, c) for c in range(nc)]
        now = sum(math.log(t[4]) for t in tm) / nc
        if best is None or now < best[0] - 1e-9:
            best, since = (now, order), 0
        since += 1
        if since > P["stall"]:
            order, since, ban, kick = best[1], 0, {}, P["kick"]
            continue
        pos = {j: x for x, j in enumerate(order)}
        rows = [[] for _ in range(5)]
        for j in order:
            rows[eng[j]].append(j)
        seed = (seed * 1103515245 + 12345) % (1 << 31)
        c0 = (seed >> 16) % nc
        ready, st, own, tail, end = tm[c0]
        co = cost[c0]
        cand = []
        for e in range(4):
            row = rows[e]
            for x in range(1, len(row)):
                j, p = row[x], row[x - 1]
                if st[j] + tail[j] > end - 1.0 and st[p] + tail[p] > end - 1.0 and st[j] > ready[j] + 0.5:
                    y = x - 1
                    while y >= 0 and x - y <= span and st[row[y]] + co[row[y]] > ready[j]:
                        if row[y] in hard[j] or row[y] in soft[j]:
                            break
                        cand.append((e, y, x, True))
                        y -= 1
                    y = x
                    while y < len(row) and y - x < span:
                        if p in hard[row[y]] or p in soft[row[y]]:
                            break
                        if y > x:
                            cand.append((e, x - 1, y, False))
                        if own[p] + co[p] >= tail[row[y]]:
                            break
                        y += 1
        marks = []
        for e, y, x, forth in cand:
            row = rows[e]
            seq = [row[x]] + row[y:x] if forth else row[y + 1:x + 1] + [row[y]]
            val = 0.0
            for c in range(nc):
                ready, st, own, tail, end = tm[c]
                co = cost[c]
                r = st[row[y - 1]] + co[row[y - 1]] if y else 0.0
                heads = []
                crit = False
                for j in seq:
                    if ready[j] > r:
                        r = ready[j]
                    heads.append(r)
                    r += co[j]
                    if st[j] + tail[j] > end - 1.0:
                        crit = True
                q = tail[row[x + 1]] if x + 1 < len(row) else 0.0
                top = 0.0
                for k in range(len(seq) - 1, -1, -1):
                    j = seq[k]
                    if own[j] > q:
                        q = own[j]
                    q += co[j]
                    if heads[k] + q > top:
                        top = heads[k] + q
                val += math.log(max(top, end - 300.0) if crit else max(top, end))
            val /= nc
            a, b = row[y], row[x]
            pairs = [(b, z) for z in row[y:x]] if forth else [(z, a) for z in row[y + 1:x + 1]]
            if any(ban.get(p, -1) > it for p in pairs) and val >= best[0]:
                continue
            seed = (seed * 1103515245 + 12345) % (1 << 31)
            marks.append((val + (P["wild"] if kick else 1e-7) * (seed >> 20), a, b, forth, pairs))
        kick = max(kick - 1, 0)
        marks.sort(key=lambda m: m[0])
        spots = []
        for val, a, b, forth, pairs in marks:
            if spots and (val > now - P["gain"] or any(pos[a] < y + P["far"] and x < pos[b] + P["far"] for x, y in spots)):
                continue
            new = moved(order, pos, a, b, forth)
            if new is not None:
                order = new
                spots.append((pos[a], pos[b]))
                for u, v in pairs:
                    ban[v, u] = it + keep + (seed >> 12) % keep
        if not spots:
            ban = {}
    return best


def backward(ops, succ, done):
    n = len(ops)
    left = [len(succ[j]) for j in range(n)]
    fin = [0.0] * n
    free, ready, rt = {}, {}, {}

    def arm(j):
        o = ops[j]
        rt[j] = max([o.get("lat", 0.0)] + [fin[s] + ((HOP + o.get("lat", 0.0)) if j in ops[s]["hard"] else 0.0) for s in succ[j]])
        ready.setdefault(o["eng"], set()).add(j)
    for j in range(n):
        if left[j] == 0:
            arm(j)
    for _ in range(n):
        best = None
        for e, rs in ready.items():
            if rs:
                t0 = max(free.get(e, 0.0), min(rt[j] for j in rs))
                j = max((x for x in rs if rt[x] <= t0), key=lambda x: (done[x], x))
                st = max(free.get(e, 0.0), rt[j])
                if best is None or st < best[0]:
                    best = (st, j, e)
        st, j, e = best
        ready[e].discard(j)
        fin[j] = free[e] = st + ops[j]["cost"]
        for m in ops[j]["hard"] + ops[j]["soft"]:
            left[m] -= 1
            if left[m] == 0:
                arm(m)
    return fin


def forward(ops, succ, pri):
    n = len(ops)
    left = [len(o["hard"]) + len(o["soft"]) for o in ops]
    free = {e: 0.0 for e in "vatgs"}
    ready = {e: [] for e in "vatgs"}
    pick = {}
    done, endq, rt = [0.0] * n, [0.0] * n, [0.0] * n
    dmafree = 0.0
    look = P["look"]

    def arm(j):
        o = ops[j]
        r = 0.0
        for m in o["hard"]:
            if done[m] + HOP > r:
                r = done[m] + HOP
        for m in o["soft"]:
            if endq[m] > r:
                r = endq[m]
        rt[j] = r
        ready[o["eng"]].append(j)
        pick.pop(o["eng"], None)
    for j in range(n):
        if left[j] == 0:
            arm(j)
    order = []
    while len(order) < n:
        best = None
        for e, rs in ready.items():
            if not rs:
                continue
            if e not in pick:
                f = free[e]
                t0 = max(f, min([rt[j] for j in rs]))
                j = max([(pri[x], -x) for x in rs if rt[x] <= t0])
                j = -j[1]
                c = ops[j]["cost"]
                t1, p1 = t0 + min(look, 0.6 * c), pri[j] + c
                soon = [(pri[x], -x) for x in rs if t0 < rt[x] <= t1 and pri[x] > p1]
                if soon:
                    j = -max(soon)[1]
                pick[e] = (max(f, rt[j]), j, e)
            if best is None or pick[e][0] < best[0]:
                best = pick[e]
        st, j, e = best
        o = ops[j]
        ready[e].remove(j)
        del pick[e]
        endq[j] = free[e] = st + o["cost"]
        done[j] = endq[j] + o.get("lat", 0.0)
        if "bw" in o:
            dmafree = done[j] = max(dmafree + o["bw"], done[j])
        order.append(j)
        for s in succ[j]:
            left[s] -= 1
            if left[s] == 0:
                arm(s)
    return max(done), order, done


ORDER = {}


def plan(g, core, T, topo):
    ops = build_ops(g, core, T, topo)
    link(ops)
    if "order" not in ORDER:
        cases = [[(o["cost"], o.get("lat", 0.0) + c.get("wake", 0.0), o.get("bw", 0.0)) for o in build_ops(g, core, T, topo, c)] for c in CASES]
        ORDER["order"] = schedule(ops, cases)
    return ops, ORDER["order"]


def rank_program(g, core, T, topo):
    if T.rank_of(core) is None:
        return
    ops, best = plan(g, core, T, topo)
    order = best[1]
    Q = {"v": g.vector, "a": g.scalar, "t": g.tensor, "g": g, "s": g.sync}
    esem = {"v": T.sem.ev, "a": T.sem.ea, "t": T.sem.et, "g": T.sem.eg}
    pos = {j: x for x, j in enumerate(order)}
    final = {}
    for j in order:
        if "group" in ops[j]:
            final[ops[j]["group"]] = j
    for j in order:
        o = ops[j]
        if "group" in o and not (o["flags"]["start"] and o["flags"]["stop"]):
            for s in o["subs"]:
                s["stop"] = False
            o["subs"][-1]["stop"] = final[o["group"]] == j
    known = {e: {} for e in Q}
    after = {}
    waits = {}
    signals = set()
    for j in order:
        o = ops[j]
        kn = known[o["eng"]]
        need = {}
        for m in o["hard"]:
            key = ("own", m) if "sem" in ops[m] else ops[m]["eng"]
            if kn.get(key, -1) < pos[m] and (key not in need or pos[need[key]] < pos[m]):
                need[key] = m
        ws = []
        for key, m in sorted(need.items(), key=lambda kv: -pos[kv[1]]):
            if kn.get(key, -1) >= pos[m]:
                continue
            ws.append(m)
            signals.add(m)
            kn[key] = pos[m]
            if not ops[m].get("remote"):
                for k2, v2 in after[m].items():
                    if kn.get(k2, -1) < v2:
                        kn[k2] = v2
        waits[j] = ws
        after[j] = dict(kn)
    count = {e: 0 for e in esem}
    val = {}
    sent = 0
    for j in order:
        o = ops[j]
        q = Q[o["eng"]]
        for m in waits[j]:
            p = ops[m]
            if "sem" in p:
                q.wait_ge(p["sem"], p["inc"])
            else:
                q.wait_ge(esem[p["eng"]], val[m])
        ins = [f() for f in o["fn"]][-1] if o["eng"] == "t" else o["fn"]()
        if o.get("remote"):
            sent += o["inc"]
        elif "sem" in o:
            ins.then_inc(o["sem"], 16)
        elif j in signals:
            count[o["eng"]] += 1
            val[j] = count[o["eng"]]
            ins.then_inc(esem[o["eng"]], 1)
    g.wait_ge(T.sem.sent, sent)
    for e in esem:
        if count[e]:
            g.wait_ge(esem[e], count[e])
    for o in ops:
        if "sem" in o and (o["w"] + ["out"])[0][:3] == "out":
            g.wait_ge(o["sem"], 16)
